import numpy as np
import ml_dtypes


def mxq(x, axis, fmt="e4m3"):
    dtype, down = {"e4m3": (ml_dtypes.float8_e4m3fn, 7), "e5m2": (ml_dtypes.float8_e5m2, 14)}[fmt]
    v = np.moveaxis(np.asarray(x, np.float32).astype(ml_dtypes.bfloat16).astype(np.float64), axis, -1)
    blocks = v.reshape(v.shape[:-1] + (-1, 32))
    amax = np.abs(blocks).max(-1, keepdims=True)
    byte = np.maximum(np.where(amax > 0, np.frexp(amax)[1] - 1 + 127, 0) - down, 1)
    scale = np.exp2(byte - 127.0)
    codes = (blocks / scale).astype(np.float32).astype(dtype).astype(np.float64)
    return np.moveaxis((codes * scale).reshape(v.shape), -1, axis)


WIDE = False


def mx_kscale(k):
    if not WIDE:
        return np.ones(k)
    levels = np.array([10, -10, 5, -5, 0])
    if k % 512:
        return np.exp2(np.random.permutation(np.resize(levels, k // 32))).repeat(32)
    a = np.empty((k // 512, 16))
    for p in range(k // 512):
        a[p, :8] = np.random.permutation(np.resize(levels, 8))
        for g in range(8):
            far = levels[np.abs(levels - a[p, g]) >= 10]
            a[p, g + 8] = far[np.random.randint(len(far))]
    return np.exp2(a.ravel()).repeat(32)


BF16 = ml_dtypes.bfloat16


def bf(x):
    return np.asarray(x, np.float32).astype(BF16)


def f64(x):
    return np.asarray(x).astype(np.float64)


B, S, D = 4, 1024, 512
TWO = 2


def softmax_last(logit):
    top = np.max(logit, axis=-1, keepdims=True)
    e = np.exp(logit - top)
    return e / np.sum(e, axis=-1, keepdims=True)


def draw0():
    s, t = mx_kscale(D), mx_kscale(S)
    x = bf(np.random.standard_normal((B, S, D)) * s)
    w = bf(np.random.standard_normal((D, S)) * (2.0 / np.sqrt(D)) / s[:, None])
    rnd = bf(np.random.standard_normal((S, S)) * 1.5)
    mix = bf(np.random.uniform(0.5, 0.9, (TWO,)))
    wv = bf(np.random.standard_normal((D, D)) / np.sqrt(D) / s[:, None])
    c = bf(np.random.standard_normal(S) * (0.25 * np.sqrt(S)) * t)
    u = bf((1.0 + 0.1 * np.random.standard_normal(S)) / t)
    return {"x": x, "w": w, "rnd": rnd, "mix": mix, "wv": wv, "c": c, "u": u}


def core(x, w, rnd, mix, wv, c, u):
    mix = f64(mix)
    xq = mxq(f64(x), 2, "e4m3")
    syn = xq @ mxq(f64(w), 0, "e4m3")
    logit = mix[0] * syn + mix[1] * f64(rnd)[None, :, :]
    p = softmax_last(logit)
    pc = p * f64(c)[None, None, :]
    v = f64(u)[None, :, None] * (xq @ mxq(f64(wv), 0, "e4m3"))
    return mxq(pc, 2, "e4m3") @ mxq(v, 1, "e4m3")


def e4m3fn_bytes(y):
    return np.clip(np.asarray(y, np.float64), -448.0, 448.0).astype(np.float32).astype(ml_dtypes.float8_e4m3fn).view(np.uint8)


def e4m3fn_values(b):
    return np.asarray(b, np.uint8).view(ml_dtypes.float8_e4m3fn).astype(np.float64)


def setup_inputs():
    d = draw0()
    x0 = np.asarray(d['x']).astype(np.float64)
    s = (np.max(np.abs(x0), axis=(0, 1), keepdims=True) / 448.0).astype(np.float32)
    out = {}
    for k, v in d.items():
        if k == 'x':
            out['x_bytes'] = e4m3fn_bytes(x0 / s.astype(np.float64))
            out['x_scale'] = s
        else:
            out[k] = v
    return out


def reference(x_bytes, x_scale, w, rnd, mix, wv, c, u):
    return core(e4m3fn_values(x_bytes) * x_scale.astype(np.float64), w, rnd, mix, wv, c, u)

@@ -1,0 +1,461 @@
+from contextlib import ExitStack
+
+import concourse.mybir as mybir
+from concourse.masks import make_identity
+
+B, S, D = 4, 1024, 512
+P = 128
+PACK = 4
+HALF = P * PACK
+HALVES = S // HALF
+TILES = S // P
+N_TILES = B * TILES
+BANK = 512
+
+F32 = mybir.dt.float32
+BF16 = mybir.dt.bfloat16
+U32 = mybir.dt.uint32
+U8 = mybir.dt.uint8
+FP8 = mybir.dt.float8_e4m3fn
+FP8X4 = mybir.dt.float8_e4m3fn_x4
+Alu = mybir.AluOpType
+Act = mybir.ActivationFunctionType
+AX = mybir.AxisListType
+
+FLOPS = 2 * B * S * D * S + 2 * B * S * D * D + 2 * B * S * S * D
+
+VECTOR_TILES = (N_TILES - 3, N_TILES - 2, N_TILES - 1)
+
+SPARE_BANK_TILES = range(N_TILES - 4, N_TILES)
+
+
+def tile_mixturedenserandomsynthesizer_t_kernel(tc, x_bytes, x_scale, w, rnd, mix, wv, c, u, out):
+    nc = tc.nc
+    with ExitStack() as ctx:
+        keep = ctx.enter_context(tc.tile_pool(name="keep", bufs=1))
+        work = ctx.enter_context(tc.tile_pool(name="work", bufs=2))
+        ps_score = ctx.enter_context(tc.psum_pool(name="ps_score", bufs=3))
+        ps_turn = ctx.enter_context(tc.psum_pool(name="ps_turn", bufs=1))
+        ps_sum = ctx.enter_context(tc.psum_pool(name="ps_sum", bufs=1))
+        ps_prep = ctx.enter_context(tc.psum_pool(name="ps_prep", bufs=3))
+
+        x_scale_flat = x_scale.rearrange("a b k -> (a b k)")
+        scale_4 = keep.tile([P, PACK], F32, name="scale_4")
+        nc.scalar.dma_start(out=scale_4[:], in_=x_scale_flat.rearrange("(p t) -> p t", t=PACK))
+        mix_raw = keep.tile([P, 2], BF16, name="mix_raw")
+        nc.scalar.dma_start(out=mix_raw[:], in_=mix.partition_broadcast(P))
+        u_raw = keep.tile([P, HALVES, PACK], BF16, name="u_raw")
+        nc.scalar.dma_start(out=u_raw[:], in_=u.rearrange("(h p t) -> p h t", p=P, t=PACK))
+        c_row = keep.tile([P, S], BF16, name="c_row")
+        nc.gpsimd.memset(c_row[:], 0.0)
+        ones = keep.tile([P, P], BF16, name="ones")
+        nc.gpsimd.memset(ones[:], 1.0)
+        nc.scalar.dma_start(out=c_row[0:1, :], in_=c.rearrange("(o k) -> o k", o=1))
+
+        x_rows = x_bytes.rearrange("b (h m t) k -> b m h t k", m=P, t=PACK)
+        x_raw = []
+        for b in range(B):
+            x_raw.append(keep.tile([P, HALVES, PACK, D], U8, name="x_raw%d" % b, align_bytes=64))
+        rnd_rows = rnd.rearrange("(h m t) k -> m h t k", m=P, t=PACK)
+        rnd_raw = keep.tile([P, TILES, S], BF16, name="rnd_raw")
+        w_rows = w.rearrange("(p j) n -> p j n", j=PACK)
+        w_raw = keep.tile([P, PACK, S], BF16, name="w_raw")
+        wv_raw = keep.tile([P, PACK, D], BF16, name="wv_raw")
+        scale_row = keep.tile([P, 2 * D], F32, name="scale_row")
+
+        nc.sync.dma_start(out=w_raw[:, :, 0:BANK], in_=w_rows[:, :, 0:BANK])
+        nc.sync.dma_start(out=x_raw[0][:, 0], in_=x_rows[0, :, 0])
+        nc.sync.dma_start(out=w_raw[:, :, BANK:S], in_=w_rows[:, :, BANK:S])
+        nc.sync.dma_start(out=rnd_raw[:, 0:2], in_=rnd_rows[:, 0, 0:2])
+        nc.sync.dma_start(out=x_raw[0][:, 1], in_=x_rows[0, :, 1])
+        nc.sync.dma_start(out=scale_row[:, 0:D], in_=x_scale_flat.partition_broadcast(P))
+        nc.sync.dma_start(out=wv_raw[:], in_=wv.rearrange("(p j) n -> p j n", j=PACK))
+        nc.sync.dma_start(out=rnd_raw[:, 2:4], in_=rnd_rows[:, 0, 2:4])
+        nc.sync.dma_start(out=rnd_raw[:, 4:8], in_=rnd_rows[:, 1])
+        for b in range(1, B):
+            nc.sync.dma_start(out=x_raw[b][:], in_=x_rows[b])
+
+        ident = keep.tile([P, P], F32, name="ident")
+        make_identity(nc, ident[:])
+        warm = keep.tile([P, 1], F32, name="warm")
+        nc.vector.memset(warm[:], 0.0)
+        nc.scalar.activation(out=warm[:], in_=warm[:], func=Act.Exp)
+        mix_f = keep.tile([P, 2], F32, name="mix_f")
+        u_f = keep.tile([P, HALVES, PACK], F32, name="u_f")
+        c_f = keep.tile([P, S], F32, name="c_f")
+        rnd_f = keep.tile([P, TILES, S], F32, name="rnd_f")
+
+        w_grouped = []
+        for g in range(HALVES):
+            w_grouped.append(keep.tile([P, BANK, PACK], BF16, name="w_grouped%d" % g, align_bytes=64))
+        wv_grouped = keep.tile([P, D, PACK], BF16, name="wv_grouped", align_bytes=64)
+        w_codes = keep.tile([P, S], U32, name="w_codes", align_bytes=64)
+        w_scales = keep.tile([P, S], U8, name="w_scales", align_bytes=64)
+        wv_codes = keep.tile([P, D], U32, name="wv_codes", align_bytes=64)
+        wv_scales = keep.tile([P, D], U8, name="wv_scales", align_bytes=64)
+        x_codes, x_scales, v_codes, v_scales = [], [], [], []
+        for b in range(B):
+            x_codes.append(keep.tile([P, S], U32, name="x_codes%d" % b, align_bytes=64))
+            x_scales.append(keep.tile([P, S], U8, name="x_scales%d" % b, align_bytes=64))
+            v_codes.append(keep.tile([P, HALVES, D], U32, name="v_codes%d" % b, align_bytes=64))
+            v_scales.append(keep.tile([P, HALVES, D], U8, name="v_scales%d" % b, align_bytes=64))
+
+        out_rows = out.rearrange("b (h m t) d -> b m h t d", m=P, t=PACK)
+
+        def key_columns(ap):
+            return ap.rearrange("p (m h e) -> p h m e", h=2, e=2)
+
+        def columns_split(ap):
+            return ap.rearrange("p (h m e) -> p h m e", h=2, e=2)
+
+        def w_group(g):
+            src = w_raw[:, :, g * BANK : (g + 1) * BANK].rearrange("p j (m h e) -> p h m e j", h=2, e=2)
+            dst = w_grouped[g][:].rearrange("p (h m e) j -> p h m e j", h=2, e=2)
+            for h in range(2):
+                nc.vector.tensor_copy(out=dst[:, h], in_=src[:, h])
+
+        def w_quantize(g):
+            cols = slice(g * BANK, (g + 1) * BANK)
+            nc.vector.quantize_mx(
+                out=w_codes[:, cols].bitcast(FP8X4),
+                scales=w_scales[:, cols],
+                in_=w_grouped[g][:].rearrange("p n j -> p (n j)"),
+            )
+
+        def wv_group():
+            nc.scalar.copy(out=wv_grouped[:], in_=wv_raw[:].rearrange("p j n -> p n j"))
+
+        def wv_quantize():
+            nc.vector.quantize_mx(
+                out=wv_codes[:].bitcast(FP8X4),
+                scales=wv_scales[:],
+                in_=wv_grouped[:].rearrange("p n j -> p (n j)"),
+            )
+
+        def rnd_scale(r):
+            for g in range(HALVES):
+                cols = slice(g * BANK, (g + 1) * BANK)
+                nc.scalar.activation(
+                    out=columns_split(rnd_f[:, r, cols]),
+                    in_=key_columns(rnd_raw[:, r, cols]),
+                    func=Act.Copy,
+                    scale=mix_f[:, 1:2],
+                )
+
+        def c_spread():
+            for g in range(HALVES):
+                cols = slice(g * BANK, (g + 1) * BANK)
+                spread = ps_prep.tile([P, BANK], F32, name="prep")
+                nc.tensor.matmul(spread[:], lhsT=ones[:], rhs=c_row[:, cols], start=True, stop=True)
+                nc.scalar.copy(out=columns_split(c_f[:, cols]), in_=key_columns(spread[:]))
+
+        x_wide, x_turned, x_grouped = {}, {}, {}
+
+        def x_codes_of(b, k):
+            h, t = k // 2, 2 * (k % 2)
+            return x_raw[b][:, h, t : t + 2, :].rearrange("p t k -> p (t k)").bitcast(FP8)
+
+        def x_scaled(b, k):
+            wide = work.tile([P, 2 * D], BF16, name="wide")
+            nc.vector.tensor_tensor(out=wide[:], in0=x_codes_of(b, k), in1=scale_row[:], op=Alu.mult)
+            x_wide[(b, k)] = wide
+
+        def x_plain(b, k):
+            wide = work.tile([P, 2 * D], BF16, name="wide")
+            nc.scalar.copy(out=wide[:], in_=x_codes_of(b, k))
+            x_wide[(b, k)] = wide
+
+        def x_turn(b, k):
+            words = x_wide.get((b, k))[:].bitcast(F32)
+            turned = ps_prep.tile([P, 2, 2, P], F32, name="prep")
+            for j in range(2):
+                for e in range(2):
+                    nc.tensor.transpose(turned[:, j, e, :], words[:, 256 * j + e : 256 * (j + 1) : 2], ident[:])
+            x_turned[(b, k)] = turned
+
+        def x_copy_out(b, k):
+            grouped = work.tile([P, 2, P, PACK], BF16, name="x_grouped", align_bytes=64)
+            nc.scalar.copy(
+                out=grouped[:].bitcast(F32), in_=x_turned.get((b, k))[:].rearrange("p j e q -> p j q e")
+            )
+            x_grouped[(b, k)] = grouped
+
+        def x_scaled_late(b, k):
+            turned = x_turned.get((b, k))
+            grouped = work.tile([P, 2, P, PACK], BF16, name="x_grouped", align_bytes=64)
+            for j in range(2):
+                nc.vector.tensor_tensor(
+                    out=grouped[:, j].rearrange("p q (h e) -> p q h e", e=2),
+                    in0=turned[:, j]
+                    .rearrange("p h q -> p (h q)")
+                    .bitcast(BF16)
+                    .rearrange("p (h q e) -> p q h e", h=2, e=2),
+                    in1=scale_4[:].rearrange("p (o h e) -> p o h e", o=1, e=2).to_broadcast([P, P, 2, 2]),
+                    op=Alu.mult,
+                )
+            x_grouped[(b, k)] = grouped
+
+        def x_quantize(b, k):
+            cols = slice(2 * P * k, 2 * P * (k + 1))
+            nc.vector.quantize_mx(
+                out=x_codes[b][:, cols].bitcast(FP8X4),
+                scales=x_scales[b][:, cols],
+                in_=x_grouped.get((b, k))[:].rearrange("p j q t -> p (j q t)"),
+            )
+
+        v_sums, v_grouped = {}, {}
+
+        def v_product(b, h, n):
+            sums = ps_prep.tile([P, PACK, P], F32, name="prep")
+            d_cols = slice(n * P, (n + 1) * P)
+            for t in range(PACK):
+                rows = slice((h * PACK + t) * P, (h * PACK + t + 1) * P)
+                nc.tensor.matmul_mx(
+                    out=sums[:, t, :],
+                    lhsT=x_codes[b][:, rows].bitcast(FP8X4),
+                    lhsT_scale=x_scales[b][:, rows],
+                    rhs=wv_codes[:, d_cols].bitcast(FP8X4),
+                    rhs_scale=wv_scales[:, d_cols],
+                    start=True,
+                    stop=True,
+                )
+            v_sums[(b, h, n)] = sums
+
+        def v_gain(b, h, n):
+            if n == 0:
+                v_grouped[(b, h)] = work.tile([P, D, PACK], BF16, name="v_grouped", align_bytes=64)
+            nc.vector.tensor_tensor(
+                out=v_grouped.get((b, h))[:, n * P : (n + 1) * P, :],
+                in0=v_sums.get((b, h, n))[:].rearrange("p t d -> p d t"),
+                in1=u_f[:, h : h + 1, :].to_broadcast([P, P, PACK]),
+                op=Alu.mult,
+            )
+
+        def v_quantize(b, h):
+            nc.vector.quantize_mx(
+                out=v_codes[b][:, h, :].bitcast(FP8X4),
+                scales=v_scales[b][:, h, :],
+                in_=v_grouped.get((b, h))[:].rearrange("p d t -> p (d t)"),
+            )
+
+        scores, logits, maxima, exps, totals, inverses = {}, {}, {}, {}, {}, {}
+        gained, pcs, turned_pcs, grouped_pcs, pc_codes, sums_out = {}, {}, {}, {}, {}, {}
+
+        def score(i):
+            b, r = i // TILES, i % TILES
+            rows = slice(r * P, (r + 1) * P)
+            scores[i] = []
+            for g in range(HALVES):
+                bank = ps_score.tile([P, BANK], F32, name="score")
+                keys = slice(g * BANK, (g + 1) * BANK)
+                nc.tensor.matmul_mx(
+                    out=bank[:],
+                    lhsT=x_codes[b][:, rows].bitcast(FP8X4),
+                    lhsT_scale=x_scales[b][:, rows],
+                    rhs=w_codes[:, keys].bitcast(FP8X4),
+                    rhs_scale=w_scales[:, keys],
+                    start=True,
+                    stop=True,
+                )
+                scores[i].append(bank)
+
+        def blend(i):
+            logits[i] = work.tile([P, S], F32, name="logit", bufs=3)
+            for g in range(HALVES):
+                keys = slice(g * BANK, (g + 1) * BANK)
+                nc.vector.scalar_tensor_tensor(
+                    out=logits[i][:, keys],
+                    in0=scores[i][g][:],
+                    scalar=mix_f[:, 0:1],
+                    in1=rnd_f[:, i % TILES, keys],
+                    op0=Alu.mult,
+                    op1=Alu.add,
+                )
+
+        def maximum(i):
+            maxima[i] = work.tile([P, 1], F32, name="maximum", bufs=4)
+            nc.vector.tensor_reduce(out=maxima[i][:], in_=logits[i][:], axis=AX.X, op=Alu.max, negate=True)
+
+        def exponent(i):
+            exps[i] = work.tile([P, S], F32, name="exp", bufs=3)
+            totals[i] = work.tile([P, 1], F32, name="total", bufs=4)
+            nc.scalar.activation(
+                out=exps[i][:], in_=logits[i][:], func=Act.Exp, bias=maxima[i][:], accum_out=totals[i][:]
+            )
+
+        def invert(i):
+            inverses[i] = work.tile([P, 1], F32, name="inverse", bufs=4)
+            nc.vector.reciprocal(out=inverses[i][:], in_=totals[i][:])
+
+        def gain(i):
+            if i not in VECTOR_TILES:
+                gained[i] = work.tile([P, S], F32, name="gained", bufs=3)
+                nc.gpsimd.tensor_tensor(out=gained[i][:], in0=exps[i][:], in1=c_f[:], op=Alu.mult)
+
+        def normalise(i):
+            pcs[i] = work.tile([P, S], BF16, name="pc")
+            if i in VECTOR_TILES:
+                nc.vector.scalar_tensor_tensor(
+                    out=pcs[i][:],
+                    in0=exps[i][:],
+                    scalar=inverses[i][:],
+                    in1=c_f[:],
+                    op0=Alu.mult,
+                    op1=Alu.mult,
+                )
+            else:
+                nc.scalar.activation(
+                    out=pcs[i][:], in_=gained[i][:], func=Act.Copy, scale=inverses[i][:]
+                )
+
+        def turn(i):
+            words = pcs[i][:].bitcast(F32)
+            turned_pcs[i] = ps_turn.tile([P, HALVES, 2, P], F32, name="turned")
+            for g in range(HALVES):
+                for h in range(2):
+                    first = g * 2 * P + h * P
+                    nc.tensor.transpose(turned_pcs[i][:, g, h, :], words[:, first : first + P], ident[:])
+
+        def turn_out(i):
+            grouped_pcs[i] = work.tile([P, HALVES, P, PACK], BF16, name="p_grouped", bufs=3, align_bytes=64)
+            nc.scalar.copy(
+                out=grouped_pcs[i][:].bitcast(F32),
+                in_=turned_pcs[i][:].rearrange("p g h q -> p g q h"),
+            )
+
+        def p_quantize(i):
+            p_codes = work.tile([P, HALVES, P], U32, name="p_codes", bufs=4, align_bytes=64)
+            p_scales = work.tile([P, HALVES, P], U8, name="p_scales", bufs=4, align_bytes=64)
+            nc.vector.quantize_mx(
+                out=p_codes[:].rearrange("p g q -> p (g q)").bitcast(FP8X4),
+                scales=p_scales[:].rearrange("p g q -> p (g q)"),
+                in_=grouped_pcs[i][:].rearrange("p g q t -> p (g q t)"),
+            )
+            pc_codes[i] = (p_codes, p_scales)
+
+        def product(i):
+            b = i // TILES
+            p_codes, p_scales = pc_codes[i]
+            if i in SPARE_BANK_TILES:
+                sums_out[i] = ps_prep.tile([P, D], F32, name="prep")
+            else:
+                sums_out[i] = ps_sum.tile([P, D], F32, name="sum")
+            for g in range(HALVES):
+                nc.tensor.matmul_mx(
+                    out=sums_out[i][:],
+                    lhsT=p_codes[:, g, :].bitcast(FP8X4),
+                    lhsT_scale=p_scales[:, g, :],
+                    rhs=v_codes[b][:, g, :].bitcast(FP8X4),
+                    rhs_scale=v_scales[b][:, g, :],
+                    start=(g == 0),
+                    stop=(g == HALVES - 1),
+                )
+
+        def store(i):
+            b, r = i // TILES, i % TILES
+            rows_out = work.tile([P, D], F32, name="rows_out", bufs=4)
+            nc.scalar.copy(out=rows_out[:], in_=sums_out[i][:])
+            nc.sync.dma_start(out=out_rows[b, :, r // PACK, r % PACK], in_=rows_out[:])
+
+        before, head, opening, middle, closing, rnd_plan = {}, {}, {}, {}, {}, {}
+
+        def put(plan, step, stage, *args):
+            plan.setdefault(step, []).append((stage, args))
+
+        def run(plan, step):
+            for stage, args in plan.get(step, []):
+                stage(*args)
+
+        for b in range(B):
+            if b > 0:
+                for k in range(4):
+                    put(before, 8 * b - 3 + k, x_copy_out, b, k)
+                    put(head, 8 * b - 2 + k, x_quantize, b, k)
+                    put(head, 8 * b - 4 + k, x_scaled, b, k)
+                    put(closing, 8 * b - 4 + k, x_turn, b, k)
+            put(head, 8 * b + 3, v_quantize, b, 0)
+            put(head, 8 * b + 4, v_quantize, b, 1)
+            for h in range(HALVES):
+                for n in range(4):
+                    if b > 0:
+                        step = 8 * b + 2 * h + n // 2
+                        put(closing, step - 1, v_product, b, h, n)
+                    else:
+                        step = 2 + h
+                        put(opening if n < 2 else middle, step, v_product, b, h, n)
+                    put(middle, step, v_gain, b, h, n)
+        for r in range(3, TILES):
+            put(rnd_plan, max(2, r - 3), rnd_scale, r)
+
+        with tc.manual_schedule():
+            w_group(0)
+            x_plain(0, 0)
+            x_turn(0, 0)
+            w_quantize(0)
+            nc.vector.tensor_copy(out=mix_f[:], in_=mix_raw[:])
+            nc.vector.tensor_copy(out=u_f[:], in_=u_raw[:])
+            w_group(1)
+            x_plain(0, 1)
+            x_turn(0, 1)
+            x_scaled_late(0, 0)
+            rnd_scale(0)
+            w_quantize(1)
+            x_scaled_late(0, 1)
+            x_quantize(0, 0)
+            score(0)
+            x_quantize(0, 1)
+            rnd_scale(1)
+            c_spread()
+            wv_group()
+            nc.vector.tensor_copy(out=scale_row[:, D : 2 * D], in_=scale_row[:, 0:D])
+            blend(0)
+            score(1)
+            x_scaled(0, 2)
+            x_turn(0, 2)
+            maximum(0)
+            x_scaled(0, 3)
+            x_turn(0, 3)
+            x_copy_out(0, 2)
+            blend(1)
+            score(2)
+            rnd_scale(2)
+            x_copy_out(0, 3)
+            exponent(0)
+            gain(0)
+            maximum(1)
+            x_quantize(0, 2)
+            x_quantize(0, 3)
+
+            for s in range(2, N_TILES + 4):
+                if s <= N_TILES:
+                    exponent(s - 1)
+                    gain(s - 1)
+                run(before, s)
+                if 0 <= s - 3 < N_TILES:
+                    turn_out(s - 3)
+                if 0 <= s - 4 < N_TILES:
+                    p_quantize(s - 4)
+                run(head, s)
+                if s == 2:
+                    wv_quantize()
+                    invert(0)
+                if 0 <= s - 2 < N_TILES:
+                    normalise(s - 2)
+                run(rnd_plan, s)
+                if 0 <= s - 4 < N_TILES:
+                    product(s - 4)
+                run(opening, s)
+                if s < N_TILES:
+                    blend(s)
+                if s + 1 < N_TILES:
+                    score(s + 1)
+                run(middle, s)
+                if s <= N_TILES:
+                    invert(s - 1)
+                if s < N_TILES:
+                    maximum(s)
+                if 0 <= s - 2 < N_TILES:
+                    turn(s - 2)
+                if 0 <= s - 4 < N_TILES:
+                    store(s - 4)
+                run(closing, s)

@@ -8,9 +8,10 @@ P = 128
 PACK = 4
 HALF = P * PACK
 HALVES = S // HALF
-TILES = S // P
-N_TILES = B * TILES
+PAIRS = S // (2 * P)
+N_PAIRS = B * PAIRS
 BANK = 512
+QUARTERS = D // P
 
 F32 = mybir.dt.float32
 BF16 = mybir.dt.bfloat16
@@ -24,9 +25,10 @@ AX = mybir.AxisListType
 
 FLOPS = 2 * B * S * D * S + 2 * B * S * D * D + 2 * B * S * S * D
 
-VECTOR_TILES = (N_TILES - 3, N_TILES - 2, N_TILES - 1)
-
-SPARE_BANK_TILES = range(N_TILES - 4, N_TILES)
+VECTOR_PAIRS = (N_PAIRS - 1,)
+BOTH, FIRST, SECOND = slice(0, 2), slice(0, 1), slice(1, 2)
+SCORE_BANKS = 4
+SHARED_BANKS = 4
 
 
 def tile_mixturedenserandomsynthesizer_t_kernel(tc, x_bytes, x_scale, w, rnd, mix, wv, c, u, out):
@@ -34,46 +36,58 @@ def tile_mixturedenserandomsynthesizer_t_kernel(tc, x_bytes, x_scale, w, rnd, mi
     with ExitStack() as ctx:
         keep = ctx.enter_context(tc.tile_pool(name="keep", bufs=1))
         work = ctx.enter_context(tc.tile_pool(name="work", bufs=2))
-        ps_score = ctx.enter_context(tc.psum_pool(name="ps_score", bufs=3))
-        ps_turn = ctx.enter_context(tc.psum_pool(name="ps_turn", bufs=1))
-        ps_sum = ctx.enter_context(tc.psum_pool(name="ps_sum", bufs=1))
-        ps_prep = ctx.enter_context(tc.psum_pool(name="ps_prep", bufs=3))
+        psum = ctx.enter_context(tc.psum_pool(name="psum", bufs=1))
+        score_count, shared_count = [], []
 
-        x_scale_flat = x_scale.rearrange("a b k -> (a b k)")
+        def score_bank():
+            score_count.append(0)
+            return psum.tile([P, BANK], F32, name="score%d" % (len(score_count) % SCORE_BANKS))
+
+        def shared_bank():
+            shared_count.append(0)
+            return psum.tile([P, PACK, P], F32, name="shared%d" % (len(shared_count) % SHARED_BANKS))
+
         scale_4 = keep.tile([P, PACK], F32, name="scale_4")
-        nc.scalar.dma_start(out=scale_4[:], in_=x_scale_flat.rearrange("(p t) -> p t", t=PACK))
+        nc.scalar.dma_start(out=scale_4[:], in_=x_scale.rearrange("a b (p t) -> p (a b t)", t=PACK))
         mix_raw = keep.tile([P, 2], BF16, name="mix_raw")
         nc.scalar.dma_start(out=mix_raw[:], in_=mix.partition_broadcast(P))
+        c_raw = keep.tile([P, HALVES, PACK], BF16, name="c_raw")
+        nc.scalar.dma_start(out=c_raw[:], in_=c.rearrange("(g p t) -> p g t", p=P, t=PACK))
         u_raw = keep.tile([P, HALVES, PACK], BF16, name="u_raw")
         nc.scalar.dma_start(out=u_raw[:], in_=u.rearrange("(h p t) -> p h t", p=P, t=PACK))
-        c_row = keep.tile([P, S], BF16, name="c_row")
-        nc.gpsimd.memset(c_row[:], 0.0)
-        ones = keep.tile([P, P], BF16, name="ones")
-        nc.gpsimd.memset(ones[:], 1.0)
-        nc.scalar.dma_start(out=c_row[0:1, :], in_=c.rearrange("(o k) -> o k", o=1))
 
-        x_rows = x_bytes.rearrange("b (h m t) k -> b m h t k", m=P, t=PACK)
-        x_raw = []
-        for b in range(B):
-            x_raw.append(keep.tile([P, HALVES, PACK, D], U8, name="x_raw%d" % b, align_bytes=64))
-        rnd_rows = rnd.rearrange("(h m t) k -> m h t k", m=P, t=PACK)
-        rnd_raw = keep.tile([P, TILES, S], BF16, name="rnd_raw")
+        x_rows = x_bytes.rearrange("b (h m t) k -> b h m t k", m=P, t=PACK)
+        rnd_rows = rnd.rearrange("(h m t) k -> h m t k", m=P, t=PACK)
         w_rows = w.rearrange("(p j) n -> p j n", j=PACK)
-        w_raw = keep.tile([P, PACK, S], BF16, name="w_raw")
+        x_raw, rnd_raw, w_raw = {}, {}, {}
         wv_raw = keep.tile([P, PACK, D], BF16, name="wv_raw")
-        scale_row = keep.tile([P, 2 * D], F32, name="scale_row")
 
-        nc.sync.dma_start(out=w_raw[:, :, 0:BANK], in_=w_rows[:, :, 0:BANK])
-        nc.sync.dma_start(out=x_raw[0][:, 0], in_=x_rows[0, :, 0])
-        nc.sync.dma_start(out=w_raw[:, :, BANK:S], in_=w_rows[:, :, BANK:S])
-        nc.sync.dma_start(out=rnd_raw[:, 0:2], in_=rnd_rows[:, 0, 0:2])
-        nc.sync.dma_start(out=x_raw[0][:, 1], in_=x_rows[0, :, 1])
-        nc.sync.dma_start(out=scale_row[:, 0:D], in_=x_scale_flat.partition_broadcast(P))
+        def load_x(b, h):
+            x_raw[(b, h)] = keep.tile([P, PACK, D], U8, name="x_raw%d%d" % (b, h), align_bytes=64)
+            nc.sync.dma_start(out=x_raw.get((b, h))[:], in_=x_rows[b, h])
+
+        def load_w(g):
+            w_raw[g] = keep.tile([P, PACK, BANK], BF16, name="w_raw%d" % g)
+            nc.sync.dma_start(out=w_raw[g][:], in_=w_rows[:, :, g * BANK : (g + 1) * BANK])
+
+        def load_rnd(k):
+            rnd_raw[k] = keep.tile([P, 2, S], BF16, name="rnd_raw%d" % k)
+            nc.sync.dma_start(out=rnd_raw[k][:], in_=rnd_rows[k // 2, :, 2 * (k % 2) : 2 * (k % 2) + 2])
+
+        load_w(0)
+        load_x(0, 0)
+        load_w(1)
+        load_rnd(0)
+        load_x(0, 1)
         nc.sync.dma_start(out=wv_raw[:], in_=wv.rearrange("(p j) n -> p j n", j=PACK))
-        nc.sync.dma_start(out=rnd_raw[:, 2:4], in_=rnd_rows[:, 0, 2:4])
-        nc.sync.dma_start(out=rnd_raw[:, 4:8], in_=rnd_rows[:, 1])
-        for b in range(1, B):
-            nc.sync.dma_start(out=x_raw[b][:], in_=x_rows[b])
+        load_rnd(1)
+        load_x(1, 0)
+        load_rnd(2)
+        load_rnd(3)
+        load_x(1, 1)
+        for b in range(2, B):
+            for h in range(HALVES):
+                load_x(b, h)
 
         ident = keep.tile([P, P], F32, name="ident")
         make_identity(nc, ident[:])
@@ -82,380 +96,441 @@ def tile_mixturedenserandomsynthesizer_t_kernel(tc, x_bytes, x_scale, w, rnd, mi
         nc.scalar.activation(out=warm[:], in_=warm[:], func=Act.Exp)
         mix_f = keep.tile([P, 2], F32, name="mix_f")
         u_f = keep.tile([P, HALVES, PACK], F32, name="u_f")
-        c_f = keep.tile([P, S], F32, name="c_f")
-        rnd_f = keep.tile([P, TILES, S], F32, name="rnd_f")
-
-        w_grouped = []
+        c_4 = keep.tile([P, HALVES * PACK], F32, name="c_4")
+        c_f = keep.tile([P, 1, S], F32, name="c_f")
+        scale_row = keep.tile([P, 2, P, PACK], F32, name="scale_row")
+        rnd_f = []
+        for r in range(2 * PAIRS):
+            rnd_f.append(keep.tile([P, S], F32, name="rnd_f%d" % r))
+        w_grouped, w_codes, w_scales = [], [], []
         for g in range(HALVES):
             w_grouped.append(keep.tile([P, BANK, PACK], BF16, name="w_grouped%d" % g, align_bytes=64))
-        wv_grouped = keep.tile([P, D, PACK], BF16, name="wv_grouped", align_bytes=64)
-        w_codes = keep.tile([P, S], U32, name="w_codes", align_bytes=64)
-        w_scales = keep.tile([P, S], U8, name="w_scales", align_bytes=64)
+            w_codes.append(keep.tile([P, BANK], U32, name="w_codes%d" % g, align_bytes=64))
+            w_scales.append(keep.tile([P, BANK], U8, name="w_scales%d" % g, align_bytes=64))
+        grouped = {}
         wv_codes = keep.tile([P, D], U32, name="wv_codes", align_bytes=64)
         wv_scales = keep.tile([P, D], U8, name="wv_scales", align_bytes=64)
-        x_codes, x_scales, v_codes, v_scales = [], [], [], []
-        for b in range(B):
-            x_codes.append(keep.tile([P, S], U32, name="x_codes%d" % b, align_bytes=64))
-            x_scales.append(keep.tile([P, S], U8, name="x_scales%d" % b, align_bytes=64))
-            v_codes.append(keep.tile([P, HALVES, D], U32, name="v_codes%d" % b, align_bytes=64))
-            v_scales.append(keep.tile([P, HALVES, D], U8, name="v_scales%d" % b, align_bytes=64))
 
-        out_rows = out.rearrange("b (h m t) d -> b m h t d", m=P, t=PACK)
+        out_rows = out.rearrange("b (h m t) d -> b h m t d", m=P, t=PACK)
 
-        def key_columns(ap):
+        def quantize(codes, scales, grouped):
+            nc.vector.quantize_mx(out=codes.bitcast(FP8X4), scales=scales, in_=grouped)
+
+        def multiply(sums, lhs_codes, lhs_scales, rhs_codes, rhs_scales, start, stop):
+            nc.tensor.matmul_mx(
+                out=sums,
+                lhsT=lhs_codes.bitcast(FP8X4),
+                lhsT_scale=lhs_scales,
+                rhs=rhs_codes.bitcast(FP8X4),
+                rhs_scale=rhs_scales,
+                start=start,
+                stop=stop,
+            )
+
+        def key_split(ap):
             return ap.rearrange("p (m h e) -> p h m e", h=2, e=2)
 
-        def columns_split(ap):
+        def column_split(ap):
             return ap.rearrange("p (h m e) -> p h m e", h=2, e=2)
 
-        def w_group(g):
-            src = w_raw[:, :, g * BANK : (g + 1) * BANK].rearrange("p j (m h e) -> p h m e j", h=2, e=2)
+        def spread(columns):
+            bank = shared_bank()
+            for t in range(PACK):
+                nc.tensor.transpose(bank[:, t, :], columns[:, t : t + 1].to_broadcast([P, P]), ident[:])
+            return bank
+
+        def scale_spread():
+            bank = spread(scale_4[:])
+            nc.scalar.copy(
+                out=scale_row[:], in_=bank[:].rearrange("p (o t) m -> p o m t", o=1).to_broadcast([P, 2, P, PACK])
+            )
+
+        def c_spread(g):
+            bank = spread(c_4[:, g * PACK : (g + 1) * PACK])
+            nc.scalar.copy(
+                out=column_split(c_f[:, 0, g * BANK : (g + 1) * BANK]),
+                in_=bank[:].rearrange("p (h e) m -> p h m e", h=2),
+            )
+
+        def w_group(g, copy):
+            src = w_raw[g][:].rearrange("p j (m h e) -> p h m e j", h=2, e=2)
             dst = w_grouped[g][:].rearrange("p (h m e) j -> p h m e j", h=2, e=2)
             for h in range(2):
-                nc.vector.tensor_copy(out=dst[:, h], in_=src[:, h])
+                copy(out=dst[:, h], in_=src[:, h])
 
         def w_quantize(g):
-            cols = slice(g * BANK, (g + 1) * BANK)
-            nc.vector.quantize_mx(
-                out=w_codes[:, cols].bitcast(FP8X4),
-                scales=w_scales[:, cols],
-                in_=w_grouped[g][:].rearrange("p n j -> p (n j)"),
-            )
+            quantize(w_codes[g][:], w_scales[g][:], w_grouped[g][:].rearrange("p n j -> p (n j)"))
 
         def wv_group():
-            nc.scalar.copy(out=wv_grouped[:], in_=wv_raw[:].rearrange("p j n -> p n j"))
+            grouped["wv"] = keep.tile([P, BANK, PACK], BF16, name="w_grouped1", align_bytes=64)
+            nc.gpsimd.tensor_scalar(
+                out=grouped.get("wv")[:],
+                in0=wv_raw[:].rearrange("p j n -> p n j"),
+                scalar1=1.0,
+                scalar2=0.0,
+                op0=Alu.mult,
+                op1=Alu.add,
+            )
 
         def wv_quantize():
-            nc.vector.quantize_mx(
-                out=wv_codes[:].bitcast(FP8X4),
-                scales=wv_scales[:],
-                in_=wv_grouped[:].rearrange("p n j -> p (n j)"),
-            )
+            quantize(wv_codes[:], wv_scales[:], grouped.get("wv")[:].rearrange("p n j -> p (n j)"))
 
         def rnd_scale(r):
             for g in range(HALVES):
                 cols = slice(g * BANK, (g + 1) * BANK)
                 nc.scalar.activation(
-                    out=columns_split(rnd_f[:, r, cols]),
-                    in_=key_columns(rnd_raw[:, r, cols]),
+                    out=column_split(rnd_f[r][:, cols]),
+                    in_=key_split(rnd_raw[r // 2][:, r % 2, cols]),
                     func=Act.Copy,
                     scale=mix_f[:, 1:2],
                 )
 
-        def c_spread():
-            for g in range(HALVES):
-                cols = slice(g * BANK, (g + 1) * BANK)
-                spread = ps_prep.tile([P, BANK], F32, name="prep")
-                nc.tensor.matmul(spread[:], lhsT=ones[:], rhs=c_row[:, cols], start=True, stop=True)
-                nc.scalar.copy(out=columns_split(c_f[:, cols]), in_=key_columns(spread[:]))
+        x_wide, x_turned, x_grouped, x_codes, x_scales = {}, {}, {}, {}, {}
 
-        x_wide, x_turned, x_grouped = {}, {}, {}
+        def x_scaled(q):
+            b, h, t = q // PAIRS, (q % PAIRS) // 2, 2 * (q % 2)
+            x_wide[q] = work.tile([P, 2 * D], BF16, name="wide")
+            nc.vector.tensor_tensor(
+                out=x_wide[q][:],
+                in0=x_raw.get((b, h))[:, t : t + 2, :].rearrange("p t k -> p (t k)").bitcast(FP8),
+                in1=scale_row[:].rearrange("p o m t -> p (o m t)"),
+                op=Alu.mult,
+            )
 
-        def x_codes_of(b, k):
-            h, t = k // 2, 2 * (k % 2)
-            return x_raw[b][:, h, t : t + 2, :].rearrange("p t k -> p (t k)").bitcast(FP8)
-
-        def x_scaled(b, k):
-            wide = work.tile([P, 2 * D], BF16, name="wide")
-            nc.vector.tensor_tensor(out=wide[:], in0=x_codes_of(b, k), in1=scale_row[:], op=Alu.mult)
-            x_wide[(b, k)] = wide
-
-        def x_plain(b, k):
-            wide = work.tile([P, 2 * D], BF16, name="wide")
-            nc.scalar.copy(out=wide[:], in_=x_codes_of(b, k))
-            x_wide[(b, k)] = wide
-
-        def x_turn(b, k):
-            words = x_wide.get((b, k))[:].bitcast(F32)
-            turned = ps_prep.tile([P, 2, 2, P], F32, name="prep")
+        def x_turn(q):
+            words = x_wide[q][:].bitcast(F32)
+            x_turned[q] = shared_bank()
             for j in range(2):
                 for e in range(2):
-                    nc.tensor.transpose(turned[:, j, e, :], words[:, 256 * j + e : 256 * (j + 1) : 2], ident[:])
-            x_turned[(b, k)] = turned
+                    nc.tensor.transpose(
+                        x_turned[q][:, 2 * j + e, :], words[:, 256 * j + e : 256 * (j + 1) : 2], ident[:]
+                    )
 
-        def x_copy_out(b, k):
-            grouped = work.tile([P, 2, P, PACK], BF16, name="x_grouped", align_bytes=64)
+        def x_copy_out(q):
+            x_grouped[q] = work.tile([P, 2, P, PACK], BF16, name="x_grouped", align_bytes=64)
             nc.scalar.copy(
-                out=grouped[:].bitcast(F32), in_=x_turned.get((b, k))[:].rearrange("p j e q -> p j q e")
-            )
-            x_grouped[(b, k)] = grouped
-
-        def x_scaled_late(b, k):
-            turned = x_turned.get((b, k))
-            grouped = work.tile([P, 2, P, PACK], BF16, name="x_grouped", align_bytes=64)
-            for j in range(2):
-                nc.vector.tensor_tensor(
-                    out=grouped[:, j].rearrange("p q (h e) -> p q h e", e=2),
-                    in0=turned[:, j]
-                    .rearrange("p h q -> p (h q)")
-                    .bitcast(BF16)
-                    .rearrange("p (h q e) -> p q h e", h=2, e=2),
-                    in1=scale_4[:].rearrange("p (o h e) -> p o h e", o=1, e=2).to_broadcast([P, P, 2, 2]),
-                    op=Alu.mult,
-                )
-            x_grouped[(b, k)] = grouped
-
-        def x_quantize(b, k):
-            cols = slice(2 * P * k, 2 * P * (k + 1))
-            nc.vector.quantize_mx(
-                out=x_codes[b][:, cols].bitcast(FP8X4),
-                scales=x_scales[b][:, cols],
-                in_=x_grouped.get((b, k))[:].rearrange("p j q t -> p (j q t)"),
+                out=x_grouped[q][:].bitcast(F32), in_=x_turned[q][:].rearrange("p (j e) q -> p j q e", e=2)
             )
 
-        v_sums, v_grouped = {}, {}
+        def x_quantize(q):
+            x_codes[q] = work.tile([P, 2 * P], U32, name="x_codes", bufs=7, align_bytes=64)
+            x_scales[q] = work.tile([P, 2 * P], U8, name="x_scales", bufs=7, align_bytes=64)
+            quantize(x_codes[q][:], x_scales[q][:], x_grouped[q][:].rearrange("p j q t -> p (j q t)"))
 
-        def v_product(b, h, n):
-            sums = ps_prep.tile([P, PACK, P], F32, name="prep")
+        v_sums, v_grouped, v_codes, v_scales = {}, {}, {}, {}
+
+        def v_product(hh, n):
+            sums = shared_bank()
             d_cols = slice(n * P, (n + 1) * P)
             for t in range(PACK):
-                rows = slice((h * PACK + t) * P, (h * PACK + t + 1) * P)
-                nc.tensor.matmul_mx(
-                    out=sums[:, t, :],
-                    lhsT=x_codes[b][:, rows].bitcast(FP8X4),
-                    lhsT_scale=x_scales[b][:, rows],
-                    rhs=wv_codes[:, d_cols].bitcast(FP8X4),
-                    rhs_scale=wv_scales[:, d_cols],
-                    start=True,
-                    stop=True,
+                q, rows = 2 * hh + t // 2, slice((t % 2) * P, (t % 2 + 1) * P)
+                multiply(
+                    sums[:, t, :], x_codes[q][:, rows], x_scales[q][:, rows],
+                    wv_codes[:, d_cols], wv_scales[:, d_cols], True, True,
                 )
-            v_sums[(b, h, n)] = sums
+            v_sums[(hh, n)] = sums
 
-        def v_gain(b, h, n):
+        def v_gain(hh, n):
             if n == 0:
-                v_grouped[(b, h)] = work.tile([P, D, PACK], BF16, name="v_grouped", align_bytes=64)
+                v_grouped[hh] = work.tile([P, D, PACK], BF16, name="v_grouped", align_bytes=64)
+            h = hh % HALVES
             nc.vector.tensor_tensor(
-                out=v_grouped.get((b, h))[:, n * P : (n + 1) * P, :],
-                in0=v_sums.get((b, h, n))[:].rearrange("p t d -> p d t"),
+                out=v_grouped[hh][:, n * P : (n + 1) * P, :],
+                in0=v_sums.get((hh, n))[:].rearrange("p t d -> p d t"),
                 in1=u_f[:, h : h + 1, :].to_broadcast([P, P, PACK]),
                 op=Alu.mult,
             )
 
-        def v_quantize(b, h):
-            nc.vector.quantize_mx(
-                out=v_codes[b][:, h, :].bitcast(FP8X4),
-                scales=v_scales[b][:, h, :],
-                in_=v_grouped.get((b, h))[:].rearrange("p d t -> p (d t)"),
-            )
+        def v_quantize(hh):
+            v_codes[hh] = work.tile([P, D], U32, name="v_codes", bufs=4, align_bytes=64)
+            v_scales[hh] = work.tile([P, D], U8, name="v_scales", bufs=4, align_bytes=64)
+            quantize(v_codes[hh][:], v_scales[hh][:], v_grouped[hh][:].rearrange("p d t -> p (d t)"))
 
         scores, logits, maxima, exps, totals, inverses = {}, {}, {}, {}, {}, {}
-        gained, pcs, turned_pcs, grouped_pcs, pc_codes, sums_out = {}, {}, {}, {}, {}, {}
+        gained, pcs, turned_pcs, grouped_pcs, p_codes, p_scales, sums_out, rows_out = {}, {}, {}, {}, {}, {}, {}, {}
 
-        def score(i):
-            b, r = i // TILES, i % TILES
-            rows = slice(r * P, (r + 1) * P)
-            scores[i] = []
-            for g in range(HALVES):
-                bank = ps_score.tile([P, BANK], F32, name="score")
-                keys = slice(g * BANK, (g + 1) * BANK)
-                nc.tensor.matmul_mx(
-                    out=bank[:],
-                    lhsT=x_codes[b][:, rows].bitcast(FP8X4),
-                    lhsT_scale=x_scales[b][:, rows],
-                    rhs=w_codes[:, keys].bitcast(FP8X4),
-                    rhs_scale=w_scales[:, keys],
-                    start=True,
-                    stop=True,
-                )
-                scores[i].append(bank)
+        def score(q, j, g):
+            rows = slice(j * P, (j + 1) * P)
+            bank = score_bank()
+            multiply(bank[:], x_codes[q][:, rows], x_scales[q][:, rows], w_codes[g][:], w_scales[g][:], True, True)
+            scores[(q, j, g)] = bank
 
-        def blend(i):
-            logits[i] = work.tile([P, S], F32, name="logit", bufs=3)
-            for g in range(HALVES):
-                keys = slice(g * BANK, (g + 1) * BANK)
-                nc.vector.scalar_tensor_tensor(
-                    out=logits[i][:, keys],
-                    in0=scores[i][g][:],
-                    scalar=mix_f[:, 0:1],
-                    in1=rnd_f[:, i % TILES, keys],
-                    op0=Alu.mult,
-                    op1=Alu.add,
-                )
-
-        def maximum(i):
-            maxima[i] = work.tile([P, 1], F32, name="maximum", bufs=4)
-            nc.vector.tensor_reduce(out=maxima[i][:], in_=logits[i][:], axis=AX.X, op=Alu.max, negate=True)
-
-        def exponent(i):
-            exps[i] = work.tile([P, S], F32, name="exp", bufs=3)
-            totals[i] = work.tile([P, 1], F32, name="total", bufs=4)
-            nc.scalar.activation(
-                out=exps[i][:], in_=logits[i][:], func=Act.Exp, bias=maxima[i][:], accum_out=totals[i][:]
+        def blend(q, j, g):
+            if (j, g) == (0, 0):
+                logits[q] = work.tile([P, 2, S], F32, name="logit")
+            keys = slice(g * BANK, (g + 1) * BANK)
+            nc.vector.scalar_tensor_tensor(
+                out=logits[q][:, j, keys],
+                in0=scores.get((q, j, g))[:],
+                scalar=mix_f[:, 0:1],
+                in1=rnd_f[2 * (q % PAIRS) + j][:, keys],
+                op0=Alu.mult,
+                op1=Alu.add,
             )
 
-        def invert(i):
-            inverses[i] = work.tile([P, 1], F32, name="inverse", bufs=4)
-            nc.vector.reciprocal(out=inverses[i][:], in_=totals[i][:])
+        def maximum(q, tiles=BOTH):
+            if tiles.start == 0:
+                maxima[q] = work.tile([P, 2], F32, name="maximum")
+            nc.vector.tensor_reduce(
+                out=maxima[q][:, tiles], in_=logits[q][:, tiles], axis=AX.X, op=Alu.max, negate=True
+            )
 
-        def gain(i):
-            if i not in VECTOR_TILES:
-                gained[i] = work.tile([P, S], F32, name="gained", bufs=3)
-                nc.gpsimd.tensor_tensor(out=gained[i][:], in0=exps[i][:], in1=c_f[:], op=Alu.mult)
+        def exponent(q, j):
+            if j == 0:
+                exps[q] = work.tile([P, 2, S], F32, name="exp")
+                totals[q] = work.tile([P, 2], F32, name="total")
+            nc.scalar.activation(
+                out=exps[q][:, j],
+                in_=logits[q][:, j],
+                func=Act.Exp,
+                bias=maxima[q][:, j : j + 1],
+                accum_out=totals[q][:, j : j + 1],
+            )
 
-        def normalise(i):
-            pcs[i] = work.tile([P, S], BF16, name="pc")
-            if i in VECTOR_TILES:
+        def invert(q, tiles=BOTH):
+            if tiles.start == 0:
+                inverses[q] = work.tile([P, 2], F32, name="inverse")
+            nc.vector.reciprocal(out=inverses[q][:, tiles], in_=totals[q][:, tiles])
+
+        def gain(q):
+            gained[q] = work.tile([P, 2, S], F32, name="relay%d" % (q % 2), bufs=1, align_bytes=64)
+            nc.gpsimd.tensor_tensor(
+                out=gained[q][:], in0=exps[q][:], in1=c_f[:].to_broadcast([P, 2, S]), op=Alu.mult
+            )
+
+        def normalise(q, j):
+            if j == 0:
+                pcs[q] = work.tile([P, 2, S], BF16, name="pc")
+            if q in VECTOR_PAIRS:
                 nc.vector.scalar_tensor_tensor(
-                    out=pcs[i][:],
-                    in0=exps[i][:],
-                    scalar=inverses[i][:],
-                    in1=c_f[:],
+                    out=pcs[q][:, j],
+                    in0=exps[q][:, j],
+                    scalar=inverses[q][:, j : j + 1],
+                    in1=c_f[:, 0],
                     op0=Alu.mult,
                     op1=Alu.mult,
                 )
             else:
                 nc.scalar.activation(
-                    out=pcs[i][:], in_=gained[i][:], func=Act.Copy, scale=inverses[i][:]
+                    out=pcs[q][:, j], in_=gained[q][:, j], func=Act.Copy, scale=inverses[q][:, j : j + 1]
                 )
 
-        def turn(i):
-            words = pcs[i][:].bitcast(F32)
-            turned_pcs[i] = ps_turn.tile([P, HALVES, 2, P], F32, name="turned")
+        def turn(q, j):
+            words = pcs[q][:, j].bitcast(F32)
+            bank = shared_bank()
+            for n in range(PACK):
+                nc.tensor.transpose(bank[:, n, :], words[:, n * P : (n + 1) * P], ident[:])
+            turned_pcs[(q, j)] = bank
+
+        def turn_out(q, j, copy):
+            if j == 0:
+                grouped_pcs[q] = work.tile(
+                    [P, 2, HALVES, P, PACK], BF16, name="relay%d" % (q % 2), bufs=1, align_bytes=64
+                )
+            copy(
+                out=grouped_pcs[q][:, j].bitcast(F32),
+                in_=turned_pcs.get((q, j))[:].rearrange("p (g h) q -> p g q h", h=2),
+            )
+
+        def p_quantize(q, tiles=BOTH):
+            if tiles.start == 0:
+                p_codes[q] = work.tile([P, 2 * HALVES * P], U32, name="p_codes", bufs=3, align_bytes=64)
+                p_scales[q] = work.tile([P, 2 * HALVES * P], U8, name="p_scales", bufs=3, align_bytes=64)
+            cols = slice(tiles.start * HALVES * P, tiles.stop * HALVES * P)
+            quantize(
+                p_codes[q][:, cols], p_scales[q][:, cols], grouped_pcs[q][:, tiles].rearrange("p j g q t -> p (j g q t)")
+            )
+
+        def product(q, j):
+            bank = shared_bank()
             for g in range(HALVES):
-                for h in range(2):
-                    first = g * 2 * P + h * P
-                    nc.tensor.transpose(turned_pcs[i][:, g, h, :], words[:, first : first + P], ident[:])
+                cols = slice((2 * j + g) * P, (2 * j + g + 1) * P)
+                hh = HALVES * (q // PAIRS) + g
+                multiply(
+                    bank[:].rearrange("p t d -> p (t d)"), p_codes[q][:, cols], p_scales[q][:, cols],
+                    v_codes[hh][:], v_scales[hh][:], g == 0, g == HALVES - 1,
+                )
+            sums_out[(q, j)] = bank
 
-        def turn_out(i):
-            grouped_pcs[i] = work.tile([P, HALVES, P, PACK], BF16, name="p_grouped", bufs=3, align_bytes=64)
-            nc.scalar.copy(
-                out=grouped_pcs[i][:].bitcast(F32),
-                in_=turned_pcs[i][:].rearrange("p g h q -> p g q h"),
-            )
+        def store(q, j, copy):
+            b, h, t = q // PAIRS, (q % PAIRS) // 2, 2 * (q % 2) + j
+            rows = work.tile([P, D], F32, name="rows_out", bufs=4)
+            copy(out=rows[:], in_=sums_out.get((q, j))[:].rearrange("p t d -> p (t d)"))
+            nc.sync.dma_start(out=out_rows[b, h, :, t], in_=rows[:])
 
-        def p_quantize(i):
-            p_codes = work.tile([P, HALVES, P], U32, name="p_codes", bufs=4, align_bytes=64)
-            p_scales = work.tile([P, HALVES, P], U8, name="p_scales", bufs=4, align_bytes=64)
-            nc.vector.quantize_mx(
-                out=p_codes[:].rearrange("p g q -> p (g q)").bitcast(FP8X4),
-                scales=p_scales[:].rearrange("p g q -> p (g q)"),
-                in_=grouped_pcs[i][:].rearrange("p g q t -> p (g q t)"),
-            )
-            pc_codes[i] = (p_codes, p_scales)
+        def live(q):
+            return 0 <= q < N_PAIRS
 
-        def product(i):
-            b = i // TILES
-            p_codes, p_scales = pc_codes[i]
-            if i in SPARE_BANK_TILES:
-                sums_out[i] = ps_prep.tile([P, D], F32, name="prep")
+        by_scalar, by_vector = nc.scalar.copy, nc.vector.tensor_copy
+
+        def blends(q):
+            for j in range(2):
+                for g in range(HALVES):
+                    blend(q, j, g)
+
+        def v_quarters(s):
+            if s < 2:
+                quarters = [divmod(3 * s + i, QUARTERS) for i in range(3)]
             else:
-                sums_out[i] = ps_sum.tile([P, D], F32, name="sum")
-            for g in range(HALVES):
-                nc.tensor.matmul_mx(
-                    out=sums_out[i][:],
-                    lhsT=p_codes[:, g, :].bitcast(FP8X4),
-                    lhsT_scale=p_scales[:, g, :],
-                    rhs=v_codes[b][:, g, :].bitcast(FP8X4),
-                    rhs_scale=v_scales[b][:, g, :],
-                    start=(g == 0),
-                    stop=(g == HALVES - 1),
-                )
-
-        def store(i):
-            b, r = i // TILES, i % TILES
-            rows_out = work.tile([P, D], F32, name="rows_out", bufs=4)
-            nc.scalar.copy(out=rows_out[:], in_=sums_out[i][:])
-            nc.sync.dma_start(out=out_rows[b, :, r // PACK, r % PACK], in_=rows_out[:])
-
-        before, head, opening, middle, closing, rnd_plan = {}, {}, {}, {}, {}, {}
-
-        def put(plan, step, stage, *args):
-            plan.setdefault(step, []).append((stage, args))
-
-        def run(plan, step):
-            for stage, args in plan.get(step, []):
-                stage(*args)
-
-        for b in range(B):
-            if b > 0:
-                for k in range(4):
-                    put(before, 8 * b - 3 + k, x_copy_out, b, k)
-                    put(head, 8 * b - 2 + k, x_quantize, b, k)
-                    put(head, 8 * b - 4 + k, x_scaled, b, k)
-                    put(closing, 8 * b - 4 + k, x_turn, b, k)
-            put(head, 8 * b + 3, v_quantize, b, 0)
-            put(head, 8 * b + 4, v_quantize, b, 1)
-            for h in range(HALVES):
-                for n in range(4):
-                    if b > 0:
-                        step = 8 * b + 2 * h + n // 2
-                        put(closing, step - 1, v_product, b, h, n)
-                    else:
-                        step = 2 + h
-                        put(opening if n < 2 else middle, step, v_product, b, h, n)
-                    put(middle, step, v_gain, b, h, n)
-        for r in range(3, TILES):
-            put(rnd_plan, max(2, r - 3), rnd_scale, r)
+                quarters = [divmod(2 * s + 2 + i, QUARTERS) for i in range(2)]
+            if s == 0:
+                return [], quarters
+            return quarters[:1], quarters[1:]
 
         with tc.manual_schedule():
-            w_group(0)
-            x_plain(0, 0)
-            x_turn(0, 0)
-            w_quantize(0)
+            scale_spread()
             nc.vector.tensor_copy(out=mix_f[:], in_=mix_raw[:])
+            nc.vector.tensor_copy(out=c_4[:], in_=c_raw[:].rearrange("p g t -> p (g t)"))
             nc.vector.tensor_copy(out=u_f[:], in_=u_raw[:])
-            w_group(1)
-            x_plain(0, 1)
-            x_turn(0, 1)
-            x_scaled_late(0, 0)
+            w_group(0, by_vector)
+            x_scaled(0)
+            x_turn(0)
+            w_group(1, by_scalar)
+            w_quantize(0)
+            x_scaled(1)
+            x_copy_out(0)
+            x_turn(1)
             rnd_scale(0)
+            x_scaled(2)
+            x_quantize(0)
+            score(0, 0, 0)
+            score(0, 1, 0)
             w_quantize(1)
-            x_scaled_late(0, 1)
-            x_quantize(0, 0)
-            score(0)
-            x_quantize(0, 1)
-            rnd_scale(1)
-            c_spread()
             wv_group()
-            nc.vector.tensor_copy(out=scale_row[:, D : 2 * D], in_=scale_row[:, 0:D])
-            blend(0)
-            score(1)
-            x_scaled(0, 2)
-            x_turn(0, 2)
-            maximum(0)
-            x_scaled(0, 3)
-            x_turn(0, 3)
-            x_copy_out(0, 2)
-            blend(1)
-            score(2)
+            score(0, 0, 1)
+            score(0, 1, 1)
+            x_turn(2)
+            x_copy_out(1)
+            rnd_scale(1)
+            x_copy_out(2)
+            for g in range(HALVES):
+                for j in range(2):
+                    blend(0, j, g)
+            for g in range(HALVES):
+                c_spread(g)
             rnd_scale(2)
-            x_copy_out(0, 3)
-            exponent(0)
-            gain(0)
-            maximum(1)
-            x_quantize(0, 2)
-            x_quantize(0, 3)
+            rnd_scale(3)
+            maximum(0)
+            x_quantize(1)
+            for j in range(2):
+                for g in range(HALVES):
+                    score(1, j, g)
+            wv_quantize()
 
-            for s in range(2, N_TILES + 4):
-                if s <= N_TILES:
-                    exponent(s - 1)
-                    gain(s - 1)
-                run(before, s)
-                if 0 <= s - 3 < N_TILES:
-                    turn_out(s - 3)
-                if 0 <= s - 4 < N_TILES:
-                    p_quantize(s - 4)
-                run(head, s)
-                if s == 2:
-                    wv_quantize()
-                    invert(0)
-                if 0 <= s - 2 < N_TILES:
-                    normalise(s - 2)
-                run(rnd_plan, s)
-                if 0 <= s - 4 < N_TILES:
-                    product(s - 4)
-                run(opening, s)
-                if s < N_TILES:
-                    blend(s)
-                if s + 1 < N_TILES:
-                    score(s + 1)
-                run(middle, s)
-                if s <= N_TILES:
-                    invert(s - 1)
-                if s < N_TILES:
-                    maximum(s)
-                if 0 <= s - 2 < N_TILES:
-                    turn(s - 2)
-                if 0 <= s - 4 < N_TILES:
-                    store(s - 4)
-                run(closing, s)
+            for s in range(N_PAIRS - 2):
+                early, late = v_quarters(s)
+                exponent(s, 0)
+                exponent(s, 1)
+                x_quantize(s + 2)
+                for hh, n in early:
+                    v_product(hh, n)
+                if live(s + 3):
+                    x_scaled(s + 3)
+                    x_turn(s + 3)
+                    x_copy_out(s + 3)
+                if s == 2 or s % 2 == 1 and s > 1:
+                    v_quantize((s - 1) // 2)
+                if live(s - 2):
+                    p_quantize(s - 2)
+                if live(s - 3):
+                    product(s - 3, 0)
+                gain(s)
+                for hh, n in early:
+                    v_gain(hh, n)
+                for hh, n in late:
+                    v_product(hh, n)
+                if live(s - 3):
+                    product(s - 3, 1)
+                if live(s - 1):
+                    normalise(s - 1, 0)
+                if live(s - 3):
+                    store(s - 3, 0, by_scalar)
+                if live(s - 1):
+                    turn(s - 1, 0)
+                blends(s + 1)
+                if live(s - 1):
+                    normalise(s - 1, 1)
+                if live(s - 3):
+                    store(s - 3, 1, by_scalar)
+                score(s + 2, 0, 0)
+                score(s + 2, 0, 1)
+                for hh, n in late:
+                    v_gain(hh, n)
+                if live(s - 1):
+                    turn(s - 1, 1)
+                score(s + 2, 1, 0)
+                score(s + 2, 1, 1)
+                invert(s)
+                maximum(s + 1)
+                if live(s - 1):
+                    turn_out(s - 1, 0, by_scalar)
+                    turn_out(s - 1, 1, by_scalar)
+                if s == 0:
+                    for r in range(4, 2 * PAIRS):
+                        rnd_scale(r)
+
+            z, a, b, c3, d = N_PAIRS - 5, N_PAIRS - 4, N_PAIRS - 3, N_PAIRS - 2, N_PAIRS - 1
+            last = B * HALVES - 1
+            v_product(last, 2)
+            v_product(last, 3)
+            exponent(c3, 0)
+            exponent(c3, 1)
+            v_gain(last, 2)
+            v_gain(last, 3)
+            p_quantize(a)
+            v_quantize(last)
+            gain(c3)
+            product(z, 0)
+            product(z, 1)
+            normalise(b, 0)
+            store(z, 0, by_scalar)
+            product(a, 0)
+            turn(b, 0)
+            blend(d, 0, 0)
+            blend(d, 0, 1)
+            blend(d, 1, 0)
+            maximum(d, FIRST)
+            blend(d, 1, 1)
+            invert(c3)
+            normalise(b, 1)
+            store(z, 1, by_scalar)
+            store(a, 0, by_vector)
+            turn(b, 1)
+            product(a, 1)
+            maximum(d, SECOND)
+            exponent(d, 0)
+            turn_out(b, 0, by_scalar)
+            turn_out(b, 1, by_vector)
+            exponent(d, 1)
+            store(a, 1, by_vector)
+            invert(d, FIRST)
+            p_quantize(b)
+            product(b, 0)
+            product(b, 1)
+            normalise(c3, 0)
+            normalise(d, 0)
+            invert(d, SECOND)
+            normalise(c3, 1)
+            store(b, 0, by_vector)
+            turn(c3, 0)
+            turn(d, 0)
+            normalise(d, 1)
+            store(b, 1, by_scalar)
+            turn(c3, 1)
+            turn_out(c3, 0, by_scalar)
+            turn_out(d, 0, by_scalar)
+            turn(d, 1)
+            turn_out(c3, 1, by_vector)
+            p_quantize(c3, FIRST)
+            product(c3, 0)
+            p_quantize(d, FIRST)
+            product(d, 0)
+            turn_out(d, 1, by_scalar)
+            p_quantize(c3, SECOND)
+            product(c3, 1)
+            p_quantize(d, SECOND)
+            product(d, 1)
+            store(c3, 0, by_scalar)
+            store(d, 0, by_vector)
+            store(c3, 1, by_scalar)
+            store(d, 1, by_vector)

@@ -37,15 +37,15 @@ def tile_mixturedenserandomsynthesizer_t_kernel(tc, x_bytes, x_scale, w, rnd, mi
         keep = ctx.enter_context(tc.tile_pool(name="keep", bufs=1))
         work = ctx.enter_context(tc.tile_pool(name="work", bufs=2))
         psum = ctx.enter_context(tc.psum_pool(name="psum", bufs=1))
-        score_count, shared_count = [], []
+        score_count = []
 
         def score_bank():
             score_count.append(0)
             return psum.tile([P, BANK], F32, name="score%d" % (len(score_count) % SCORE_BANKS))
 
-        def shared_bank():
-            shared_count.append(0)
-            return psum.tile([P, PACK, P], F32, name="shared%d" % (len(shared_count) % SHARED_BANKS))
+        def shared_bank(k):
+            name = "shared%d" % k if k < SHARED_BANKS else "score%d" % (k - SHARED_BANKS)
+            return psum.tile([P, PACK, P], F32, name=name)
 
         scale_4 = keep.tile([P, PACK], F32, name="scale_4")
         nc.scalar.dma_start(out=scale_4[:], in_=x_scale.rearrange("a b (p t) -> p (a b t)", t=PACK))
@@ -97,7 +97,7 @@ def tile_mixturedenserandomsynthesizer_t_kernel(tc, x_bytes, x_scale, w, rnd, mi
         mix_f = keep.tile([P, 2], F32, name="mix_f")
         u_f = keep.tile([P, HALVES, PACK], F32, name="u_f")
         c_4 = keep.tile([P, HALVES * PACK], F32, name="c_4")
-        c_f = keep.tile([P, 1, S], F32, name="c_f")
+        c_f = keep.tile([P, 2, S], F32, name="c_f")
         scale_row = keep.tile([P, 2, P, PACK], F32, name="scale_row")
         rnd_f = []
         for r in range(2 * PAIRS):
@@ -133,23 +133,23 @@ def tile_mixturedenserandomsynthesizer_t_kernel(tc, x_bytes, x_scale, w, rnd, mi
         def column_split(ap):
             return ap.rearrange("p (h m e) -> p h m e", h=2, e=2)
 
-        def spread(columns):
-            bank = shared_bank()
+        def spread(columns, k):
+            bank = shared_bank(k)
             for t in range(PACK):
                 nc.tensor.transpose(bank[:, t, :], columns[:, t : t + 1].to_broadcast([P, P]), ident[:])
             return bank
 
         def scale_spread():
-            bank = spread(scale_4[:])
+            bank = spread(scale_4[:], 3)
             nc.scalar.copy(
                 out=scale_row[:], in_=bank[:].rearrange("p (o t) m -> p o m t", o=1).to_broadcast([P, 2, P, PACK])
             )
 
         def c_spread(g):
-            bank = spread(c_4[:, g * PACK : (g + 1) * PACK])
+            bank = spread(c_4[:, g * PACK : (g + 1) * PACK], 2 + g)
             nc.scalar.copy(
-                out=column_split(c_f[:, 0, g * BANK : (g + 1) * BANK]),
-                in_=bank[:].rearrange("p (h e) m -> p h m e", h=2),
+                out=c_f[:, :, g * BANK : (g + 1) * BANK].rearrange("p o (h m e) -> p o h m e", h=2, e=2),
+                in_=bank[:].rearrange("p (o h e) m -> p o h m e", o=1, h=2).to_broadcast([P, 2, 2, P, 2]),
             )
 
         def w_group(g, copy):
@@ -197,9 +197,9 @@ def tile_mixturedenserandomsynthesizer_t_kernel(tc, x_bytes, x_scale, w, rnd, mi
                 op=Alu.mult,
             )
 
-        def x_turn(q):
+        def x_turn(q, k=0):
             words = x_wide[q][:].bitcast(F32)
-            x_turned[q] = shared_bank()
+            x_turned[q] = shared_bank(k)
             for j in range(2):
                 for e in range(2):
                     nc.tensor.transpose(
@@ -219,8 +219,8 @@ def tile_mixturedenserandomsynthesizer_t_kernel(tc, x_bytes, x_scale, w, rnd, mi
 
         v_sums, v_grouped, v_codes, v_scales = {}, {}, {}, {}
 
-        def v_product(hh, n):
-            sums = shared_bank()
+        def v_product(hh, n, k):
+            sums = shared_bank(k)
             d_cols = slice(n * P, (n + 1) * P)
             for t in range(PACK):
                 q, rows = 2 * hh + t // 2, slice((t % 2) * P, (t % 2 + 1) * P)
@@ -294,9 +294,7 @@ def tile_mixturedenserandomsynthesizer_t_kernel(tc, x_bytes, x_scale, w, rnd, mi
 
         def gain(q):
             gained[q] = work.tile([P, 2, S], F32, name="relay%d" % (q % 2), bufs=1, align_bytes=64)
-            nc.gpsimd.tensor_tensor(
-                out=gained[q][:], in0=exps[q][:], in1=c_f[:].to_broadcast([P, 2, S]), op=Alu.mult
-            )
+            nc.gpsimd.tensor_tensor(out=gained[q][:], in0=exps[q][:], in1=c_f[:], op=Alu.mult)
 
         def normalise(q, j):
             if j == 0:
@@ -315,9 +313,9 @@ def tile_mixturedenserandomsynthesizer_t_kernel(tc, x_bytes, x_scale, w, rnd, mi
                     out=pcs[q][:, j], in_=gained[q][:, j], func=Act.Copy, scale=inverses[q][:, j : j + 1]
                 )
 
-        def turn(q, j):
+        def turn(q, j, k):
             words = pcs[q][:, j].bitcast(F32)
-            bank = shared_bank()
+            bank = shared_bank(k)
             for n in range(PACK):
                 nc.tensor.transpose(bank[:, n, :], words[:, n * P : (n + 1) * P], ident[:])
             turned_pcs[(q, j)] = bank
@@ -334,15 +332,15 @@ def tile_mixturedenserandomsynthesizer_t_kernel(tc, x_bytes, x_scale, w, rnd, mi
 
         def p_quantize(q, tiles=BOTH):
             if tiles.start == 0:
-                p_codes[q] = work.tile([P, 2 * HALVES * P], U32, name="p_codes", bufs=3, align_bytes=64)
-                p_scales[q] = work.tile([P, 2 * HALVES * P], U8, name="p_scales", bufs=3, align_bytes=64)
+                p_codes[q] = work.tile([P, 2 * HALVES * P], U32, name="p_codes", bufs=4, align_bytes=64)
+                p_scales[q] = work.tile([P, 2 * HALVES * P], U8, name="p_scales", bufs=4, align_bytes=64)
             cols = slice(tiles.start * HALVES * P, tiles.stop * HALVES * P)
             quantize(
                 p_codes[q][:, cols], p_scales[q][:, cols], grouped_pcs[q][:, tiles].rearrange("p j g q t -> p (j g q t)")
             )
 
-        def product(q, j):
-            bank = shared_bank()
+        def product(q, j, k):
+            bank = shared_bank(k)
             for g in range(HALVES):
                 cols = slice((2 * j + g) * P, (2 * j + g + 1) * P)
                 hh = HALVES * (q // PAIRS) + g
@@ -354,7 +352,7 @@ def tile_mixturedenserandomsynthesizer_t_kernel(tc, x_bytes, x_scale, w, rnd, mi
 
         def store(q, j, copy):
             b, h, t = q // PAIRS, (q % PAIRS) // 2, 2 * (q % 2) + j
-            rows = work.tile([P, D], F32, name="rows_out", bufs=4)
+            rows = work.tile([P, D], F32, name="rows_out", bufs=7)
             copy(out=rows[:], in_=sums_out.get((q, j))[:].rearrange("p t d -> p (t d)"))
             nc.sync.dma_start(out=out_rows[b, h, :, t], in_=rows[:])
 
@@ -369,13 +367,9 @@ def tile_mixturedenserandomsynthesizer_t_kernel(tc, x_bytes, x_scale, w, rnd, mi
                     blend(q, j, g)
 
         def v_quarters(s):
-            if s < 2:
-                quarters = [divmod(3 * s + i, QUARTERS) for i in range(3)]
-            else:
-                quarters = [divmod(2 * s + 2 + i, QUARTERS) for i in range(2)]
             if s == 0:
-                return [], quarters
-            return quarters[:1], quarters[1:]
+                return [], [(0, 0), (0, 1), (0, 2)]
+            return [divmod(2 * s + 1, QUARTERS)], [divmod(2 * s + 2, QUARTERS)]
 
         with tc.manual_schedule():
             scale_spread()
@@ -389,7 +383,7 @@ def tile_mixturedenserandomsynthesizer_t_kernel(tc, x_bytes, x_scale, w, rnd, mi
             w_quantize(0)
             x_scaled(1)
             x_copy_out(0)
-            x_turn(1)
+            x_turn(1, 1)
             rnd_scale(0)
             x_scaled(2)
             x_quantize(0)
@@ -399,15 +393,15 @@ def tile_mixturedenserandomsynthesizer_t_kernel(tc, x_bytes, x_scale, w, rnd, mi
             wv_group()
             score(0, 0, 1)
             score(0, 1, 1)
-            x_turn(2)
             x_copy_out(1)
             rnd_scale(1)
+            for g in range(HALVES):
+                c_spread(g)
+            x_turn(2)
             x_copy_out(2)
             for g in range(HALVES):
                 for j in range(2):
                     blend(0, j, g)
-            for g in range(HALVES):
-                c_spread(g)
             rnd_scale(2)
             rnd_scale(3)
             maximum(0)
@@ -417,75 +411,109 @@ def tile_mixturedenserandomsynthesizer_t_kernel(tc, x_bytes, x_scale, w, rnd, mi
                     score(1, j, g)
             wv_quantize()
 
-            for s in range(N_PAIRS - 2):
+            for s in range(N_PAIRS - 3):
                 early, late = v_quarters(s)
                 exponent(s, 0)
                 exponent(s, 1)
-                x_quantize(s + 2)
                 for hh, n in early:
-                    v_product(hh, n)
+                    v_gain(hh, n)
+                x_quantize(s + 2)
+                for k, (hh, n) in enumerate(late):
+                    v_product(hh, n, 1 + k)
+                if s > 0:
+                    score(s + 1, 1, 1)
                 if live(s + 3):
                     x_scaled(s + 3)
                     x_turn(s + 3)
-                    x_copy_out(s + 3)
-                if s == 2 or s % 2 == 1 and s > 1:
+                if s % 2 == 1:
                     v_quantize((s - 1) // 2)
                 if live(s - 2):
                     p_quantize(s - 2)
-                if live(s - 3):
-                    product(s - 3, 0)
                 gain(s)
-                for hh, n in early:
-                    v_gain(hh, n)
-                for hh, n in late:
-                    v_product(hh, n)
-                if live(s - 3):
-                    product(s - 3, 1)
+                if live(s - 4):
+                    product(s - 4, 1, 3)
+                    store(s - 4, 0, by_scalar)
                 if live(s - 1):
                     normalise(s - 1, 0)
-                if live(s - 3):
-                    store(s - 3, 0, by_scalar)
-                if live(s - 1):
-                    turn(s - 1, 0)
+                if live(s - 4):
+                    store(s - 4, 1, by_scalar)
                 blends(s + 1)
-                if live(s - 1):
-                    normalise(s - 1, 1)
-                if live(s - 3):
-                    store(s - 3, 1, by_scalar)
                 score(s + 2, 0, 0)
+                if live(s - 1):
+                    turn(s - 1, 0, 2)
+                    normalise(s - 1, 1)
                 score(s + 2, 0, 1)
+                score(s + 2, 1, 0)
                 for hh, n in late:
                     v_gain(hh, n)
                 if live(s - 1):
-                    turn(s - 1, 1)
-                score(s + 2, 1, 0)
-                score(s + 2, 1, 1)
+                    turn(s - 1, 1, 3)
+                for hh, n in v_quarters(s + 1)[0]:
+                    v_product(hh, n, 1)
                 invert(s)
                 maximum(s + 1)
+                if live(s + 3):
+                    x_copy_out(s + 3)
                 if live(s - 1):
                     turn_out(s - 1, 0, by_scalar)
+                if live(s - 3):
+                    product(s - 3, 0, 2)
+                if live(s - 1):
                     turn_out(s - 1, 1, by_scalar)
                 if s == 0:
                     for r in range(4, 2 * PAIRS):
                         rnd_scale(r)
 
-            z, a, b, c3, d = N_PAIRS - 5, N_PAIRS - 4, N_PAIRS - 3, N_PAIRS - 2, N_PAIRS - 1
+            x, y, z, a, b, c3, d = range(N_PAIRS - 7, N_PAIRS)
             last = B * HALVES - 1
-            v_product(last, 2)
-            v_product(last, 3)
+            exponent(b, 0)
+            exponent(b, 1)
+            v_gain(last - 1, 3)
+            x_quantize(d)
+            v_product(last, 0, 1)
+            score(c3, 1, 1)
+            v_product(last, 1, 0)
+            v_quantize(last - 1)
+            p_quantize(z)
+            gain(b)
+            product(x, 1, 3)
+            store(x, 0, by_scalar)
+            product(y, 0, 2)
+            normalise(a, 0)
+            store(x, 1, by_scalar)
+            v_gain(last, 0)
+            v_product(last, 2, 1)
+            blends(c3)
+            store(y, 0, by_scalar)
+            score(d, 0, 0)
+            turn(a, 0, 3)
+            normalise(a, 1)
+            v_gain(last, 1)
+            product(y, 1, 0)
+            score(d, 0, 1)
+            turn(a, 1, 2)
+            v_gain(last, 2)
+            v_product(last, 3, 1)
+            score(d, 1, 0)
+            score(d, 1, 1)
+            invert(b)
+            maximum(c3)
+            turn_out(a, 0, by_scalar)
+            product(z, 0, 3)
+            turn_out(a, 1, by_scalar)
+            product(z, 1, 2)
+            store(y, 1, by_scalar)
             exponent(c3, 0)
             exponent(c3, 1)
-            v_gain(last, 2)
             v_gain(last, 3)
             p_quantize(a)
             v_quantize(last)
             gain(c3)
-            product(z, 0)
-            product(z, 1)
+            product(a, 0, 0)
+            product(a, 1, 1)
             normalise(b, 0)
             store(z, 0, by_scalar)
-            product(a, 0)
-            turn(b, 0)
+            turn(b, 0, 3)
             blend(d, 0, 0)
             blend(d, 0, 1)
             blend(d, 1, 0)
@@ -493,44 +521,43 @@ def tile_mixturedenserandomsynthesizer_t_kernel(tc, x_bytes, x_scale, w, rnd, mi
             blend(d, 1, 1)
             invert(c3)
             normalise(b, 1)
-            store(z, 1, by_scalar)
-            store(a, 0, by_vector)
-            turn(b, 1)
-            product(a, 1)
+            turn(b, 1, 4)
+            store(z, 1, by_vector)
             maximum(d, SECOND)
             exponent(d, 0)
             turn_out(b, 0, by_scalar)
             turn_out(b, 1, by_vector)
             exponent(d, 1)
-            store(a, 1, by_vector)
             invert(d, FIRST)
             p_quantize(b)
-            product(b, 0)
-            product(b, 1)
-            normalise(c3, 0)
+            product(b, 0, 2)
+            product(b, 1, 3)
             normalise(d, 0)
+            normalise(c3, 0)
+            turn(c3, 0, 6)
+            turn(d, 0, 5)
             invert(d, SECOND)
+            store(a, 0, by_vector)
             normalise(c3, 1)
-            store(b, 0, by_vector)
-            turn(c3, 0)
-            turn(d, 0)
             normalise(d, 1)
-            store(b, 1, by_scalar)
-            turn(c3, 1)
+            turn(c3, 1, 7)
+            turn(d, 1, 4)
             turn_out(c3, 0, by_scalar)
             turn_out(d, 0, by_scalar)
-            turn(d, 1)
-            turn_out(c3, 1, by_vector)
+            store(a, 1, by_vector)
             p_quantize(c3, FIRST)
-            product(c3, 0)
+            product(c3, 0, 0)
             p_quantize(d, FIRST)
-            product(d, 0)
+            product(d, 0, 1)
+            turn_out(c3, 1, by_scalar)
+            store(b, 0, by_vector)
             turn_out(d, 1, by_scalar)
             p_quantize(c3, SECOND)
-            product(c3, 1)
+            product(c3, 1, 5)
+            store(b, 1, by_scalar)
             p_quantize(d, SECOND)
-            product(d, 1)
-            store(c3, 0, by_scalar)
-            store(d, 0, by_vector)
-            store(c3, 1, by_scalar)
-            store(d, 1, by_vector)
+            product(d, 1, 6)
+            store(c3, 0, by_vector)
+            store(d, 0, by_scalar)
+            store(c3, 1, by_vector)
+            store(d, 1, by_scalar)

@@ -25,8 +25,9 @@ AX = mybir.AxisListType
 
 FLOPS = 2 * B * S * D * S + 2 * B * S * D * D + 2 * B * S * S * D
 
-VECTOR_PAIRS = (N_PAIRS - 1,)
+FIRST_VECTOR_TILE = 2 * N_PAIRS - 3
 BOTH, FIRST, SECOND = slice(0, 2), slice(0, 1), slice(1, 2)
+CATCH_UP = N_PAIRS - 5
 SCORE_BANKS = 4
 SHARED_BANKS = 4
 
@@ -97,7 +98,7 @@ def tile_mixturedenserandomsynthesizer_t_kernel(tc, x_bytes, x_scale, w, rnd, mi
         mix_f = keep.tile([P, 2], F32, name="mix_f")
         u_f = keep.tile([P, HALVES, PACK], F32, name="u_f")
         c_4 = keep.tile([P, HALVES * PACK], F32, name="c_4")
-        c_f = keep.tile([P, 2, S], F32, name="c_f")
+        c_f = keep.tile([P, 1, S], F32, name="c_f")
         scale_row = keep.tile([P, 2, P, PACK], F32, name="scale_row")
         rnd_f = []
         for r in range(2 * PAIRS):
@@ -148,8 +149,8 @@ def tile_mixturedenserandomsynthesizer_t_kernel(tc, x_bytes, x_scale, w, rnd, mi
         def c_spread(g):
             bank = spread(c_4[:, g * PACK : (g + 1) * PACK], 2 + g)
             nc.scalar.copy(
-                out=c_f[:, :, g * BANK : (g + 1) * BANK].rearrange("p o (h m e) -> p o h m e", h=2, e=2),
-                in_=bank[:].rearrange("p (o h e) m -> p o h m e", o=1, h=2).to_broadcast([P, 2, 2, P, 2]),
+                out=column_split(c_f[:, 0, g * BANK : (g + 1) * BANK]),
+                in_=bank[:].rearrange("p (h e) m -> p h m e", h=2),
             )
 
         def w_group(g, copy):
@@ -207,7 +208,7 @@ def tile_mixturedenserandomsynthesizer_t_kernel(tc, x_bytes, x_scale, w, rnd, mi
                     )
 
         def x_copy_out(q):
-            x_grouped[q] = work.tile([P, 2, P, PACK], BF16, name="x_grouped", align_bytes=64)
+            x_grouped[q] = work.tile([P, 2, P, PACK], BF16, name="x_grouped", bufs=3, align_bytes=64)
             nc.scalar.copy(
                 out=x_grouped[q][:].bitcast(F32), in_=x_turned[q][:].rearrange("p (j e) q -> p j q e", e=2)
             )
@@ -292,14 +293,19 @@ def tile_mixturedenserandomsynthesizer_t_kernel(tc, x_bytes, x_scale, w, rnd, mi
                 inverses[q] = work.tile([P, 2], F32, name="inverse")
             nc.vector.reciprocal(out=inverses[q][:, tiles], in_=totals[q][:, tiles])
 
-        def gain(q):
+        def gain(q, tiles=BOTH):
             gained[q] = work.tile([P, 2, S], F32, name="relay%d" % (q % 2), bufs=1, align_bytes=64)
-            nc.gpsimd.tensor_tensor(out=gained[q][:], in0=exps[q][:], in1=c_f[:], op=Alu.mult)
+            nc.gpsimd.tensor_tensor(
+                out=gained[q][:, tiles],
+                in0=exps[q][:, tiles],
+                in1=c_f[:].to_broadcast([P, tiles.stop - tiles.start, S]),
+                op=Alu.mult,
+            )
 
         def normalise(q, j):
-            if j == 0:
+            if q not in pcs:
                 pcs[q] = work.tile([P, 2, S], BF16, name="pc")
-            if q in VECTOR_PAIRS:
+            if 2 * q + j >= FIRST_VECTOR_TILE:
                 nc.vector.scalar_tensor_tensor(
                     out=pcs[q][:, j],
                     in0=exps[q][:, j],
@@ -307,6 +313,15 @@ def tile_mixturedenserandomsynthesizer_t_kernel(tc, x_bytes, x_scale, w, rnd, mi
                     in1=c_f[:, 0],
                     op0=Alu.mult,
                     op1=Alu.mult,
+                )
+            elif q == N_PAIRS - 3:
+                nc.gpsimd.tensor_scalar(
+                    out=pcs[q][:, j],
+                    in0=gained[q][:, j],
+                    scalar1=inverses[q][:, j : j + 1],
+                    scalar2=0.0,
+                    op0=Alu.mult,
+                    op1=Alu.add,
                 )
             else:
                 nc.scalar.activation(
@@ -321,7 +336,7 @@ def tile_mixturedenserandomsynthesizer_t_kernel(tc, x_bytes, x_scale, w, rnd, mi
             turned_pcs[(q, j)] = bank
 
         def turn_out(q, j, copy):
-            if j == 0:
+            if q not in grouped_pcs:
                 grouped_pcs[q] = work.tile(
                     [P, 2, HALVES, P, PACK], BF16, name="relay%d" % (q % 2), bufs=1, align_bytes=64
                 )
@@ -331,7 +346,7 @@ def tile_mixturedenserandomsynthesizer_t_kernel(tc, x_bytes, x_scale, w, rnd, mi
             )
 
         def p_quantize(q, tiles=BOTH):
-            if tiles.start == 0:
+            if q not in p_codes:
                 p_codes[q] = work.tile([P, 2 * HALVES * P], U32, name="p_codes", bufs=4, align_bytes=64)
                 p_scales[q] = work.tile([P, 2 * HALVES * P], U8, name="p_scales", bufs=4, align_bytes=64)
             cols = slice(tiles.start * HALVES * P, tiles.stop * HALVES * P)
@@ -352,7 +367,7 @@ def tile_mixturedenserandomsynthesizer_t_kernel(tc, x_bytes, x_scale, w, rnd, mi
 
         def store(q, j, copy):
             b, h, t = q // PAIRS, (q % PAIRS) // 2, 2 * (q % 2) + j
-            rows = work.tile([P, D], F32, name="rows_out", bufs=7)
+            rows = work.tile([P, D], F32, name="rows_out", bufs=8)
             copy(out=rows[:], in_=sums_out.get((q, j))[:].rearrange("p t d -> p (t d)"))
             nc.sync.dma_start(out=out_rows[b, h, :, t], in_=rows[:])
 
@@ -370,6 +385,11 @@ def tile_mixturedenserandomsynthesizer_t_kernel(tc, x_bytes, x_scale, w, rnd, mi
             if s == 0:
                 return [], [(0, 0), (0, 1), (0, 2)]
             return [divmod(2 * s + 1, QUARTERS)], [divmod(2 * s + 2, QUARTERS)]
+
+        def stores_of(s):
+            first = 2 * (s - 4) + max(0, s - CATCH_UP)
+            count = 3 if s >= CATCH_UP else 2
+            return [divmod(i, 2) for i in range(first, first + count) if i >= 0]
 
         with tc.manual_schedule():
             scale_spread()
@@ -389,30 +409,34 @@ def tile_mixturedenserandomsynthesizer_t_kernel(tc, x_bytes, x_scale, w, rnd, mi
             x_quantize(0)
             score(0, 0, 0)
             score(0, 1, 0)
+            x_copy_out(1)
+            x_turn(2)
+            rnd_scale(1)
+            x_scaled(3)
+            x_quantize(1)
             w_quantize(1)
             wv_group()
             score(0, 0, 1)
             score(0, 1, 1)
-            x_copy_out(1)
-            rnd_scale(1)
+            x_copy_out(2)
+            x_turn(3, 1)
             for g in range(HALVES):
                 c_spread(g)
-            x_turn(2)
-            x_copy_out(2)
             for g in range(HALVES):
                 for j in range(2):
                     blend(0, j, g)
-            rnd_scale(2)
-            rnd_scale(3)
-            maximum(0)
-            x_quantize(1)
             for j in range(2):
                 for g in range(HALVES):
                     score(1, j, g)
+            maximum(0, FIRST)
+            maximum(0, SECOND)
+            x_copy_out(3)
+            rnd_scale(2)
             wv_quantize()
 
             for s in range(N_PAIRS - 3):
                 early, late = v_quarters(s)
+                stores = stores_of(s)
                 exponent(s, 0)
                 exponent(s, 1)
                 for hh, n in early:
@@ -422,7 +446,9 @@ def tile_mixturedenserandomsynthesizer_t_kernel(tc, x_bytes, x_scale, w, rnd, mi
                     v_product(hh, n, 1 + k)
                 if s > 0:
                     score(s + 1, 1, 1)
-                if live(s + 3):
+                if s == 0:
+                    rnd_scale(3)
+                elif live(s + 3):
                     x_scaled(s + 3)
                     x_turn(s + 3)
                 if s % 2 == 1:
@@ -430,14 +456,25 @@ def tile_mixturedenserandomsynthesizer_t_kernel(tc, x_bytes, x_scale, w, rnd, mi
                 if live(s - 2):
                     p_quantize(s - 2)
                 gain(s)
-                if live(s - 4):
-                    product(s - 4, 1, 3)
-                    store(s - 4, 0, by_scalar)
+                if stores:
+                    product(*stores[1], 3)
+                    store(*stores[0], by_scalar)
+                if len(stores) > 2:
+                    product(*stores[2], 2)
                 if live(s - 1):
                     normalise(s - 1, 0)
-                if live(s - 4):
-                    store(s - 4, 1, by_scalar)
-                blends(s + 1)
+                for q, j in stores[1:]:
+                    store(q, j, by_scalar)
+                if s == 0:
+                    blend(1, 0, 0)
+                    blend(1, 0, 1)
+                    v_gain(0, 0)
+                    v_gain(0, 1)
+                    blend(1, 1, 0)
+                    blend(1, 1, 1)
+                    late = late[2:]
+                else:
+                    blends(s + 1)
                 score(s + 2, 0, 0)
                 if live(s - 1):
                     turn(s - 1, 0, 2)
@@ -446,25 +483,25 @@ def tile_mixturedenserandomsynthesizer_t_kernel(tc, x_bytes, x_scale, w, rnd, mi
                 score(s + 2, 1, 0)
                 for hh, n in late:
                     v_gain(hh, n)
-                if live(s - 1):
-                    turn(s - 1, 1, 3)
                 for hh, n in v_quarters(s + 1)[0]:
                     v_product(hh, n, 1)
+                if live(s - 1):
+                    turn(s - 1, 1, 3)
                 invert(s)
                 maximum(s + 1)
-                if live(s + 3):
+                if s > 0:
                     x_copy_out(s + 3)
                 if live(s - 1):
                     turn_out(s - 1, 0, by_scalar)
-                if live(s - 3):
-                    product(s - 3, 0, 2)
+                for q, j in stores_of(s + 1)[:1]:
+                    product(q, j, 2)
                 if live(s - 1):
                     turn_out(s - 1, 1, by_scalar)
                 if s == 0:
                     for r in range(4, 2 * PAIRS):
                         rnd_scale(r)
 
-            x, y, z, a, b, c3, d = range(N_PAIRS - 7, N_PAIRS)
+            y, z, a, b, c3, d = range(N_PAIRS - 6, N_PAIRS)
             last = B * HALVES - 1
             exponent(b, 0)
             exponent(b, 1)
@@ -476,20 +513,20 @@ def tile_mixturedenserandomsynthesizer_t_kernel(tc, x_bytes, x_scale, w, rnd, mi
             v_quantize(last - 1)
             p_quantize(z)
             gain(b)
-            product(x, 1, 3)
-            store(x, 0, by_scalar)
-            product(y, 0, 2)
+            product(y, 1, 3)
+            store(y, 0, by_scalar)
+            product(z, 0, 2)
             normalise(a, 0)
-            store(x, 1, by_scalar)
+            store(y, 1, by_scalar)
             v_gain(last, 0)
             v_product(last, 2, 1)
             blends(c3)
-            store(y, 0, by_scalar)
             score(d, 0, 0)
             turn(a, 0, 3)
             normalise(a, 1)
+            store(z, 0, by_scalar)
             v_gain(last, 1)
-            product(y, 1, 0)
+            product(z, 1, 0)
             score(d, 0, 1)
             turn(a, 1, 2)
             v_gain(last, 2)
@@ -499,65 +536,58 @@ def tile_mixturedenserandomsynthesizer_t_kernel(tc, x_bytes, x_scale, w, rnd, mi
             invert(b)
             maximum(c3)
             turn_out(a, 0, by_scalar)
-            product(z, 0, 3)
             turn_out(a, 1, by_scalar)
-            product(z, 1, 2)
-            store(y, 1, by_scalar)
+            store(z, 1, by_scalar)
             exponent(c3, 0)
             exponent(c3, 1)
             v_gain(last, 3)
-            p_quantize(a)
+            normalise(b, 0)
+            normalise(b, 1)
+            turn(b, 0, 3)
+            turn(b, 1, 2)
+            blends(d)
             v_quantize(last)
-            gain(c3)
+            p_quantize(a)
+            gain(c3, FIRST)
             product(a, 0, 0)
             product(a, 1, 1)
-            normalise(b, 0)
-            store(z, 0, by_scalar)
-            turn(b, 0, 3)
-            blend(d, 0, 0)
-            blend(d, 0, 1)
-            blend(d, 1, 0)
+            turn_out(b, 0, by_scalar)
+            turn_out(b, 1, by_scalar)
             maximum(d, FIRST)
-            blend(d, 1, 1)
             invert(c3)
-            normalise(b, 1)
-            turn(b, 1, 4)
-            store(z, 1, by_vector)
             maximum(d, SECOND)
             exponent(d, 0)
-            turn_out(b, 0, by_scalar)
-            turn_out(b, 1, by_vector)
+            store(a, 0, by_vector)
             exponent(d, 1)
-            invert(d, FIRST)
             p_quantize(b)
             product(b, 0, 2)
+            invert(d, FIRST)
+            normalise(c3, 1)
+            normalise(c3, 0)
+            turn(c3, 1, 4)
             product(b, 1, 3)
             normalise(d, 0)
-            normalise(c3, 0)
-            turn(c3, 0, 6)
-            turn(d, 0, 5)
             invert(d, SECOND)
-            store(a, 0, by_vector)
-            normalise(c3, 1)
-            normalise(d, 1)
-            turn(c3, 1, 7)
-            turn(d, 1, 4)
-            turn_out(c3, 0, by_scalar)
-            turn_out(d, 0, by_scalar)
-            store(a, 1, by_vector)
-            p_quantize(c3, FIRST)
-            product(c3, 0, 0)
-            p_quantize(d, FIRST)
-            product(d, 0, 1)
+            turn(c3, 0, 5)
+            store(a, 1, by_scalar)
             turn_out(c3, 1, by_scalar)
-            store(b, 0, by_vector)
-            turn_out(d, 1, by_scalar)
+            turn_out(c3, 0, by_scalar)
+            turn(d, 0, 6)
+            normalise(d, 1)
             p_quantize(c3, SECOND)
-            product(c3, 1, 5)
-            store(b, 1, by_scalar)
+            turn(d, 1, 7)
+            product(c3, 1, 0)
+            store(b, 0, by_scalar)
+            turn_out(d, 0, by_scalar)
+            p_quantize(c3, FIRST)
+            product(c3, 0, 1)
+            store(b, 1, by_vector)
+            turn_out(d, 1, by_scalar)
+            p_quantize(d, FIRST)
+            product(d, 0, 2)
+            store(c3, 1, by_scalar)
             p_quantize(d, SECOND)
-            product(d, 1, 6)
+            product(d, 1, 4)
             store(c3, 0, by_vector)
             store(d, 0, by_scalar)
-            store(c3, 1, by_vector)
-            store(d, 1, by_scalar)
+            store(d, 1, by_vector)

@@ -27,7 +27,9 @@ FLOPS = 2 * B * S * D * S + 2 * B * S * D * D + 2 * B * S * S * D
 
 FIRST_VECTOR_TILE = 2 * N_PAIRS - 3
 BOTH, FIRST, SECOND = slice(0, 2), slice(0, 1), slice(1, 2)
-CATCH_UP = N_PAIRS - 5
+CATCH_UP = N_PAIRS
+FIRST_SINGLE_STORE = N_PAIRS - 4
+GPSIMD_TILE = 2 * (N_PAIRS - 3)
 SCORE_BANKS = 4
 SHARED_BANKS = 4
 
@@ -294,7 +296,7 @@ def tile_mixturedenserandomsynthesizer_t_kernel(tc, x_bytes, x_scale, w, rnd, mi
             nc.vector.reciprocal(out=inverses[q][:, tiles], in_=totals[q][:, tiles])
 
         def gain(q, tiles=BOTH):
-            gained[q] = work.tile([P, 2, S], F32, name="relay%d" % (q % 2), bufs=1, align_bytes=64)
+            gained[q] = work.tile([P, 2, S], F32, name="gained")
             nc.gpsimd.tensor_tensor(
                 out=gained[q][:, tiles],
                 in0=exps[q][:, tiles],
@@ -314,7 +316,7 @@ def tile_mixturedenserandomsynthesizer_t_kernel(tc, x_bytes, x_scale, w, rnd, mi
                     op0=Alu.mult,
                     op1=Alu.mult,
                 )
-            elif q == N_PAIRS - 3:
+            elif 2 * q + j == GPSIMD_TILE:
                 nc.gpsimd.tensor_scalar(
                     out=pcs[q][:, j],
                     in0=gained[q][:, j],
@@ -338,7 +340,7 @@ def tile_mixturedenserandomsynthesizer_t_kernel(tc, x_bytes, x_scale, w, rnd, mi
         def turn_out(q, j, copy):
             if q not in grouped_pcs:
                 grouped_pcs[q] = work.tile(
-                    [P, 2, HALVES, P, PACK], BF16, name="relay%d" % (q % 2), bufs=1, align_bytes=64
+                    [P, 2, HALVES, P, PACK], BF16, name="p_grouped", bufs=3, align_bytes=64
                 )
             copy(
                 out=grouped_pcs[q][:, j].bitcast(F32),
@@ -367,9 +369,13 @@ def tile_mixturedenserandomsynthesizer_t_kernel(tc, x_bytes, x_scale, w, rnd, mi
 
         def store(q, j, copy):
             b, h, t = q // PAIRS, (q % PAIRS) // 2, 2 * (q % 2) + j
-            rows = work.tile([P, D], F32, name="rows_out", bufs=8)
-            copy(out=rows[:], in_=sums_out.get((q, j))[:].rearrange("p t d -> p (t d)"))
-            nc.sync.dma_start(out=out_rows[b, h, :, t], in_=rows[:])
+            if q not in rows_out:
+                rows_out[q] = work.tile([P, 2, D], F32, name="rows_out", bufs=4)
+            copy(out=rows_out[q][:, j], in_=sums_out.get((q, j))[:].rearrange("p t d -> p (t d)"))
+            if q >= FIRST_SINGLE_STORE:
+                nc.sync.dma_start(out=out_rows[b, h, :, t], in_=rows_out[q][:, j])
+            elif j == 1:
+                nc.sync.dma_start(out=out_rows[b, h, :, t - 1 : t + 1], in_=rows_out[q][:])
 
         def live(q):
             return 0 <= q < N_PAIRS
@@ -437,34 +443,38 @@ def tile_mixturedenserandomsynthesizer_t_kernel(tc, x_bytes, x_scale, w, rnd, mi
             for s in range(N_PAIRS - 3):
                 early, late = v_quarters(s)
                 stores = stores_of(s)
+                this_bank, other_bank = 1 + 2 * (s % 2), 3 - 2 * (s % 2)
                 exponent(s, 0)
                 exponent(s, 1)
                 for hh, n in early:
                     v_gain(hh, n)
                 x_quantize(s + 2)
-                for k, (hh, n) in enumerate(late):
-                    v_product(hh, n, 1 + k)
+                if live(s - 1):
+                    invert(s - 1)
+                if s % 2 == 0 and s > 0:
+                    v_quantize(s // 2 - 1)
+                if stores and s % PAIRS == 0:
+                    product(*stores[0], 2)
                 if s > 0:
-                    score(s + 1, 1, 1)
+                    v_product(*late[0], other_bank)
+                if live(s - 3):
+                    p_quantize(s - 3)
                 if s == 0:
                     rnd_scale(3)
-                elif live(s + 3):
+                    for k in range(3):
+                        v_product(0, k, 1 + k)
+                else:
                     x_scaled(s + 3)
+                    if stores:
+                        product(*stores[1], this_bank)
                     x_turn(s + 3)
-                if s % 2 == 1:
-                    v_quantize((s - 1) // 2)
-                if live(s - 2):
-                    p_quantize(s - 2)
                 gain(s)
                 if stores:
-                    product(*stores[1], 3)
                     store(*stores[0], by_scalar)
-                if len(stores) > 2:
-                    product(*stores[2], 2)
                 if live(s - 1):
                     normalise(s - 1, 0)
-                for q, j in stores[1:]:
-                    store(q, j, by_scalar)
+                if s > 0:
+                    x_copy_out(s + 3)
                 if s == 0:
                     blend(1, 0, 0)
                     blend(1, 0, 1)
@@ -475,119 +485,124 @@ def tile_mixturedenserandomsynthesizer_t_kernel(tc, x_bytes, x_scale, w, rnd, mi
                     late = late[2:]
                 else:
                     blends(s + 1)
-                score(s + 2, 0, 0)
+                for j in range(2):
+                    for g in range(HALVES):
+                        score(s + 2, j, g)
                 if live(s - 1):
                     turn(s - 1, 0, 2)
                     normalise(s - 1, 1)
-                score(s + 2, 0, 1)
-                score(s + 2, 1, 0)
+                    turn(s - 1, 1, 0)
+                if stores:
+                    store(*stores[1], by_scalar)
+                for hh, n in v_quarters(s + 1)[0]:
+                    v_product(hh, n, this_bank)
                 for hh, n in late:
                     v_gain(hh, n)
-                for hh, n in v_quarters(s + 1)[0]:
-                    v_product(hh, n, 1)
-                if live(s - 1):
-                    turn(s - 1, 1, 3)
-                invert(s)
                 maximum(s + 1)
-                if s > 0:
-                    x_copy_out(s + 3)
-                if live(s - 1):
-                    turn_out(s - 1, 0, by_scalar)
-                for q, j in stores_of(s + 1)[:1]:
-                    product(q, j, 2)
                 if live(s - 1):
                     turn_out(s - 1, 1, by_scalar)
+                    turn_out(s - 1, 0, by_scalar)
+                if (s + 1) % PAIRS > 0:
+                    for q, j in stores_of(s + 1)[:1]:
+                        product(q, j, 2)
                 if s == 0:
                     for r in range(4, 2 * PAIRS):
                         rnd_scale(r)
 
-            y, z, a, b, c3, d = range(N_PAIRS - 6, N_PAIRS)
+            x, y, z, a, b, c3, d = range(N_PAIRS - 7, N_PAIRS)
             last = B * HALVES - 1
             exponent(b, 0)
             exponent(b, 1)
             v_gain(last - 1, 3)
             x_quantize(d)
+            invert(a)
             v_product(last, 0, 1)
-            score(c3, 1, 1)
             v_product(last, 1, 0)
+            product(x, 1, 3)
+            p_quantize(y)
             v_quantize(last - 1)
             p_quantize(z)
             gain(b)
-            product(y, 1, 3)
-            store(y, 0, by_scalar)
-            product(z, 0, 2)
-            normalise(a, 0)
-            store(y, 1, by_scalar)
+            store(x, 0, by_scalar)
+            product(y, 0, 2)
             v_gain(last, 0)
             v_product(last, 2, 1)
+            normalise(a, 0)
+            store(x, 1, by_scalar)
             blends(c3)
+            store(y, 0, by_scalar)
             score(d, 0, 0)
             turn(a, 0, 3)
             normalise(a, 1)
-            store(z, 0, by_scalar)
-            v_gain(last, 1)
-            product(z, 1, 0)
             score(d, 0, 1)
-            turn(a, 1, 2)
-            v_gain(last, 2)
-            v_product(last, 3, 1)
             score(d, 1, 0)
             score(d, 1, 1)
-            invert(b)
+            v_gain(last, 1)
+            product(y, 1, 0)
+            v_gain(last, 2)
+            turn(a, 1, 2)
+            v_product(last, 3, 1)
             maximum(c3)
             turn_out(a, 0, by_scalar)
+            product(z, 0, 3)
+            store(y, 1, by_scalar)
             turn_out(a, 1, by_scalar)
-            store(z, 1, by_scalar)
+            product(z, 1, 0)
             exponent(c3, 0)
             exponent(c3, 1)
             v_gain(last, 3)
-            normalise(b, 0)
-            normalise(b, 1)
-            turn(b, 0, 3)
-            turn(b, 1, 2)
-            blends(d)
-            v_quantize(last)
             p_quantize(a)
+            v_quantize(last)
+            invert(b)
             gain(c3, FIRST)
-            product(a, 0, 0)
-            product(a, 1, 1)
-            turn_out(b, 0, by_scalar)
-            turn_out(b, 1, by_scalar)
-            maximum(d, FIRST)
+            normalise(b, 0)
+            store(z, 0, by_scalar)
+            store(z, 1, by_scalar)
+            normalise(b, 1)
+            blend(d, 0, 0)
+            blend(d, 0, 1)
             invert(c3)
-            maximum(d, SECOND)
-            exponent(d, 0)
-            store(a, 0, by_vector)
-            exponent(d, 1)
-            p_quantize(b)
-            product(b, 0, 2)
-            invert(d, FIRST)
-            normalise(c3, 1)
+            blend(d, 1, 0)
+            blend(d, 1, 1)
+            turn(b, 1, 2)
             normalise(c3, 0)
-            turn(c3, 1, 4)
-            product(b, 1, 3)
+            maximum(d, FIRST)
+            maximum(d, SECOND)
+            turn(b, 0, 0)
+            turn(c3, 0, 4)
+            exponent(d, 0)
+            exponent(d, 1)
+            normalise(c3, 1)
+            product(a, 0, 1)
+            turn(c3, 1, 5)
+            product(a, 1, 3)
+            invert(d, FIRST)
+            turn_out(b, 1, by_vector)
             normalise(d, 0)
-            invert(d, SECOND)
-            turn(c3, 0, 5)
-            store(a, 1, by_scalar)
-            turn_out(c3, 1, by_scalar)
-            turn_out(c3, 0, by_scalar)
             turn(d, 0, 6)
+            turn_out(b, 0, by_scalar)
+            turn_out(c3, 0, by_scalar)
+            invert(d, SECOND)
+            p_quantize(b)
+            product(b, 0, 0)
+            turn_out(c3, 1, by_scalar)
+            store(a, 0, by_scalar)
             normalise(d, 1)
-            p_quantize(c3, SECOND)
+            product(b, 1, 2)
             turn(d, 1, 7)
-            product(c3, 1, 0)
-            store(b, 0, by_scalar)
             turn_out(d, 0, by_scalar)
-            p_quantize(c3, FIRST)
+            store(a, 1, by_scalar)
+            p_quantize(c3)
             product(c3, 0, 1)
-            store(b, 1, by_vector)
             turn_out(d, 1, by_scalar)
             p_quantize(d, FIRST)
-            product(d, 0, 2)
-            store(c3, 1, by_scalar)
+            product(c3, 1, 3)
+            product(d, 0, 4)
+            store(b, 0, by_vector)
             p_quantize(d, SECOND)
-            product(d, 1, 4)
+            product(d, 1, 5)
+            store(b, 1, by_scalar)
             store(c3, 0, by_vector)
-            store(d, 0, by_scalar)
-            store(d, 1, by_vector)
+            store(c3, 1, by_scalar)
+            store(d, 0, by_vector)
+            store(d, 1, by_scalar)

@@ -29,7 +29,8 @@ FIRST_VECTOR_TILE = 2 * N_PAIRS - 3
 BOTH, FIRST, SECOND = slice(0, 2), slice(0, 1), slice(1, 2)
 CATCH_UP = N_PAIRS
 FIRST_SINGLE_STORE = N_PAIRS - 4
-GPSIMD_TILE = 2 * (N_PAIRS - 3)
+GPSIMD_X_STEPS = (1, 2, 3, 5, 7, 9, 11)
+GPSIMD_PC_STEPS = (4, 6, 8, 10, 12, 13)
 SCORE_BANKS = 4
 SHARED_BANKS = 4
 
@@ -103,7 +104,7 @@ def tile_mixturedenserandomsynthesizer_t_kernel(tc, x_bytes, x_scale, w, rnd, mi
         c_f = keep.tile([P, 1, S], F32, name="c_f")
         scale_row = keep.tile([P, 2, P, PACK], F32, name="scale_row")
         rnd_f = []
-        for r in range(2 * PAIRS):
+        for r in range(2 * PAIRS - 1):
             rnd_f.append(keep.tile([P, S], F32, name="rnd_f%d" % r))
         w_grouped, w_codes, w_scales = [], [], []
         for g in range(HALVES):
@@ -188,11 +189,25 @@ def tile_mixturedenserandomsynthesizer_t_kernel(tc, x_bytes, x_scale, w, rnd, mi
                     scale=mix_f[:, 1:2],
                 )
 
+        def rnd_scale_by_gpsimd(r):
+            if r == len(rnd_f):
+                rnd_f.append(keep.tile([P, S], F32, name="w_grouped1", align_bytes=64))
+            for g in range(HALVES):
+                cols = slice(g * BANK, (g + 1) * BANK)
+                nc.gpsimd.tensor_scalar(
+                    out=column_split(rnd_f[r][:, cols]),
+                    in0=key_split(rnd_raw[r // 2][:, r % 2, cols]),
+                    scalar1=mix_f[:, 1:2],
+                    scalar2=0.0,
+                    op0=Alu.mult,
+                    op1=Alu.add,
+                )
+
         x_wide, x_turned, x_grouped, x_codes, x_scales = {}, {}, {}, {}, {}
 
         def x_scaled(q):
             b, h, t = q // PAIRS, (q % PAIRS) // 2, 2 * (q % 2)
-            x_wide[q] = work.tile([P, 2 * D], BF16, name="wide")
+            x_wide[q] = work.tile([P, 2 * D], BF16, name="wide", bufs=3)
             nc.vector.tensor_tensor(
                 out=x_wide[q][:],
                 in0=x_raw.get((b, h))[:, t : t + 2, :].rearrange("p t k -> p (t k)").bitcast(FP8),
@@ -200,19 +215,47 @@ def tile_mixturedenserandomsynthesizer_t_kernel(tc, x_bytes, x_scale, w, rnd, mi
                 op=Alu.mult,
             )
 
+        def x_widen(q):
+            b, h, t = q // PAIRS, (q % PAIRS) // 2, 2 * (q % 2)
+            x_wide[q] = work.tile([P, 2 * D], BF16, name="wide", bufs=3)
+            nc.scalar.copy(
+                out=x_wide[q][:], in_=x_raw.get((b, h))[:, t : t + 2, :].rearrange("p t k -> p (t k)").bitcast(FP8)
+            )
+
+        def x_scale_second(q):
+            nc.gpsimd.tensor_tensor(
+                out=x_wide[q][:, D : 2 * D],
+                in0=x_wide[q][:, D : 2 * D],
+                in1=scale_row[:, 0].rearrange("p m t -> p (m t)"),
+                op=Alu.mult,
+            )
+
         def x_turn(q, k=0):
             words = x_wide[q][:].bitcast(F32)
             x_turned[q] = shared_bank(k)
+            x_grouped[q] = work.tile([P, 2, P, PACK], BF16, name="x_grouped", bufs=3, align_bytes=64)
             for j in range(2):
-                for e in range(2):
+                for h in range(2):
                     nc.tensor.transpose(
-                        x_turned[q][:, 2 * j + e, :], words[:, 256 * j + e : 256 * (j + 1) : 2], ident[:]
+                        x_turned[q][:, 2 * h + j, :], words[:, 256 * j + h : 256 * (j + 1) : 2], ident[:]
                     )
 
-        def x_copy_out(q):
-            x_grouped[q] = work.tile([P, 2, P, PACK], BF16, name="x_grouped", bufs=3, align_bytes=64)
+        def x_copy_out(q, tiles=BOTH):
             nc.scalar.copy(
-                out=x_grouped[q][:].bitcast(F32), in_=x_turned[q][:].rearrange("p (j e) q -> p j q e", e=2)
+                out=x_grouped[q][:, tiles].bitcast(F32),
+                in_=x_turned[q][:].rearrange("p (h j) q -> p j q h", h=2)[:, tiles],
+            )
+
+        def x_scale_out(q, tiles):
+            rows = slice(tiles.start * P, tiles.stop * P)
+            values = x_turned[q][:].rearrange("p (h j) q -> p h (j q)", h=2)[:, :, rows].bitcast(BF16)
+            nc.vector.tensor_tensor(
+                out=x_grouped[q][:, tiles].rearrange("p j q (h e) -> p (j q) h e", e=2),
+                in0=values.rearrange("p h (q e) -> p q h e", e=2),
+                in1=scale_4[:]
+                .rearrange("p (o h e) -> p o h e", o=1, e=2)
+                .to_broadcast([P, rows.stop - rows.start, 2, 2]),
+                op=Alu.mult,
             )
 
         def x_quantize(q):
@@ -316,7 +359,7 @@ def tile_mixturedenserandomsynthesizer_t_kernel(tc, x_bytes, x_scale, w, rnd, mi
                     op0=Alu.mult,
                     op1=Alu.mult,
                 )
-            elif 2 * q + j == GPSIMD_TILE:
+            elif j == 0 and q in GPSIMD_PC_STEPS:
                 nc.gpsimd.tensor_scalar(
                     out=pcs[q][:, j],
                     in0=gained[q][:, j],
@@ -422,6 +465,7 @@ def tile_mixturedenserandomsynthesizer_t_kernel(tc, x_bytes, x_scale, w, rnd, mi
             x_quantize(1)
             w_quantize(1)
             wv_group()
+            rnd_scale_by_gpsimd(6)
             score(0, 0, 1)
             score(0, 1, 1)
             x_copy_out(2)
@@ -438,22 +482,31 @@ def tile_mixturedenserandomsynthesizer_t_kernel(tc, x_bytes, x_scale, w, rnd, mi
             maximum(0, SECOND)
             x_copy_out(3)
             rnd_scale(2)
-            wv_quantize()
 
             for s in range(N_PAIRS - 3):
                 early, late = v_quarters(s)
                 stores = stores_of(s)
                 this_bank, other_bank = 1 + 2 * (s % 2), 3 - 2 * (s % 2)
+                split = s - 1 in GPSIMD_X_STEPS
                 exponent(s, 0)
                 exponent(s, 1)
                 for hh, n in early:
                     v_gain(hh, n)
-                x_quantize(s + 2)
-                if live(s - 1):
+                if live(s - 1) and s - 1 not in GPSIMD_PC_STEPS:
                     invert(s - 1)
+                if s > 0:
+                    blend(s + 1, 0, 0)
+                if s % 2 == 1 and s > 1:
+                    blend(s + 1, 0, 1)
+                x_quantize(s + 2)
+                if s == 0:
+                    wv_quantize()
+                    rnd_scale_by_gpsimd(7)
                 if s % 2 == 0 and s > 0:
                     v_quantize(s // 2 - 1)
-                if stores and s % PAIRS == 0:
+                if s > 1:
+                    x_turn(s + 3)
+                if stores:
                     product(*stores[0], 2)
                 if s > 0:
                     v_product(*late[0], other_bank)
@@ -463,18 +516,20 @@ def tile_mixturedenserandomsynthesizer_t_kernel(tc, x_bytes, x_scale, w, rnd, mi
                     rnd_scale(3)
                     for k in range(3):
                         v_product(0, k, 1 + k)
-                else:
+                elif s == 1:
                     x_scaled(s + 3)
-                    if stores:
-                        product(*stores[1], this_bank)
                     x_turn(s + 3)
+                if stores:
+                    product(*stores[1], this_bank)
                 gain(s)
+                if live(s - 1) and s - 1 not in GPSIMD_PC_STEPS:
+                    normalise(s - 1, 0)
+                if s in GPSIMD_X_STEPS:
+                    if s > 1:
+                        x_widen(s + 4)
+                    x_scale_second(s + 4)
                 if stores:
                     store(*stores[0], by_scalar)
-                if live(s - 1):
-                    normalise(s - 1, 0)
-                if s > 0:
-                    x_copy_out(s + 3)
                 if s == 0:
                     blend(1, 0, 0)
                     blend(1, 0, 1)
@@ -484,38 +539,53 @@ def tile_mixturedenserandomsynthesizer_t_kernel(tc, x_bytes, x_scale, w, rnd, mi
                     blend(1, 1, 1)
                     late = late[2:]
                 else:
-                    blends(s + 1)
+                    if s % 2 == 0 or s == 1:
+                        blend(s + 1, 0, 1)
+                    blend(s + 1, 1, 0)
+                    if s > 1:
+                        x_scale_out(s + 3, FIRST if split else BOTH)
+                    if s == 1 or split:
+                        x_copy_out(s + 3, SECOND if split else BOTH)
+                    blend(s + 1, 1, 1)
                 for j in range(2):
                     for g in range(HALVES):
                         score(s + 2, j, g)
+                if stores and s % 2 == 1:
+                    store(*stores[1], by_scalar)
                 if live(s - 1):
                     turn(s - 1, 0, 2)
+                if s % 2 == 1 or not stores:
+                    v_product(*v_quarters(s + 1)[0][0], this_bank)
+                if live(s - 1):
                     normalise(s - 1, 1)
                     turn(s - 1, 1, 0)
-                if stores:
+                if stores and s % 2 == 0:
                     store(*stores[1], by_scalar)
-                for hh, n in v_quarters(s + 1)[0]:
-                    v_product(hh, n, this_bank)
+                    v_product(*v_quarters(s + 1)[0][0], this_bank)
+                if s + 1 in GPSIMD_PC_STEPS and live(s + 5):
+                    x_widen(s + 5)
                 for hh, n in late:
                     v_gain(hh, n)
+                if s in GPSIMD_PC_STEPS:
+                    invert(s)
+                    normalise(s, 0)
                 maximum(s + 1)
                 if live(s - 1):
-                    turn_out(s - 1, 1, by_scalar)
                     turn_out(s - 1, 0, by_scalar)
-                if (s + 1) % PAIRS > 0:
-                    for q, j in stores_of(s + 1)[:1]:
-                        product(q, j, 2)
+                    turn_out(s - 1, 1, by_scalar)
                 if s == 0:
-                    for r in range(4, 2 * PAIRS):
+                    for r in (4, 5):
                         rnd_scale(r)
+                    x_widen(5)
 
             x, y, z, a, b, c3, d = range(N_PAIRS - 7, N_PAIRS)
             last = B * HALVES - 1
             exponent(b, 0)
             exponent(b, 1)
             v_gain(last - 1, 3)
+            blend(c3, 0, 0)
             x_quantize(d)
-            invert(a)
+            product(x, 0, 2)
             v_product(last, 0, 1)
             v_product(last, 1, 0)
             product(x, 1, 3)
@@ -527,9 +597,10 @@ def tile_mixturedenserandomsynthesizer_t_kernel(tc, x_bytes, x_scale, w, rnd, mi
             product(y, 0, 2)
             v_gain(last, 0)
             v_product(last, 2, 1)
-            normalise(a, 0)
             store(x, 1, by_scalar)
-            blends(c3)
+            blend(c3, 0, 1)
+            blend(c3, 1, 0)
+            blend(c3, 1, 1)
             store(y, 0, by_scalar)
             score(d, 0, 0)
             turn(a, 0, 3)

@@ -25,11 +25,11 @@ AX = mybir.AxisListType
 
 FLOPS = 2 * B * S * D * S + 2 * B * S * D * D + 2 * B * S * S * D
 
-FIRST_VECTOR_TILE = 2 * N_PAIRS - 3
+FIRST_VECTOR_TILE = 2 * N_PAIRS - 2
 BOTH, FIRST, SECOND = slice(0, 2), slice(0, 1), slice(1, 2)
 CATCH_UP = N_PAIRS
 FIRST_SINGLE_STORE = N_PAIRS - 4
-GPSIMD_X_STEPS = (1, 2, 3, 5, 7, 9, 11)
+GPSIMD_X_STEPS = (0, 1, 2, 3, 5, 7, 9, 11)
 GPSIMD_PC_STEPS = (4, 6, 8, 10, 12, 13)
 SCORE_BANKS = 4
 SHARED_BANKS = 4
@@ -70,9 +70,9 @@ def tile_mixturedenserandomsynthesizer_t_kernel(tc, x_bytes, x_scale, w, rnd, mi
             x_raw[(b, h)] = keep.tile([P, PACK, D], U8, name="x_raw%d%d" % (b, h), align_bytes=64)
             nc.sync.dma_start(out=x_raw.get((b, h))[:], in_=x_rows[b, h])
 
-        def load_w(g):
-            w_raw[g] = keep.tile([P, PACK, BANK], BF16, name="w_raw%d" % g)
-            nc.sync.dma_start(out=w_raw[g][:], in_=w_rows[:, :, g * BANK : (g + 1) * BANK])
+        def load_w(n):
+            w_raw[n] = keep.tile([P, PACK, BANK], BF16, name="w_raw%d" % n)
+            nc.sync.dma_start(out=w_raw[n][:], in_=w_rows[:, :, n * BANK : (n + 1) * BANK])
 
         def load_rnd(k):
             rnd_raw[k] = keep.tile([P, 2, S], BF16, name="rnd_raw%d" % k)
@@ -102,7 +102,7 @@ def tile_mixturedenserandomsynthesizer_t_kernel(tc, x_bytes, x_scale, w, rnd, mi
         u_f = keep.tile([P, HALVES, PACK], F32, name="u_f")
         c_4 = keep.tile([P, HALVES * PACK], F32, name="c_4")
         c_f = keep.tile([P, 1, S], F32, name="c_f")
-        scale_row = keep.tile([P, 2, P, PACK], F32, name="scale_row")
+        scale_row = keep.tile([P, P, PACK], F32, name="scale_row")
         rnd_f = []
         for r in range(2 * PAIRS - 1):
             rnd_f.append(keep.tile([P, S], F32, name="rnd_f%d" % r))
@@ -145,9 +145,7 @@ def tile_mixturedenserandomsynthesizer_t_kernel(tc, x_bytes, x_scale, w, rnd, mi
 
         def scale_spread():
             bank = spread(scale_4[:], 3)
-            nc.scalar.copy(
-                out=scale_row[:], in_=bank[:].rearrange("p (o t) m -> p o m t", o=1).to_broadcast([P, 2, P, PACK])
-            )
+            nc.scalar.copy(out=scale_row[:], in_=bank[:].rearrange("p t m -> p m t"))
 
         def c_spread(g):
             bank = spread(c_4[:, g * PACK : (g + 1) * PACK], 2 + g)
@@ -158,9 +156,7 @@ def tile_mixturedenserandomsynthesizer_t_kernel(tc, x_bytes, x_scale, w, rnd, mi
 
         def w_group(g, copy):
             src = w_raw[g][:].rearrange("p j (m h e) -> p h m e j", h=2, e=2)
-            dst = w_grouped[g][:].rearrange("p (h m e) j -> p h m e j", h=2, e=2)
-            for h in range(2):
-                copy(out=dst[:, h], in_=src[:, h])
+            copy(out=w_grouped[g][:].rearrange("p (h m e) j -> p h m e j", h=2, e=2), in_=src)
 
         def w_quantize(g):
             quantize(w_codes[g][:], w_scales[g][:], w_grouped[g][:].rearrange("p n j -> p (n j)"))
@@ -205,13 +201,14 @@ def tile_mixturedenserandomsynthesizer_t_kernel(tc, x_bytes, x_scale, w, rnd, mi
 
         x_wide, x_turned, x_grouped, x_codes, x_scales = {}, {}, {}, {}, {}
 
-        def x_scaled(q):
-            b, h, t = q // PAIRS, (q % PAIRS) // 2, 2 * (q % 2)
-            x_wide[q] = work.tile([P, 2 * D], BF16, name="wide", bufs=3)
+        def x_scaled(q, j):
+            b, h, t = q // PAIRS, (q % PAIRS) // 2, 2 * (q % 2) + j
+            if j == 0:
+                x_wide[q] = work.tile([P, 2 * D], BF16, name="wide", bufs=3)
             nc.vector.tensor_tensor(
-                out=x_wide[q][:],
-                in0=x_raw.get((b, h))[:, t : t + 2, :].rearrange("p t k -> p (t k)").bitcast(FP8),
-                in1=scale_row[:].rearrange("p o m t -> p (o m t)"),
+                out=x_wide[q][:, j * D : (j + 1) * D],
+                in0=x_raw.get((b, h))[:, t, :].bitcast(FP8),
+                in1=scale_row[:].rearrange("p m t -> p (m t)"),
                 op=Alu.mult,
             )
 
@@ -226,7 +223,7 @@ def tile_mixturedenserandomsynthesizer_t_kernel(tc, x_bytes, x_scale, w, rnd, mi
             nc.gpsimd.tensor_tensor(
                 out=x_wide[q][:, D : 2 * D],
                 in0=x_wide[q][:, D : 2 * D],
-                in1=scale_row[:, 0].rearrange("p m t -> p (m t)"),
+                in1=scale_row[:].rearrange("p m t -> p (m t)"),
                 op=Alu.mult,
             )
 
@@ -442,33 +439,38 @@ def tile_mixturedenserandomsynthesizer_t_kernel(tc, x_bytes, x_scale, w, rnd, mi
 
         with tc.manual_schedule():
             scale_spread()
+            w_group(0, by_vector)
+            x_scaled(0, 0)
+            w_quantize(0)
             nc.vector.tensor_copy(out=mix_f[:], in_=mix_raw[:])
             nc.vector.tensor_copy(out=c_4[:], in_=c_raw[:].rearrange("p g t -> p (g t)"))
             nc.vector.tensor_copy(out=u_f[:], in_=u_raw[:])
-            w_group(0, by_vector)
-            x_scaled(0)
+            x_scaled(0, 1)
             x_turn(0)
             w_group(1, by_scalar)
-            w_quantize(0)
-            x_scaled(1)
+            x_scaled(1, 0)
+            x_scaled(1, 1)
             x_copy_out(0)
             x_turn(1, 1)
             rnd_scale(0)
-            x_scaled(2)
+            x_scaled(2, 0)
+            x_scaled(2, 1)
             x_quantize(0)
             score(0, 0, 0)
             score(0, 1, 0)
             x_copy_out(1)
             x_turn(2)
             rnd_scale(1)
-            x_scaled(3)
+            x_scaled(3, 0)
+            x_scaled(3, 1)
             x_quantize(1)
             w_quantize(1)
             wv_group()
-            rnd_scale_by_gpsimd(6)
+            rnd_scale_by_gpsimd(3)
             score(0, 0, 1)
             score(0, 1, 1)
             x_copy_out(2)
+            x_widen(4)
             x_turn(3, 1)
             for g in range(HALVES):
                 c_spread(g)
@@ -496,7 +498,7 @@ def tile_mixturedenserandomsynthesizer_t_kernel(tc, x_bytes, x_scale, w, rnd, mi
                     invert(s - 1)
                 if s > 0:
                     blend(s + 1, 0, 0)
-                if s % 2 == 1 and s > 1:
+                if s % 2 == 1 or s == 2:
                     blend(s + 1, 0, 1)
                 x_quantize(s + 2)
                 if s == 0:
@@ -504,7 +506,7 @@ def tile_mixturedenserandomsynthesizer_t_kernel(tc, x_bytes, x_scale, w, rnd, mi
                     rnd_scale_by_gpsimd(7)
                 if s % 2 == 0 and s > 0:
                     v_quantize(s // 2 - 1)
-                if s > 1:
+                if s > 0:
                     x_turn(s + 3)
                 if stores:
                     product(*stores[0], 2)
@@ -513,12 +515,8 @@ def tile_mixturedenserandomsynthesizer_t_kernel(tc, x_bytes, x_scale, w, rnd, mi
                 if live(s - 3):
                     p_quantize(s - 3)
                 if s == 0:
-                    rnd_scale(3)
                     for k in range(3):
                         v_product(0, k, 1 + k)
-                elif s == 1:
-                    x_scaled(s + 3)
-                    x_turn(s + 3)
                 if stores:
                     product(*stores[1], this_bank)
                 gain(s)
@@ -539,13 +537,12 @@ def tile_mixturedenserandomsynthesizer_t_kernel(tc, x_bytes, x_scale, w, rnd, mi
                     blend(1, 1, 1)
                     late = late[2:]
                 else:
-                    if s % 2 == 0 or s == 1:
+                    if s % 2 == 0 and s > 2:
                         blend(s + 1, 0, 1)
                     blend(s + 1, 1, 0)
-                    if s > 1:
-                        x_scale_out(s + 3, FIRST if split else BOTH)
-                    if s == 1 or split:
-                        x_copy_out(s + 3, SECOND if split else BOTH)
+                    x_scale_out(s + 3, FIRST if split else BOTH)
+                    if split:
+                        x_copy_out(s + 3, SECOND)
                     blend(s + 1, 1, 1)
                 for j in range(2):
                     for g in range(HALVES):
@@ -574,7 +571,7 @@ def tile_mixturedenserandomsynthesizer_t_kernel(tc, x_bytes, x_scale, w, rnd, mi
                     turn_out(s - 1, 0, by_scalar)
                     turn_out(s - 1, 1, by_scalar)
                 if s == 0:
-                    for r in (4, 5):
+                    for r in (4, 5, 6):
                         rnd_scale(r)
                     x_widen(5)
 
@@ -596,84 +593,82 @@ def tile_mixturedenserandomsynthesizer_t_kernel(tc, x_bytes, x_scale, w, rnd, mi
             store(x, 0, by_scalar)
             product(y, 0, 2)
             v_gain(last, 0)
-            v_product(last, 2, 1)
             store(x, 1, by_scalar)
+            product(y, 1, 3)
+            v_product(last, 2, 1)
+            normalise(a, 1)
+            v_gain(last, 1)
+            turn(a, 0, 0)
             blend(c3, 0, 1)
             blend(c3, 1, 0)
             blend(c3, 1, 1)
             store(y, 0, by_scalar)
+            turn(a, 1, 2)
+            store(y, 1, by_scalar)
             score(d, 0, 0)
-            turn(a, 0, 3)
-            normalise(a, 1)
             score(d, 0, 1)
+            product(z, 0, 3)
+            v_gain(last, 2)
+            invert(b)
+            normalise(b, 0)
+            turn_out(a, 0, by_scalar)
+            product(z, 1, 0)
+            v_product(last, 3, 1)
             score(d, 1, 0)
             score(d, 1, 1)
-            v_gain(last, 1)
-            product(y, 1, 0)
-            v_gain(last, 2)
-            turn(a, 1, 2)
-            v_product(last, 3, 1)
             maximum(c3)
-            turn_out(a, 0, by_scalar)
-            product(z, 0, 3)
-            store(y, 1, by_scalar)
             turn_out(a, 1, by_scalar)
-            product(z, 1, 0)
+            store(z, 0, by_scalar)
+            store(z, 1, by_scalar)
             exponent(c3, 0)
             exponent(c3, 1)
             v_gain(last, 3)
             p_quantize(a)
             v_quantize(last)
-            invert(b)
-            gain(c3, FIRST)
-            normalise(b, 0)
-            store(z, 0, by_scalar)
-            store(z, 1, by_scalar)
+            gain(c3)
+            turn(b, 0, 2)
+            product(a, 0, 1)
             normalise(b, 1)
-            blend(d, 0, 0)
-            blend(d, 0, 1)
+            turn(b, 1, 3)
+            blends(d)
             invert(c3)
-            blend(d, 1, 0)
-            blend(d, 1, 1)
-            turn(b, 1, 2)
-            normalise(c3, 0)
             maximum(d, FIRST)
             maximum(d, SECOND)
-            turn(b, 0, 0)
-            turn(c3, 0, 4)
+            product(a, 1, 0)
+            turn_out(b, 0, by_scalar)
+            turn_out(b, 1, by_scalar)
             exponent(d, 0)
             exponent(d, 1)
-            normalise(c3, 1)
-            product(a, 0, 1)
-            turn(c3, 1, 5)
-            product(a, 1, 3)
+            store(a, 0, by_vector)
             invert(d, FIRST)
-            turn_out(b, 1, by_vector)
-            normalise(d, 0)
-            turn(d, 0, 6)
-            turn_out(b, 0, by_scalar)
-            turn_out(c3, 0, by_scalar)
-            invert(d, SECOND)
             p_quantize(b)
-            product(b, 0, 0)
-            turn_out(c3, 1, by_scalar)
-            store(a, 0, by_scalar)
+            product(b, 0, 2)
+            normalise(d, 0)
+            normalise(c3, 0)
+            turn(d, 0, 4)
+            turn(c3, 0, 5)
+            product(b, 1, 3)
+            invert(d, SECOND)
+            store(a, 1, by_vector)
             normalise(d, 1)
-            product(b, 1, 2)
-            turn(d, 1, 7)
+            normalise(c3, 1)
+            turn(c3, 1, 7)
+            turn(d, 1, 6)
             turn_out(d, 0, by_scalar)
-            store(a, 1, by_scalar)
-            p_quantize(c3)
+            turn_out(c3, 0, by_scalar)
+            p_quantize(d, FIRST)
+            product(d, 0, 0)
+            store(b, 0, by_vector)
+            store(b, 1, by_vector)
+            turn_out(c3, 1, by_scalar)
+            p_quantize(c3, FIRST)
             product(c3, 0, 1)
             turn_out(d, 1, by_scalar)
-            p_quantize(d, FIRST)
-            product(c3, 1, 3)
-            product(d, 0, 4)
-            store(b, 0, by_vector)
+            p_quantize(c3, SECOND)
+            product(c3, 1, 4)
+            store(d, 0, by_scalar)
             p_quantize(d, SECOND)
-            product(d, 1, 5)
-            store(b, 1, by_scalar)
-            store(c3, 0, by_vector)
-            store(c3, 1, by_scalar)
-            store(d, 0, by_vector)
+            product(d, 1, 2)
+            store(c3, 0, by_scalar)
+            store(c3, 1, by_vector)
             store(d, 1, by_scalar)

@@ -52,13 +52,9 @@ def tile_mixturedenserandomsynthesizer_t_kernel(tc, x_bytes, x_scale, w, rnd, mi
             return psum.tile([P, PACK, P], F32, name=name)
 
         scale_4 = keep.tile([P, PACK], F32, name="scale_4")
-        nc.scalar.dma_start(out=scale_4[:], in_=x_scale.rearrange("a b (p t) -> p (a b t)", t=PACK))
         mix_raw = keep.tile([P, 2], BF16, name="mix_raw")
-        nc.scalar.dma_start(out=mix_raw[:], in_=mix.partition_broadcast(P))
         c_raw = keep.tile([P, HALVES, PACK], BF16, name="c_raw")
-        nc.scalar.dma_start(out=c_raw[:], in_=c.rearrange("(g p t) -> p g t", p=P, t=PACK))
         u_raw = keep.tile([P, HALVES, PACK], BF16, name="u_raw")
-        nc.scalar.dma_start(out=u_raw[:], in_=u.rearrange("(h p t) -> p h t", p=P, t=PACK))
 
         x_rows = x_bytes.rearrange("b (h m t) k -> b h m t k", m=P, t=PACK)
         rnd_rows = rnd.rearrange("(h m t) k -> h m t k", m=P, t=PACK)
@@ -78,14 +74,18 @@ def tile_mixturedenserandomsynthesizer_t_kernel(tc, x_bytes, x_scale, w, rnd, mi
             rnd_raw[k] = keep.tile([P, 2, S], BF16, name="rnd_raw%d" % k)
             nc.sync.dma_start(out=rnd_raw[k][:], in_=rnd_rows[k // 2, :, 2 * (k % 2) : 2 * (k % 2) + 2])
 
+        nc.sync.dma_start(out=scale_4[:], in_=x_scale.rearrange("a b (p t) -> p (a b t)", t=PACK))
         load_w(0)
         load_x(0, 0)
         load_w(1)
+        nc.sync.dma_start(out=mix_raw[:], in_=mix.partition_broadcast(P))
         load_rnd(0)
         load_x(0, 1)
         nc.sync.dma_start(out=wv_raw[:], in_=wv.rearrange("(p j) n -> p j n", j=PACK))
-        load_rnd(1)
+        nc.sync.dma_start(out=c_raw[:], in_=c.rearrange("(g p t) -> p g t", p=P, t=PACK))
         load_x(1, 0)
+        load_rnd(1)
+        nc.sync.dma_start(out=u_raw[:], in_=u.rearrange("(h p t) -> p h t", p=P, t=PACK))
         load_rnd(2)
         load_rnd(3)
         load_x(1, 1)
@@ -442,14 +442,12 @@ def tile_mixturedenserandomsynthesizer_t_kernel(tc, x_bytes, x_scale, w, rnd, mi
             w_group(0, by_vector)
             x_scaled(0, 0)
             w_quantize(0)
-            nc.vector.tensor_copy(out=mix_f[:], in_=mix_raw[:])
-            nc.vector.tensor_copy(out=c_4[:], in_=c_raw[:].rearrange("p g t -> p (g t)"))
-            nc.vector.tensor_copy(out=u_f[:], in_=u_raw[:])
             x_scaled(0, 1)
             x_turn(0)
             w_group(1, by_scalar)
             x_scaled(1, 0)
             x_scaled(1, 1)
+            nc.scalar.copy(out=mix_f[:], in_=mix_raw[:])
             x_copy_out(0)
             x_turn(1, 1)
             rnd_scale(0)
@@ -461,6 +459,7 @@ def tile_mixturedenserandomsynthesizer_t_kernel(tc, x_bytes, x_scale, w, rnd, mi
             x_copy_out(1)
             x_turn(2)
             rnd_scale(1)
+            nc.scalar.copy(out=c_4[:], in_=c_raw[:].rearrange("p g t -> p (g t)"))
             x_scaled(3, 0)
             x_scaled(3, 1)
             x_quantize(1)
@@ -483,6 +482,7 @@ def tile_mixturedenserandomsynthesizer_t_kernel(tc, x_bytes, x_scale, w, rnd, mi
             maximum(0, FIRST)
             maximum(0, SECOND)
             x_copy_out(3)
+            nc.scalar.copy(out=u_f[:], in_=u_raw[:])
             rnd_scale(2)
 
             for s in range(N_PAIRS - 3):

@@ -25,14 +25,21 @@ AX = mybir.AxisListType
 
 FLOPS = 2 * B * S * D * S + 2 * B * S * D * D + 2 * B * S * S * D
 
-FIRST_VECTOR_TILE = 2 * N_PAIRS - 2
 BOTH, FIRST, SECOND = slice(0, 2), slice(0, 1), slice(1, 2)
-CATCH_UP = N_PAIRS
-FIRST_SINGLE_STORE = N_PAIRS - 4
-GPSIMD_X_STEPS = (0, 1, 2, 3, 5, 7, 9, 11)
-GPSIMD_PC_STEPS = (4, 6, 8, 10, 12, 13)
+
 SCORE_BANKS = 4
 SHARED_BANKS = 4
+
+STORE_LAG = 4
+
+X_LEAD = 4
+
+GPSIMD_X_STEPS = [s for s in range(N_PAIRS - X_LEAD) if s < STORE_LAG or s % 2 == 1]
+GPSIMD_PC_STEPS = [s for s in range(N_PAIRS - 2) if s not in GPSIMD_X_STEPS]
+
+WIDE_BUFS = 3
+
+FIRST_TILEWISE_PAIR = N_PAIRS - 4
 
 
 def tile_mixturedenserandomsynthesizer_t_kernel(tc, x_bytes, x_scale, w, rnd, mix, wv, c, u, out):
@@ -41,11 +48,6 @@ def tile_mixturedenserandomsynthesizer_t_kernel(tc, x_bytes, x_scale, w, rnd, mi
         keep = ctx.enter_context(tc.tile_pool(name="keep", bufs=1))
         work = ctx.enter_context(tc.tile_pool(name="work", bufs=2))
         psum = ctx.enter_context(tc.psum_pool(name="psum", bufs=1))
-        score_count = []
-
-        def score_bank():
-            score_count.append(0)
-            return psum.tile([P, BANK], F32, name="score%d" % (len(score_count) % SCORE_BANKS))
 
         def shared_bank(k):
             name = "shared%d" % k if k < SHARED_BANKS else "score%d" % (k - SHARED_BANKS)
@@ -66,9 +68,9 @@ def tile_mixturedenserandomsynthesizer_t_kernel(tc, x_bytes, x_scale, w, rnd, mi
             x_raw[(b, h)] = keep.tile([P, PACK, D], U8, name="x_raw%d%d" % (b, h), align_bytes=64)
             nc.sync.dma_start(out=x_raw.get((b, h))[:], in_=x_rows[b, h])
 
-        def load_w(n):
-            w_raw[n] = keep.tile([P, PACK, BANK], BF16, name="w_raw%d" % n)
-            nc.sync.dma_start(out=w_raw[n][:], in_=w_rows[:, :, n * BANK : (n + 1) * BANK])
+        def load_w(g):
+            w_raw[g] = keep.tile([P, PACK, BANK], BF16, name="w_raw%d" % g)
+            nc.sync.dma_start(out=w_raw[g][:], in_=w_rows[:, :, g * BANK : (g + 1) * BANK])
 
         def load_rnd(k):
             rnd_raw[k] = keep.tile([P, 2, S], BF16, name="rnd_raw%d" % k)
@@ -111,7 +113,7 @@ def tile_mixturedenserandomsynthesizer_t_kernel(tc, x_bytes, x_scale, w, rnd, mi
             w_grouped.append(keep.tile([P, BANK, PACK], BF16, name="w_grouped%d" % g, align_bytes=64))
             w_codes.append(keep.tile([P, BANK], U32, name="w_codes%d" % g, align_bytes=64))
             w_scales.append(keep.tile([P, BANK], U8, name="w_scales%d" % g, align_bytes=64))
-        grouped = {}
+        wv_grouped = []
         wv_codes = keep.tile([P, D], U32, name="wv_codes", align_bytes=64)
         wv_scales = keep.tile([P, D], U8, name="wv_scales", align_bytes=64)
 
@@ -162,9 +164,9 @@ def tile_mixturedenserandomsynthesizer_t_kernel(tc, x_bytes, x_scale, w, rnd, mi
             quantize(w_codes[g][:], w_scales[g][:], w_grouped[g][:].rearrange("p n j -> p (n j)"))
 
         def wv_group():
-            grouped["wv"] = keep.tile([P, BANK, PACK], BF16, name="w_grouped1", align_bytes=64)
+            wv_grouped.append(keep.tile([P, D, PACK], BF16, name="w_grouped1", align_bytes=64))
             nc.gpsimd.tensor_scalar(
-                out=grouped.get("wv")[:],
+                out=wv_grouped[0][:],
                 in0=wv_raw[:].rearrange("p j n -> p n j"),
                 scalar1=1.0,
                 scalar2=0.0,
@@ -173,7 +175,7 @@ def tile_mixturedenserandomsynthesizer_t_kernel(tc, x_bytes, x_scale, w, rnd, mi
             )
 
         def wv_quantize():
-            quantize(wv_codes[:], wv_scales[:], grouped.get("wv")[:].rearrange("p n j -> p (n j)"))
+            quantize(wv_codes[:], wv_scales[:], wv_grouped[0][:].rearrange("p n j -> p (n j)"))
 
         def rnd_scale(r):
             for g in range(HALVES):
@@ -204,7 +206,7 @@ def tile_mixturedenserandomsynthesizer_t_kernel(tc, x_bytes, x_scale, w, rnd, mi
         def x_scaled(q, j):
             b, h, t = q // PAIRS, (q % PAIRS) // 2, 2 * (q % 2) + j
             if j == 0:
-                x_wide[q] = work.tile([P, 2 * D], BF16, name="wide", bufs=3)
+                x_wide[q] = work.tile([P, 2 * D], BF16, name="wide", bufs=WIDE_BUFS)
             nc.vector.tensor_tensor(
                 out=x_wide[q][:, j * D : (j + 1) * D],
                 in0=x_raw.get((b, h))[:, t, :].bitcast(FP8),
@@ -214,7 +216,7 @@ def tile_mixturedenserandomsynthesizer_t_kernel(tc, x_bytes, x_scale, w, rnd, mi
 
         def x_widen(q):
             b, h, t = q // PAIRS, (q % PAIRS) // 2, 2 * (q % 2)
-            x_wide[q] = work.tile([P, 2 * D], BF16, name="wide", bufs=3)
+            x_wide[q] = work.tile([P, 2 * D], BF16, name="wide", bufs=WIDE_BUFS)
             nc.scalar.copy(
                 out=x_wide[q][:], in_=x_raw.get((b, h))[:, t : t + 2, :].rearrange("p t k -> p (t k)").bitcast(FP8)
             )
@@ -227,14 +229,14 @@ def tile_mixturedenserandomsynthesizer_t_kernel(tc, x_bytes, x_scale, w, rnd, mi
                 op=Alu.mult,
             )
 
-        def x_turn(q, k=0):
+        def x_turn(q, k):
             words = x_wide[q][:].bitcast(F32)
             x_turned[q] = shared_bank(k)
-            x_grouped[q] = work.tile([P, 2, P, PACK], BF16, name="x_grouped", bufs=3, align_bytes=64)
+            x_grouped[q] = work.tile([P, 2, P, PACK], BF16, name="x_grouped", bufs=WIDE_BUFS, align_bytes=64)
             for j in range(2):
                 for h in range(2):
                     nc.tensor.transpose(
-                        x_turned[q][:, 2 * h + j, :], words[:, 256 * j + h : 256 * (j + 1) : 2], ident[:]
+                        x_turned[q][:, 2 * h + j, :], words[:, 2 * P * j + h : 2 * P * (j + 1) : 2], ident[:]
                     )
 
         def x_copy_out(q, tiles=BOTH):
@@ -294,7 +296,7 @@ def tile_mixturedenserandomsynthesizer_t_kernel(tc, x_bytes, x_scale, w, rnd, mi
 
         def score(q, j, g):
             rows = slice(j * P, (j + 1) * P)
-            bank = score_bank()
+            bank = psum.tile([P, BANK], F32, name="score%d" % (HALVES * j + g))
             multiply(bank[:], x_codes[q][:, rows], x_scales[q][:, rows], w_codes[g][:], w_scales[g][:], True, True)
             scores[(q, j, g)] = bank
 
@@ -335,19 +337,16 @@ def tile_mixturedenserandomsynthesizer_t_kernel(tc, x_bytes, x_scale, w, rnd, mi
                 inverses[q] = work.tile([P, 2], F32, name="inverse")
             nc.vector.reciprocal(out=inverses[q][:, tiles], in_=totals[q][:, tiles])
 
-        def gain(q, tiles=BOTH):
+        def gain(q):
             gained[q] = work.tile([P, 2, S], F32, name="gained")
             nc.gpsimd.tensor_tensor(
-                out=gained[q][:, tiles],
-                in0=exps[q][:, tiles],
-                in1=c_f[:].to_broadcast([P, tiles.stop - tiles.start, S]),
-                op=Alu.mult,
+                out=gained[q][:], in0=exps[q][:], in1=c_f[:].to_broadcast([P, 2, S]), op=Alu.mult
             )
 
         def normalise(q, j):
             if q not in pcs:
                 pcs[q] = work.tile([P, 2, S], BF16, name="pc")
-            if 2 * q + j >= FIRST_VECTOR_TILE:
+            if q == N_PAIRS - 1:
                 nc.vector.scalar_tensor_tensor(
                     out=pcs[q][:, j],
                     in0=exps[q][:, j],
@@ -377,12 +376,12 @@ def tile_mixturedenserandomsynthesizer_t_kernel(tc, x_bytes, x_scale, w, rnd, mi
                 nc.tensor.transpose(bank[:, n, :], words[:, n * P : (n + 1) * P], ident[:])
             turned_pcs[(q, j)] = bank
 
-        def turn_out(q, j, copy):
+        def turn_out(q, j):
             if q not in grouped_pcs:
                 grouped_pcs[q] = work.tile(
                     [P, 2, HALVES, P, PACK], BF16, name="p_grouped", bufs=3, align_bytes=64
                 )
-            copy(
+            nc.scalar.copy(
                 out=grouped_pcs[q][:, j].bitcast(F32),
                 in_=turned_pcs.get((q, j))[:].rearrange("p (g h) q -> p g q h", h=2),
             )
@@ -412,30 +411,13 @@ def tile_mixturedenserandomsynthesizer_t_kernel(tc, x_bytes, x_scale, w, rnd, mi
             if q not in rows_out:
                 rows_out[q] = work.tile([P, 2, D], F32, name="rows_out", bufs=4)
             copy(out=rows_out[q][:, j], in_=sums_out.get((q, j))[:].rearrange("p t d -> p (t d)"))
-            if q >= FIRST_SINGLE_STORE:
+            if q >= FIRST_TILEWISE_PAIR:
                 nc.sync.dma_start(out=out_rows[b, h, :, t], in_=rows_out[q][:, j])
             elif j == 1:
                 nc.sync.dma_start(out=out_rows[b, h, :, t - 1 : t + 1], in_=rows_out[q][:])
 
-        def live(q):
-            return 0 <= q < N_PAIRS
-
         by_scalar, by_vector = nc.scalar.copy, nc.vector.tensor_copy
-
-        def blends(q):
-            for j in range(2):
-                for g in range(HALVES):
-                    blend(q, j, g)
-
-        def v_quarters(s):
-            if s == 0:
-                return [], [(0, 0), (0, 1), (0, 2)]
-            return [divmod(2 * s + 1, QUARTERS)], [divmod(2 * s + 2, QUARTERS)]
-
-        def stores_of(s):
-            first = 2 * (s - 4) + max(0, s - CATCH_UP)
-            count = 3 if s >= CATCH_UP else 2
-            return [divmod(i, 2) for i in range(first, first + count) if i >= 0]
+        in_order = [(j, g) for j in range(2) for g in range(HALVES)]
 
         with tc.manual_schedule():
             scale_spread()
@@ -443,232 +425,221 @@ def tile_mixturedenserandomsynthesizer_t_kernel(tc, x_bytes, x_scale, w, rnd, mi
             x_scaled(0, 0)
             w_quantize(0)
             x_scaled(0, 1)
-            x_turn(0)
+            x_turn(0, 0)
             w_group(1, by_scalar)
-            x_scaled(1, 0)
-            x_scaled(1, 1)
-            nc.scalar.copy(out=mix_f[:], in_=mix_raw[:])
-            x_copy_out(0)
-            x_turn(1, 1)
-            rnd_scale(0)
-            x_scaled(2, 0)
-            x_scaled(2, 1)
-            x_quantize(0)
-            score(0, 0, 0)
-            score(0, 1, 0)
-            x_copy_out(1)
-            x_turn(2)
-            rnd_scale(1)
-            nc.scalar.copy(out=c_4[:], in_=c_raw[:].rearrange("p g t -> p (g t)"))
-            x_scaled(3, 0)
-            x_scaled(3, 1)
-            x_quantize(1)
+            by_scalar(out=mix_f[:], in_=mix_raw[:])
+            for q in range(1, X_LEAD):
+                x_scaled(q, 0)
+                x_scaled(q, 1)
+                if q > 1:
+                    x_quantize(q - 2)
+                if q == 2:
+                    score(0, 0, 0)
+                    score(0, 1, 0)
+                if q < X_LEAD - 1:
+                    x_copy_out(q - 1)
+                    x_turn(q, q % 2)
+                    rnd_scale(q - 1)
+            by_scalar(out=c_4[:], in_=c_raw[:].rearrange("p g t -> p (g t)"))
             w_quantize(1)
             wv_group()
             rnd_scale_by_gpsimd(3)
             score(0, 0, 1)
             score(0, 1, 1)
             x_copy_out(2)
-            x_widen(4)
+            x_widen(X_LEAD)
             x_turn(3, 1)
             for g in range(HALVES):
                 c_spread(g)
             for g in range(HALVES):
                 for j in range(2):
                     blend(0, j, g)
-            for j in range(2):
-                for g in range(HALVES):
-                    score(1, j, g)
+            for j, g in in_order:
+                score(1, j, g)
             maximum(0, FIRST)
             maximum(0, SECOND)
             x_copy_out(3)
-            nc.scalar.copy(out=u_f[:], in_=u_raw[:])
+            by_scalar(out=u_f[:], in_=u_raw[:])
             rnd_scale(2)
 
-            for s in range(N_PAIRS - 3):
-                early, late = v_quarters(s)
-                stores = stores_of(s)
+            exponent(0, 0)
+            exponent(0, 1)
+            x_quantize(2)
+            wv_quantize()
+            rnd_scale_by_gpsimd(2 * PAIRS - 1)
+            for n in range(3):
+                v_product(0, n, 1 + n)
+            gain(0)
+            x_scale_second(X_LEAD)
+            for j in range(2):
+                blend(1, j, 0)
+                blend(1, j, 1)
+                v_gain(0, 2 * j)
+                if j == 0:
+                    v_gain(0, 1)
+            for j, g in in_order:
+                score(2, j, g)
+            v_product(0, 3, 1)
+            maximum(1)
+            for r in range(4, 2 * PAIRS - 1):
+                rnd_scale(r)
+            x_widen(X_LEAD + 1)
+
+            for s in range(1, N_PAIRS - 3):
+                opening, closing = divmod(2 * s + 1, QUARTERS), divmod(2 * s + 2, QUARTERS)
+                next_opening = divmod(2 * s + 3, QUARTERS)
                 this_bank, other_bank = 1 + 2 * (s % 2), 3 - 2 * (s % 2)
+                stored = s - STORE_LAG
                 split = s - 1 in GPSIMD_X_STEPS
+                ahead = 1 if s % 2 == 0 and s >= 3 else 2
+
                 exponent(s, 0)
                 exponent(s, 1)
-                for hh, n in early:
-                    v_gain(hh, n)
-                if live(s - 1) and s - 1 not in GPSIMD_PC_STEPS:
+                v_gain(*opening)
+                if split:
                     invert(s - 1)
-                if s > 0:
-                    blend(s + 1, 0, 0)
-                if s % 2 == 1 or s == 2:
-                    blend(s + 1, 0, 1)
+                for j, g in in_order[:ahead]:
+                    blend(s + 1, j, g)
                 x_quantize(s + 2)
-                if s == 0:
-                    wv_quantize()
-                    rnd_scale_by_gpsimd(7)
-                if s % 2 == 0 and s > 0:
+                if s % 2 == 0:
                     v_quantize(s // 2 - 1)
-                if s > 0:
-                    x_turn(s + 3)
-                if stores:
-                    product(*stores[0], 2)
-                if s > 0:
-                    v_product(*late[0], other_bank)
-                if live(s - 3):
+                x_turn(s + 3, 0)
+                if stored >= 0 and stored % PAIRS == 0:
+                    product(stored, 0, 2)
+                v_product(*closing, other_bank)
+                if s >= 3:
                     p_quantize(s - 3)
-                if s == 0:
-                    for k in range(3):
-                        v_product(0, k, 1 + k)
-                if stores:
-                    product(*stores[1], this_bank)
+                if stored >= 0:
+                    product(stored, 1, this_bank)
                 gain(s)
-                if live(s - 1) and s - 1 not in GPSIMD_PC_STEPS:
+                if split:
                     normalise(s - 1, 0)
                 if s in GPSIMD_X_STEPS:
                     if s > 1:
-                        x_widen(s + 4)
-                    x_scale_second(s + 4)
-                if stores:
-                    store(*stores[0], by_scalar)
-                if s == 0:
-                    blend(1, 0, 0)
-                    blend(1, 0, 1)
-                    v_gain(0, 0)
-                    v_gain(0, 1)
-                    blend(1, 1, 0)
-                    blend(1, 1, 1)
-                    late = late[2:]
-                else:
-                    if s % 2 == 0 and s > 2:
-                        blend(s + 1, 0, 1)
-                    blend(s + 1, 1, 0)
-                    x_scale_out(s + 3, FIRST if split else BOTH)
-                    if split:
-                        x_copy_out(s + 3, SECOND)
-                    blend(s + 1, 1, 1)
-                for j in range(2):
-                    for g in range(HALVES):
-                        score(s + 2, j, g)
-                if stores and s % 2 == 1:
-                    store(*stores[1], by_scalar)
-                if live(s - 1):
-                    turn(s - 1, 0, 2)
-                if s % 2 == 1 or not stores:
-                    v_product(*v_quarters(s + 1)[0][0], this_bank)
-                if live(s - 1):
-                    normalise(s - 1, 1)
-                    turn(s - 1, 1, 0)
-                if stores and s % 2 == 0:
-                    store(*stores[1], by_scalar)
-                    v_product(*v_quarters(s + 1)[0][0], this_bank)
-                if s + 1 in GPSIMD_PC_STEPS and live(s + 5):
-                    x_widen(s + 5)
-                for hh, n in late:
-                    v_gain(hh, n)
+                        x_widen(s + X_LEAD)
+                    x_scale_second(s + X_LEAD)
+                if stored >= 0:
+                    store(stored, 0, by_scalar)
+                for j, g in in_order[ahead:3]:
+                    blend(s + 1, j, g)
+                x_scale_out(s + 3, FIRST if split else BOTH)
+                if split:
+                    x_copy_out(s + 3, SECOND)
+                blend(s + 1, 1, 1)
+                score(s + 2, 0, 0)
+                score(s + 2, 0, 1)
+                turn(s - 1, 0, 2)
+                score(s + 2, 1, 0)
+                score(s + 2, 1, 1)
+                if stored >= 0 and s % 2 == 1:
+                    store(stored, 1, by_scalar)
+                if stored < 0 or s % 2 == 1:
+                    v_product(*next_opening, this_bank)
+                normalise(s - 1, 1)
+                turn(s - 1, 1, 0)
+                if stored >= 0 and s % 2 == 0:
+                    store(stored, 1, by_scalar)
+                    v_product(*next_opening, this_bank)
+                if s + 1 in GPSIMD_PC_STEPS and s + 1 + X_LEAD < N_PAIRS:
+                    x_widen(s + 1 + X_LEAD)
+                v_gain(*closing)
                 if s in GPSIMD_PC_STEPS:
                     invert(s)
                     normalise(s, 0)
                 maximum(s + 1)
-                if live(s - 1):
-                    turn_out(s - 1, 0, by_scalar)
-                    turn_out(s - 1, 1, by_scalar)
-                if s == 0:
-                    for r in (4, 5, 6):
-                        rnd_scale(r)
-                    x_widen(5)
+                turn_out(s - 1, 0)
+                if stored + 1 >= 0 and (stored + 1) % PAIRS > 0:
+                    product(stored + 1, 0, 2)
+                turn_out(s - 1, 1)
 
-            x, y, z, a, b, c3, d = range(N_PAIRS - 7, N_PAIRS)
-            last = B * HALVES - 1
-            exponent(b, 0)
-            exponent(b, 1)
-            v_gain(last - 1, 3)
-            blend(c3, 0, 0)
-            x_quantize(d)
-            product(x, 0, 2)
-            v_product(last, 0, 1)
-            v_product(last, 1, 0)
-            product(x, 1, 3)
-            p_quantize(y)
-            v_quantize(last - 1)
-            p_quantize(z)
-            gain(b)
-            store(x, 0, by_scalar)
-            product(y, 0, 2)
-            v_gain(last, 0)
-            store(x, 1, by_scalar)
-            product(y, 1, 3)
-            v_product(last, 2, 1)
-            normalise(a, 1)
-            v_gain(last, 1)
-            turn(a, 0, 0)
-            blend(c3, 0, 1)
-            blend(c3, 1, 0)
-            blend(c3, 1, 1)
-            store(y, 0, by_scalar)
-            turn(a, 1, 2)
-            store(y, 1, by_scalar)
-            score(d, 0, 0)
-            score(d, 0, 1)
-            product(z, 0, 3)
-            v_gain(last, 2)
-            invert(b)
-            normalise(b, 0)
-            turn_out(a, 0, by_scalar)
-            product(z, 1, 0)
-            v_product(last, 3, 1)
-            score(d, 1, 0)
-            score(d, 1, 1)
-            maximum(c3)
-            turn_out(a, 1, by_scalar)
-            store(z, 0, by_scalar)
-            store(z, 1, by_scalar)
-            exponent(c3, 0)
-            exponent(c3, 1)
-            v_gain(last, 3)
-            p_quantize(a)
-            v_quantize(last)
-            gain(c3)
-            turn(b, 0, 2)
-            product(a, 0, 1)
-            normalise(b, 1)
-            turn(b, 1, 3)
-            blends(d)
-            invert(c3)
-            maximum(d, FIRST)
-            maximum(d, SECOND)
-            product(a, 1, 0)
-            turn_out(b, 0, by_scalar)
-            turn_out(b, 1, by_scalar)
-            exponent(d, 0)
-            exponent(d, 1)
-            store(a, 0, by_vector)
-            invert(d, FIRST)
-            p_quantize(b)
-            product(b, 0, 2)
-            normalise(d, 0)
-            normalise(c3, 0)
-            turn(d, 0, 4)
-            turn(c3, 0, 5)
-            product(b, 1, 3)
-            invert(d, SECOND)
-            store(a, 1, by_vector)
-            normalise(d, 1)
-            normalise(c3, 1)
-            turn(c3, 1, 7)
-            turn(d, 1, 6)
-            turn_out(d, 0, by_scalar)
-            turn_out(c3, 0, by_scalar)
-            p_quantize(d, FIRST)
-            product(d, 0, 0)
-            store(b, 0, by_vector)
-            store(b, 1, by_vector)
-            turn_out(c3, 1, by_scalar)
-            p_quantize(c3, FIRST)
-            product(c3, 0, 1)
-            turn_out(d, 1, by_scalar)
-            p_quantize(c3, SECOND)
-            product(c3, 1, 4)
-            store(d, 0, by_scalar)
-            p_quantize(d, SECOND)
-            product(d, 1, 2)
-            store(c3, 0, by_scalar)
-            store(c3, 1, by_vector)
-            store(d, 1, by_scalar)
+            s = N_PAIRS - 3
+            last_half = B * HALVES - 1
+            exponent(s, 0)
+            exponent(s, 1)
+            v_gain(last_half - 1, 3)
+            blend(s + 1, 0, 0)
+            x_quantize(s + 2)
+            v_product(last_half, 0, 1)
+            v_product(last_half, 1, 0)
+            product(s - 4, 1, 3)
+            p_quantize(s - 3)
+            v_quantize(last_half - 1)
+            p_quantize(s - 2)
+            gain(s)
+            for j in range(2):
+                store(s - 4, j, by_scalar)
+                product(s - 3, j, 2 + j)
+                v_gain(last_half, j)
+            v_product(last_half, 2, 1)
+            normalise(s - 1, 1)
+            turn(s - 1, 0, 0)
+            for j, g in in_order[1:]:
+                blend(s + 1, j, g)
+            store(s - 3, 0, by_scalar)
+            turn(s - 1, 1, 2)
+            store(s - 3, 1, by_scalar)
+            score(s + 2, 0, 0)
+            score(s + 2, 0, 1)
+            product(s - 2, 0, 3)
+            v_gain(last_half, 2)
+            invert(s)
+            normalise(s, 0)
+            turn_out(s - 1, 0)
+            product(s - 2, 1, 0)
+            v_product(last_half, 3, 1)
+            score(s + 2, 1, 0)
+            score(s + 2, 1, 1)
+            maximum(s + 1)
+            turn_out(s - 1, 1)
+            store(s - 2, 0, by_scalar)
+            store(s - 2, 1, by_scalar)
+
+            s = N_PAIRS - 2
+            exponent(s, 0)
+            exponent(s, 1)
+            v_gain(last_half, 3)
+            p_quantize(s - 2)
+            v_quantize(last_half)
+            gain(s)
+            turn(s - 1, 0, 2)
+            product(s - 2, 0, 1)
+            normalise(s - 1, 1)
+            turn(s - 1, 1, 3)
+            product(s - 2, 1, 0)
+            for j, g in in_order:
+                blend(s + 1, j, g)
+            invert(s)
+            for j, tile in enumerate((FIRST, SECOND)):
+                maximum(s + 1, tile)
+                turn_out(s - 1, j)
+
+            s = N_PAIRS - 1
+            exponent(s, 0)
+            exponent(s, 1)
+            store(s - 3, 0, by_vector)
+            invert(s, FIRST)
+            p_quantize(s - 2)
+            product(s - 2, 0, 2)
+            normalise(s, 0)
+            normalise(s - 1, 0)
+            turn(s, 0, 4)
+            turn(s - 1, 0, 5)
+            product(s - 2, 1, 3)
+            invert(s, SECOND)
+            store(s - 3, 1, by_vector)
+            normalise(s, 1)
+            normalise(s - 1, 1)
+            turn(s - 1, 1, 7)
+            turn(s, 1, 6)
+
+            last_tiles = [(s, 0), (s - 1, 0), (s - 1, 1), (s, 1)]
+            for q, j in last_tiles:
+                turn_out(q, j)
+            for (q, j), k in zip(last_tiles, (0, 1, 4, 2)):
+                p_quantize(q, (FIRST, SECOND)[j])
+                product(q, j, k)
+                if (q, j) == last_tiles[0]:
+                    store(s - 2, 0, by_vector)
+                    store(s - 2, 1, by_vector)
+            for (q, j), copy in zip(last_tiles, (by_scalar, by_scalar, by_vector, by_scalar)):
+                store(q, j, copy)

@@ -97,9 +97,6 @@ def tile_mixturedenserandomsynthesizer_t_kernel(tc, x_bytes, x_scale, w, rnd, mi
 
         ident = keep.tile([P, P], F32, name="ident")
         make_identity(nc, ident[:])
-        warm = keep.tile([P, 1], F32, name="warm")
-        nc.vector.memset(warm[:], 0.0)
-        nc.scalar.activation(out=warm[:], in_=warm[:], func=Act.Exp)
         mix_f = keep.tile([P, 2], F32, name="mix_f")
         u_f = keep.tile([P, HALVES, PACK], F32, name="u_f")
         c_4 = keep.tile([P, HALVES * PACK], F32, name="c_4")

@@ -54,7 +54,7 @@ def tile_mixturedenserandomsynthesizer_t_kernel(tc, x_bytes, x_scale, w, rnd, mi
             return psum.tile([P, PACK, P], F32, name=name)
 
         scale_4 = keep.tile([P, PACK], F32, name="scale_4")
-        mix_raw = keep.tile([P, 2], BF16, name="mix_raw")
+        mix_raw = keep.tile([2, 1], BF16, name="mix_raw")
         c_raw = keep.tile([P, HALVES, PACK], BF16, name="c_raw")
         u_raw = keep.tile([P, HALVES, PACK], BF16, name="u_raw")
 
@@ -79,8 +79,8 @@ def tile_mixturedenserandomsynthesizer_t_kernel(tc, x_bytes, x_scale, w, rnd, mi
         nc.sync.dma_start(out=scale_4[:], in_=x_scale.rearrange("a b (p t) -> p (a b t)", t=PACK))
         load_w(0)
         load_x(0, 0)
+        nc.sync.dma_start(out=mix_raw[:], in_=mix.rearrange("(p o) -> p o", o=1))
         load_w(1)
-        nc.sync.dma_start(out=mix_raw[:], in_=mix.partition_broadcast(P))
         load_rnd(0)
         load_x(0, 1)
         nc.sync.dma_start(out=wv_raw[:], in_=wv.rearrange("(p j) n -> p j n", j=PACK))
@@ -97,6 +97,8 @@ def tile_mixturedenserandomsynthesizer_t_kernel(tc, x_bytes, x_scale, w, rnd, mi
 
         ident = keep.tile([P, P], F32, name="ident")
         make_identity(nc, ident[:])
+        mix_column = keep.tile([P, 1], F32, name="mix_column")
+        nc.vector.memset(mix_column[:], 0.0)
         mix_f = keep.tile([P, 2], F32, name="mix_f")
         u_f = keep.tile([P, HALVES, PACK], F32, name="u_f")
         c_4 = keep.tile([P, HALVES * PACK], F32, name="c_4")
@@ -145,6 +147,11 @@ def tile_mixturedenserandomsynthesizer_t_kernel(tc, x_bytes, x_scale, w, rnd, mi
         def scale_spread():
             bank = spread(scale_4[:], 3)
             nc.scalar.copy(out=scale_row[:], in_=bank[:].rearrange("p t m -> p m t"))
+
+        def mix_spread():
+            bank = shared_bank(2)
+            nc.tensor.transpose(bank[:, 0, :], mix_column[:].to_broadcast([P, P]), ident[:])
+            nc.scalar.copy(out=mix_f[:], in_=bank[:, 0, 0:2])
 
         def c_spread(g):
             bank = spread(c_4[:, g * PACK : (g + 1) * PACK], 2 + g)
@@ -418,13 +425,14 @@ def tile_mixturedenserandomsynthesizer_t_kernel(tc, x_bytes, x_scale, w, rnd, mi
 
         with tc.manual_schedule():
             scale_spread()
+            by_scalar(out=mix_column[0:2], in_=mix_raw[:])
             w_group(0, by_vector)
             x_scaled(0, 0)
             w_quantize(0)
             x_scaled(0, 1)
             x_turn(0, 0)
             w_group(1, by_scalar)
-            by_scalar(out=mix_f[:], in_=mix_raw[:])
+            mix_spread()
             for q in range(1, X_LEAD):
                 x_scaled(q, 0)
                 x_scaled(q, 1)

@@ -27,17 +27,12 @@ FLOPS = 2 * B * S * D * S + 2 * B * S * D * D + 2 * B * S * S * D
 
 BOTH, FIRST, SECOND = slice(0, 2), slice(0, 1), slice(1, 2)
 
-SCORE_BANKS = 4
-SHARED_BANKS = 4
+LOGIT_BANK, RING_BANK, OUT_BANK, V_BANK, X_BANK = 0, 2, 4, 6, 7
+RING_BANKS, RING_USES = 4, 6
 
-STORE_LAG = 4
+STORE_LAG = 3
 
-X_LEAD = 4
-
-GPSIMD_X_STEPS = [s for s in range(N_PAIRS - X_LEAD) if s < STORE_LAG or s % 2 == 1]
-GPSIMD_PC_STEPS = [s for s in range(N_PAIRS - 2) if s not in GPSIMD_X_STEPS]
-
-WIDE_BUFS = 3
+WIDE_BUFS = 2
 
 FIRST_TILEWISE_PAIR = N_PAIRS - 4
 
@@ -50,8 +45,7 @@ def tile_mixturedenserandomsynthesizer_t_kernel(tc, x_bytes, x_scale, w, rnd, mi
         psum = ctx.enter_context(tc.psum_pool(name="psum", bufs=1))
 
         def shared_bank(k):
-            name = "shared%d" % k if k < SHARED_BANKS else "score%d" % (k - SHARED_BANKS)
-            return psum.tile([P, PACK, P], F32, name=name)
+            return psum.tile([P, PACK, P], F32, name="bank%d" % k)
 
         scale_4 = keep.tile([P, PACK], F32, name="scale_4")
         mix_raw = keep.tile([2, 1], BF16, name="mix_raw")
@@ -77,18 +71,18 @@ def tile_mixturedenserandomsynthesizer_t_kernel(tc, x_bytes, x_scale, w, rnd, mi
             nc.sync.dma_start(out=rnd_raw[k][:], in_=rnd_rows[k // 2, :, 2 * (k % 2) : 2 * (k % 2) + 2])
 
         nc.sync.dma_start(out=scale_4[:], in_=x_scale.rearrange("a b (p t) -> p (a b t)", t=PACK))
-        load_w(0)
-        load_x(0, 0)
         nc.sync.dma_start(out=mix_raw[:], in_=mix.rearrange("(p o) -> p o", o=1))
+        load_x(0, 0)
+        load_w(0)
         load_w(1)
         load_rnd(0)
         load_x(0, 1)
         nc.sync.dma_start(out=wv_raw[:], in_=wv.rearrange("(p j) n -> p j n", j=PACK))
-        nc.sync.dma_start(out=c_raw[:], in_=c.rearrange("(g p t) -> p g t", p=P, t=PACK))
-        load_x(1, 0)
         load_rnd(1)
+        nc.sync.dma_start(out=c_raw[:], in_=c.rearrange("(g p t) -> p g t", p=P, t=PACK))
         nc.sync.dma_start(out=u_raw[:], in_=u.rearrange("(h p t) -> p h t", p=P, t=PACK))
         load_rnd(2)
+        load_x(1, 0)
         load_rnd(3)
         load_x(1, 1)
         for b in range(2, B):
@@ -103,13 +97,13 @@ def tile_mixturedenserandomsynthesizer_t_kernel(tc, x_bytes, x_scale, w, rnd, mi
         u_f = keep.tile([P, HALVES, PACK], F32, name="u_f")
         c_4 = keep.tile([P, HALVES * PACK], F32, name="c_4")
         c_f = keep.tile([P, 1, S], F32, name="c_f")
-        scale_row = keep.tile([P, P, PACK], F32, name="scale_row")
+        mix_diag = keep.tile([P, P], BF16, name="mix_diag")
         rnd_f = []
-        for r in range(2 * PAIRS - 1):
-            rnd_f.append(keep.tile([P, S], F32, name="rnd_f%d" % r))
+        for k in range(PAIRS):
+            rnd_f.append(keep.tile([P, S], F32, name="rnd_f%d" % k))
         w_grouped, w_codes, w_scales = [], [], []
         for g in range(HALVES):
-            w_grouped.append(keep.tile([P, BANK, PACK], BF16, name="w_grouped%d" % g, align_bytes=64))
+            w_grouped.append(keep.tile([P, BANK, PACK], BF16, name="gained%d" % (1 - g), align_bytes=64))
             w_codes.append(keep.tile([P, BANK], U32, name="w_codes%d" % g, align_bytes=64))
             w_scales.append(keep.tile([P, BANK], U8, name="w_scales%d" % g, align_bytes=64))
         wv_grouped = []
@@ -144,93 +138,63 @@ def tile_mixturedenserandomsynthesizer_t_kernel(tc, x_bytes, x_scale, w, rnd, mi
                 nc.tensor.transpose(bank[:, t, :], columns[:, t : t + 1].to_broadcast([P, P]), ident[:])
             return bank
 
-        def scale_spread():
-            bank = spread(scale_4[:], 3)
-            nc.scalar.copy(out=scale_row[:], in_=bank[:].rearrange("p t m -> p m t"))
-
         def mix_spread():
-            bank = shared_bank(2)
+            bank = shared_bank(OUT_BANK)
             nc.tensor.transpose(bank[:, 0, :], mix_column[:].to_broadcast([P, P]), ident[:])
             nc.scalar.copy(out=mix_f[:], in_=bank[:, 0, 0:2])
 
+        def mix_diagonal():
+            nc.gpsimd.tensor_scalar(
+                out=mix_diag[:], in0=ident[:], scalar1=mix_f[:, 1:2], scalar2=0.0, op0=Alu.mult, op1=Alu.add
+            )
+
         def c_spread(g):
-            bank = spread(c_4[:, g * PACK : (g + 1) * PACK], 2 + g)
+            bank = spread(c_4[:, g * PACK : (g + 1) * PACK], RING_BANK + 1 - g)
             nc.scalar.copy(
                 out=column_split(c_f[:, 0, g * BANK : (g + 1) * BANK]),
                 in_=bank[:].rearrange("p (h e) m -> p h m e", h=2),
             )
 
-        def w_group(g, copy):
+        def copy_by_gpsimd(out, in_):
+            nc.gpsimd.tensor_scalar(out=out, in0=in_, scalar1=1.0, scalar2=0.0, op0=Alu.mult, op1=Alu.add)
+
+        def w_group(g):
             src = w_raw[g][:].rearrange("p j (m h e) -> p h m e j", h=2, e=2)
-            copy(out=w_grouped[g][:].rearrange("p (h m e) j -> p h m e j", h=2, e=2), in_=src)
+            dst = w_grouped[g][:].rearrange("p (h m e) j -> p h m e j", h=2, e=2)
+            nc.scalar.copy(out=dst[:, 0], in_=src[:, 0])
+            copy_by_gpsimd(dst[:, 1], src[:, 1])
 
         def w_quantize(g):
             quantize(w_codes[g][:], w_scales[g][:], w_grouped[g][:].rearrange("p n j -> p (n j)"))
 
         def wv_group():
-            wv_grouped.append(keep.tile([P, D, PACK], BF16, name="w_grouped1", align_bytes=64))
-            nc.gpsimd.tensor_scalar(
-                out=wv_grouped[0][:],
-                in0=wv_raw[:].rearrange("p j n -> p n j"),
-                scalar1=1.0,
-                scalar2=0.0,
-                op0=Alu.mult,
-                op1=Alu.add,
-            )
+            wv_grouped.append(keep.tile([P, D, PACK], BF16, name="gained0", align_bytes=64))
+            copy_by_gpsimd(wv_grouped[0][:], wv_raw[:].rearrange("p j n -> p n j"))
 
         def wv_quantize():
             quantize(wv_codes[:], wv_scales[:], wv_grouped[0][:].rearrange("p n j -> p (n j)"))
 
-        def rnd_scale(r):
-            for g in range(HALVES):
-                cols = slice(g * BANK, (g + 1) * BANK)
-                nc.scalar.activation(
-                    out=column_split(rnd_f[r][:, cols]),
-                    in_=key_split(rnd_raw[r // 2][:, r % 2, cols]),
-                    func=Act.Copy,
-                    scale=mix_f[:, 1:2],
-                )
-
-        def rnd_scale_by_gpsimd(r):
-            if r == len(rnd_f):
-                rnd_f.append(keep.tile([P, S], F32, name="w_grouped1", align_bytes=64))
-            for g in range(HALVES):
-                cols = slice(g * BANK, (g + 1) * BANK)
-                nc.gpsimd.tensor_scalar(
-                    out=column_split(rnd_f[r][:, cols]),
-                    in0=key_split(rnd_raw[r // 2][:, r % 2, cols]),
-                    scalar1=mix_f[:, 1:2],
-                    scalar2=0.0,
-                    op0=Alu.mult,
-                    op1=Alu.add,
-                )
+        def rnd_scale(k):
+            nc.scalar.activation(
+                out=rnd_f[k][:].rearrange("p (g h m e) -> p g h m e", g=HALVES, h=2, e=2)[:, 0],
+                in_=key_split(rnd_raw[k][:, 0, 0:BANK]),
+                func=Act.Copy,
+                scale=mix_f[:, 1:2],
+            )
+            nc.scalar.activation(
+                out=rnd_f[k][:].rearrange("p (g h m e) -> p g h m e", g=HALVES, h=2, e=2)[:, 1],
+                in_=key_split(rnd_raw[k][:, 0, BANK:S]),
+                func=Act.Copy,
+                scale=mix_f[:, 1:2],
+            )
 
         x_wide, x_turned, x_grouped, x_codes, x_scales = {}, {}, {}, {}, {}
-
-        def x_scaled(q, j):
-            b, h, t = q // PAIRS, (q % PAIRS) // 2, 2 * (q % 2) + j
-            if j == 0:
-                x_wide[q] = work.tile([P, 2 * D], BF16, name="wide", bufs=WIDE_BUFS)
-            nc.vector.tensor_tensor(
-                out=x_wide[q][:, j * D : (j + 1) * D],
-                in0=x_raw.get((b, h))[:, t, :].bitcast(FP8),
-                in1=scale_row[:].rearrange("p m t -> p (m t)"),
-                op=Alu.mult,
-            )
 
         def x_widen(q):
             b, h, t = q // PAIRS, (q % PAIRS) // 2, 2 * (q % 2)
             x_wide[q] = work.tile([P, 2 * D], BF16, name="wide", bufs=WIDE_BUFS)
             nc.scalar.copy(
                 out=x_wide[q][:], in_=x_raw.get((b, h))[:, t : t + 2, :].rearrange("p t k -> p (t k)").bitcast(FP8)
-            )
-
-        def x_scale_second(q):
-            nc.gpsimd.tensor_tensor(
-                out=x_wide[q][:, D : 2 * D],
-                in0=x_wide[q][:, D : 2 * D],
-                in1=scale_row[:].rearrange("p m t -> p (m t)"),
-                op=Alu.mult,
             )
 
         def x_turn(q, k):
@@ -242,12 +206,6 @@ def tile_mixturedenserandomsynthesizer_t_kernel(tc, x_bytes, x_scale, w, rnd, mi
                     nc.tensor.transpose(
                         x_turned[q][:, 2 * h + j, :], words[:, 2 * P * j + h : 2 * P * (j + 1) : 2], ident[:]
                     )
-
-        def x_copy_out(q, tiles=BOTH):
-            nc.scalar.copy(
-                out=x_grouped[q][:, tiles].bitcast(F32),
-                in_=x_turned[q][:].rearrange("p (h j) q -> p j q h", h=2)[:, tiles],
-            )
 
         def x_scale_out(q, tiles):
             rows = slice(tiles.start * P, tiles.stop * P)
@@ -280,7 +238,7 @@ def tile_mixturedenserandomsynthesizer_t_kernel(tc, x_bytes, x_scale, w, rnd, mi
             v_sums[(hh, n)] = sums
 
         def v_gain(hh, n):
-            if n == 0:
+            if hh not in v_grouped:
                 v_grouped[hh] = work.tile([P, D, PACK], BF16, name="v_grouped", align_bytes=64)
             h = hh % HALVES
             nc.vector.tensor_tensor(
@@ -295,37 +253,82 @@ def tile_mixturedenserandomsynthesizer_t_kernel(tc, x_bytes, x_scale, w, rnd, mi
             v_scales[hh] = work.tile([P, D], U8, name="v_scales", bufs=4, align_bytes=64)
             quantize(v_codes[hh][:], v_scales[hh][:], v_grouped[hh][:].rearrange("p d t -> p (d t)"))
 
+        turned_scores, mixed_scores, psum_logits = {}, {}, {}
         scores, logits, maxima, exps, totals, inverses = {}, {}, {}, {}, {}, {}
         gained, pcs, turned_pcs, grouped_pcs, p_codes, p_scales, sums_out, rows_out = {}, {}, {}, {}, {}, {}, {}, {}
 
-        def score(q, j, g):
-            rows = slice(j * P, (j + 1) * P)
-            bank = psum.tile([P, BANK], F32, name="score%d" % (HALVES * j + g))
-            multiply(bank[:], x_codes[q][:, rows], x_scales[q][:, rows], w_codes[g][:], w_scales[g][:], True, True)
-            scores[(q, j, g)] = bank
+        def score(q, g):
+            bank = psum.tile([P, BANK], F32, name="bank%d" % (LOGIT_BANK + g))
+            multiply(bank[:], x_codes[q][:, 0:P], x_scales[q][:, 0:P], w_codes[g][:], w_scales[g][:], True, True)
+            scores[(q, g)] = bank
 
-        def blend(q, j, g):
-            if (j, g) == (0, 0):
+        def blend(q, g):
+            if q not in logits:
                 logits[q] = work.tile([P, 2, S], F32, name="logit")
+                maxima[q] = work.tile([P, 4], F32, name="maximum")
             keys = slice(g * BANK, (g + 1) * BANK)
             nc.vector.scalar_tensor_tensor(
-                out=logits[q][:, j, keys],
-                in0=scores.get((q, j, g))[:],
+                out=logits[q][:, 0, keys],
+                in0=scores.get((q, g))[:],
                 scalar=mix_f[:, 0:1],
-                in1=rnd_f[2 * (q % PAIRS) + j][:, keys],
+                in1=rnd_f[q % PAIRS][:, keys],
                 op0=Alu.mult,
                 op1=Alu.add,
             )
 
-        def maximum(q, tiles=BOTH):
-            if tiles.start == 0:
-                maxima[q] = work.tile([P, 2], F32, name="maximum")
-            nc.vector.tensor_reduce(
-                out=maxima[q][:, tiles], in_=logits[q][:, tiles], axis=AX.X, op=Alu.max, negate=True
+        def maximum(q):
+            nc.vector.tensor_reduce(out=maxima[q][:, 0:1], in_=logits[q][:, 0], axis=AX.X, op=Alu.max, negate=True)
+
+        def score_turned(q, g, k):
+            bank = shared_bank(k)
+            for n in range(PACK):
+                keys = slice(n * P, (n + 1) * P)
+                multiply(
+                    bank[:, n, :], w_codes[g][:, keys], w_scales[g][:, keys],
+                    x_codes[q][:, P : 2 * P], x_scales[q][:, P : 2 * P], True, True,
+                )
+            turned_scores[(q, g)] = bank
+
+        def score_out(q, g):
+            if q not in mixed_scores:
+                mixed_scores[q] = work.tile([P, HALVES, PACK, P], F32, name="mixed_scores")
+            nc.scalar.activation(
+                out=mixed_scores[q][:, g], in_=turned_scores.get((q, g))[:], func=Act.Copy, scale=mix_f[:, 0:1]
+            )
+
+        def blend_in_psum(q, g):
+            bank = psum.tile([P, BANK], F32, name="bank%d" % (LOGIT_BANK + g))
+            nc.tensor.matmul(
+                bank[:].rearrange("p (h m e) -> p m h e", h=2, e=2),
+                lhsT=mix_diag[:],
+                rhs=rnd_raw[q % PAIRS][:, 1, g * BANK : (g + 1) * BANK].rearrange("p (m h e) -> p m h e", h=2, e=2),
+                start=True,
+                stop=False,
+            )
+            for n in range(PACK):
+                nc.tensor.matmul(
+                    bank[:, n * P : (n + 1) * P],
+                    lhsT=mixed_scores[q][:, g, n, :],
+                    rhs=ident[:],
+                    start=False,
+                    stop=n == PACK - 1,
+                    is_transpose=True,
+                )
+            psum_logits[(q, g)] = bank
+
+        def logit_out(q, g):
+            nc.vector.tensor_scalar(
+                out=logits[q][:, 1, g * BANK : (g + 1) * BANK],
+                in0=psum_logits.get((q, g))[:],
+                scalar1=-1.0,
+                scalar2=None if g == 0 else maxima[q][:, 2:3],
+                op0=Alu.mult,
+                op1=Alu.min,
+                accum_out=maxima[q][:, 2:3] if g == 0 else maxima[q][:, 1:2],
             )
 
         def exponent(q, j):
-            if j == 0:
+            if q not in exps:
                 exps[q] = work.tile([P, 2, S], F32, name="exp")
                 totals[q] = work.tile([P, 2], F32, name="total")
             nc.scalar.activation(
@@ -333,6 +336,7 @@ def tile_mixturedenserandomsynthesizer_t_kernel(tc, x_bytes, x_scale, w, rnd, mi
                 in_=logits[q][:, j],
                 func=Act.Exp,
                 bias=maxima[q][:, j : j + 1],
+                scale=1.0 if j == 0 else -1.0,
                 accum_out=totals[q][:, j : j + 1],
             )
 
@@ -342,7 +346,7 @@ def tile_mixturedenserandomsynthesizer_t_kernel(tc, x_bytes, x_scale, w, rnd, mi
             nc.vector.reciprocal(out=inverses[q][:, tiles], in_=totals[q][:, tiles])
 
         def gain(q):
-            gained[q] = work.tile([P, 2, S], F32, name="gained")
+            gained[q] = keep.tile([P, 2, S], F32, name="gained%d" % (q % 2), align_bytes=64)
             nc.gpsimd.tensor_tensor(
                 out=gained[q][:], in0=exps[q][:], in1=c_f[:].to_broadcast([P, 2, S]), op=Alu.mult
             )
@@ -359,7 +363,7 @@ def tile_mixturedenserandomsynthesizer_t_kernel(tc, x_bytes, x_scale, w, rnd, mi
                     op0=Alu.mult,
                     op1=Alu.mult,
                 )
-            elif j == 0 and q in GPSIMD_PC_STEPS:
+            elif j == 0 and q != N_PAIRS - 3:
                 nc.gpsimd.tensor_scalar(
                     out=pcs[q][:, j],
                     in0=gained[q][:, j],
@@ -380,12 +384,12 @@ def tile_mixturedenserandomsynthesizer_t_kernel(tc, x_bytes, x_scale, w, rnd, mi
                 nc.tensor.transpose(bank[:, n, :], words[:, n * P : (n + 1) * P], ident[:])
             turned_pcs[(q, j)] = bank
 
-        def turn_out(q, j):
+        def turn_out(q, j, copy=nc.scalar.copy):
             if q not in grouped_pcs:
                 grouped_pcs[q] = work.tile(
                     [P, 2, HALVES, P, PACK], BF16, name="p_grouped", bufs=3, align_bytes=64
                 )
-            nc.scalar.copy(
+            copy(
                 out=grouped_pcs[q][:, j].bitcast(F32),
                 in_=turned_pcs.get((q, j))[:].rearrange("p (g h) q -> p g q h", h=2),
             )
@@ -421,230 +425,241 @@ def tile_mixturedenserandomsynthesizer_t_kernel(tc, x_bytes, x_scale, w, rnd, mi
                 nc.sync.dma_start(out=out_rows[b, h, :, t - 1 : t + 1], in_=rows_out[q][:])
 
         by_scalar, by_vector = nc.scalar.copy, nc.vector.tensor_copy
-        in_order = [(j, g) for j in range(2) for g in range(HALVES)]
 
         with tc.manual_schedule():
-            scale_spread()
-            by_scalar(out=mix_column[0:2], in_=mix_raw[:])
-            w_group(0, by_vector)
-            x_scaled(0, 0)
-            w_quantize(0)
-            x_scaled(0, 1)
-            x_turn(0, 0)
-            w_group(1, by_scalar)
+            nc.scalar.activation(out=mix_column[0:2], in_=mix_raw[:], func=Act.Copy)
+            x_widen(0)
             mix_spread()
-            for q in range(1, X_LEAD):
-                x_scaled(q, 0)
-                x_scaled(q, 1)
-                if q > 1:
-                    x_quantize(q - 2)
-                if q == 2:
-                    score(0, 0, 0)
-                    score(0, 1, 0)
-                if q < X_LEAD - 1:
-                    x_copy_out(q - 1)
-                    x_turn(q, q % 2)
-                    rnd_scale(q - 1)
-            by_scalar(out=c_4[:], in_=c_raw[:].rearrange("p g t -> p (g t)"))
+            x_turn(0, X_BANK)
+            x_widen(1)
+            x_turn(1, V_BANK)
+            w_group(0)
+            w_group(1)
+            mix_diagonal()
+            x_scale_out(0, BOTH)
+            x_scale_out(1, BOTH)
+            rnd_scale(0)
+            w_quantize(0)
+            x_quantize(0)
+            x_quantize(1)
             w_quantize(1)
+            x_widen(2)
             wv_group()
-            rnd_scale_by_gpsimd(3)
-            score(0, 0, 1)
-            score(0, 1, 1)
-            x_copy_out(2)
-            x_widen(X_LEAD)
-            x_turn(3, 1)
+            copy_by_gpsimd(u_f[:], u_raw[:])
+            score(0, 0)
+            score_turned(0, 0, 3)
+            score(0, 1)
+            score_turned(0, 1, 2)
+            x_turn(2, X_BANK)
+            x_widen(3)
+            by_scalar(out=c_4[:], in_=c_raw[:].rearrange("p g t -> p (g t)"))
+            score_out(0, 0)
+            score_out(0, 1)
+            blend(0, 0)
+            blend(0, 1)
+            blend_in_psum(0, 0)
+            blend_in_psum(0, 1)
+            rnd_scale(1)
             for g in range(HALVES):
                 c_spread(g)
-            for g in range(HALVES):
-                for j in range(2):
-                    blend(0, j, g)
-            for j, g in in_order:
-                score(1, j, g)
-            maximum(0, FIRST)
-            maximum(0, SECOND)
-            x_copy_out(3)
-            by_scalar(out=u_f[:], in_=u_raw[:])
-            rnd_scale(2)
-
-            exponent(0, 0)
-            exponent(0, 1)
-            x_quantize(2)
+            score_turned(1, 0, 4)
+            score_turned(1, 1, 5)
+            x_scale_out(2, BOTH)
+            logit_out(0, 0)
             wv_quantize()
-            rnd_scale_by_gpsimd(2 * PAIRS - 1)
-            for n in range(3):
-                v_product(0, n, 1 + n)
+            logit_out(0, 1)
+            x_quantize(2)
+            maximum(0)
+            x_turn(3, X_BANK)
+            score(1, 0)
+            score(1, 1)
+            v_product(0, 0, V_BANK)
+            score_out(1, 0)
+            score_out(1, 1)
+
+            exponent(0, 1)
+            exponent(0, 0)
             gain(0)
-            x_scale_second(X_LEAD)
-            for j in range(2):
-                blend(1, j, 0)
-                blend(1, j, 1)
-                v_gain(0, 2 * j)
-                if j == 0:
-                    v_gain(0, 1)
-            for j, g in in_order:
-                score(2, j, g)
-            v_product(0, 3, 1)
+            blend(1, 0)
+            blend(1, 1)
+            blend_in_psum(1, 0)
+            blend_in_psum(1, 1)
+            v_product(0, 1, 2)
+            v_product(0, 2, 3)
+            x_widen(4)
+            rnd_scale(2)
+            x_scale_out(3, BOTH)
+            logit_out(1, 0)
+            v_gain(0, 0)
+            logit_out(1, 1)
+            score_turned(2, 0, 4)
+            score_turned(2, 1, 5)
+            v_product(0, 3, V_BANK)
+            x_turn(4, X_BANK)
+            score(2, 0)
+            score(2, 1)
+            score_out(2, 0)
+            score_out(2, 1)
+            rnd_scale(3)
+            v_gain(0, 1)
             maximum(1)
-            for r in range(4, 2 * PAIRS - 1):
-                rnd_scale(r)
-            x_widen(X_LEAD + 1)
+            v_gain(0, 2)
 
             for s in range(1, N_PAIRS - 3):
-                opening, closing = divmod(2 * s + 1, QUARTERS), divmod(2 * s + 2, QUARTERS)
-                next_opening = divmod(2 * s + 3, QUARTERS)
-                this_bank, other_bank = 1 + 2 * (s % 2), 3 - 2 * (s % 2)
+                opening, closing, next_opening = (divmod(2 * s + n, QUARTERS) for n in (1, 2, 3))
+                ring = [RING_BANK + (RING_USES * s + n) % RING_BANKS for n in range(RING_USES)]
                 stored = s - STORE_LAG
-                split = s - 1 in GPSIMD_X_STEPS
-                ahead = 1 if s % 2 == 0 and s >= 3 else 2
-
                 exponent(s, 0)
                 exponent(s, 1)
                 v_gain(*opening)
-                if split:
-                    invert(s - 1)
-                for j, g in in_order[:ahead]:
-                    blend(s + 1, j, g)
                 x_quantize(s + 2)
                 if s % 2 == 0:
-                    v_quantize(s // 2 - 1)
-                x_turn(s + 3, 0)
-                if stored >= 0 and stored % PAIRS == 0:
-                    product(stored, 0, 2)
-                v_product(*closing, other_bank)
-                if s >= 3:
-                    p_quantize(s - 3)
+                    invert(s - 1)
                 if stored >= 0:
-                    product(stored, 1, this_bank)
+                    p_quantize(stored)
+                if s % 2 == 1:
+                    invert(s - 1)
+                    v_quantize(s // 2)
+                normalise(s - 1, 0)
                 gain(s)
-                if split:
-                    normalise(s - 1, 0)
-                if s in GPSIMD_X_STEPS:
-                    if s > 1:
-                        x_widen(s + X_LEAD)
-                    x_scale_second(s + X_LEAD)
+                v_product(*closing, V_BANK)
                 if stored >= 0:
-                    store(stored, 0, by_scalar)
-                for j, g in in_order[ahead:3]:
-                    blend(s + 1, j, g)
-                x_scale_out(s + 3, FIRST if split else BOTH)
-                if split:
-                    x_copy_out(s + 3, SECOND)
-                blend(s + 1, 1, 1)
-                score(s + 2, 0, 0)
-                score(s + 2, 0, 1)
-                turn(s - 1, 0, 2)
-                score(s + 2, 1, 0)
-                score(s + 2, 1, 1)
-                if stored >= 0 and s % 2 == 1:
-                    store(stored, 1, by_scalar)
-                if stored < 0 or s % 2 == 1:
-                    v_product(*next_opening, this_bank)
+                    product(stored, 0, ring[0])
+                blend(s + 1, 0)
+                blend(s + 1, 1)
+                blend_in_psum(s + 1, 0)
+                blend_in_psum(s + 1, 1)
+                turn(s - 1, 0, ring[1])
                 normalise(s - 1, 1)
-                turn(s - 1, 1, 0)
-                if stored >= 0 and s % 2 == 0:
-                    store(stored, 1, by_scalar)
-                    v_product(*next_opening, this_bank)
-                if s + 1 in GPSIMD_PC_STEPS and s + 1 + X_LEAD < N_PAIRS:
-                    x_widen(s + 1 + X_LEAD)
-                v_gain(*closing)
-                if s in GPSIMD_PC_STEPS:
-                    invert(s)
-                    normalise(s, 0)
-                maximum(s + 1)
+                turn(s - 1, 1, ring[2])
+                if stored >= 0:
+                    product(stored, 1, ring[3])
+                    store(stored, 0, by_scalar)
+                if s + 4 < N_PAIRS:
+                    x_widen(s + 4)
                 turn_out(s - 1, 0)
-                if stored + 1 >= 0 and (stored + 1) % PAIRS > 0:
-                    product(stored + 1, 0, 2)
                 turn_out(s - 1, 1)
+                x_scale_out(s + 3, BOTH)
+                logit_out(s + 1, 0)
+                v_gain(*closing)
+                logit_out(s + 1, 1)
+                score_turned(s + 2, 0, ring[4])
+                score_turned(s + 2, 1, ring[5])
+                v_product(*next_opening, V_BANK)
+                if s + 4 < N_PAIRS:
+                    x_turn(s + 4, X_BANK)
+                score(s + 2, 0)
+                score(s + 2, 1)
+                if stored >= 0:
+                    store(stored, 1, by_vector if s % 2 == 0 and s + 4 < N_PAIRS else by_scalar)
+                score_out(s + 2, 0)
+                score_out(s + 2, 1)
+                maximum(s + 1)
 
             s = N_PAIRS - 3
             last_half = B * HALVES - 1
             exponent(s, 0)
             exponent(s, 1)
             v_gain(last_half - 1, 3)
-            blend(s + 1, 0, 0)
             x_quantize(s + 2)
-            v_product(last_half, 0, 1)
-            v_product(last_half, 1, 0)
-            product(s - 4, 1, 3)
             p_quantize(s - 3)
+            invert(s - 1)
             v_quantize(last_half - 1)
-            p_quantize(s - 2)
+            normalise(s - 1, 0)
             gain(s)
-            for j in range(2):
-                store(s - 4, j, by_scalar)
-                product(s - 3, j, 2 + j)
-                v_gain(last_half, j)
-            v_product(last_half, 2, 1)
+            v_product(last_half, 1, X_BANK)
+            v_product(last_half, 0, V_BANK)
+            product(s - 3, 0, 4)
+            blend(s + 1, 0)
+            blend(s + 1, 1)
+            blend_in_psum(s + 1, 0)
+            blend_in_psum(s + 1, 1)
+            v_gain(last_half, 1)
+            turn(s - 1, 0, 5)
             normalise(s - 1, 1)
-            turn(s - 1, 0, 0)
-            for j, g in in_order[1:]:
-                blend(s + 1, j, g)
-            store(s - 3, 0, by_scalar)
             turn(s - 1, 1, 2)
-            store(s - 3, 1, by_scalar)
-            score(s + 2, 0, 0)
-            score(s + 2, 0, 1)
-            product(s - 2, 0, 3)
-            v_gain(last_half, 2)
-            invert(s)
-            normalise(s, 0)
+            product(s - 3, 1, 3)
+            store(s - 3, 0, by_scalar)
             turn_out(s - 1, 0)
-            product(s - 2, 1, 0)
-            v_product(last_half, 3, 1)
-            score(s + 2, 1, 0)
-            score(s + 2, 1, 1)
-            maximum(s + 1)
             turn_out(s - 1, 1)
-            store(s - 2, 0, by_scalar)
-            store(s - 2, 1, by_scalar)
+            logit_out(s + 1, 0)
+            v_gain(last_half, 0)
+            logit_out(s + 1, 1)
+            score_turned(s + 2, 0, 4)
+            score_turned(s + 2, 1, 5)
+            v_product(last_half, 2, X_BANK)
+            v_product(last_half, 3, V_BANK)
+            score(s + 2, 0)
+            score(s + 2, 1)
+            store(s - 3, 1, by_scalar)
+            score_out(s + 2, 0)
+            score_out(s + 2, 1)
+            maximum(s + 1)
+            v_gain(last_half, 2)
 
             s = N_PAIRS - 2
             exponent(s, 0)
             exponent(s, 1)
             v_gain(last_half, 3)
+            p_quantize(s - 3)
+            invert(s - 1)
             p_quantize(s - 2)
             v_quantize(last_half)
             gain(s)
-            turn(s - 1, 0, 2)
-            product(s - 2, 0, 1)
+            product(s - 3, 0, 2)
+            product(s - 3, 1, 3)
+            blend(s + 1, 0)
+            blend(s + 1, 1)
+            blend_in_psum(s + 1, 0)
+            blend_in_psum(s + 1, 1)
+            product(s - 2, 0, 6)
+            normalise(s - 1, 0)
+            turn(s - 1, 0, 4)
+            product(s - 2, 1, 7)
             normalise(s - 1, 1)
-            turn(s - 1, 1, 3)
-            product(s - 2, 1, 0)
-            for j, g in in_order:
-                blend(s + 1, j, g)
+            turn(s - 1, 1, 5)
+            maximum(s + 1)
+            logit_out(s + 1, 0)
             invert(s)
-            for j, tile in enumerate((FIRST, SECOND)):
-                maximum(s + 1, tile)
-                turn_out(s - 1, j)
+            logit_out(s + 1, 1)
+            normalise(s, 0)
 
             s = N_PAIRS - 1
             exponent(s, 0)
+            turn_out(s - 2, 0)
             exponent(s, 1)
-            store(s - 3, 0, by_vector)
+            turn_out(s - 2, 1)
+            store(s - 4, 0, by_vector)
+            store(s - 4, 1, by_vector)
             invert(s, FIRST)
-            p_quantize(s - 2)
-            product(s - 2, 0, 2)
-            normalise(s, 0)
-            normalise(s - 1, 0)
-            turn(s, 0, 4)
-            turn(s - 1, 0, 5)
-            product(s - 2, 1, 3)
-            invert(s, SECOND)
+            store(s - 3, 0, by_vector)
             store(s - 3, 1, by_vector)
-            normalise(s, 1)
+            p_quantize(s - 2)
+            normalise(s, 0)
+            invert(s, SECOND)
             normalise(s - 1, 1)
-            turn(s - 1, 1, 7)
-            turn(s, 1, 6)
-
-            last_tiles = [(s, 0), (s - 1, 0), (s - 1, 1), (s, 1)]
-            for q, j in last_tiles:
-                turn_out(q, j)
-            for (q, j), k in zip(last_tiles, (0, 1, 4, 2)):
-                p_quantize(q, (FIRST, SECOND)[j])
-                product(q, j, k)
-                if (q, j) == last_tiles[0]:
-                    store(s - 2, 0, by_vector)
-                    store(s - 2, 1, by_vector)
-            for (q, j), copy in zip(last_tiles, (by_scalar, by_scalar, by_vector, by_scalar)):
-                store(q, j, copy)
+            turn(s - 1, 0, 1)
+            product(s - 2, 0, 2)
+            product(s - 2, 1, 3)
+            turn(s - 1, 1, 4)
+            turn(s, 0, 0)
+            turn_out(s - 1, 0)
+            turn_out(s - 1, 1)
+            p_quantize(s - 1, FIRST)
+            normalise(s, 1)
+            product(s - 1, 0, 6)
+            turn(s, 1, 5)
+            turn_out(s, 0)
+            p_quantize(s - 1, SECOND)
+            product(s - 1, 1, 7)
+            p_quantize(s, FIRST)
+            product(s, 0, 1)
+            store(s - 2, 0, by_scalar)
+            turn_out(s, 1)
+            store(s - 2, 1, by_vector)
+            p_quantize(s, SECOND)
+            product(s, 1, 0)
+            store(s - 1, 0, by_scalar)
+            store(s - 1, 1, by_vector)
+            store(s, 0, by_scalar)
+            store(s, 1, by_vector)

@@ -34,7 +34,7 @@ STORE_LAG = 3
 
 WIDE_BUFS = 2
 
-FIRST_TILEWISE_PAIR = N_PAIRS - 4
+FIRST_TILEWISE_PAIR = N_PAIRS - 5
 
 
 def tile_mixturedenserandomsynthesizer_t_kernel(tc, x_bytes, x_scale, w, rnd, mix, wv, c, u, out):
@@ -77,9 +77,9 @@ def tile_mixturedenserandomsynthesizer_t_kernel(tc, x_bytes, x_scale, w, rnd, mi
         load_w(1)
         load_rnd(0)
         load_x(0, 1)
+        nc.sync.dma_start(out=c_raw[:], in_=c.rearrange("(g p t) -> p g t", p=P, t=PACK))
         nc.sync.dma_start(out=wv_raw[:], in_=wv.rearrange("(p j) n -> p j n", j=PACK))
         load_rnd(1)
-        nc.sync.dma_start(out=c_raw[:], in_=c.rearrange("(g p t) -> p g t", p=P, t=PACK))
         nc.sync.dma_start(out=u_raw[:], in_=u.rearrange("(h p t) -> p h t", p=P, t=PACK))
         load_rnd(2)
         load_x(1, 0)
@@ -149,7 +149,7 @@ def tile_mixturedenserandomsynthesizer_t_kernel(tc, x_bytes, x_scale, w, rnd, mi
             )
 
         def c_spread(g):
-            bank = spread(c_4[:, g * PACK : (g + 1) * PACK], RING_BANK + 1 - g)
+            bank = spread(c_4[:, g * PACK : (g + 1) * PACK], V_BANK + g)
             nc.scalar.copy(
                 out=column_split(c_f[:, 0, g * BANK : (g + 1) * BANK]),
                 in_=bank[:].rearrange("p (h e) m -> p h m e", h=2),
@@ -173,6 +173,18 @@ def tile_mixturedenserandomsynthesizer_t_kernel(tc, x_bytes, x_scale, w, rnd, mi
 
         def wv_quantize():
             quantize(wv_codes[:], wv_scales[:], wv_grouped[0][:].rearrange("p n j -> p (n j)"))
+
+        def rnd_scale_by_gpsimd(k):
+            for g in range(HALVES):
+                cols = slice(g * BANK, (g + 1) * BANK)
+                nc.gpsimd.tensor_scalar(
+                    out=column_split(rnd_f[k][:, cols]),
+                    in0=key_split(rnd_raw[k][:, 0, cols]),
+                    scalar1=mix_f[:, 1:2],
+                    scalar2=0.0,
+                    op0=Alu.mult,
+                    op1=Alu.add,
+                )
 
         def rnd_scale(k):
             nc.scalar.activation(
@@ -200,29 +212,26 @@ def tile_mixturedenserandomsynthesizer_t_kernel(tc, x_bytes, x_scale, w, rnd, mi
         def x_turn(q, k):
             words = x_wide[q][:].bitcast(F32)
             x_turned[q] = shared_bank(k)
-            x_grouped[q] = work.tile([P, 2, P, PACK], BF16, name="x_grouped", bufs=WIDE_BUFS, align_bytes=64)
             for j in range(2):
                 for h in range(2):
                     nc.tensor.transpose(
                         x_turned[q][:, 2 * h + j, :], words[:, 2 * P * j + h : 2 * P * (j + 1) : 2], ident[:]
                     )
 
-        def x_scale_out(q, tiles):
-            rows = slice(tiles.start * P, tiles.stop * P)
-            values = x_turned[q][:].rearrange("p (h j) q -> p h (j q)", h=2)[:, :, rows].bitcast(BF16)
+        def x_scale_out(q):
+            x_grouped[q] = work.tile([P, 2 * P, PACK], BF16, name="x_grouped", align_bytes=64)
+            values = x_turned[q][:].rearrange("p (h j) q -> p h (j q)", h=2).bitcast(BF16)
             nc.vector.tensor_tensor(
-                out=x_grouped[q][:, tiles].rearrange("p j q (h e) -> p (j q) h e", e=2),
+                out=x_grouped[q][:].rearrange("p q (h e) -> p q h e", e=2),
                 in0=values.rearrange("p h (q e) -> p q h e", e=2),
-                in1=scale_4[:]
-                .rearrange("p (o h e) -> p o h e", o=1, e=2)
-                .to_broadcast([P, rows.stop - rows.start, 2, 2]),
+                in1=scale_4[:].rearrange("p (o h e) -> p o h e", o=1, e=2).to_broadcast([P, 2 * P, 2, 2]),
                 op=Alu.mult,
             )
 
         def x_quantize(q):
             x_codes[q] = work.tile([P, 2 * P], U32, name="x_codes", bufs=7, align_bytes=64)
             x_scales[q] = work.tile([P, 2 * P], U8, name="x_scales", bufs=7, align_bytes=64)
-            quantize(x_codes[q][:], x_scales[q][:], x_grouped[q][:].rearrange("p j q t -> p (j q t)"))
+            quantize(x_codes[q][:], x_scales[q][:], x_grouped[q][:].rearrange("p q t -> p (q t)"))
 
         v_sums, v_grouped, v_codes, v_scales = {}, {}, {}, {}
 
@@ -279,52 +288,66 @@ def tile_mixturedenserandomsynthesizer_t_kernel(tc, x_bytes, x_scale, w, rnd, mi
         def maximum(q):
             nc.vector.tensor_reduce(out=maxima[q][:, 0:1], in_=logits[q][:, 0], axis=AX.X, op=Alu.max, negate=True)
 
-        def score_turned(q, g, k):
+        def score_turned(q, g, k, j=1):
             bank = shared_bank(k)
+            rows = slice(j * P, (j + 1) * P)
             for n in range(PACK):
                 keys = slice(n * P, (n + 1) * P)
                 multiply(
                     bank[:, n, :], w_codes[g][:, keys], w_scales[g][:, keys],
-                    x_codes[q][:, P : 2 * P], x_scales[q][:, P : 2 * P], True, True,
+                    x_codes[q][:, rows], x_scales[q][:, rows], True, True,
                 )
-            turned_scores[(q, g)] = bank
+            turned_scores[(q, j, g)] = bank
 
-        def score_out(q, g):
-            if q not in mixed_scores:
-                mixed_scores[q] = work.tile([P, HALVES, PACK, P], F32, name="mixed_scores")
+        def score_out(q, g, j=1):
+            if (q, j) not in mixed_scores:
+                mixed_scores[(q, j)] = work.tile([P, HALVES, PACK, P], F32, name="mixed_scores")
             nc.scalar.activation(
-                out=mixed_scores[q][:, g], in_=turned_scores.get((q, g))[:], func=Act.Copy, scale=mix_f[:, 0:1]
+                out=mixed_scores.get((q, j))[:, g],
+                in_=turned_scores.get((q, j, g))[:],
+                func=Act.Copy,
+                scale=mix_f[:, 0:1],
             )
 
-        def blend_in_psum(q, g):
-            bank = psum.tile([P, BANK], F32, name="bank%d" % (LOGIT_BANK + g))
+        def rnd_into_psum(q, g, k, j=1):
+            bank = psum.tile([P, BANK], F32, name="bank%d" % k)
             nc.tensor.matmul(
                 bank[:].rearrange("p (h m e) -> p m h e", h=2, e=2),
                 lhsT=mix_diag[:],
-                rhs=rnd_raw[q % PAIRS][:, 1, g * BANK : (g + 1) * BANK].rearrange("p (m h e) -> p m h e", h=2, e=2),
+                rhs=rnd_raw[q % PAIRS][:, j, g * BANK : (g + 1) * BANK].rearrange("p (m h e) -> p m h e", h=2, e=2),
                 start=True,
                 stop=False,
             )
+            psum_logits[(q, j, g)] = bank
+
+        def score_into_psum(q, g, j=1):
             for n in range(PACK):
                 nc.tensor.matmul(
-                    bank[:, n * P : (n + 1) * P],
-                    lhsT=mixed_scores[q][:, g, n, :],
+                    psum_logits.get((q, j, g))[:, n * P : (n + 1) * P],
+                    lhsT=mixed_scores.get((q, j))[:, g, n, :],
                     rhs=ident[:],
                     start=False,
                     stop=n == PACK - 1,
                     is_transpose=True,
                 )
-            psum_logits[(q, g)] = bank
 
-        def logit_out(q, g):
+        def blend_in_psum(q, g):
+            rnd_into_psum(q, g, LOGIT_BANK + g)
+            score_into_psum(q, g)
+
+        def logit_out(q, g, j=1):
+            if q not in logits:
+                logits[q] = work.tile([P, 2, S], F32, name="logit")
+                maxima[q] = work.tile([P, 4], F32, name="maximum")
+            first = maxima[q][:, 2 + j : 3 + j]
             nc.vector.tensor_scalar(
-                out=logits[q][:, 1, g * BANK : (g + 1) * BANK],
-                in0=psum_logits.get((q, g))[:],
+                out=logits[q][:, j, g * BANK : (g + 1) * BANK],
+                in0=psum_logits.get((q, j, g))[:],
                 scalar1=-1.0,
-                scalar2=None if g == 0 else maxima[q][:, 2:3],
+                scalar2=None if g == 0 else first,
                 op0=Alu.mult,
                 op1=Alu.min,
-                accum_out=maxima[q][:, 2:3] if g == 0 else maxima[q][:, 1:2],
+                accum_out=first if g == 0 else maxima[q][:, j : j + 1],
             )
 
         def exponent(q, j):
@@ -345,37 +368,47 @@ def tile_mixturedenserandomsynthesizer_t_kernel(tc, x_bytes, x_scale, w, rnd, mi
                 inverses[q] = work.tile([P, 2], F32, name="inverse")
             nc.vector.reciprocal(out=inverses[q][:, tiles], in_=totals[q][:, tiles])
 
-        def gain(q):
+        def gain(q, tiles=BOTH):
             gained[q] = keep.tile([P, 2, S], F32, name="gained%d" % (q % 2), align_bytes=64)
             nc.gpsimd.tensor_tensor(
-                out=gained[q][:], in0=exps[q][:], in1=c_f[:].to_broadcast([P, 2, S]), op=Alu.mult
+                out=gained[q][:, tiles],
+                in0=exps[q][:, tiles],
+                in1=c_f[:].to_broadcast([P, tiles.stop - tiles.start, S]),
+                op=Alu.mult,
             )
 
-        def normalise(q, j):
+        def pc_tile(q):
             if q not in pcs:
                 pcs[q] = work.tile([P, 2, S], BF16, name="pc")
-            if q == N_PAIRS - 1:
-                nc.vector.scalar_tensor_tensor(
-                    out=pcs[q][:, j],
-                    in0=exps[q][:, j],
-                    scalar=inverses[q][:, j : j + 1],
-                    in1=c_f[:, 0],
-                    op0=Alu.mult,
-                    op1=Alu.mult,
-                )
-            elif j == 0 and q != N_PAIRS - 3:
-                nc.gpsimd.tensor_scalar(
-                    out=pcs[q][:, j],
-                    in0=gained[q][:, j],
-                    scalar1=inverses[q][:, j : j + 1],
-                    scalar2=0.0,
-                    op0=Alu.mult,
-                    op1=Alu.add,
-                )
-            else:
-                nc.scalar.activation(
-                    out=pcs[q][:, j], in_=gained[q][:, j], func=Act.Copy, scale=inverses[q][:, j : j + 1]
-                )
+            return pcs[q]
+
+        def divide_and_gain(q, j):
+            nc.vector.scalar_tensor_tensor(
+                out=pc_tile(q)[:, j],
+                in0=exps[q][:, j],
+                scalar=inverses[q][:, j : j + 1],
+                in1=c_f[:, 0],
+                op0=Alu.mult,
+                op1=Alu.mult,
+            )
+
+        def divide_by_gpsimd(q, j, keys=slice(0, S)):
+            nc.gpsimd.tensor_scalar(
+                out=pc_tile(q)[:, j, keys],
+                in0=gained[q][:, j, keys],
+                scalar1=inverses[q][:, j : j + 1],
+                scalar2=0.0,
+                op0=Alu.mult,
+                op1=Alu.add,
+            )
+
+        def divide_by_scalar(q, j, keys=slice(0, S)):
+            nc.scalar.activation(
+                out=pc_tile(q)[:, j, keys],
+                in_=gained[q][:, j, keys],
+                func=Act.Copy,
+                scale=inverses[q][:, j : j + 1],
+            )
 
         def turn(q, j, k):
             words = pcs[q][:, j].bitcast(F32)
@@ -417,12 +450,63 @@ def tile_mixturedenserandomsynthesizer_t_kernel(tc, x_bytes, x_scale, w, rnd, mi
         def store(q, j, copy):
             b, h, t = q // PAIRS, (q % PAIRS) // 2, 2 * (q % 2) + j
             if q not in rows_out:
-                rows_out[q] = work.tile([P, 2, D], F32, name="rows_out", bufs=4)
+                rows_out[q] = work.tile([P, 2, D], F32, name="rows_out", bufs=5)
             copy(out=rows_out[q][:, j], in_=sums_out.get((q, j))[:].rearrange("p t d -> p (t d)"))
             if q >= FIRST_TILEWISE_PAIR:
                 nc.sync.dma_start(out=out_rows[b, h, :, t], in_=rows_out[q][:, j])
             elif j == 1:
                 nc.sync.dma_start(out=out_rows[b, h, :, t - 1 : t + 1], in_=rows_out[q][:])
+
+        last_q, last_j = N_PAIRS - 1, 1
+        last_turned, last_sums = {}, {}
+
+        def last_divide(g):
+            keys = slice(g * BANK, (g + 1) * BANK)
+            nc.vector.scalar_tensor_tensor(
+                out=pcs[last_q][:, last_j, keys],
+                in0=exps[last_q][:, last_j, keys],
+                scalar=inverses[last_q][:, last_j : last_j + 1],
+                in1=c_f[:, 0, keys],
+                op0=Alu.mult,
+                op1=Alu.mult,
+            )
+
+        def last_turn(g, k):
+            words = pcs[last_q][:, last_j].bitcast(F32)
+            last_turned[g] = shared_bank(k)
+            for h in range(2):
+                n = 2 * g + h
+                nc.tensor.transpose(last_turned[g][:, h, :], words[:, n * P : (n + 1) * P], ident[:])
+
+        def last_turn_out(g):
+            nc.scalar.copy(
+                out=grouped_pcs[last_q][:, last_j, g].bitcast(F32),
+                in_=last_turned[g][:, 0:2].rearrange("p h q -> p q h"),
+            )
+
+        def last_quantize(g):
+            cols = slice((2 * last_j + g) * P, (2 * last_j + g + 1) * P)
+            quantize(
+                p_codes[last_q][:, cols], p_scales[last_q][:, cols],
+                grouped_pcs[last_q][:, last_j, g].rearrange("p q t -> p (q t)"),
+            )
+
+        def last_product(g, banks):
+            cols = slice((2 * last_j + g) * P, (2 * last_j + g + 1) * P)
+            hh = HALVES * (B - 1) + g
+            for n, k in enumerate(banks):
+                if g == 0:
+                    last_sums[n] = psum.tile([P, D // 2], F32, name="bank%d" % k)
+                d_cols = slice(n * D // 2, (n + 1) * D // 2)
+                multiply(
+                    last_sums[n][:], p_codes[last_q][:, cols], p_scales[last_q][:, cols],
+                    v_codes[hh][:, d_cols], v_scales[hh][:, d_cols], g == 0, g == HALVES - 1,
+                )
+
+        def last_store(n, copy):
+            d_cols = slice(n * D // 2, (n + 1) * D // 2)
+            copy(out=rows_out[last_q][:, last_j, d_cols], in_=last_sums[n][:])
+            nc.sync.dma_start(out=out_rows[B - 1, HALVES - 1, :, PACK - 1, d_cols], in_=rows_out[last_q][:, last_j, d_cols])
 
         by_scalar, by_vector = nc.scalar.copy, nc.vector.tensor_copy
 
@@ -432,80 +516,121 @@ def tile_mixturedenserandomsynthesizer_t_kernel(tc, x_bytes, x_scale, w, rnd, mi
             mix_spread()
             x_turn(0, X_BANK)
             x_widen(1)
+            mix_diagonal()
             x_turn(1, V_BANK)
             w_group(0)
             w_group(1)
-            mix_diagonal()
-            x_scale_out(0, BOTH)
-            x_scale_out(1, BOTH)
+            x_scale_out(0)
+            x_scale_out(1)
             rnd_scale(0)
+            x_widen(2)
+            rnd_into_psum(0, 0, 4)
+            rnd_into_psum(0, 1, 5)
             w_quantize(0)
             x_quantize(0)
             x_quantize(1)
             w_quantize(1)
-            x_widen(2)
+            x_widen(3)
             wv_group()
             copy_by_gpsimd(u_f[:], u_raw[:])
-            score(0, 0)
-            score_turned(0, 0, 3)
-            score(0, 1)
-            score_turned(0, 1, 2)
-            x_turn(2, X_BANK)
-            x_widen(3)
             by_scalar(out=c_4[:], in_=c_raw[:].rearrange("p g t -> p (g t)"))
+            rnd_scale(1)
+            rnd_scale_by_gpsimd(2)
+            score(0, 0)
+            x_turn(2, X_BANK)
+            score(0, 1)
+            score_turned(0, 0, 2)
+            score_turned(0, 1, 3)
+            blend(0, 0)
+            x_scale_out(2)
+            blend(0, 1)
+            score(1, 0)
             score_out(0, 0)
             score_out(0, 1)
-            blend(0, 0)
-            blend(0, 1)
-            blend_in_psum(0, 0)
-            blend_in_psum(0, 1)
-            rnd_scale(1)
             for g in range(HALVES):
                 c_spread(g)
-            score_turned(1, 0, 4)
-            score_turned(1, 1, 5)
-            x_scale_out(2, BOTH)
-            logit_out(0, 0)
-            wv_quantize()
-            logit_out(0, 1)
-            x_quantize(2)
-            maximum(0)
-            x_turn(3, X_BANK)
-            score(1, 0)
+            score_into_psum(0, 0)
             score(1, 1)
-            v_product(0, 0, V_BANK)
-            score_out(1, 0)
-            score_out(1, 1)
-
-            exponent(0, 1)
-            exponent(0, 0)
-            gain(0)
+            score_turned(1, 0, 2)
+            score_into_psum(0, 1)
+            score_turned(1, 1, 3)
+            x_turn(3, V_BANK)
+            maximum(0)
+            logit_out(0, 0)
             blend(1, 0)
-            blend(1, 1)
-            blend_in_psum(1, 0)
-            blend_in_psum(1, 1)
+            logit_out(0, 1)
+            wv_quantize()
+            x_quantize(2)
+
+            exponent(0, 0)
+            score_out(1, 0)
+            exponent(0, 1)
+            score_out(1, 1)
+            gain(0)
+            rnd_into_psum(1, 0, 4)
+            rnd_into_psum(1, 1, 5)
+            score_into_psum(1, 0)
+            v_product(0, 0, X_BANK)
+            score(2, 0)
             v_product(0, 1, 2)
-            v_product(0, 2, 3)
+            score_into_psum(1, 1)
+            blend(1, 1)
+            x_scale_out(3)
+            score_turned(2, 0, 3)
+            v_product(0, 2, V_BANK)
             x_widen(4)
-            rnd_scale(2)
-            x_scale_out(3, BOTH)
+            rnd_scale(3)
             logit_out(1, 0)
             v_gain(0, 0)
             logit_out(1, 1)
-            score_turned(2, 0, 4)
-            score_turned(2, 1, 5)
-            v_product(0, 3, V_BANK)
+            score_turned(2, 1, 4)
             x_turn(4, X_BANK)
-            score(2, 0)
             score(2, 1)
             score_out(2, 0)
             score_out(2, 1)
-            rnd_scale(3)
-            v_gain(0, 1)
             maximum(1)
-            v_gain(0, 2)
+            v_gain(0, 1)
 
-            for s in range(1, N_PAIRS - 3):
+            for s in range(1, STORE_LAG):
+                ring = [RING_BANK + (RING_USES * s + n) % RING_BANKS for n in range(RING_USES)]
+                opening, closing = divmod(2 * s, QUARTERS), divmod(2 * s + 1, QUARTERS)
+                exponent(s, 0)
+                exponent(s, 1)
+                v_gain(*opening)
+                x_quantize(s + 2)
+                invert(s - 1)
+                if s == 2:
+                    v_quantize(0)
+                divide_by_gpsimd(s - 1, 0)
+                gain(s)
+                v_product(*closing, V_BANK)
+                score_turned(s + 2, 0, ring[0])
+                blend(s + 1, 0)
+                blend(s + 1, 1)
+                blend_in_psum(s + 1, 0)
+                blend_in_psum(s + 1, 1)
+                turn(s - 1, 0, ring[1])
+                score_turned(s + 2, 1, ring[3])
+                divide_by_scalar(s - 1, 1)
+                turn(s - 1, 1, ring[2])
+                x_widen(s + 4)
+                score_out(s + 2, 0)
+                turn_out(s - 1, 0)
+                turn_out(s - 1, 1)
+                x_scale_out(s + 3)
+                logit_out(s + 1, 0)
+                v_gain(*closing)
+                logit_out(s + 1, 1)
+                score(s + 2, 0)
+                v_product(*divmod(2 * s + 2, QUARTERS), V_BANK)
+                x_turn(s + 4, X_BANK)
+                score(s + 2, 1)
+                score_out(s + 2, 1)
+                maximum(s + 1)
+            v_product(1, 3, ring[4])
+            v_gain(1, 2)
+
+            for s in range(STORE_LAG, N_PAIRS - 3):
                 opening, closing, next_opening = (divmod(2 * s + n, QUARTERS) for n in (1, 2, 3))
                 ring = [RING_BANK + (RING_USES * s + n) % RING_BANKS for n in range(RING_USES)]
                 stored = s - STORE_LAG
@@ -515,31 +640,28 @@ def tile_mixturedenserandomsynthesizer_t_kernel(tc, x_bytes, x_scale, w, rnd, mi
                 x_quantize(s + 2)
                 if s % 2 == 0:
                     invert(s - 1)
-                if stored >= 0:
-                    p_quantize(stored)
+                p_quantize(stored)
                 if s % 2 == 1:
                     invert(s - 1)
                     v_quantize(s // 2)
-                normalise(s - 1, 0)
+                divide_by_gpsimd(s - 1, 0)
                 gain(s)
                 v_product(*closing, V_BANK)
-                if stored >= 0:
-                    product(stored, 0, ring[0])
+                product(stored, 0, ring[0])
                 blend(s + 1, 0)
                 blend(s + 1, 1)
                 blend_in_psum(s + 1, 0)
                 blend_in_psum(s + 1, 1)
                 turn(s - 1, 0, ring[1])
-                normalise(s - 1, 1)
+                divide_by_scalar(s - 1, 1)
                 turn(s - 1, 1, ring[2])
-                if stored >= 0:
-                    product(stored, 1, ring[3])
-                    store(stored, 0, by_scalar)
+                product(stored, 1, ring[3])
+                store(stored, 0, by_scalar)
                 if s + 4 < N_PAIRS:
                     x_widen(s + 4)
                 turn_out(s - 1, 0)
                 turn_out(s - 1, 1)
-                x_scale_out(s + 3, BOTH)
+                x_scale_out(s + 3)
                 logit_out(s + 1, 0)
                 v_gain(*closing)
                 logit_out(s + 1, 1)
@@ -550,8 +672,7 @@ def tile_mixturedenserandomsynthesizer_t_kernel(tc, x_bytes, x_scale, w, rnd, mi
                     x_turn(s + 4, X_BANK)
                 score(s + 2, 0)
                 score(s + 2, 1)
-                if stored >= 0:
-                    store(stored, 1, by_vector if s % 2 == 0 and s + 4 < N_PAIRS else by_scalar)
+                store(stored, 1, by_vector if s % 2 == 0 and s + 4 < N_PAIRS else by_scalar)
                 score_out(s + 2, 0)
                 score_out(s + 2, 1)
                 maximum(s + 1)
@@ -565,7 +686,7 @@ def tile_mixturedenserandomsynthesizer_t_kernel(tc, x_bytes, x_scale, w, rnd, mi
             p_quantize(s - 3)
             invert(s - 1)
             v_quantize(last_half - 1)
-            normalise(s - 1, 0)
+            divide_by_gpsimd(s - 1, 0)
             gain(s)
             v_product(last_half, 1, X_BANK)
             v_product(last_half, 0, V_BANK)
@@ -576,7 +697,7 @@ def tile_mixturedenserandomsynthesizer_t_kernel(tc, x_bytes, x_scale, w, rnd, mi
             blend_in_psum(s + 1, 1)
             v_gain(last_half, 1)
             turn(s - 1, 0, 5)
-            normalise(s - 1, 1)
+            divide_by_scalar(s - 1, 1)
             turn(s - 1, 1, 2)
             product(s - 3, 1, 3)
             store(s - 3, 0, by_scalar)
@@ -598,68 +719,74 @@ def tile_mixturedenserandomsynthesizer_t_kernel(tc, x_bytes, x_scale, w, rnd, mi
             v_gain(last_half, 2)
 
             s = N_PAIRS - 2
-            exponent(s, 0)
             exponent(s, 1)
+            exponent(s, 0)
             v_gain(last_half, 3)
             p_quantize(s - 3)
             invert(s - 1)
             p_quantize(s - 2)
             v_quantize(last_half)
-            gain(s)
+            gain(s, FIRST)
             product(s - 3, 0, 2)
-            product(s - 3, 1, 3)
             blend(s + 1, 0)
             blend(s + 1, 1)
+            invert(s)
+            divide_by_gpsimd(s, 0)
             blend_in_psum(s + 1, 0)
             blend_in_psum(s + 1, 1)
-            product(s - 2, 0, 6)
-            normalise(s - 1, 0)
+            divide_by_scalar(s - 1, 0)
+            divide_by_scalar(s - 1, 1)
             turn(s - 1, 0, 4)
-            product(s - 2, 1, 7)
-            normalise(s - 1, 1)
             turn(s - 1, 1, 5)
+            product(s - 3, 1, 3)
+            product(s - 2, 0, 6)
             maximum(s + 1)
             logit_out(s + 1, 0)
-            invert(s)
+            store(s - 3, 0, by_vector)
             logit_out(s + 1, 1)
-            normalise(s, 0)
+            turn(s, 0, 0)
+            product(s - 2, 1, 7)
+            divide_and_gain(s, 1)
+            turn(s, 1, 1)
 
             s = N_PAIRS - 1
             exponent(s, 0)
             turn_out(s - 2, 0)
-            exponent(s, 1)
             turn_out(s - 2, 1)
-            store(s - 4, 0, by_vector)
-            store(s - 4, 1, by_vector)
+            exponent(s, 1)
             invert(s, FIRST)
-            store(s - 3, 0, by_vector)
-            store(s - 3, 1, by_vector)
             p_quantize(s - 2)
-            normalise(s, 0)
-            invert(s, SECOND)
-            normalise(s - 1, 1)
-            turn(s - 1, 0, 1)
             product(s - 2, 0, 2)
-            product(s - 2, 1, 3)
-            turn(s - 1, 1, 4)
-            turn(s, 0, 0)
+            product(s - 2, 1, 4)
+            divide_and_gain(s, 0)
+            store(s - 4, 1, by_scalar)
             turn_out(s - 1, 0)
+            store(s - 3, 0, by_scalar)
             turn_out(s - 1, 1)
+            invert(s, SECOND)
+            store(s - 3, 1, by_vector)
+            last_divide(0)
             p_quantize(s - 1, FIRST)
-            normalise(s, 1)
-            product(s - 1, 0, 6)
-            turn(s, 1, 5)
-            turn_out(s, 0)
+            last_divide(1)
             p_quantize(s - 1, SECOND)
-            product(s - 1, 1, 7)
-            p_quantize(s, FIRST)
-            product(s, 0, 1)
+            turn(s, 0, 5)
+            last_turn(0, 3)
+            product(s - 1, 0, 0)
+            last_turn(1, 6)
+            product(s - 1, 1, 1)
+            turn_out(s, 0)
             store(s - 2, 0, by_scalar)
-            turn_out(s, 1)
+            last_turn_out(0)
+            last_turn_out(1)
             store(s - 2, 1, by_vector)
-            p_quantize(s, SECOND)
-            product(s, 1, 0)
+            p_quantize(s, FIRST)
+            product(s, 0, 7)
+            last_quantize(0)
+            last_quantize(1)
+            last_product(0, (3, 5))
+            last_product(1, (3, 5))
             store(s - 1, 0, by_scalar)
             store(s - 1, 1, by_vector)
             store(s, 0, by_scalar)
-            store(s, 1, by_vector)
+            last_store(0, by_vector)
+            last_store(1, by_scalar)

@@ -31,6 +31,7 @@ LOGIT_BANK, RING_BANK, OUT_BANK, V_BANK, X_BANK = 0, 2, 4, 6, 7
 RING_BANKS, RING_USES = 4, 6
 
 STORE_LAG = 3
+VECTOR_COLUMNS = 192
 
 WIDE_BUFS = 2
 
@@ -379,7 +380,7 @@ def tile_mixturedenserandomsynthesizer_t_kernel(tc, x_bytes, x_scale, w, rnd, mi
 
         def pc_tile(q):
             if q not in pcs:
-                pcs[q] = work.tile([P, 2, S], BF16, name="pc")
+                pcs[q] = work.tile([P, 2, S], BF16, name="pc", bufs=3)
             return pcs[q]
 
         def divide_and_gain(q, j):
@@ -447,11 +448,14 @@ def tile_mixturedenserandomsynthesizer_t_kernel(tc, x_bytes, x_scale, w, rnd, mi
                 )
             sums_out[(q, j)] = bank
 
-        def store(q, j, copy):
+        def store_part(q, j, copy, cols):
+            copy(out=rows_out[q][:, j, cols], in_=sums_out.get((q, j))[:].rearrange("p t d -> p (t d)")[:, cols])
+
+        def store(q, j, copy, cols=slice(0, D)):
             b, h, t = q // PAIRS, (q % PAIRS) // 2, 2 * (q % 2) + j
             if q not in rows_out:
                 rows_out[q] = work.tile([P, 2, D], F32, name="rows_out", bufs=5)
-            copy(out=rows_out[q][:, j], in_=sums_out.get((q, j))[:].rearrange("p t d -> p (t d)"))
+            store_part(q, j, copy, cols)
             if q >= FIRST_TILEWISE_PAIR:
                 nc.sync.dma_start(out=out_rows[b, h, :, t], in_=rows_out[q][:, j])
             elif j == 1:
@@ -672,10 +676,15 @@ def tile_mixturedenserandomsynthesizer_t_kernel(tc, x_bytes, x_scale, w, rnd, mi
                     x_turn(s + 4, X_BANK)
                 score(s + 2, 0)
                 score(s + 2, 1)
-                store(stored, 1, by_vector if s % 2 == 0 and s + 4 < N_PAIRS else by_scalar)
+                if s + 4 < N_PAIRS:
+                    store_part(stored, 1, by_scalar, slice(VECTOR_COLUMNS, D))
+                else:
+                    store(stored, 1, by_scalar)
                 score_out(s + 2, 0)
                 score_out(s + 2, 1)
                 maximum(s + 1)
+                if s + 4 < N_PAIRS:
+                    store(stored, 1, by_vector, slice(0, VECTOR_COLUMNS))
 
             s = N_PAIRS - 3
             last_half = B * HALVES - 1
@@ -728,6 +737,7 @@ def tile_mixturedenserandomsynthesizer_t_kernel(tc, x_bytes, x_scale, w, rnd, mi
             v_quantize(last_half)
             gain(s, FIRST)
             product(s - 3, 0, 2)
+            product(s - 2, 0, 6)
             blend(s + 1, 0)
             blend(s + 1, 1)
             invert(s)
@@ -737,17 +747,15 @@ def tile_mixturedenserandomsynthesizer_t_kernel(tc, x_bytes, x_scale, w, rnd, mi
             divide_by_scalar(s - 1, 0)
             divide_by_scalar(s - 1, 1)
             turn(s - 1, 0, 4)
-            turn(s - 1, 1, 5)
             product(s - 3, 1, 3)
-            product(s - 2, 0, 6)
+            turn(s - 1, 1, 5)
+            product(s - 2, 1, 7)
             maximum(s + 1)
             logit_out(s + 1, 0)
             store(s - 3, 0, by_vector)
             logit_out(s + 1, 1)
             turn(s, 0, 0)
-            product(s - 2, 1, 7)
             divide_and_gain(s, 1)
-            turn(s, 1, 1)
 
             s = N_PAIRS - 1
             exponent(s, 0)
@@ -757,6 +765,7 @@ def tile_mixturedenserandomsynthesizer_t_kernel(tc, x_bytes, x_scale, w, rnd, mi
             invert(s, FIRST)
             p_quantize(s - 2)
             product(s - 2, 0, 2)
+            turn(s - 1, 1, 1)
             product(s - 2, 1, 4)
             divide_and_gain(s, 0)
             store(s - 4, 1, by_scalar)

@@ -12,6 +12,7 @@ PAIRS = S // (2 * P)
 N_PAIRS = B * PAIRS
 BANK = 512
 QUARTERS = D // P
+N_QUARTERS = B * HALVES * QUARTERS
 
 F32 = mybir.dt.float32
 BF16 = mybir.dt.bfloat16
@@ -26,15 +27,7 @@ AX = mybir.AxisListType
 FLOPS = 2 * B * S * D * S + 2 * B * S * D * D + 2 * B * S * S * D
 
 BOTH, FIRST, SECOND = slice(0, 2), slice(0, 1), slice(1, 2)
-
-LOGIT_BANK, RING_BANK, OUT_BANK, V_BANK, X_BANK = 0, 2, 4, 6, 7
-RING_BANKS, RING_USES = 4, 6
-
-STORE_LAG = 3
-VECTOR_COLUMNS = 192
-
-WIDE_BUFS = 2
-
+RING = 4
 FIRST_TILEWISE_PAIR = N_PAIRS - 5
 
 
@@ -45,8 +38,19 @@ def tile_mixturedenserandomsynthesizer_t_kernel(tc, x_bytes, x_scale, w, rnd, mi
         work = ctx.enter_context(tc.tile_pool(name="work", bufs=2))
         psum = ctx.enter_context(tc.psum_pool(name="psum", bufs=1))
 
-        def shared_bank(k):
-            return psum.tile([P, PACK, P], F32, name="bank%d" % k)
+        free_banks = {"vector": list(range(RING)), "scalar": list(range(RING, 2 * RING))}
+        held = {}
+
+        def take_bank(ring, key, shape=(P, PACK, P)):
+            k = free_banks[ring][0]
+            free_banks[ring].remove(k)
+            held[key] = (ring, k, psum.tile(list(shape), F32, name="bank%d" % k))
+            return held.get(key)[2]
+
+        def give_bank(key):
+            ring, k, bank = held.get(key)
+            free_banks[ring].append(k)
+            return bank
 
         scale_4 = keep.tile([P, PACK], F32, name="scale_4")
         mix_raw = keep.tile([2, 1], BF16, name="mix_raw")
@@ -71,19 +75,19 @@ def tile_mixturedenserandomsynthesizer_t_kernel(tc, x_bytes, x_scale, w, rnd, mi
             rnd_raw[k] = keep.tile([P, 2, S], BF16, name="rnd_raw%d" % k)
             nc.sync.dma_start(out=rnd_raw[k][:], in_=rnd_rows[k // 2, :, 2 * (k % 2) : 2 * (k % 2) + 2])
 
-        nc.sync.dma_start(out=scale_4[:], in_=x_scale.rearrange("a b (p t) -> p (a b t)", t=PACK))
-        nc.sync.dma_start(out=mix_raw[:], in_=mix.rearrange("(p o) -> p o", o=1))
         load_x(0, 0)
         load_w(0)
+        nc.sync.dma_start(out=scale_4[:], in_=x_scale.rearrange("a b (p t) -> p (a b t)", t=PACK))
+        nc.sync.dma_start(out=mix_raw[:], in_=mix.rearrange("(p o) -> p o", o=1))
+        load_x(0, 1)
         load_w(1)
         load_rnd(0)
-        load_x(0, 1)
-        nc.sync.dma_start(out=c_raw[:], in_=c.rearrange("(g p t) -> p g t", p=P, t=PACK))
         nc.sync.dma_start(out=wv_raw[:], in_=wv.rearrange("(p j) n -> p j n", j=PACK))
-        load_rnd(1)
+        nc.sync.dma_start(out=c_raw[:], in_=c.rearrange("(g p t) -> p g t", p=P, t=PACK))
         nc.sync.dma_start(out=u_raw[:], in_=u.rearrange("(h p t) -> p h t", p=P, t=PACK))
-        load_rnd(2)
+        load_rnd(1)
         load_x(1, 0)
+        load_rnd(2)
         load_rnd(3)
         load_x(1, 1)
         for b in range(2, B):
@@ -94,14 +98,11 @@ def tile_mixturedenserandomsynthesizer_t_kernel(tc, x_bytes, x_scale, w, rnd, mi
         make_identity(nc, ident[:])
         mix_column = keep.tile([P, 1], F32, name="mix_column")
         nc.vector.memset(mix_column[:], 0.0)
-        mix_f = keep.tile([P, 2], F32, name="mix_f")
+        mix_f = keep.tile([P, 1], F32, name="mix_f")
         u_f = keep.tile([P, HALVES, PACK], F32, name="u_f")
         c_4 = keep.tile([P, HALVES * PACK], F32, name="c_4")
-        c_f = keep.tile([P, 1, S], F32, name="c_f")
+        c_f = keep.tile([P, S + BANK], F32, name="c_f")
         mix_diag = keep.tile([P, P], BF16, name="mix_diag")
-        rnd_f = []
-        for k in range(PAIRS):
-            rnd_f.append(keep.tile([P, S], F32, name="rnd_f%d" % k))
         w_grouped, w_codes, w_scales = [], [], []
         for g in range(HALVES):
             w_grouped.append(keep.tile([P, BANK, PACK], BF16, name="gained%d" % (1 - g), align_bytes=64))
@@ -133,37 +134,39 @@ def tile_mixturedenserandomsynthesizer_t_kernel(tc, x_bytes, x_scale, w, rnd, mi
         def column_split(ap):
             return ap.rearrange("p (h m e) -> p h m e", h=2, e=2)
 
-        def spread(columns, k):
-            bank = shared_bank(k)
+        def spread(columns, key):
+            bank = take_bank("scalar", key)
             for t in range(PACK):
                 nc.tensor.transpose(bank[:, t, :], columns[:, t : t + 1].to_broadcast([P, P]), ident[:])
-            return bank
 
         def mix_spread():
-            bank = shared_bank(OUT_BANK)
+            bank = take_bank("scalar", "mix")
             nc.tensor.transpose(bank[:, 0, :], mix_column[:].to_broadcast([P, P]), ident[:])
-            nc.scalar.copy(out=mix_f[:], in_=bank[:, 0, 0:2])
 
-        def mix_diagonal():
-            nc.gpsimd.tensor_scalar(
-                out=mix_diag[:], in0=ident[:], scalar1=mix_f[:, 1:2], scalar2=0.0, op0=Alu.mult, op1=Alu.add
-            )
+        def mix_out():
+            bank = give_bank("mix")
+            nc.vector.tensor_copy(out=mix_f[:], in_=bank[:, 0, 0:1])
+            nc.vector.tensor_scalar(out=mix_diag[:], in0=ident[:], scalar1=bank[:, 0, 1:2], scalar2=None, op0=Alu.mult)
 
         def c_spread(g):
-            bank = spread(c_4[:, g * PACK : (g + 1) * PACK], V_BANK + g)
-            nc.scalar.copy(
-                out=column_split(c_f[:, 0, g * BANK : (g + 1) * BANK]),
-                in_=bank[:].rearrange("p (h e) m -> p h m e", h=2),
+            spread(c_4[:, g * PACK : (g + 1) * PACK], ("c", g))
+
+        def c_out(g, copy):
+            copy(
+                out=column_split(c_f[:, g * BANK : (g + 1) * BANK]),
+                in_=give_bank(("c", g))[:].rearrange("p (h e) m -> p h m e", h=2),
             )
+
+        def c_again():
+            copy_by_gpsimd(c_f[:, S : S + BANK], c_f[:, 0:BANK])
 
         def copy_by_gpsimd(out, in_):
             nc.gpsimd.tensor_scalar(out=out, in0=in_, scalar1=1.0, scalar2=0.0, op0=Alu.mult, op1=Alu.add)
 
-        def w_group(g):
+        def w_group(g, h, copy):
             src = w_raw[g][:].rearrange("p j (m h e) -> p h m e j", h=2, e=2)
             dst = w_grouped[g][:].rearrange("p (h m e) j -> p h m e j", h=2, e=2)
-            nc.scalar.copy(out=dst[:, 0], in_=src[:, 0])
-            copy_by_gpsimd(dst[:, 1], src[:, 1])
+            copy(out=dst[:, h], in_=src[:, h])
 
         def w_quantize(g):
             quantize(w_codes[g][:], w_scales[g][:], w_grouped[g][:].rearrange("p n j -> p (n j)"))
@@ -175,53 +178,27 @@ def tile_mixturedenserandomsynthesizer_t_kernel(tc, x_bytes, x_scale, w, rnd, mi
         def wv_quantize():
             quantize(wv_codes[:], wv_scales[:], wv_grouped[0][:].rearrange("p n j -> p (n j)"))
 
-        def rnd_scale_by_gpsimd(k):
-            for g in range(HALVES):
-                cols = slice(g * BANK, (g + 1) * BANK)
-                nc.gpsimd.tensor_scalar(
-                    out=column_split(rnd_f[k][:, cols]),
-                    in0=key_split(rnd_raw[k][:, 0, cols]),
-                    scalar1=mix_f[:, 1:2],
-                    scalar2=0.0,
-                    op0=Alu.mult,
-                    op1=Alu.add,
-                )
-
-        def rnd_scale(k):
-            nc.scalar.activation(
-                out=rnd_f[k][:].rearrange("p (g h m e) -> p g h m e", g=HALVES, h=2, e=2)[:, 0],
-                in_=key_split(rnd_raw[k][:, 0, 0:BANK]),
-                func=Act.Copy,
-                scale=mix_f[:, 1:2],
-            )
-            nc.scalar.activation(
-                out=rnd_f[k][:].rearrange("p (g h m e) -> p g h m e", g=HALVES, h=2, e=2)[:, 1],
-                in_=key_split(rnd_raw[k][:, 0, BANK:S]),
-                func=Act.Copy,
-                scale=mix_f[:, 1:2],
-            )
-
-        x_wide, x_turned, x_grouped, x_codes, x_scales = {}, {}, {}, {}, {}
+        x_wide, x_grouped, x_codes, x_scales = {}, {}, {}, {}
 
         def x_widen(q):
             b, h, t = q // PAIRS, (q % PAIRS) // 2, 2 * (q % 2)
-            x_wide[q] = work.tile([P, 2 * D], BF16, name="wide", bufs=WIDE_BUFS)
+            x_wide[q] = work.tile([P, 2 * D], BF16, name="wide", bufs=2)
             nc.scalar.copy(
                 out=x_wide[q][:], in_=x_raw.get((b, h))[:, t : t + 2, :].rearrange("p t k -> p (t k)").bitcast(FP8)
             )
 
-        def x_turn(q, k):
+        def x_turn(q, tiles=BOTH):
             words = x_wide[q][:].bitcast(F32)
-            x_turned[q] = shared_bank(k)
-            for j in range(2):
+            if tiles.start == 0:
+                take_bank("vector", ("x", q))
+            bank = held.get(("x", q))[2]
+            for j in range(tiles.start, tiles.stop):
                 for h in range(2):
-                    nc.tensor.transpose(
-                        x_turned[q][:, 2 * h + j, :], words[:, 2 * P * j + h : 2 * P * (j + 1) : 2], ident[:]
-                    )
+                    nc.tensor.transpose(bank[:, 2 * h + j, :], words[:, 2 * P * j + h : 2 * P * (j + 1) : 2], ident[:])
 
         def x_scale_out(q):
             x_grouped[q] = work.tile([P, 2 * P, PACK], BF16, name="x_grouped", align_bytes=64)
-            values = x_turned[q][:].rearrange("p (h j) q -> p h (j q)", h=2).bitcast(BF16)
+            values = give_bank(("x", q))[:].rearrange("p (h j) q -> p h (j q)", h=2).bitcast(BF16)
             nc.vector.tensor_tensor(
                 out=x_grouped[q][:].rearrange("p q (h e) -> p q h e", e=2),
                 in0=values.rearrange("p h (q e) -> p q h e", e=2),
@@ -234,10 +211,10 @@ def tile_mixturedenserandomsynthesizer_t_kernel(tc, x_bytes, x_scale, w, rnd, mi
             x_scales[q] = work.tile([P, 2 * P], U8, name="x_scales", bufs=7, align_bytes=64)
             quantize(x_codes[q][:], x_scales[q][:], x_grouped[q][:].rearrange("p q t -> p (q t)"))
 
-        v_sums, v_grouped, v_codes, v_scales = {}, {}, {}, {}
+        v_grouped, v_codes, v_scales = {}, {}, {}
 
-        def v_product(hh, n, k):
-            sums = shared_bank(k)
+        def v_product(hh, n):
+            sums = take_bank("vector", ("v", hh, n))
             d_cols = slice(n * P, (n + 1) * P)
             for t in range(PACK):
                 q, rows = 2 * hh + t // 2, slice((t % 2) * P, (t % 2 + 1) * P)
@@ -245,7 +222,6 @@ def tile_mixturedenserandomsynthesizer_t_kernel(tc, x_bytes, x_scale, w, rnd, mi
                     sums[:, t, :], x_codes[q][:, rows], x_scales[q][:, rows],
                     wv_codes[:, d_cols], wv_scales[:, d_cols], True, True,
                 )
-            v_sums[(hh, n)] = sums
 
         def v_gain(hh, n):
             if hh not in v_grouped:
@@ -253,65 +229,46 @@ def tile_mixturedenserandomsynthesizer_t_kernel(tc, x_bytes, x_scale, w, rnd, mi
             h = hh % HALVES
             nc.vector.tensor_tensor(
                 out=v_grouped[hh][:, n * P : (n + 1) * P, :],
-                in0=v_sums.get((hh, n))[:].rearrange("p t d -> p d t"),
+                in0=give_bank(("v", hh, n))[:].rearrange("p t d -> p d t"),
                 in1=u_f[:, h : h + 1, :].to_broadcast([P, P, PACK]),
                 op=Alu.mult,
             )
 
-        def v_quantize(hh):
-            v_codes[hh] = work.tile([P, D], U32, name="v_codes", bufs=4, align_bytes=64)
-            v_scales[hh] = work.tile([P, D], U8, name="v_scales", bufs=4, align_bytes=64)
-            quantize(v_codes[hh][:], v_scales[hh][:], v_grouped[hh][:].rearrange("p d t -> p (d t)"))
-
-        turned_scores, mixed_scores, psum_logits = {}, {}, {}
-        scores, logits, maxima, exps, totals, inverses = {}, {}, {}, {}, {}, {}
-        gained, pcs, turned_pcs, grouped_pcs, p_codes, p_scales, sums_out, rows_out = {}, {}, {}, {}, {}, {}, {}, {}
-
-        def score(q, g):
-            bank = psum.tile([P, BANK], F32, name="bank%d" % (LOGIT_BANK + g))
-            multiply(bank[:], x_codes[q][:, 0:P], x_scales[q][:, 0:P], w_codes[g][:], w_scales[g][:], True, True)
-            scores[(q, g)] = bank
-
-        def blend(q, g):
-            if q not in logits:
-                logits[q] = work.tile([P, 2, S], F32, name="logit")
-                maxima[q] = work.tile([P, 4], F32, name="maximum")
-            keys = slice(g * BANK, (g + 1) * BANK)
-            nc.vector.scalar_tensor_tensor(
-                out=logits[q][:, 0, keys],
-                in0=scores.get((q, g))[:],
-                scalar=mix_f[:, 0:1],
-                in1=rnd_f[q % PAIRS][:, keys],
-                op0=Alu.mult,
-                op1=Alu.add,
+        def v_quantize(hh, features=slice(0, D)):
+            if hh not in v_codes:
+                v_codes[hh] = work.tile([P, D], U32, name="v_codes", bufs=4, align_bytes=64)
+                v_scales[hh] = work.tile([P, D], U8, name="v_scales", bufs=4, align_bytes=64)
+            quantize(
+                v_codes[hh][:, features], v_scales[hh][:, features],
+                v_grouped[hh][:, features].rearrange("p d t -> p (d t)"),
             )
 
-        def maximum(q):
-            nc.vector.tensor_reduce(out=maxima[q][:, 0:1], in_=logits[q][:, 0], axis=AX.X, op=Alu.max, negate=True)
+        mixed_scores = {}
+        logits, maxima, exps, totals, inverses = {}, {}, {}, {}, {}
+        gained, pcs, divided, grouped_pcs = {}, {}, {}, {}
+        p_codes, p_scales, rows_out = {}, {}, {}
 
-        def score_turned(q, g, k, j=1):
-            bank = shared_bank(k)
-            rows = slice(j * P, (j + 1) * P)
-            for n in range(PACK):
-                keys = slice(n * P, (n + 1) * P)
+        def score_turned(q, n):
+            bank = take_bank("scalar", ("score", q, n), (P, 2, 2 * P))
+            for i in range(2):
+                keys = slice((2 * (n % 2) + i) * P, (2 * (n % 2) + i + 1) * P)
                 multiply(
-                    bank[:, n, :], w_codes[g][:, keys], w_scales[g][:, keys],
-                    x_codes[q][:, rows], x_scales[q][:, rows], True, True,
+                    bank[:, i, :], w_codes[n // 2][:, keys], w_scales[n // 2][:, keys],
+                    x_codes[q][:], x_scales[q][:], True, True,
                 )
-            turned_scores[(q, j, g)] = bank
 
-        def score_out(q, g, j=1):
-            if (q, j) not in mixed_scores:
-                mixed_scores[(q, j)] = work.tile([P, HALVES, PACK, P], F32, name="mixed_scores")
+        def score_out(q, n):
+            if (q, n // 2) not in mixed_scores:
+                mixed_scores[(q, n // 2)] = work.tile([P, PACK, 2 * P], F32, name="mixed_scores%d" % (n // 2))
             nc.scalar.activation(
-                out=mixed_scores.get((q, j))[:, g],
-                in_=turned_scores.get((q, j, g))[:],
+                out=mixed_scores.get((q, n // 2))[:, 2 * (n % 2) : 2 * (n % 2) + 2],
+                in_=give_bank(("score", q, n))[:],
                 func=Act.Copy,
-                scale=mix_f[:, 0:1],
+                scale=mix_f[:],
             )
 
-        def rnd_into_psum(q, g, k, j=1):
-            bank = psum.tile([P, BANK], F32, name="bank%d" % k)
+        def blend_open(q, j, g):
+            bank = take_bank("vector", ("logit", q, j, g), (P, BANK))
             nc.tensor.matmul(
                 bank[:].rearrange("p (h m e) -> p m h e", h=2, e=2),
                 lhsT=mix_diag[:],
@@ -319,31 +276,30 @@ def tile_mixturedenserandomsynthesizer_t_kernel(tc, x_bytes, x_scale, w, rnd, mi
                 start=True,
                 stop=False,
             )
-            psum_logits[(q, j, g)] = bank
 
-        def score_into_psum(q, g, j=1):
+        def blend_close(q, j, g):
             for n in range(PACK):
                 nc.tensor.matmul(
-                    psum_logits.get((q, j, g))[:, n * P : (n + 1) * P],
-                    lhsT=mixed_scores.get((q, j))[:, g, n, :],
+                    held.get(("logit", q, j, g))[2][:, n * P : (n + 1) * P],
+                    lhsT=mixed_scores.get((q, g))[:, n, j * P : (j + 1) * P],
                     rhs=ident[:],
                     start=False,
                     stop=n == PACK - 1,
                     is_transpose=True,
                 )
 
-        def blend_in_psum(q, g):
-            rnd_into_psum(q, g, LOGIT_BANK + g)
-            score_into_psum(q, g)
+        def blend(q, j, g):
+            blend_open(q, j, g)
+            blend_close(q, j, g)
 
-        def logit_out(q, g, j=1):
+        def logit_out(q, j, g):
             if q not in logits:
                 logits[q] = work.tile([P, 2, S], F32, name="logit")
                 maxima[q] = work.tile([P, 4], F32, name="maximum")
             first = maxima[q][:, 2 + j : 3 + j]
             nc.vector.tensor_scalar(
                 out=logits[q][:, j, g * BANK : (g + 1) * BANK],
-                in0=psum_logits.get((q, j, g))[:],
+                in0=give_bank(("logit", q, j, g))[:],
                 scalar1=-1.0,
                 scalar2=None if g == 0 else first,
                 op0=Alu.mult,
@@ -353,79 +309,98 @@ def tile_mixturedenserandomsynthesizer_t_kernel(tc, x_bytes, x_scale, w, rnd, mi
 
         def exponent(q, j):
             if q not in exps:
-                exps[q] = work.tile([P, 2, S], F32, name="exp")
+                exps[q] = work.tile([P, 2 * S], F32, name="exp")
                 totals[q] = work.tile([P, 2], F32, name="total")
             nc.scalar.activation(
-                out=exps[q][:, j],
+                out=exps[q][:, j * S : (j + 1) * S],
                 in_=logits[q][:, j],
                 func=Act.Exp,
                 bias=maxima[q][:, j : j + 1],
-                scale=1.0 if j == 0 else -1.0,
+                scale=-1.0,
                 accum_out=totals[q][:, j : j + 1],
             )
 
         def invert(q, tiles=BOTH):
-            if tiles.start == 0:
+            if q not in inverses:
                 inverses[q] = work.tile([P, 2], F32, name="inverse")
             nc.vector.reciprocal(out=inverses[q][:, tiles], in_=totals[q][:, tiles])
 
-        def gain(q, tiles=BOTH):
-            gained[q] = keep.tile([P, 2, S], F32, name="gained%d" % (q % 2), align_bytes=64)
-            nc.gpsimd.tensor_tensor(
-                out=gained[q][:, tiles],
-                in0=exps[q][:, tiles],
-                in1=c_f[:].to_broadcast([P, tiles.stop - tiles.start, S]),
-                op=Alu.mult,
-            )
+        def gain(q, columns=slice(0, S + BANK)):
+            if q not in gained:
+                gained[q] = keep.tile([P, S + BANK], F32, name="gained%d" % (q % 2), align_bytes=64)
+            nc.gpsimd.tensor_tensor(out=gained[q][:, columns], in0=exps[q][:, columns], in1=c_f[:, columns], op=Alu.mult)
 
         def pc_tile(q):
             if q not in pcs:
-                pcs[q] = work.tile([P, 2, S], BF16, name="pc", bufs=3)
+                pcs[q] = work.tile([P, 2 * S], BF16, name="pc")
             return pcs[q]
 
-        def divide_and_gain(q, j):
-            nc.vector.scalar_tensor_tensor(
-                out=pc_tile(q)[:, j],
-                in0=exps[q][:, j],
-                scalar=inverses[q][:, j : j + 1],
-                in1=c_f[:, 0],
-                op0=Alu.mult,
-                op1=Alu.mult,
-            )
-
-        def divide_by_gpsimd(q, j, keys=slice(0, S)):
-            nc.gpsimd.tensor_scalar(
-                out=pc_tile(q)[:, j, keys],
-                in0=gained[q][:, j, keys],
+        def divide(q, j, columns, engine=nc.gpsimd):
+            engine.tensor_scalar(
+                out=pc_tile(q)[:, columns],
+                in0=gained[q][:, columns],
                 scalar1=inverses[q][:, j : j + 1],
                 scalar2=0.0,
                 op0=Alu.mult,
                 op1=Alu.add,
             )
 
-        def divide_by_scalar(q, j, keys=slice(0, S)):
-            nc.scalar.activation(
-                out=pc_tile(q)[:, j, keys],
-                in_=gained[q][:, j, keys],
-                func=Act.Copy,
-                scale=inverses[q][:, j : j + 1],
+        def divide_ungained(q, j=1, g=1):
+            divided[(q, j, g)] = work.tile([P, PACK, P], F32, name="divided", bufs=3)
+            nc.gpsimd.tensor_scalar(
+                out=divided.get((q, j, g))[:].rearrange("p (h e) m -> p h e m", e=2),
+                in0=exps[q][:, j * S + g * BANK : j * S + (g + 1) * BANK].rearrange("p (h m e) -> p h e m", h=2, e=2),
+                scalar1=inverses[q][:, j : j + 1],
+                scalar2=0.0,
+                op0=Alu.mult,
+                op1=Alu.add,
             )
 
-        def turn(q, j, k):
-            words = pcs[q][:, j].bitcast(F32)
-            bank = shared_bank(k)
-            for n in range(PACK):
-                nc.tensor.transpose(bank[:, n, :], words[:, n * P : (n + 1) * P], ident[:])
-            turned_pcs[(q, j)] = bank
+        def divide_by_scalar(q, j, columns):
+            nc.scalar.activation(
+                out=pc_tile(q)[:, columns], in_=gained[q][:, columns], func=Act.Copy, scale=inverses[q][:, j : j + 1]
+            )
 
-        def turn_out(q, j, copy=nc.scalar.copy):
+        def divide_and_gain(q, j, g):
+            columns = slice(j * S + g * BANK, j * S + (g + 1) * BANK)
+            nc.vector.scalar_tensor_tensor(
+                out=pc_tile(q)[:, columns],
+                in0=exps[q][:, columns],
+                scalar=inverses[q][:, j : j + 1],
+                in1=c_f[:, g * BANK : (g + 1) * BANK],
+                op0=Alu.mult,
+                op1=Alu.mult,
+            )
+
+        def grouped_tile(q):
             if q not in grouped_pcs:
-                grouped_pcs[q] = work.tile(
-                    [P, 2, HALVES, P, PACK], BF16, name="p_grouped", bufs=3, align_bytes=64
-                )
+                grouped_pcs[q] = work.tile([P, 2, HALVES, P, PACK], BF16, name="p_grouped", bufs=4, align_bytes=64)
+            return grouped_pcs[q]
+
+        def turn(q, j, halves=BOTH, ring="scalar"):
+            words = pcs[q][:, j * S : (j + 1) * S].bitcast(F32)
+            bank = take_bank(ring, ("pc", q, j, halves.start))
+            for n in range(2 * halves.start, 2 * halves.stop):
+                nc.tensor.transpose(bank[:, n, :], words[:, n * P : (n + 1) * P], ident[:])
+
+        def turn_out(q, j, halves=BOTH, copy=nc.scalar.copy):
+            bank = give_bank(("pc", q, j, halves.start))
             copy(
-                out=grouped_pcs[q][:, j].bitcast(F32),
-                in_=turned_pcs.get((q, j))[:].rearrange("p (g h) q -> p g q h", h=2),
+                out=grouped_tile(q)[:, j, halves].bitcast(F32),
+                in_=bank[:, 2 * halves.start : 2 * halves.stop].rearrange("p (g h) q -> p g q h", h=2),
+            )
+
+        def turn_ungained(q, j=1, g=1):
+            bank = take_bank("vector", ("divided", q, j, g))
+            for t in range(PACK):
+                nc.tensor.transpose(bank[:, t, :], divided.get((q, j, g))[:, t, :], ident[:])
+
+        def gain_out(q, j=1, g=1):
+            nc.vector.tensor_tensor(
+                out=grouped_tile(q)[:, j, g],
+                in0=give_bank(("divided", q, j, g))[:].rearrange("p t q -> p q t"),
+                in1=c_4[:, g * PACK : (g + 1) * PACK].rearrange("p (o t) -> p o t", o=1).to_broadcast([P, P, PACK]),
+                op=Alu.mult,
             )
 
         def p_quantize(q, tiles=BOTH):
@@ -437,365 +412,356 @@ def tile_mixturedenserandomsynthesizer_t_kernel(tc, x_bytes, x_scale, w, rnd, mi
                 p_codes[q][:, cols], p_scales[q][:, cols], grouped_pcs[q][:, tiles].rearrange("p j g q t -> p (j g q t)")
             )
 
-        def product(q, j, k):
-            bank = shared_bank(k)
+        def product(q, j, ring="scalar"):
+            bank = take_bank(ring, ("out", q, j), (P, D))
             for g in range(HALVES):
                 cols = slice((2 * j + g) * P, (2 * j + g + 1) * P)
                 hh = HALVES * (q // PAIRS) + g
                 multiply(
-                    bank[:].rearrange("p t d -> p (t d)"), p_codes[q][:, cols], p_scales[q][:, cols],
+                    bank[:], p_codes[q][:, cols], p_scales[q][:, cols],
                     v_codes[hh][:], v_scales[hh][:], g == 0, g == HALVES - 1,
                 )
-            sums_out[(q, j)] = bank
 
-        def store_part(q, j, copy, cols):
-            copy(out=rows_out[q][:, j, cols], in_=sums_out.get((q, j))[:].rearrange("p t d -> p (t d)")[:, cols])
+        def quantize_half(q, j, g):
+            cols = slice((2 * j + g) * P, (2 * j + g + 1) * P)
+            quantize(p_codes[q][:, cols], p_scales[q][:, cols], grouped_pcs[q][:, j, g].rearrange("p q t -> p (q t)"))
 
-        def store(q, j, copy, cols=slice(0, D)):
-            b, h, t = q // PAIRS, (q % PAIRS) // 2, 2 * (q % 2) + j
-            if q not in rows_out:
-                rows_out[q] = work.tile([P, 2, D], F32, name="rows_out", bufs=5)
-            store_part(q, j, copy, cols)
-            if q >= FIRST_TILEWISE_PAIR:
-                nc.sync.dma_start(out=out_rows[b, h, :, t], in_=rows_out[q][:, j])
-            elif j == 1:
-                nc.sync.dma_start(out=out_rows[b, h, :, t - 1 : t + 1], in_=rows_out[q][:])
+        last_sums = {}
 
-        last_q, last_j = N_PAIRS - 1, 1
-        last_turned, last_sums = {}, {}
-
-        def last_divide(g):
-            keys = slice(g * BANK, (g + 1) * BANK)
-            nc.vector.scalar_tensor_tensor(
-                out=pcs[last_q][:, last_j, keys],
-                in0=exps[last_q][:, last_j, keys],
-                scalar=inverses[last_q][:, last_j : last_j + 1],
-                in1=c_f[:, 0, keys],
-                op0=Alu.mult,
-                op1=Alu.mult,
-            )
-
-        def last_turn(g, k):
-            words = pcs[last_q][:, last_j].bitcast(F32)
-            last_turned[g] = shared_bank(k)
-            for h in range(2):
-                n = 2 * g + h
-                nc.tensor.transpose(last_turned[g][:, h, :], words[:, n * P : (n + 1) * P], ident[:])
-
-        def last_turn_out(g):
-            nc.scalar.copy(
-                out=grouped_pcs[last_q][:, last_j, g].bitcast(F32),
-                in_=last_turned[g][:, 0:2].rearrange("p h q -> p q h"),
-            )
-
-        def last_quantize(g):
-            cols = slice((2 * last_j + g) * P, (2 * last_j + g + 1) * P)
-            quantize(
-                p_codes[last_q][:, cols], p_scales[last_q][:, cols],
-                grouped_pcs[last_q][:, last_j, g].rearrange("p q t -> p (q t)"),
-            )
-
-        def last_product(g, banks):
-            cols = slice((2 * last_j + g) * P, (2 * last_j + g + 1) * P)
+        def last_product(g):
+            cols = slice((2 + g) * P, (3 + g) * P)
             hh = HALVES * (B - 1) + g
-            for n, k in enumerate(banks):
+            for n, ring in enumerate(("vector", "scalar")):
                 if g == 0:
-                    last_sums[n] = psum.tile([P, D // 2], F32, name="bank%d" % k)
+                    last_sums[n] = take_bank(ring, ("last", n), (P, D // 2))
                 d_cols = slice(n * D // 2, (n + 1) * D // 2)
                 multiply(
-                    last_sums[n][:], p_codes[last_q][:, cols], p_scales[last_q][:, cols],
+                    last_sums[n][:], p_codes[N_PAIRS - 1][:, cols], p_scales[N_PAIRS - 1][:, cols],
                     v_codes[hh][:, d_cols], v_scales[hh][:, d_cols], g == 0, g == HALVES - 1,
                 )
 
         def last_store(n, copy):
             d_cols = slice(n * D // 2, (n + 1) * D // 2)
-            copy(out=rows_out[last_q][:, last_j, d_cols], in_=last_sums[n][:])
-            nc.sync.dma_start(out=out_rows[B - 1, HALVES - 1, :, PACK - 1, d_cols], in_=rows_out[last_q][:, last_j, d_cols])
+            copy(out=rows_out[N_PAIRS - 1][:, 1, d_cols], in_=give_bank(("last", n))[:])
+            nc.sync.dma_start(
+                out=out_rows[B - 1, HALVES - 1, :, PACK - 1, d_cols], in_=rows_out[N_PAIRS - 1][:, 1, d_cols]
+            )
+
+        stored_tiles = {}
+
+        def store(q, j, copy=nc.scalar.copy):
+            b, h, t = q // PAIRS, (q % PAIRS) // 2, 2 * (q % 2)
+            if q not in rows_out:
+                rows_out[q] = work.tile([P, 2, D], F32, name="rows_out", bufs=4)
+            copy(out=rows_out[q][:, j], in_=give_bank(("out", q, j))[:])
+            stored_tiles[q] = stored_tiles.get(q, 0) + 1
+            if q >= FIRST_TILEWISE_PAIR:
+                nc.sync.dma_start(out=out_rows[b, h, :, t + j], in_=rows_out[q][:, j])
+            elif stored_tiles[q] == 2:
+                nc.sync.dma_start(out=out_rows[b, h, :, t : t + 2], in_=rows_out[q][:])
 
         by_scalar, by_vector = nc.scalar.copy, nc.vector.tensor_copy
 
+        def live(q):
+            return 0 <= q < N_PAIRS
+
+        def quarter(n):
+            return divmod(n, QUARTERS)
+
+        def step(s):
+            exponent(s, 1)
+            exponent(s, 0)
+            blend(s + 1, 0, 1)
+            if live(s - 2):
+                turn(s - 2, 1, FIRST)
+                turn(s - 2, 0)
+            x_quantize(s + 2)
+            features = slice(0 if s == 1 else s % 2 * D // 2, (s % 2 + 1) * D // 2)
+            if not live(s - 3):
+                invert(s - 1)
+                v_quantize(s // 2, features)
+                divide_by_scalar(s - 1, 1, slice(S, S + BANK))
+            elif live(s + 4):
+                v_quantize(s // 2, features)
+                invert(s - 1, SECOND)
+                p_quantize(s - 3)
+                invert(s - 1, FIRST)
+                divide(s - 1, 1, slice(S, S + BANK), nc.vector)
+            else:
+                v_quantize(s // 2, features)
+                invert(s - 1)
+                p_quantize(s - 3)
+                divide_by_scalar(s - 1, 1, slice(S, S + BANK))
+            divide(s - 1, 0, slice(0, S))
+            divide_ungained(s - 1)
+            gain(s)
+            if live(s - 3):
+                product(s - 3, 0)
+                product(s - 3, 1)
+            else:
+                score_turned(s + 2, 0)
+                score_turned(s + 2, 1)
+            if live(s - 2):
+                turn_out(s - 2, 0)
+                turn_out(s - 2, 1, FIRST)
+            logit_out(s + 1, 0, 0)
+            logit_out(s + 1, 1, 0)
+            blend(s + 1, 1, 1)
+            if live(s - 2):
+                turn_ungained(s - 2)
+            if live(s + 4):
+                x_widen(s + 4)
+            logit_out(s + 1, 0, 1)
+            x_scale_out(s + 3)
+            if live(s - 3):
+                store(s - 3, 1)
+                store(s - 3, 0)
+                score_turned(s + 2, 0)
+                score_turned(s + 2, 1)
+            v_product(*quarter(2 * s + 2))
+            if live(s - 3):
+                v_product(*quarter(2 * s + 3))
+            score_turned(s + 2, 2)
+            score_turned(s + 2, 3)
+            if not live(s - 3):
+                v_product(*quarter(2 * s + 3))
+            if live(s - 2):
+                gain_out(s - 2)
+            logit_out(s + 1, 1, 1)
+            if live(s + 4):
+                x_turn(s + 4)
+            score_out(s + 2, 1)
+            score_out(s + 2, 0)
+            blend(s + 2, 1, 0)
+            v_gain(*quarter(2 * s + 3))
+            score_out(s + 2, 3)
+            score_out(s + 2, 2)
+            blend(s + 2, 0, 0)
+            v_gain(*quarter(2 * s + 2))
+
         with tc.manual_schedule():
-            nc.scalar.activation(out=mix_column[0:2], in_=mix_raw[:], func=Act.Copy)
             x_widen(0)
-            mix_spread()
-            x_turn(0, X_BANK)
+            x_turn(0)
             x_widen(1)
-            mix_diagonal()
-            x_turn(1, V_BANK)
-            w_group(0)
-            w_group(1)
-            x_scale_out(0)
-            x_scale_out(1)
-            rnd_scale(0)
+            w_group(0, 0, by_vector)
+            w_group(0, 1, by_scalar)
+            by_vector(out=mix_column[0:2], in_=mix_raw[:])
+            mix_spread()
+            x_turn(1)
             x_widen(2)
-            rnd_into_psum(0, 0, 4)
-            rnd_into_psum(0, 1, 5)
+            w_group(1, 0, by_scalar)
+            w_group(1, 1, by_scalar)
+            x_scale_out(0)
+            mix_out()
+            x_turn(2)
+            blend_open(0, 0, 0)
             w_quantize(0)
             x_quantize(0)
+            score_turned(0, 0)
+            score_turned(0, 1)
+            blend_open(0, 1, 0)
+            x_scale_out(1)
+            by_vector(out=c_4[:], in_=c_raw[:].rearrange("p g t -> p (g t)"))
+            by_vector(out=u_f[:], in_=u_raw[:])
             x_quantize(1)
             w_quantize(1)
-            x_widen(3)
             wv_group()
-            copy_by_gpsimd(u_f[:], u_raw[:])
-            by_scalar(out=c_4[:], in_=c_raw[:].rearrange("p g t -> p (g t)"))
-            rnd_scale(1)
-            rnd_scale_by_gpsimd(2)
-            score(0, 0)
-            x_turn(2, X_BANK)
-            score(0, 1)
-            score_turned(0, 0, 2)
-            score_turned(0, 1, 3)
-            blend(0, 0)
-            x_scale_out(2)
-            blend(0, 1)
-            score(1, 0)
             score_out(0, 0)
             score_out(0, 1)
-            for g in range(HALVES):
-                c_spread(g)
-            score_into_psum(0, 0)
-            score(1, 1)
-            score_turned(1, 0, 2)
-            score_into_psum(0, 1)
-            score_turned(1, 1, 3)
-            x_turn(3, V_BANK)
-            maximum(0)
-            logit_out(0, 0)
-            blend(1, 0)
-            logit_out(0, 1)
-            wv_quantize()
-            x_quantize(2)
-
-            exponent(0, 0)
+            score_turned(1, 0)
+            blend_close(0, 0, 0)
+            score_turned(0, 2)
+            score_turned(0, 3)
+            x_widen(3)
+            blend_close(0, 1, 0)
+            x_turn(3)
+            score_turned(1, 1)
+            x_scale_out(2)
+            score_out(0, 2)
+            score_out(0, 3)
+            logit_out(0, 0, 0)
+            logit_out(0, 1, 0)
+            blend(0, 0, 1)
+            score_turned(1, 2)
+            score_turned(1, 3)
+            blend(0, 1, 1)
             score_out(1, 0)
-            exponent(0, 1)
             score_out(1, 1)
-            gain(0)
-            rnd_into_psum(1, 0, 4)
-            rnd_into_psum(1, 1, 5)
-            score_into_psum(1, 0)
-            v_product(0, 0, X_BANK)
-            score(2, 0)
-            v_product(0, 1, 2)
-            score_into_psum(1, 1)
-            blend(1, 1)
             x_scale_out(3)
-            score_turned(2, 0, 3)
-            v_product(0, 2, V_BANK)
-            x_widen(4)
-            rnd_scale(3)
-            logit_out(1, 0)
+            logit_out(0, 0, 1)
+            c_spread(0)
+            blend(1, 1, 0)
+            c_spread(1)
+            blend(1, 0, 0)
+            x_quantize(2)
+            wv_quantize()
+            logit_out(0, 1, 1)
+            score_out(1, 2)
+            score_out(1, 3)
+
+            c_out(0, by_scalar)
+            c_again()
+            c_out(1, by_scalar)
+            exponent(0, 0)
+            gain(0, slice(0, S))
+            exponent(0, 1)
+            gain(0, slice(S, S + BANK))
+            v_product(0, 0)
+            v_product(0, 1)
+            score_turned(2, 0)
+            score_turned(2, 1)
+            logit_out(1, 0, 0)
+            logit_out(1, 1, 0)
+            blend(1, 0, 1)
+            blend(1, 1, 1)
             v_gain(0, 0)
-            logit_out(1, 1)
-            score_turned(2, 1, 4)
-            x_turn(4, X_BANK)
-            score(2, 1)
-            score_out(2, 0)
-            score_out(2, 1)
-            maximum(1)
             v_gain(0, 1)
+            x_widen(4)
+            v_product(0, 2)
+            score_turned(2, 2)
+            score_turned(2, 3)
+            v_product(0, 3)
+            logit_out(1, 0, 1)
+            logit_out(1, 1, 1)
+            x_turn(4)
+            score_out(2, 1)
+            score_out(2, 0)
+            blend(2, 1, 0)
+            v_gain(0, 3)
+            score_out(2, 3)
+            score_out(2, 2)
+            blend(2, 0, 0)
+            v_gain(0, 2)
 
-            for s in range(1, STORE_LAG):
-                ring = [RING_BANK + (RING_USES * s + n) % RING_BANKS for n in range(RING_USES)]
-                opening, closing = divmod(2 * s, QUARTERS), divmod(2 * s + 1, QUARTERS)
-                exponent(s, 0)
-                exponent(s, 1)
-                v_gain(*opening)
-                x_quantize(s + 2)
-                invert(s - 1)
-                if s == 2:
-                    v_quantize(0)
-                divide_by_gpsimd(s - 1, 0)
-                gain(s)
-                v_product(*closing, V_BANK)
-                score_turned(s + 2, 0, ring[0])
-                blend(s + 1, 0)
-                blend(s + 1, 1)
-                blend_in_psum(s + 1, 0)
-                blend_in_psum(s + 1, 1)
-                turn(s - 1, 0, ring[1])
-                score_turned(s + 2, 1, ring[3])
-                divide_by_scalar(s - 1, 1)
-                turn(s - 1, 1, ring[2])
-                x_widen(s + 4)
-                score_out(s + 2, 0)
-                turn_out(s - 1, 0)
-                turn_out(s - 1, 1)
-                x_scale_out(s + 3)
-                logit_out(s + 1, 0)
-                v_gain(*closing)
-                logit_out(s + 1, 1)
-                score(s + 2, 0)
-                v_product(*divmod(2 * s + 2, QUARTERS), V_BANK)
-                x_turn(s + 4, X_BANK)
-                score(s + 2, 1)
-                score_out(s + 2, 1)
-                maximum(s + 1)
-            v_product(1, 3, ring[4])
-            v_gain(1, 2)
+            for s in range(1, N_PAIRS - 3):
+                step(s)
 
-            for s in range(STORE_LAG, N_PAIRS - 3):
-                opening, closing, next_opening = (divmod(2 * s + n, QUARTERS) for n in (1, 2, 3))
-                ring = [RING_BANK + (RING_USES * s + n) % RING_BANKS for n in range(RING_USES)]
-                stored = s - STORE_LAG
-                exponent(s, 0)
-                exponent(s, 1)
-                v_gain(*opening)
-                x_quantize(s + 2)
-                if s % 2 == 0:
-                    invert(s - 1)
-                p_quantize(stored)
-                if s % 2 == 1:
-                    invert(s - 1)
-                    v_quantize(s // 2)
-                divide_by_gpsimd(s - 1, 0)
-                gain(s)
-                v_product(*closing, V_BANK)
-                product(stored, 0, ring[0])
-                blend(s + 1, 0)
-                blend(s + 1, 1)
-                blend_in_psum(s + 1, 0)
-                blend_in_psum(s + 1, 1)
-                turn(s - 1, 0, ring[1])
-                divide_by_scalar(s - 1, 1)
-                turn(s - 1, 1, ring[2])
-                product(stored, 1, ring[3])
-                store(stored, 0, by_scalar)
-                if s + 4 < N_PAIRS:
-                    x_widen(s + 4)
-                turn_out(s - 1, 0)
-                turn_out(s - 1, 1)
-                x_scale_out(s + 3)
-                logit_out(s + 1, 0)
-                v_gain(*closing)
-                logit_out(s + 1, 1)
-                score_turned(s + 2, 0, ring[4])
-                score_turned(s + 2, 1, ring[5])
-                v_product(*next_opening, V_BANK)
-                if s + 4 < N_PAIRS:
-                    x_turn(s + 4, X_BANK)
-                score(s + 2, 0)
-                score(s + 2, 1)
-                if s + 4 < N_PAIRS:
-                    store_part(stored, 1, by_scalar, slice(VECTOR_COLUMNS, D))
-                else:
-                    store(stored, 1, by_scalar)
-                score_out(s + 2, 0)
-                score_out(s + 2, 1)
-                maximum(s + 1)
-                if s + 4 < N_PAIRS:
-                    store(stored, 1, by_vector, slice(0, VECTOR_COLUMNS))
-
-            s = N_PAIRS - 3
-            last_half = B * HALVES - 1
-            exponent(s, 0)
+            s = 13
             exponent(s, 1)
-            v_gain(last_half - 1, 3)
+            exponent(s, 0)
+            blend(s + 1, 0, 1)
+            turn(s - 2, 1, FIRST)
+            turn(s - 2, 0)
             x_quantize(s + 2)
+            v_quantize(6, slice(D // 2, D))
+            invert(s - 1, SECOND)
             p_quantize(s - 3)
-            invert(s - 1)
-            v_quantize(last_half - 1)
-            divide_by_gpsimd(s - 1, 0)
+            invert(s - 1, FIRST)
+            divide(s - 1, 1, slice(S, S + BANK), nc.vector)
+            divide(s - 1, 0, slice(0, S))
+            divide_ungained(s - 1)
             gain(s)
-            v_product(last_half, 1, X_BANK)
-            v_product(last_half, 0, V_BANK)
-            product(s - 3, 0, 4)
-            blend(s + 1, 0)
-            blend(s + 1, 1)
-            blend_in_psum(s + 1, 0)
-            blend_in_psum(s + 1, 1)
-            v_gain(last_half, 1)
-            turn(s - 1, 0, 5)
-            divide_by_scalar(s - 1, 1)
-            turn(s - 1, 1, 2)
-            product(s - 3, 1, 3)
-            store(s - 3, 0, by_scalar)
-            turn_out(s - 1, 0)
-            turn_out(s - 1, 1)
-            logit_out(s + 1, 0)
-            v_gain(last_half, 0)
-            logit_out(s + 1, 1)
-            score_turned(s + 2, 0, 4)
-            score_turned(s + 2, 1, 5)
-            v_product(last_half, 2, X_BANK)
-            v_product(last_half, 3, V_BANK)
-            score(s + 2, 0)
-            score(s + 2, 1)
-            store(s - 3, 1, by_scalar)
-            score_out(s + 2, 0)
+            v_product(7, 0)
+            product(s - 3, 0)
+            product(s - 3, 1)
+            turn_out(s - 2, 0)
+            turn_out(s - 2, 1, FIRST)
+            logit_out(s + 1, 0, 0)
+            v_product(7, 1)
+            logit_out(s + 1, 1, 0)
+            blend(s + 1, 1, 1)
+            logit_out(s + 1, 0, 1)
+            turn_ungained(s - 2)
+            v_gain(7, 1)
+            v_gain(7, 0)
+            store(s - 3, 1)
+            store(s - 3, 0)
+            score_turned(s + 2, 0)
+            score_turned(s + 2, 1)
+            v_product(7, 2)
+            v_product(7, 3)
+            score_turned(s + 2, 2)
+            score_turned(s + 2, 3)
+            gain_out(s - 2)
+            logit_out(s + 1, 1, 1)
             score_out(s + 2, 1)
-            maximum(s + 1)
-            v_gain(last_half, 2)
+            score_out(s + 2, 0)
+            blend(s + 2, 1, 0)
+            v_gain(7, 3)
+            score_out(s + 2, 3)
+            score_out(s + 2, 2)
+            blend(s + 2, 0, 0)
+            v_gain(7, 2)
 
-            s = N_PAIRS - 2
+            s = 14
             exponent(s, 1)
             exponent(s, 0)
-            v_gain(last_half, 3)
+            blend(s + 1, 0, 1)
+            blend(s + 1, 1, 1)
+            turn(s - 2, 1, FIRST)
+            turn(s - 2, 0)
             p_quantize(s - 3)
             invert(s - 1)
-            p_quantize(s - 2)
-            v_quantize(last_half)
-            gain(s, FIRST)
-            product(s - 3, 0, 2)
-            product(s - 2, 0, 6)
-            blend(s + 1, 0)
-            blend(s + 1, 1)
-            invert(s)
-            divide_by_gpsimd(s, 0)
-            blend_in_psum(s + 1, 0)
-            blend_in_psum(s + 1, 1)
-            divide_by_scalar(s - 1, 0)
-            divide_by_scalar(s - 1, 1)
-            turn(s - 1, 0, 4)
-            product(s - 3, 1, 3)
-            turn(s - 1, 1, 5)
-            product(s - 2, 1, 7)
-            maximum(s + 1)
-            logit_out(s + 1, 0)
-            store(s - 3, 0, by_vector)
-            logit_out(s + 1, 1)
-            turn(s, 0, 0)
-            divide_and_gain(s, 1)
-
-            s = N_PAIRS - 1
-            exponent(s, 0)
+            v_quantize(7)
+            divide_by_scalar(s - 1, 1, slice(S, S + BANK))
+            divide(s - 1, 0, slice(0, S))
+            divide_ungained(s - 1)
+            product(s - 3, 0)
+            product(s - 3, 1)
             turn_out(s - 2, 0)
-            turn_out(s - 2, 1)
+            turn_out(s - 2, 1, FIRST)
+            logit_out(s + 1, 0, 0)
+            turn_ungained(s - 2)
+            logit_out(s + 1, 1, 0)
+            logit_out(s + 1, 0, 1)
+            invert(s)
+            turn_ungained(s - 1)
+            turn(s - 1, 1, FIRST)
+            turn(s - 1, 0)
+            divide_ungained(s, 1, 0)
+            logit_out(s + 1, 1, 1)
+            gain_out(s - 2)
+            divide_ungained(s, 1, 1)
+
+            s = 15
+            exponent(s, 0)
             exponent(s, 1)
+            turn_ungained(s - 1, 1, 0)
+            p_quantize(s - 3)
+            gain_out(s - 2)
+            turn_ungained(s - 1, 1, 1)
+            store(s - 4, 0)
+            store(s - 4, 1)
+            product(s - 3, 0)
+            product(s - 3, 1)
             invert(s, FIRST)
-            p_quantize(s - 2)
-            product(s - 2, 0, 2)
-            turn(s - 1, 1, 1)
-            product(s - 2, 1, 4)
-            divide_and_gain(s, 0)
-            store(s - 4, 1, by_scalar)
-            turn_out(s - 1, 0)
-            store(s - 3, 0, by_scalar)
-            turn_out(s - 1, 1)
+            gain_out(s - 1, 1, 0)
+            divide_and_gain(s - 1, 0, 0)
+            divide_and_gain(s - 1, 0, 1)
+            turn_out(s - 2, 0)
+            turn_out(s - 2, 1, FIRST)
+            turn(s - 1, 0)
             invert(s, SECOND)
-            store(s - 3, 1, by_vector)
-            last_divide(0)
-            p_quantize(s - 1, FIRST)
-            last_divide(1)
-            p_quantize(s - 1, SECOND)
-            turn(s, 0, 5)
-            last_turn(0, 3)
-            product(s - 1, 0, 0)
-            last_turn(1, 6)
-            product(s - 1, 1, 1)
+            gain_out(s - 1, 1, 1)
+            p_quantize(s - 2)
+            divide_and_gain(s, 0, 0)
+            divide_and_gain(s, 0, 1)
+            store(s - 3, 0)
+            product(s - 2, 0)
+            turn_out(s - 1, 0)
+            product(s - 2, 1)
+            store(s - 3, 1)
+            turn(s, 0)
+            divide_and_gain(s, 1, 0)
+            p_quantize(s - 1)
+            divide_and_gain(s, 1, 1)
+            store(s - 2, 0)
+            turn(s, 1, FIRST)
+            product(s - 1, 0, "vector")
+            product(s - 1, 1, "vector")
             turn_out(s, 0)
-            store(s - 2, 0, by_scalar)
-            last_turn_out(0)
-            last_turn_out(1)
-            store(s - 2, 1, by_vector)
+            turn(s, 1, SECOND)
+            store(s - 2, 1)
+            turn_out(s, 1, FIRST)
+            turn_out(s, 1, SECOND)
             p_quantize(s, FIRST)
-            product(s, 0, 7)
-            last_quantize(0)
-            last_quantize(1)
-            last_product(0, (3, 5))
-            last_product(1, (3, 5))
-            store(s - 1, 0, by_scalar)
+            product(s, 0)
+            store(s - 1, 0, by_vector)
+            quantize_half(s, 1, 0)
+            quantize_half(s, 1, 1)
+            last_product(0)
+            last_product(1)
             store(s - 1, 1, by_vector)
-            store(s, 0, by_scalar)
+            store(s, 0)
             last_store(0, by_vector)
             last_store(1, by_scalar)

@@ -101,7 +101,7 @@ def tile_mixturedenserandomsynthesizer_t_kernel(tc, x_bytes, x_scale, w, rnd, mi
         mix_f = keep.tile([P, 1], F32, name="mix_f")
         u_f = keep.tile([P, HALVES, PACK], F32, name="u_f")
         c_4 = keep.tile([P, HALVES * PACK], F32, name="c_4")
-        c_f = keep.tile([P, S + BANK], F32, name="c_f")
+        c_f = keep.tile([P, S], F32, name="c_f")
         mix_diag = keep.tile([P, P], BF16, name="mix_diag")
         w_grouped, w_codes, w_scales = [], [], []
         for g in range(HALVES):
@@ -156,9 +156,6 @@ def tile_mixturedenserandomsynthesizer_t_kernel(tc, x_bytes, x_scale, w, rnd, mi
                 out=column_split(c_f[:, g * BANK : (g + 1) * BANK]),
                 in_=give_bank(("c", g))[:].rearrange("p (h e) m -> p h m e", h=2),
             )
-
-        def c_again():
-            copy_by_gpsimd(c_f[:, S : S + BANK], c_f[:, 0:BANK])
 
         def copy_by_gpsimd(out, in_):
             nc.gpsimd.tensor_scalar(out=out, in0=in_, scalar1=1.0, scalar2=0.0, op0=Alu.mult, op1=Alu.add)
@@ -297,9 +294,14 @@ def tile_mixturedenserandomsynthesizer_t_kernel(tc, x_bytes, x_scale, w, rnd, mi
                 logits[q] = work.tile([P, 2, S], F32, name="logit")
                 maxima[q] = work.tile([P, 4], F32, name="maximum")
             first = maxima[q][:, 2 + j : 3 + j]
+            bank = give_bank(("logit", q, j, g))[:]
+            columns = logits[q][:, j, g * BANK : (g + 1) * BANK]
+            if j == 1 and q < N_PAIRS - 2:
+                bank = bank.rearrange("p (h m e) -> p h e m", h=2, e=2)
+                columns = columns.rearrange("p (h e m) -> p h e m", h=2, e=2)
             nc.vector.tensor_scalar(
-                out=logits[q][:, j, g * BANK : (g + 1) * BANK],
-                in0=give_bank(("logit", q, j, g))[:],
+                out=columns,
+                in0=bank,
                 scalar1=-1.0,
                 scalar2=None if g == 0 else first,
                 op0=Alu.mult,
@@ -309,7 +311,7 @@ def tile_mixturedenserandomsynthesizer_t_kernel(tc, x_bytes, x_scale, w, rnd, mi
 
         def exponent(q, j):
             if q not in exps:
-                exps[q] = work.tile([P, 2 * S], F32, name="exp")
+                exps[q] = work.tile([P, 2 * S], F32, name="exp", bufs=3)
                 totals[q] = work.tile([P, 2], F32, name="total")
             nc.scalar.activation(
                 out=exps[q][:, j * S : (j + 1) * S],
@@ -325,40 +327,37 @@ def tile_mixturedenserandomsynthesizer_t_kernel(tc, x_bytes, x_scale, w, rnd, mi
                 inverses[q] = work.tile([P, 2], F32, name="inverse")
             nc.vector.reciprocal(out=inverses[q][:, tiles], in_=totals[q][:, tiles])
 
-        def gain(q, columns=slice(0, S + BANK)):
-            if q not in gained:
-                gained[q] = keep.tile([P, S + BANK], F32, name="gained%d" % (q % 2), align_bytes=64)
-            nc.gpsimd.tensor_tensor(out=gained[q][:, columns], in0=exps[q][:, columns], in1=c_f[:, columns], op=Alu.mult)
+        def gain(q):
+            gained[q] = keep.tile([P, S], F32, name="gained%d" % (q % 2), align_bytes=64)
+            nc.gpsimd.tensor_tensor(out=gained[q][:], in0=exps[q][:, 0:S], in1=c_f[:], op=Alu.mult)
 
         def pc_tile(q):
             if q not in pcs:
                 pcs[q] = work.tile([P, 2 * S], BF16, name="pc")
             return pcs[q]
 
-        def divide(q, j, columns, engine=nc.gpsimd):
-            engine.tensor_scalar(
-                out=pc_tile(q)[:, columns],
-                in0=gained[q][:, columns],
-                scalar1=inverses[q][:, j : j + 1],
-                scalar2=0.0,
-                op0=Alu.mult,
-                op1=Alu.add,
-            )
-
-        def divide_ungained(q, j=1, g=1):
-            divided[(q, j, g)] = work.tile([P, PACK, P], F32, name="divided", bufs=3)
+        def divide(q):
             nc.gpsimd.tensor_scalar(
-                out=divided.get((q, j, g))[:].rearrange("p (h e) m -> p h e m", e=2),
-                in0=exps[q][:, j * S + g * BANK : j * S + (g + 1) * BANK].rearrange("p (h m e) -> p h e m", h=2, e=2),
-                scalar1=inverses[q][:, j : j + 1],
+                out=pc_tile(q)[:, 0:S],
+                in0=gained[q][:],
+                scalar1=inverses[q][:, 0:1],
                 scalar2=0.0,
                 op0=Alu.mult,
                 op1=Alu.add,
             )
 
-        def divide_by_scalar(q, j, columns):
-            nc.scalar.activation(
-                out=pc_tile(q)[:, columns], in_=gained[q][:, columns], func=Act.Copy, scale=inverses[q][:, j : j + 1]
+        def divide_by_scalar(q):
+            nc.scalar.activation(out=pc_tile(q)[:, 0:S], in_=gained[q][:], func=Act.Copy, scale=inverses[q][:, 0:1])
+
+        def divide_ungained(q):
+            divided[q] = work.tile([P, S], F32, name="divided")
+            nc.gpsimd.tensor_scalar(
+                out=divided[q][:],
+                in0=exps[q][:, S : 2 * S],
+                scalar1=inverses[q][:, 1:2],
+                scalar2=0.0,
+                op0=Alu.mult,
+                op1=Alu.add,
             )
 
         def divide_and_gain(q, j, g):
@@ -390,15 +389,16 @@ def tile_mixturedenserandomsynthesizer_t_kernel(tc, x_bytes, x_scale, w, rnd, mi
                 in_=bank[:, 2 * halves.start : 2 * halves.stop].rearrange("p (g h) q -> p g q h", h=2),
             )
 
-        def turn_ungained(q, j=1, g=1):
-            bank = take_bank("vector", ("divided", q, j, g))
+        def turn_ungained(q, g, ring="vector"):
+            bank = take_bank(ring, ("divided", q, g))
             for t in range(PACK):
-                nc.tensor.transpose(bank[:, t, :], divided.get((q, j, g))[:, t, :], ident[:])
+                first = g * BANK + t * P
+                nc.tensor.transpose(bank[:, t, :], divided[q][:, first : first + P], ident[:])
 
-        def gain_out(q, j=1, g=1):
+        def gain_out(q, g):
             nc.vector.tensor_tensor(
-                out=grouped_tile(q)[:, j, g],
-                in0=give_bank(("divided", q, j, g))[:].rearrange("p t q -> p q t"),
+                out=grouped_tile(q)[:, 1, g],
+                in0=give_bank(("divided", q, g))[:].rearrange("p t q -> p q t"),
                 in1=c_4[:, g * PACK : (g + 1) * PACK].rearrange("p (o t) -> p o t", o=1).to_broadcast([P, P, PACK]),
                 op=Alu.mult,
             )
@@ -473,26 +473,17 @@ def tile_mixturedenserandomsynthesizer_t_kernel(tc, x_bytes, x_scale, w, rnd, mi
             exponent(s, 0)
             blend(s + 1, 0, 1)
             if live(s - 2):
-                turn(s - 2, 1, FIRST)
                 turn(s - 2, 0)
             x_quantize(s + 2)
             features = slice(0 if s == 1 else s % 2 * D // 2, (s % 2 + 1) * D // 2)
-            if not live(s - 3):
+            if live(s - 3):
+                v_quantize(s // 2, features)
                 invert(s - 1)
-                v_quantize(s // 2, features)
-                divide_by_scalar(s - 1, 1, slice(S, S + BANK))
-            elif live(s + 4):
-                v_quantize(s // 2, features)
-                invert(s - 1, SECOND)
                 p_quantize(s - 3)
-                invert(s - 1, FIRST)
-                divide(s - 1, 1, slice(S, S + BANK), nc.vector)
             else:
-                v_quantize(s // 2, features)
                 invert(s - 1)
-                p_quantize(s - 3)
-                divide_by_scalar(s - 1, 1, slice(S, S + BANK))
-            divide(s - 1, 0, slice(0, S))
+                v_quantize(s // 2, features)
+            divide(s - 1)
             divide_ungained(s - 1)
             gain(s)
             if live(s - 3):
@@ -503,15 +494,16 @@ def tile_mixturedenserandomsynthesizer_t_kernel(tc, x_bytes, x_scale, w, rnd, mi
                 score_turned(s + 2, 1)
             if live(s - 2):
                 turn_out(s - 2, 0)
-                turn_out(s - 2, 1, FIRST)
             logit_out(s + 1, 0, 0)
             logit_out(s + 1, 1, 0)
             blend(s + 1, 1, 1)
             if live(s - 2):
-                turn_ungained(s - 2)
+                turn_ungained(s - 2, 0)
             if live(s + 4):
                 x_widen(s + 4)
             logit_out(s + 1, 0, 1)
+            if live(s - 2):
+                turn_ungained(s - 2, 1)
             x_scale_out(s + 3)
             if live(s - 3):
                 store(s - 3, 1)
@@ -519,14 +511,13 @@ def tile_mixturedenserandomsynthesizer_t_kernel(tc, x_bytes, x_scale, w, rnd, mi
                 score_turned(s + 2, 0)
                 score_turned(s + 2, 1)
             v_product(*quarter(2 * s + 2))
-            if live(s - 3):
-                v_product(*quarter(2 * s + 3))
             score_turned(s + 2, 2)
-            score_turned(s + 2, 3)
-            if not live(s - 3):
-                v_product(*quarter(2 * s + 3))
             if live(s - 2):
-                gain_out(s - 2)
+                gain_out(s - 2, 1)
+            v_product(*quarter(2 * s + 3))
+            score_turned(s + 2, 3)
+            if live(s - 2):
+                gain_out(s - 2, 0)
             logit_out(s + 1, 1, 1)
             if live(s + 4):
                 x_turn(s + 4)
@@ -600,12 +591,10 @@ def tile_mixturedenserandomsynthesizer_t_kernel(tc, x_bytes, x_scale, w, rnd, mi
             score_out(1, 3)
 
             c_out(0, by_scalar)
-            c_again()
             c_out(1, by_scalar)
             exponent(0, 0)
-            gain(0, slice(0, S))
+            gain(0)
             exponent(0, 1)
-            gain(0, slice(S, S + BANK))
             v_product(0, 0)
             v_product(0, 1)
             score_turned(2, 0)
@@ -640,47 +629,45 @@ def tile_mixturedenserandomsynthesizer_t_kernel(tc, x_bytes, x_scale, w, rnd, mi
             exponent(s, 1)
             exponent(s, 0)
             blend(s + 1, 0, 1)
-            turn(s - 2, 1, FIRST)
             turn(s - 2, 0)
             x_quantize(s + 2)
             v_quantize(6, slice(D // 2, D))
-            invert(s - 1, SECOND)
+            invert(s - 1)
             p_quantize(s - 3)
-            invert(s - 1, FIRST)
-            divide(s - 1, 1, slice(S, S + BANK), nc.vector)
-            divide(s - 1, 0, slice(0, S))
+            divide(s - 1)
             divide_ungained(s - 1)
             gain(s)
             v_product(7, 0)
             product(s - 3, 0)
             product(s - 3, 1)
             turn_out(s - 2, 0)
-            turn_out(s - 2, 1, FIRST)
             logit_out(s + 1, 0, 0)
-            v_product(7, 1)
             logit_out(s + 1, 1, 0)
             blend(s + 1, 1, 1)
+            turn_ungained(s - 2, 0)
             logit_out(s + 1, 0, 1)
-            turn_ungained(s - 2)
-            v_gain(7, 1)
+            turn_ungained(s - 2, 1)
             v_gain(7, 0)
             store(s - 3, 1)
             store(s - 3, 0)
             score_turned(s + 2, 0)
             score_turned(s + 2, 1)
-            v_product(7, 2)
-            v_product(7, 3)
+            v_product(7, 1)
             score_turned(s + 2, 2)
+            gain_out(s - 2, 1)
+            v_product(7, 2)
             score_turned(s + 2, 3)
-            gain_out(s - 2)
+            gain_out(s - 2, 0)
+            v_product(7, 3)
             logit_out(s + 1, 1, 1)
             score_out(s + 2, 1)
             score_out(s + 2, 0)
             blend(s + 2, 1, 0)
-            v_gain(7, 3)
+            v_gain(7, 1)
             score_out(s + 2, 3)
             score_out(s + 2, 2)
             blend(s + 2, 0, 0)
+            v_gain(7, 3)
             v_gain(7, 2)
 
             s = 14
@@ -688,79 +675,76 @@ def tile_mixturedenserandomsynthesizer_t_kernel(tc, x_bytes, x_scale, w, rnd, mi
             exponent(s, 0)
             blend(s + 1, 0, 1)
             blend(s + 1, 1, 1)
-            turn(s - 2, 1, FIRST)
             turn(s - 2, 0)
             p_quantize(s - 3)
             invert(s - 1)
             v_quantize(7)
-            divide_by_scalar(s - 1, 1, slice(S, S + BANK))
-            divide(s - 1, 0, slice(0, S))
             divide_ungained(s - 1)
+            divide_by_scalar(s - 1)
+            gain(s)
             product(s - 3, 0)
             product(s - 3, 1)
             turn_out(s - 2, 0)
-            turn_out(s - 2, 1, FIRST)
             logit_out(s + 1, 0, 0)
-            turn_ungained(s - 2)
+            turn_ungained(s - 2, 0)
             logit_out(s + 1, 1, 0)
-            logit_out(s + 1, 0, 1)
-            invert(s)
-            turn_ungained(s - 1)
-            turn(s - 1, 1, FIRST)
+            turn_ungained(s - 2, 1)
             turn(s - 1, 0)
-            divide_ungained(s, 1, 0)
+            logit_out(s + 1, 0, 1)
+            turn_ungained(s - 1, 0)
+            invert(s)
             logit_out(s + 1, 1, 1)
-            gain_out(s - 2)
-            divide_ungained(s, 1, 1)
+            turn_ungained(s - 1, 1)
+            store(s - 3, 0)
+            store(s - 3, 1)
+            gain_out(s - 2, 1)
+            gain_out(s - 2, 0)
+            turn_out(s - 1, 0)
+            p_quantize(s - 2)
+            product(s - 2, 0)
+            product(s - 2, 1)
+            gain_out(s - 1, 1)
+            gain_out(s - 1, 0)
 
             s = 15
             exponent(s, 0)
+            divide_by_scalar(s - 1)
             exponent(s, 1)
-            turn_ungained(s - 1, 1, 0)
-            p_quantize(s - 3)
-            gain_out(s - 2)
-            turn_ungained(s - 1, 1, 1)
-            store(s - 4, 0)
-            store(s - 4, 1)
-            product(s - 3, 0)
-            product(s - 3, 1)
+            divide_and_gain(s - 1, 1, 0)
+            divide_and_gain(s - 1, 1, 1)
             invert(s, FIRST)
-            gain_out(s - 1, 1, 0)
-            divide_and_gain(s - 1, 0, 0)
-            divide_and_gain(s - 1, 0, 1)
-            turn_out(s - 2, 0)
-            turn_out(s - 2, 1, FIRST)
-            turn(s - 1, 0)
-            invert(s, SECOND)
-            gain_out(s - 1, 1, 1)
             p_quantize(s - 2)
+            turn(s - 1, 0, BOTH, "vector")
+            turn(s - 1, 1, BOTH, "vector")
+            product(s - 2, 0)
+            product(s - 2, 1)
             divide_and_gain(s, 0, 0)
+            invert(s, SECOND)
             divide_and_gain(s, 0, 1)
             store(s - 3, 0)
-            product(s - 2, 0)
+            turn_out(s - 1, 1)
             turn_out(s - 1, 0)
-            product(s - 2, 1)
-            store(s - 3, 1)
-            turn(s, 0)
+            turn(s, 0, BOTH, "vector")
             divide_and_gain(s, 1, 0)
-            p_quantize(s - 1)
             divide_and_gain(s, 1, 1)
-            store(s - 2, 0)
-            turn(s, 1, FIRST)
-            product(s - 1, 0, "vector")
-            product(s - 1, 1, "vector")
+            p_quantize(s - 1)
+            store(s - 3, 1)
+            turn(s, 1, FIRST, "vector")
+            turn(s, 1, SECOND, "vector")
             turn_out(s, 0)
-            turn(s, 1, SECOND)
-            store(s - 2, 1)
+            product(s - 1, 0)
+            product(s - 1, 1, "vector")
+            store(s - 2, 0, by_vector)
             turn_out(s, 1, FIRST)
             turn_out(s, 1, SECOND)
             p_quantize(s, FIRST)
-            product(s, 0)
-            store(s - 1, 0, by_vector)
+            product(s, 0, "vector")
             quantize_half(s, 1, 0)
             quantize_half(s, 1, 1)
+            store(s - 2, 1)
             last_product(0)
             last_product(1)
+            store(s - 1, 0)
             store(s - 1, 1, by_vector)
             store(s, 0)
             last_store(0, by_vector)

@@ -27,6 +27,8 @@ AX = mybir.AxisListType
 FLOPS = 2 * B * S * D * S + 2 * B * S * D * D + 2 * B * S * S * D
 
 BOTH, FIRST, SECOND = slice(0, 2), slice(0, 1), slice(1, 2)
+ROW = BANK + 8
+VECTOR_COLUMNS = 96
 RING = 4
 FIRST_TILEWISE_PAIR = N_PAIRS - 5
 
@@ -99,6 +101,10 @@ def tile_mixturedenserandomsynthesizer_t_kernel(tc, x_bytes, x_scale, w, rnd, mi
         mix_column = keep.tile([P, 1], F32, name="mix_column")
         nc.vector.memset(mix_column[:], 0.0)
         mix_f = keep.tile([P, 1], F32, name="mix_f")
+        mix_negated = keep.tile([P, 2], F32, name="mix_negated")
+        rnd_f = []
+        for k in range(PAIRS):
+            rnd_f.append(keep.tile([P, 2, BANK], F32, name="rnd_f%d" % k))
         u_f = keep.tile([P, HALVES, PACK], F32, name="u_f")
         c_4 = keep.tile([P, HALVES * PACK], F32, name="c_4")
         c_f = keep.tile([P, S], F32, name="c_f")
@@ -146,6 +152,7 @@ def tile_mixturedenserandomsynthesizer_t_kernel(tc, x_bytes, x_scale, w, rnd, mi
         def mix_out():
             bank = give_bank("mix")
             nc.vector.tensor_copy(out=mix_f[:], in_=bank[:, 0, 0:1])
+            nc.vector.tensor_scalar(out=mix_negated[:], in0=bank[:, 0, 0:2], scalar1=-1.0, scalar2=None, op0=Alu.mult)
             nc.vector.tensor_scalar(out=mix_diag[:], in0=ident[:], scalar1=bank[:, 0, 1:2], scalar2=None, op0=Alu.mult)
 
         def c_spread(g):
@@ -174,6 +181,24 @@ def tile_mixturedenserandomsynthesizer_t_kernel(tc, x_bytes, x_scale, w, rnd, mi
 
         def wv_quantize():
             quantize(wv_codes[:], wv_scales[:], wv_grouped[0][:].rearrange("p n j -> p (n j)"))
+
+        def rnd_scale(k, j):
+            nc.scalar.activation(
+                out=column_split(rnd_f[k][:, j]),
+                in_=key_split(rnd_raw[k][:, j, 0:BANK]),
+                func=Act.Copy,
+                scale=mix_negated[:, 1:2],
+            )
+
+        def rnd_scale_by_gpsimd(k, j):
+            nc.gpsimd.tensor_scalar(
+                out=column_split(rnd_f[k][:, j]),
+                in0=key_split(rnd_raw[k][:, j, 0:BANK]),
+                scalar1=mix_negated[:, 1:2],
+                scalar2=0.0,
+                op0=Alu.mult,
+                op1=Alu.add,
+            )
 
         x_wide, x_grouped, x_codes, x_scales = {}, {}, {}, {}
 
@@ -204,8 +229,8 @@ def tile_mixturedenserandomsynthesizer_t_kernel(tc, x_bytes, x_scale, w, rnd, mi
             )
 
         def x_quantize(q):
-            x_codes[q] = work.tile([P, 2 * P], U32, name="x_codes", bufs=7, align_bytes=64)
-            x_scales[q] = work.tile([P, 2 * P], U8, name="x_scales", bufs=7, align_bytes=64)
+            x_codes[q] = work.tile([P, 2 * P], U32, name="x_codes", bufs=6, align_bytes=64)
+            x_scales[q] = work.tile([P, 2 * P], U8, name="x_scales", bufs=6, align_bytes=64)
             quantize(x_codes[q][:], x_scales[q][:], x_grouped[q][:].rearrange("p q t -> p (q t)"))
 
         v_grouped, v_codes, v_scales = {}, {}, {}
@@ -242,7 +267,7 @@ def tile_mixturedenserandomsynthesizer_t_kernel(tc, x_bytes, x_scale, w, rnd, mi
 
         mixed_scores = {}
         logits, maxima, exps, totals, inverses = {}, {}, {}, {}, {}
-        gained, pcs, divided, grouped_pcs = {}, {}, {}, {}
+        gained, pcs, grouped_pcs = {}, {}, {}
         p_codes, p_scales, rows_out = {}, {}, {}
 
         def score_turned(q, n):
@@ -289,33 +314,54 @@ def tile_mixturedenserandomsynthesizer_t_kernel(tc, x_bytes, x_scale, w, rnd, mi
             blend_open(q, j, g)
             blend_close(q, j, g)
 
-        def logit_out(q, j, g):
+        def score(q, j):
+            bank = take_bank("vector", ("score", q, j, 0), (P, BANK))
+            rows = slice(j * P, (j + 1) * P)
+            multiply(bank[:], x_codes[q][:, rows], x_scales[q][:, rows], w_codes[0][:], w_scales[0][:], True, True)
+
+        def logit_tile(q):
             if q not in logits:
-                logits[q] = work.tile([P, 2, S], F32, name="logit")
-                maxima[q] = work.tile([P, 4], F32, name="maximum")
-            first = maxima[q][:, 2 + j : 3 + j]
-            bank = give_bank(("logit", q, j, g))[:]
-            columns = logits[q][:, j, g * BANK : (g + 1) * BANK]
-            if j == 1 and q < N_PAIRS - 2:
-                bank = bank.rearrange("p (h m e) -> p h e m", h=2, e=2)
-                columns = columns.rearrange("p (h e m) -> p h e m", h=2, e=2)
+                logits[q] = work.tile([P, 2, 2, ROW], F32, name="logit")
+                maxima[q] = work.tile([P, 2], F32, name="maximum")
+            return logits[q]
+
+        def mix_out_of_psum(q, j):
+            nc.vector.scalar_tensor_tensor(
+                out=logit_tile(q)[:, j, 0, 0:BANK],
+                in0=give_bank(("score", q, j, 0))[:],
+                scalar=mix_negated[:, 0:1],
+                in1=rnd_f[q % PAIRS][:, j],
+                op0=Alu.mult,
+                op1=Alu.add,
+            )
+
+        def logit_out(q, j, g=1, last=False):
+            least = logit_tile(q)[:, j, 0, BANK : BANK + 1]
             nc.vector.tensor_scalar(
-                out=columns,
-                in0=bank,
+                out=logit_tile(q)[:, j, g, 0:BANK],
+                in0=give_bank(("logit", q, j, g))[:],
                 scalar1=-1.0,
-                scalar2=None if g == 0 else first,
+                scalar2=least if last else None,
                 op0=Alu.mult,
                 op1=Alu.min,
-                accum_out=first if g == 0 else maxima[q][:, j : j + 1],
+                accum_out=maxima[q][:, j : j + 1] if last else least,
+            )
+
+        def maximum(q):
+            nc.vector.tensor_reduce(out=maxima[q][:], in_=logits[q][:, :, 0, 0 : BANK + 1], axis=AX.X, op=Alu.min)
+
+        def first_minimum(q):
+            nc.vector.tensor_reduce(
+                out=logits[q][:, :, 0, BANK], in_=logits[q][:, :, 0, 0:BANK], axis=AX.X, op=Alu.min
             )
 
         def exponent(q, j):
             if q not in exps:
-                exps[q] = work.tile([P, 2 * S], F32, name="exp", bufs=3)
+                exps[q] = work.tile([P, 2 * S], F32, name="exp")
                 totals[q] = work.tile([P, 2], F32, name="total")
             nc.scalar.activation(
-                out=exps[q][:, j * S : (j + 1) * S],
-                in_=logits[q][:, j],
+                out=exps[q][:, j * S : (j + 1) * S].rearrange("p (g k) -> p g k", g=HALVES),
+                in_=logits[q][:, j, :, 0:BANK],
                 func=Act.Exp,
                 bias=maxima[q][:, j : j + 1],
                 scale=-1.0,
@@ -327,37 +373,37 @@ def tile_mixturedenserandomsynthesizer_t_kernel(tc, x_bytes, x_scale, w, rnd, mi
                 inverses[q] = work.tile([P, 2], F32, name="inverse")
             nc.vector.reciprocal(out=inverses[q][:, tiles], in_=totals[q][:, tiles])
 
-        def gain(q):
-            gained[q] = keep.tile([P, S], F32, name="gained%d" % (q % 2), align_bytes=64)
-            nc.gpsimd.tensor_tensor(out=gained[q][:], in0=exps[q][:, 0:S], in1=c_f[:], op=Alu.mult)
+        def gain(q, tiles=BOTH):
+            gained[q] = keep.tile([P, 2, S], F32, name="gained%d" % (q % 2), align_bytes=64)
+            count = tiles.stop - tiles.start
+            nc.gpsimd.tensor_tensor(
+                out=gained[q][:, tiles],
+                in0=exps[q][:].rearrange("p (j k) -> p j k", j=2)[:, tiles],
+                in1=c_f[:].rearrange("p (o k) -> p o k", o=1).to_broadcast([P, count, S]),
+                op=Alu.mult,
+            )
 
         def pc_tile(q):
             if q not in pcs:
                 pcs[q] = work.tile([P, 2 * S], BF16, name="pc")
             return pcs[q]
 
-        def divide(q):
-            nc.gpsimd.tensor_scalar(
-                out=pc_tile(q)[:, 0:S],
-                in0=gained[q][:],
-                scalar1=inverses[q][:, 0:1],
+        def divide(q, j, keys=slice(0, S), engine=nc.gpsimd):
+            engine.tensor_scalar(
+                out=pc_tile(q)[:, j * S + keys.start : j * S + keys.stop],
+                in0=gained[q][:, j, keys],
+                scalar1=inverses[q][:, j : j + 1],
                 scalar2=0.0,
                 op0=Alu.mult,
                 op1=Alu.add,
             )
 
-        def divide_by_scalar(q):
-            nc.scalar.activation(out=pc_tile(q)[:, 0:S], in_=gained[q][:], func=Act.Copy, scale=inverses[q][:, 0:1])
-
-        def divide_ungained(q):
-            divided[q] = work.tile([P, S], F32, name="divided")
-            nc.gpsimd.tensor_scalar(
-                out=divided[q][:],
-                in0=exps[q][:, S : 2 * S],
-                scalar1=inverses[q][:, 1:2],
-                scalar2=0.0,
-                op0=Alu.mult,
-                op1=Alu.add,
+        def divide_by_scalar(q, j, keys=slice(0, S)):
+            nc.scalar.activation(
+                out=pc_tile(q)[:, j * S + keys.start : j * S + keys.stop],
+                in_=gained[q][:, j, keys],
+                func=Act.Copy,
+                scale=inverses[q][:, j : j + 1],
             )
 
         def divide_and_gain(q, j, g):
@@ -373,7 +419,7 @@ def tile_mixturedenserandomsynthesizer_t_kernel(tc, x_bytes, x_scale, w, rnd, mi
 
         def grouped_tile(q):
             if q not in grouped_pcs:
-                grouped_pcs[q] = work.tile([P, 2, HALVES, P, PACK], BF16, name="p_grouped", bufs=4, align_bytes=64)
+                grouped_pcs[q] = work.tile([P, 2, HALVES, P, PACK], BF16, name="p_grouped", bufs=3, align_bytes=64)
             return grouped_pcs[q]
 
         def turn(q, j, halves=BOTH, ring="scalar"):
@@ -387,20 +433,6 @@ def tile_mixturedenserandomsynthesizer_t_kernel(tc, x_bytes, x_scale, w, rnd, mi
             copy(
                 out=grouped_tile(q)[:, j, halves].bitcast(F32),
                 in_=bank[:, 2 * halves.start : 2 * halves.stop].rearrange("p (g h) q -> p g q h", h=2),
-            )
-
-        def turn_ungained(q, g, ring="vector"):
-            bank = take_bank(ring, ("divided", q, g))
-            for t in range(PACK):
-                first = g * BANK + t * P
-                nc.tensor.transpose(bank[:, t, :], divided[q][:, first : first + P], ident[:])
-
-        def gain_out(q, g):
-            nc.vector.tensor_tensor(
-                out=grouped_tile(q)[:, 1, g],
-                in0=give_bank(("divided", q, g))[:].rearrange("p t q -> p q t"),
-                in1=c_4[:, g * PACK : (g + 1) * PACK].rearrange("p (o t) -> p o t", o=1).to_broadcast([P, P, PACK]),
-                op=Alu.mult,
             )
 
         def p_quantize(q, tiles=BOTH):
@@ -449,11 +481,17 @@ def tile_mixturedenserandomsynthesizer_t_kernel(tc, x_bytes, x_scale, w, rnd, mi
 
         stored_tiles = {}
 
-        def store(q, j, copy=nc.scalar.copy):
-            b, h, t = q // PAIRS, (q % PAIRS) // 2, 2 * (q % 2)
+        def rows_tile(q):
             if q not in rows_out:
                 rows_out[q] = work.tile([P, 2, D], F32, name="rows_out", bufs=4)
-            copy(out=rows_out[q][:, j], in_=give_bank(("out", q, j))[:])
+            return rows_out[q]
+
+        def store_part(q, j, cols):
+            nc.scalar.copy(out=rows_tile(q)[:, j, cols], in_=held.get(("out", q, j))[2][:, cols])
+
+        def store(q, j, copy=nc.scalar.copy, cols=slice(0, D)):
+            b, h, t = q // PAIRS, (q % PAIRS) // 2, 2 * (q % 2)
+            copy(out=rows_tile(q)[:, j, cols], in_=give_bank(("out", q, j))[:, cols])
             stored_tiles[q] = stored_tiles.get(q, 0) + 1
             if q >= FIRST_TILEWISE_PAIR:
                 nc.sync.dma_start(out=out_rows[b, h, :, t + j], in_=rows_out[q][:, j])
@@ -471,64 +509,55 @@ def tile_mixturedenserandomsynthesizer_t_kernel(tc, x_bytes, x_scale, w, rnd, mi
         def step(s):
             exponent(s, 1)
             exponent(s, 0)
-            blend(s + 1, 0, 1)
-            if live(s - 2):
-                turn(s - 2, 0)
-            x_quantize(s + 2)
-            features = slice(0 if s == 1 else s % 2 * D // 2, (s % 2 + 1) * D // 2)
             if live(s - 3):
-                v_quantize(s // 2, features)
-                invert(s - 1)
                 p_quantize(s - 3)
-            else:
-                invert(s - 1)
-                v_quantize(s // 2, features)
-            divide(s - 1)
-            divide_ungained(s - 1)
+            x_quantize(s + 3)
+            invert(s - 1)
+            v_quantize(s // 2, slice(0 if s == 1 else s % 2 * D // 2, (s % 2 + 1) * D // 2))
+            divide(s - 1, 0)
+            divide_by_scalar(s - 1, 1)
             gain(s)
             if live(s - 3):
                 product(s - 3, 0)
                 product(s - 3, 1)
             else:
-                score_turned(s + 2, 0)
-                score_turned(s + 2, 1)
-            if live(s - 2):
-                turn_out(s - 2, 0)
-            logit_out(s + 1, 0, 0)
-            logit_out(s + 1, 1, 0)
-            blend(s + 1, 1, 1)
-            if live(s - 2):
-                turn_ungained(s - 2, 0)
-            if live(s + 4):
-                x_widen(s + 4)
-            logit_out(s + 1, 0, 1)
-            if live(s - 2):
-                turn_ungained(s - 2, 1)
-            x_scale_out(s + 3)
+                score_turned(s + 3, 2)
+                score_turned(s + 3, 3)
+            mix_out_of_psum(s + 1, 1)
+            x_turn(s + 4)
+            mix_out_of_psum(s + 1, 0)
+            logit_out(s + 1, 1)
+            v_product(*quarter(2 * s + 2))
+            v_product(*quarter(2 * s + 3))
             if live(s - 3):
                 store(s - 3, 1)
-                store(s - 3, 0)
-                score_turned(s + 2, 0)
-                score_turned(s + 2, 1)
-            v_product(*quarter(2 * s + 2))
-            score_turned(s + 2, 2)
+                store_part(s - 3, 0, slice(VECTOR_COLUMNS, D))
+            elif s + 2 < PAIRS:
+                rnd_scale(s + 2, 0)
+                rnd_scale(s + 2, 1)
+            logit_out(s + 1, 0)
             if live(s - 2):
-                gain_out(s - 2, 1)
-            v_product(*quarter(2 * s + 3))
-            score_turned(s + 2, 3)
-            if live(s - 2):
-                gain_out(s - 2, 0)
-            logit_out(s + 1, 1, 1)
-            if live(s + 4):
-                x_turn(s + 4)
-            score_out(s + 2, 1)
-            score_out(s + 2, 0)
-            blend(s + 2, 1, 0)
+                turn_out(s - 2, 0)
+                turn_out(s - 2, 1)
+            if live(s - 3):
+                score_turned(s + 3, 2)
+                score_turned(s + 3, 3)
+            blend(s + 2, 0, 1)
+            x_scale_out(s + 4)
+            if live(s - 3):
+                store(s - 3, 0, by_vector, slice(0, VECTOR_COLUMNS))
+            turn(s - 1, 1)
+            blend(s + 2, 1, 1)
+            turn(s - 1, 0)
+            if live(s + 5):
+                x_widen(s + 5)
             v_gain(*quarter(2 * s + 3))
-            score_out(s + 2, 3)
-            score_out(s + 2, 2)
-            blend(s + 2, 0, 0)
+            score(s + 2, 0)
+            maximum(s + 1)
             v_gain(*quarter(2 * s + 2))
+            score(s + 2, 1)
+            score_out(s + 3, 3)
+            score_out(s + 3, 2)
 
         with tc.manual_schedule():
             x_widen(0)
@@ -545,207 +574,237 @@ def tile_mixturedenserandomsynthesizer_t_kernel(tc, x_bytes, x_scale, w, rnd, mi
             x_scale_out(0)
             mix_out()
             x_turn(2)
-            blend_open(0, 0, 0)
             w_quantize(0)
             x_quantize(0)
-            score_turned(0, 0)
-            score_turned(0, 1)
-            blend_open(0, 1, 0)
+            score(0, 0)
+            score(0, 1)
             x_scale_out(1)
+            w_quantize(1)
+            x_quantize(1)
             by_vector(out=c_4[:], in_=c_raw[:].rearrange("p g t -> p (g t)"))
             by_vector(out=u_f[:], in_=u_raw[:])
-            x_quantize(1)
-            w_quantize(1)
             wv_group()
-            score_out(0, 0)
-            score_out(0, 1)
-            score_turned(1, 0)
-            blend_close(0, 0, 0)
+            rnd_scale_by_gpsimd(1, 0)
+            rnd_scale_by_gpsimd(1, 1)
+            rnd_scale(0, 0)
+            rnd_scale(0, 1)
+            x_widen(3)
+            blend_open(0, 0, 1)
             score_turned(0, 2)
             score_turned(0, 3)
-            x_widen(3)
-            blend_close(0, 1, 0)
+            mix_out_of_psum(0, 0)
             x_turn(3)
+            score_turned(1, 0)
             score_turned(1, 1)
-            x_scale_out(2)
+            mix_out_of_psum(0, 1)
+            blend_open(0, 1, 1)
             score_out(0, 2)
             score_out(0, 3)
-            logit_out(0, 0, 0)
-            logit_out(0, 1, 0)
-            blend(0, 0, 1)
-            score_turned(1, 2)
-            score_turned(1, 3)
-            blend(0, 1, 1)
-            score_out(1, 0)
-            score_out(1, 1)
-            x_scale_out(3)
-            logit_out(0, 0, 1)
             c_spread(0)
-            blend(1, 1, 0)
-            c_spread(1)
+            blend_close(0, 0, 1)
+            blend_close(0, 1, 1)
+            score_turned(1, 2)
+            x_scale_out(2)
+            first_minimum(0)
+            x_scale_out(3)
+            score_out(1, 0)
+            score_turned(1, 3)
+            score_out(1, 1)
+            c_out(0, by_scalar)
             blend(1, 0, 0)
-            x_quantize(2)
-            wv_quantize()
-            logit_out(0, 1, 1)
+            c_spread(1)
+            blend(1, 1, 0)
             score_out(1, 2)
             score_out(1, 3)
-
-            c_out(0, by_scalar)
-            c_out(1, by_scalar)
-            exponent(0, 0)
-            gain(0)
-            exponent(0, 1)
-            v_product(0, 0)
-            v_product(0, 1)
-            score_turned(2, 0)
-            score_turned(2, 1)
-            logit_out(1, 0, 0)
-            logit_out(1, 1, 0)
+            logit_out(0, 0, 1, True)
+            logit_out(0, 1, 1, True)
             blend(1, 0, 1)
             blend(1, 1, 1)
-            v_gain(0, 0)
-            v_gain(0, 1)
+            x_quantize(2)
+            wv_quantize()
+            x_quantize(3)
+
+            exponent(0, 0)
+            c_out(1, by_scalar)
+            exponent(0, 1)
+            gain(0)
             x_widen(4)
-            v_product(0, 2)
             score_turned(2, 2)
             score_turned(2, 3)
-            v_product(0, 3)
-            logit_out(1, 0, 1)
-            logit_out(1, 1, 1)
+            logit_out(1, 0, 0)
+            v_product(0, 0)
+            logit_out(1, 1, 0)
+            v_product(0, 1)
+            logit_out(1, 0, 1, True)
             x_turn(4)
-            score_out(2, 1)
-            score_out(2, 0)
-            blend(2, 1, 0)
-            v_gain(0, 3)
+            logit_out(1, 1, 1, True)
+            v_product(0, 2)
+            score_turned(3, 2)
+            score_turned(3, 3)
             score_out(2, 3)
             score_out(2, 2)
-            blend(2, 0, 0)
+            v_gain(0, 0)
+            v_product(0, 3)
+            v_gain(0, 1)
+            blend(2, 0, 1)
+            x_scale_out(4)
+            blend(2, 1, 1)
+            rnd_scale(2, 0)
+            rnd_scale(2, 1)
+            x_widen(5)
             v_gain(0, 2)
+            score(2, 0)
+            v_gain(0, 3)
+            score(2, 1)
+            score_out(3, 3)
+            score_out(3, 2)
 
-            for s in range(1, N_PAIRS - 3):
+            for s in range(1, N_PAIRS - 4):
                 step(s)
+
+            s = 12
+            exponent(s, 1)
+            exponent(s, 0)
+            p_quantize(s - 3)
+            x_quantize(s + 3)
+            invert(s - 1)
+            v_quantize(6, slice(0, D // 2))
+            divide(s - 1, 0)
+            divide_by_scalar(s - 1, 1)
+            gain(s)
+            product(s - 3, 0)
+            product(s - 3, 1)
+            mix_out_of_psum(s + 1, 1)
+            v_product(6, 2)
+            mix_out_of_psum(s + 1, 0)
+            v_product(6, 3)
+            logit_out(s + 1, 1)
+            v_product(7, 0)
+            store(s - 3, 1)
+            store(s - 3, 0)
+            logit_out(s + 1, 0)
+            v_product(7, 1)
+            turn_out(s - 2, 0)
+            turn_out(s - 2, 1)
+            score_turned(s + 3, 2)
+            score_turned(s + 3, 3)
+            v_gain(6, 3)
+            v_gain(6, 2)
+            blend(s + 2, 0, 1)
+            turn(s - 1, 1)
+            blend(s + 2, 1, 1)
+            turn(s - 1, 0)
+            v_gain(7, 1)
+            score(s + 2, 0)
+            maximum(s + 1)
+            v_gain(7, 0)
+            score(s + 2, 1)
+            score_out(s + 3, 3)
+            score_out(s + 3, 2)
 
             s = 13
             exponent(s, 1)
             exponent(s, 0)
-            blend(s + 1, 0, 1)
-            turn(s - 2, 0)
-            x_quantize(s + 2)
+            p_quantize(s - 3)
             v_quantize(6, slice(D // 2, D))
             invert(s - 1)
-            p_quantize(s - 3)
-            divide(s - 1)
-            divide_ungained(s - 1)
+            v_quantize(7, slice(0, D // 2))
+            divide(s - 1, 0, slice(0, BANK))
+            divide_by_scalar(s - 1, 1)
+            divide_by_scalar(s - 1, 0, slice(BANK, S))
             gain(s)
-            v_product(7, 0)
             product(s - 3, 0)
             product(s - 3, 1)
-            turn_out(s - 2, 0)
-            logit_out(s + 1, 0, 0)
-            logit_out(s + 1, 1, 0)
-            blend(s + 1, 1, 1)
-            turn_ungained(s - 2, 0)
-            logit_out(s + 1, 0, 1)
-            turn_ungained(s - 2, 1)
-            v_gain(7, 0)
-            store(s - 3, 1)
-            store(s - 3, 0)
-            score_turned(s + 2, 0)
-            score_turned(s + 2, 1)
-            v_product(7, 1)
-            score_turned(s + 2, 2)
-            gain_out(s - 2, 1)
+            mix_out_of_psum(s + 1, 1)
             v_product(7, 2)
-            score_turned(s + 2, 3)
-            gain_out(s - 2, 0)
+            mix_out_of_psum(s + 1, 0)
             v_product(7, 3)
-            logit_out(s + 1, 1, 1)
-            score_out(s + 2, 1)
-            score_out(s + 2, 0)
-            blend(s + 2, 1, 0)
-            v_gain(7, 1)
-            score_out(s + 2, 3)
-            score_out(s + 2, 2)
-            blend(s + 2, 0, 0)
+            logit_out(s + 1, 1)
+            turn_out(s - 2, 0)
+            turn_out(s - 2, 1)
+            logit_out(s + 1, 0)
+            blend(s + 2, 0, 1)
+            turn(s - 1, 1)
+            blend(s + 2, 1, 1)
+            turn(s - 1, 0)
             v_gain(7, 3)
+            score(s + 2, 0)
+            maximum(s + 1)
             v_gain(7, 2)
+            score(s + 2, 1)
+            store(s - 3, 1)
+            turn_out(s - 1, 1)
+            turn_out(s - 1, 0)
+            store(s - 3, 0, by_vector)
 
             s = 14
             exponent(s, 1)
             exponent(s, 0)
-            blend(s + 1, 0, 1)
-            blend(s + 1, 1, 1)
-            turn(s - 2, 0)
             p_quantize(s - 3)
+            v_quantize(7, slice(D // 2, D))
             invert(s - 1)
-            v_quantize(7)
-            divide_ungained(s - 1)
-            divide_by_scalar(s - 1)
-            gain(s)
-            product(s - 3, 0)
-            product(s - 3, 1)
-            turn_out(s - 2, 0)
-            logit_out(s + 1, 0, 0)
-            turn_ungained(s - 2, 0)
-            logit_out(s + 1, 1, 0)
-            turn_ungained(s - 2, 1)
-            turn(s - 1, 0)
-            logit_out(s + 1, 0, 1)
-            turn_ungained(s - 1, 0)
-            invert(s)
-            logit_out(s + 1, 1, 1)
-            turn_ungained(s - 1, 1)
-            store(s - 3, 0)
-            store(s - 3, 1)
-            gain_out(s - 2, 1)
-            gain_out(s - 2, 0)
-            turn_out(s - 1, 0)
             p_quantize(s - 2)
-            product(s - 2, 0)
+            divide(s - 1, 0)
+            divide_by_scalar(s - 1, 1)
+            gain(s, FIRST)
+            product(s - 3, 0)
+            logit_out(s + 1, 1)
+            product(s - 2, 0, "vector")
+            logit_out(s + 1, 0)
+            mix_out_of_psum(s + 1, 1)
+            mix_out_of_psum(s + 1, 0)
+            turn(s - 1, 0)
+            turn(s - 1, 1)
+            product(s - 3, 1)
+            invert(s)
+            store(s - 3, 0)
+            turn_out(s - 1, 0)
+            turn_out(s - 1, 1)
+            store(s - 2, 0, by_vector)
             product(s - 2, 1)
-            gain_out(s - 1, 1)
-            gain_out(s - 1, 0)
+            maximum(s + 1)
+            store(s - 3, 1)
+            p_quantize(s - 1)
+            divide(s, 0, slice(0, S), nc.vector)
+            product(s - 1, 0, "vector")
 
             s = 15
             exponent(s, 0)
-            divide_by_scalar(s - 1)
             exponent(s, 1)
             divide_and_gain(s - 1, 1, 0)
             divide_and_gain(s - 1, 1, 1)
+            turn(s - 1, 0)
+            product(s - 2, 1, "vector")
+            turn(s - 1, 1)
             invert(s, FIRST)
-            p_quantize(s - 2)
-            turn(s - 1, 0, BOTH, "vector")
-            turn(s - 1, 1, BOTH, "vector")
-            product(s - 2, 0)
-            product(s - 2, 1)
+            store(s - 2, 0, by_vector)
+            turn_out(s - 1, 0)
+            store(s - 3, 1)
+            turn_out(s - 1, 1)
+            store(s - 2, 1)
             divide_and_gain(s, 0, 0)
+            p_quantize(s - 1, FIRST)
             invert(s, SECOND)
             divide_and_gain(s, 0, 1)
-            store(s - 3, 0)
-            turn_out(s - 1, 1)
-            turn_out(s - 1, 0)
-            turn(s, 0, BOTH, "vector")
+            product(s - 1, 0, "vector")
+            turn(s, 0)
             divide_and_gain(s, 1, 0)
+            p_quantize(s - 1, SECOND)
             divide_and_gain(s, 1, 1)
-            p_quantize(s - 1)
-            store(s - 3, 1)
-            turn(s, 1, FIRST, "vector")
-            turn(s, 1, SECOND, "vector")
+            turn(s, 1, FIRST)
+            turn(s, 1, SECOND)
+            product(s - 1, 1)
             turn_out(s, 0)
-            product(s - 1, 0)
-            product(s - 1, 1, "vector")
-            store(s - 2, 0, by_vector)
             turn_out(s, 1, FIRST)
-            turn_out(s, 1, SECOND)
+            store(s - 1, 0, by_vector)
             p_quantize(s, FIRST)
-            product(s, 0, "vector")
+            turn_out(s, 1, SECOND)
+            product(s, 0)
             quantize_half(s, 1, 0)
             quantize_half(s, 1, 1)
-            store(s - 2, 1)
             last_product(0)
             last_product(1)
-            store(s - 1, 0)
-            store(s - 1, 1, by_vector)
-            store(s, 0)
-            last_store(0, by_vector)
+            store(s - 1, 1)
+            store(s, 0, by_vector)
             last_store(1, by_scalar)
+            last_store(0, by_vector)

@@ -29,6 +29,9 @@ FLOPS = 2 * B * S * D * S + 2 * B * S * D * D + 2 * B * S * S * D
 BOTH, FIRST, SECOND = slice(0, 2), slice(0, 1), slice(1, 2)
 ROW = BANK + 8
 VECTOR_COLUMNS = 96
+LAG = 3
+P_WORDS, X_WORDS, V_WORDS = slice(0, 4 * P), slice(4 * P, 6 * P), slice(6 * P, 8 * P)
+WORDS = 8 * P
 RING = 4
 FIRST_TILEWISE_PAIR = N_PAIRS - 5
 
@@ -81,11 +84,11 @@ def tile_mixturedenserandomsynthesizer_t_kernel(tc, x_bytes, x_scale, w, rnd, mi
         load_w(0)
         nc.sync.dma_start(out=scale_4[:], in_=x_scale.rearrange("a b (p t) -> p (a b t)", t=PACK))
         nc.sync.dma_start(out=mix_raw[:], in_=mix.rearrange("(p o) -> p o", o=1))
-        load_x(0, 1)
+        nc.sync.dma_start(out=c_raw[:], in_=c.rearrange("(g p t) -> p g t", p=P, t=PACK))
         load_w(1)
+        load_x(0, 1)
         load_rnd(0)
         nc.sync.dma_start(out=wv_raw[:], in_=wv.rearrange("(p j) n -> p j n", j=PACK))
-        nc.sync.dma_start(out=c_raw[:], in_=c.rearrange("(g p t) -> p g t", p=P, t=PACK))
         nc.sync.dma_start(out=u_raw[:], in_=u.rearrange("(h p t) -> p h t", p=P, t=PACK))
         load_rnd(1)
         load_x(1, 0)
@@ -200,7 +203,24 @@ def tile_mixturedenserandomsynthesizer_t_kernel(tc, x_bytes, x_scale, w, rnd, mi
                 op1=Alu.add,
             )
 
-        x_wide, x_grouped, x_codes, x_scales = {}, {}, {}, {}
+        grouped, codes, scales = {}, {}, {}
+
+        def grouped_tile(s):
+            if s not in grouped:
+                grouped[s] = work.tile([P, WORDS, PACK], BF16, name="grouped", align_bytes=64)
+            return grouped[s]
+
+        def quantize_words(s, words):
+            if s not in codes:
+                codes[s] = work.tile([P, WORDS], U32, name="codes", bufs=8, align_bytes=64)
+                scales[s] = work.tile([P, WORDS], U8, name="scales", bufs=8, align_bytes=64)
+            quantize(codes[s][:, words], scales[s][:, words], grouped[s][:, words].rearrange("p n t -> p (n t)"))
+
+        def x_operand(q, rows=slice(0, 2 * P)):
+            words = slice(X_WORDS.start + rows.start, X_WORDS.start + rows.stop)
+            return codes[q - LAG][:, words], scales[q - LAG][:, words]
+
+        x_wide = {}
 
         def x_widen(q):
             b, h, t = q // PAIRS, (q % PAIRS) // 2, 2 * (q % 2)
@@ -211,64 +231,50 @@ def tile_mixturedenserandomsynthesizer_t_kernel(tc, x_bytes, x_scale, w, rnd, mi
 
         def x_turn(q, tiles=BOTH):
             words = x_wide[q][:].bitcast(F32)
-            if tiles.start == 0:
-                take_bank("vector", ("x", q))
-            bank = held.get(("x", q))[2]
+            bank = take_bank("vector", ("x", q, tiles.start))
             for j in range(tiles.start, tiles.stop):
                 for h in range(2):
                     nc.tensor.transpose(bank[:, 2 * h + j, :], words[:, 2 * P * j + h : 2 * P * (j + 1) : 2], ident[:])
 
-        def x_scale_out(q):
-            x_grouped[q] = work.tile([P, 2 * P, PACK], BF16, name="x_grouped", align_bytes=64)
-            values = give_bank(("x", q))[:].rearrange("p (h j) q -> p h (j q)", h=2).bitcast(BF16)
+        def x_scale_out(q, tiles=BOTH):
+            bank = give_bank(("x", q, tiles.start))
+            values = bank[:].rearrange("p n q -> p (n q)").bitcast(BF16).rearrange("p (h q e) -> p q h e", h=2, e=2)
+            tokens = slice(tiles.start * P, tiles.stop * P)
+            count = tokens.stop - tokens.start
             nc.vector.tensor_tensor(
-                out=x_grouped[q][:].rearrange("p q (h e) -> p q h e", e=2),
-                in0=values.rearrange("p h (q e) -> p q h e", e=2),
-                in1=scale_4[:].rearrange("p (o h e) -> p o h e", o=1, e=2).to_broadcast([P, 2 * P, 2, 2]),
+                out=grouped_tile(q - LAG)[:, X_WORDS].rearrange("p q (h e) -> p q h e", e=2)[:, tokens],
+                in0=values[:, tokens],
+                in1=scale_4[:].rearrange("p (o h e) -> p o h e", o=1, e=2).to_broadcast([P, count, 2, 2]),
                 op=Alu.mult,
             )
 
         def x_quantize(q):
-            x_codes[q] = work.tile([P, 2 * P], U32, name="x_codes", bufs=6, align_bytes=64)
-            x_scales[q] = work.tile([P, 2 * P], U8, name="x_scales", bufs=6, align_bytes=64)
-            quantize(x_codes[q][:], x_scales[q][:], x_grouped[q][:].rearrange("p q t -> p (q t)"))
+            quantize_words(q - LAG, X_WORDS)
 
-        v_grouped, v_codes, v_scales = {}, {}, {}
-
-        def v_product(hh, n):
-            sums = take_bank("vector", ("v", hh, n))
-            d_cols = slice(n * P, (n + 1) * P)
+        def v_product(n):
+            sums = take_bank("vector", ("v", n))
+            hh, i = divmod(n, QUARTERS)
+            d_cols = slice(i * P, (i + 1) * P)
             for t in range(PACK):
-                q, rows = 2 * hh + t // 2, slice((t % 2) * P, (t % 2 + 1) * P)
-                multiply(
-                    sums[:, t, :], x_codes[q][:, rows], x_scales[q][:, rows],
-                    wv_codes[:, d_cols], wv_scales[:, d_cols], True, True,
-                )
+                x_codes, x_scales = x_operand(2 * hh + t // 2, slice((t % 2) * P, (t % 2 + 1) * P))
+                multiply(sums[:, t, :], x_codes, x_scales, wv_codes[:, d_cols], wv_scales[:, d_cols], True, True)
 
-        def v_gain(hh, n):
-            if hh not in v_grouped:
-                v_grouped[hh] = work.tile([P, D, PACK], BF16, name="v_grouped", align_bytes=64)
-            h = hh % HALVES
+        def v_gain(n):
+            h = n // QUARTERS % HALVES
+            first = V_WORDS.start + n % 2 * P
             nc.vector.tensor_tensor(
-                out=v_grouped[hh][:, n * P : (n + 1) * P, :],
-                in0=give_bank(("v", hh, n))[:].rearrange("p t d -> p d t"),
+                out=grouped_tile(n // 2)[:, first : first + P, :],
+                in0=give_bank(("v", n))[:].rearrange("p t d -> p d t"),
                 in1=u_f[:, h : h + 1, :].to_broadcast([P, P, PACK]),
                 op=Alu.mult,
             )
 
-        def v_quantize(hh, features=slice(0, D)):
-            if hh not in v_codes:
-                v_codes[hh] = work.tile([P, D], U32, name="v_codes", bufs=4, align_bytes=64)
-                v_scales[hh] = work.tile([P, D], U8, name="v_scales", bufs=4, align_bytes=64)
-            quantize(
-                v_codes[hh][:, features], v_scales[hh][:, features],
-                v_grouped[hh][:, features].rearrange("p d t -> p (d t)"),
-            )
+        def v_quantize(s):
+            quantize_words(s, V_WORDS)
 
         mixed_scores = {}
         logits, maxima, exps, totals, inverses = {}, {}, {}, {}, {}
-        gained, pcs, grouped_pcs = {}, {}, {}
-        p_codes, p_scales, rows_out = {}, {}, {}
+        gained, pcs, rows_out = {}, {}, {}
 
         def score_turned(q, n):
             bank = take_bank("scalar", ("score", q, n), (P, 2, 2 * P))
@@ -276,7 +282,7 @@ def tile_mixturedenserandomsynthesizer_t_kernel(tc, x_bytes, x_scale, w, rnd, mi
                 keys = slice((2 * (n % 2) + i) * P, (2 * (n % 2) + i + 1) * P)
                 multiply(
                     bank[:, i, :], w_codes[n // 2][:, keys], w_scales[n // 2][:, keys],
-                    x_codes[q][:], x_scales[q][:], True, True,
+                    *x_operand(q), True, True,
                 )
 
         def score_out(q, n):
@@ -316,8 +322,7 @@ def tile_mixturedenserandomsynthesizer_t_kernel(tc, x_bytes, x_scale, w, rnd, mi
 
         def score(q, j):
             bank = take_bank("vector", ("score", q, j, 0), (P, BANK))
-            rows = slice(j * P, (j + 1) * P)
-            multiply(bank[:], x_codes[q][:, rows], x_scales[q][:, rows], w_codes[0][:], w_scales[0][:], True, True)
+            multiply(bank[:], *x_operand(q, slice(j * P, (j + 1) * P)), w_codes[0][:], w_scales[0][:], True, True)
 
         def logit_tile(q):
             if q not in logits:
@@ -347,13 +352,14 @@ def tile_mixturedenserandomsynthesizer_t_kernel(tc, x_bytes, x_scale, w, rnd, mi
                 accum_out=maxima[q][:, j : j + 1] if last else least,
             )
 
-        def maximum(q):
-            nc.vector.tensor_reduce(out=maxima[q][:], in_=logits[q][:, :, 0, 0 : BANK + 1], axis=AX.X, op=Alu.min)
-
-        def first_minimum(q):
+        def maximum(q, tiles=BOTH):
             nc.vector.tensor_reduce(
-                out=logits[q][:, :, 0, BANK], in_=logits[q][:, :, 0, 0:BANK], axis=AX.X, op=Alu.min
+                out=maxima[q][:, tiles], in_=logits[q][:, tiles, 0, 0 : BANK + 1], axis=AX.X, op=Alu.min
             )
+
+        def first_minimum(q, j):
+            row = logits[q][:, j, 0]
+            nc.vector.tensor_reduce(out=row[:, BANK : BANK + 1], in_=row[:, 0:BANK], axis=AX.X, op=Alu.min)
 
         def exponent(q, j):
             if q not in exps:
@@ -417,60 +423,47 @@ def tile_mixturedenserandomsynthesizer_t_kernel(tc, x_bytes, x_scale, w, rnd, mi
                 op1=Alu.mult,
             )
 
-        def grouped_tile(q):
-            if q not in grouped_pcs:
-                grouped_pcs[q] = work.tile([P, 2, HALVES, P, PACK], BF16, name="p_grouped", bufs=3, align_bytes=64)
-            return grouped_pcs[q]
-
         def turn(q, j, halves=BOTH, ring="scalar"):
             words = pcs[q][:, j * S : (j + 1) * S].bitcast(F32)
             bank = take_bank(ring, ("pc", q, j, halves.start))
             for n in range(2 * halves.start, 2 * halves.stop):
                 nc.tensor.transpose(bank[:, n, :], words[:, n * P : (n + 1) * P], ident[:])
 
-        def turn_out(q, j, halves=BOTH, copy=nc.scalar.copy):
+        def turn_out(q, j, halves=BOTH):
+            target = grouped_tile(q + LAG)[:, P_WORDS].rearrange("p (j g q) t -> p j g q t", j=2, g=HALVES)
             bank = give_bank(("pc", q, j, halves.start))
-            copy(
-                out=grouped_tile(q)[:, j, halves].bitcast(F32),
+            nc.scalar.copy(
+                out=target[:, j, halves].bitcast(F32),
                 in_=bank[:, 2 * halves.start : 2 * halves.stop].rearrange("p (g h) q -> p g q h", h=2),
             )
 
         def p_quantize(q, tiles=BOTH):
-            if q not in p_codes:
-                p_codes[q] = work.tile([P, 2 * HALVES * P], U32, name="p_codes", bufs=4, align_bytes=64)
-                p_scales[q] = work.tile([P, 2 * HALVES * P], U8, name="p_scales", bufs=4, align_bytes=64)
-            cols = slice(tiles.start * HALVES * P, tiles.stop * HALVES * P)
-            quantize(
-                p_codes[q][:, cols], p_scales[q][:, cols], grouped_pcs[q][:, tiles].rearrange("p j g q t -> p (j g q t)")
+            quantize_words(q + LAG, slice(tiles.start * HALVES * P, tiles.stop * HALVES * P))
+
+        def quantize_half(q, j, g):
+            quantize_words(q + LAG, slice((2 * j + g) * P, (2 * j + g + 1) * P))
+
+        def product_pass(sums, q, j, g, n, start, stop):
+            words = slice((2 * j + g) * P, (2 * j + g + 1) * P)
+            s = 2 * (HALVES * (q // PAIRS) + g) + n
+            multiply(
+                sums, codes[q + LAG][:, words], scales[q + LAG][:, words],
+                codes[s][:, V_WORDS], scales[s][:, V_WORDS], start, stop,
             )
 
         def product(q, j, ring="scalar"):
             bank = take_bank(ring, ("out", q, j), (P, D))
             for g in range(HALVES):
-                cols = slice((2 * j + g) * P, (2 * j + g + 1) * P)
-                hh = HALVES * (q // PAIRS) + g
-                multiply(
-                    bank[:], p_codes[q][:, cols], p_scales[q][:, cols],
-                    v_codes[hh][:], v_scales[hh][:], g == 0, g == HALVES - 1,
-                )
-
-        def quantize_half(q, j, g):
-            cols = slice((2 * j + g) * P, (2 * j + g + 1) * P)
-            quantize(p_codes[q][:, cols], p_scales[q][:, cols], grouped_pcs[q][:, j, g].rearrange("p q t -> p (q t)"))
+                for n in range(2):
+                    product_pass(bank[:, n * D // 2 : (n + 1) * D // 2], q, j, g, n, g + n == 0, g + n == 2)
 
         last_sums = {}
 
         def last_product(g):
-            cols = slice((2 + g) * P, (3 + g) * P)
-            hh = HALVES * (B - 1) + g
             for n, ring in enumerate(("vector", "scalar")):
                 if g == 0:
                     last_sums[n] = take_bank(ring, ("last", n), (P, D // 2))
-                d_cols = slice(n * D // 2, (n + 1) * D // 2)
-                multiply(
-                    last_sums[n][:], p_codes[N_PAIRS - 1][:, cols], p_scales[N_PAIRS - 1][:, cols],
-                    v_codes[hh][:, d_cols], v_scales[hh][:, d_cols], g == 0, g == HALVES - 1,
-                )
+                product_pass(last_sums[n][:], N_PAIRS - 1, 1, g, n, g == 0, g == HALVES - 1)
 
         def last_store(n, copy):
             d_cols = slice(n * D // 2, (n + 1) * D // 2)
@@ -503,17 +496,16 @@ def tile_mixturedenserandomsynthesizer_t_kernel(tc, x_bytes, x_scale, w, rnd, mi
         def live(q):
             return 0 <= q < N_PAIRS
 
-        def quarter(n):
-            return divmod(n, QUARTERS)
-
         def step(s):
             exponent(s, 1)
             exponent(s, 0)
-            if live(s - 3):
-                p_quantize(s - 3)
-            x_quantize(s + 3)
+            if s == 1:
+                score_out(3, 3)
+                score_out(3, 2)
+            if s == 1:
+                v_quantize(0)
             invert(s - 1)
-            v_quantize(s // 2, slice(0 if s == 1 else s % 2 * D // 2, (s % 2 + 1) * D // 2))
+            quantize_words(s, slice(0 if live(s - 3) else X_WORDS.start, WORDS))
             divide(s - 1, 0)
             divide_by_scalar(s - 1, 1)
             gain(s)
@@ -521,143 +513,144 @@ def tile_mixturedenserandomsynthesizer_t_kernel(tc, x_bytes, x_scale, w, rnd, mi
                 product(s - 3, 0)
                 product(s - 3, 1)
             else:
-                score_turned(s + 3, 2)
                 score_turned(s + 3, 3)
             mix_out_of_psum(s + 1, 1)
-            x_turn(s + 4)
+            v_product(2 * s + 2)
             mix_out_of_psum(s + 1, 0)
+            v_product(2 * s + 3)
             logit_out(s + 1, 1)
-            v_product(*quarter(2 * s + 2))
-            v_product(*quarter(2 * s + 3))
+            x_turn(s + 4)
+            logit_out(s + 1, 0)
+            blend(s + 2, 0, 1)
             if live(s - 3):
                 store(s - 3, 1)
                 store_part(s - 3, 0, slice(VECTOR_COLUMNS, D))
             elif s + 2 < PAIRS:
                 rnd_scale(s + 2, 0)
                 rnd_scale(s + 2, 1)
-            logit_out(s + 1, 0)
             if live(s - 2):
                 turn_out(s - 2, 0)
                 turn_out(s - 2, 1)
+            maximum(s + 1, SECOND)
+            v_gain(2 * s + 3)
+            score_turned(s + 3, 2)
             if live(s - 3):
-                score_turned(s + 3, 2)
                 score_turned(s + 3, 3)
-            blend(s + 2, 0, 1)
+            blend(s + 2, 1, 1)
+            turn(s - 1, 1)
+            v_gain(2 * s + 2)
             x_scale_out(s + 4)
             if live(s - 3):
                 store(s - 3, 0, by_vector, slice(0, VECTOR_COLUMNS))
-            turn(s - 1, 1)
-            blend(s + 2, 1, 1)
             turn(s - 1, 0)
             if live(s + 5):
                 x_widen(s + 5)
-            v_gain(*quarter(2 * s + 3))
             score(s + 2, 0)
-            maximum(s + 1)
-            v_gain(*quarter(2 * s + 2))
             score(s + 2, 1)
-            score_out(s + 3, 3)
-            score_out(s + 3, 2)
+            maximum(s + 1, FIRST)
+            for n in (3, 2) if live(s - 3) else (2, 3):
+                score_out(s + 3, n)
 
         with tc.manual_schedule():
             x_widen(0)
-            x_turn(0)
+            x_turn(0, FIRST)
+            x_turn(0, SECOND)
             x_widen(1)
             w_group(0, 0, by_vector)
             w_group(0, 1, by_scalar)
             by_vector(out=mix_column[0:2], in_=mix_raw[:])
             mix_spread()
             x_turn(1)
-            x_widen(2)
             w_group(1, 0, by_scalar)
             w_group(1, 1, by_scalar)
-            x_scale_out(0)
+            x_widen(2)
+            x_scale_out(0, FIRST)
+            x_scale_out(0, SECOND)
+            by_vector(out=c_4[:], in_=c_raw[:].rearrange("p g t -> p (g t)"))
             mix_out()
-            x_turn(2)
+            c_spread(0)
             w_quantize(0)
             x_quantize(0)
             score(0, 0)
             score(0, 1)
+            blend_open(0, 0, 1)
             x_scale_out(1)
+            blend_open(0, 1, 1)
             w_quantize(1)
             x_quantize(1)
-            by_vector(out=c_4[:], in_=c_raw[:].rearrange("p g t -> p (g t)"))
-            by_vector(out=u_f[:], in_=u_raw[:])
             wv_group()
             rnd_scale_by_gpsimd(1, 0)
             rnd_scale_by_gpsimd(1, 1)
             rnd_scale(0, 0)
             rnd_scale(0, 1)
             x_widen(3)
-            blend_open(0, 0, 1)
+            by_scalar(out=u_f[:], in_=u_raw[:])
             score_turned(0, 2)
             score_turned(0, 3)
             mix_out_of_psum(0, 0)
-            x_turn(3)
+            x_turn(2)
             score_turned(1, 0)
-            score_turned(1, 1)
             mix_out_of_psum(0, 1)
-            blend_open(0, 1, 1)
+            c_out(0, by_scalar)
             score_out(0, 2)
             score_out(0, 3)
-            c_spread(0)
-            blend_close(0, 0, 1)
-            blend_close(0, 1, 1)
+            score_turned(1, 1)
+            x_turn(3)
             score_turned(1, 2)
+            blend_close(0, 0, 1)
+            score_turned(1, 3)
+            blend_close(0, 1, 1)
+            first_minimum(0, 0)
+            first_minimum(0, 1)
             x_scale_out(2)
-            first_minimum(0)
             x_scale_out(3)
             score_out(1, 0)
-            score_turned(1, 3)
-            score_out(1, 1)
-            c_out(0, by_scalar)
-            blend(1, 0, 0)
             c_spread(1)
-            blend(1, 1, 0)
+            score_out(1, 1)
             score_out(1, 2)
             score_out(1, 3)
+            c_out(1, by_scalar)
+            blend(1, 0, 0)
+            blend(1, 1, 0)
             logit_out(0, 0, 1, True)
             logit_out(0, 1, 1, True)
-            blend(1, 0, 1)
-            blend(1, 1, 1)
             x_quantize(2)
             wv_quantize()
             x_quantize(3)
 
             exponent(0, 0)
-            c_out(1, by_scalar)
             exponent(0, 1)
             gain(0)
-            x_widen(4)
+            v_product(0)
+            v_product(1)
             score_turned(2, 2)
             score_turned(2, 3)
+            x_widen(4)
             logit_out(1, 0, 0)
-            v_product(0, 0)
             logit_out(1, 1, 0)
-            v_product(0, 1)
-            logit_out(1, 0, 1, True)
-            x_turn(4)
-            logit_out(1, 1, 1, True)
-            v_product(0, 2)
-            score_turned(3, 2)
-            score_turned(3, 3)
+            blend(1, 0, 1)
+            blend(1, 1, 1)
+            v_gain(0)
+            v_product(2)
+            v_gain(1)
+            v_product(3)
             score_out(2, 3)
             score_out(2, 2)
-            v_gain(0, 0)
-            v_product(0, 3)
-            v_gain(0, 1)
+            logit_out(1, 0, 1, True)
+            x_turn(4)
+            score_turned(3, 2)
+            score_turned(3, 3)
+            logit_out(1, 1, 1, True)
             blend(2, 0, 1)
-            x_scale_out(4)
-            blend(2, 1, 1)
             rnd_scale(2, 0)
             rnd_scale(2, 1)
             x_widen(5)
-            v_gain(0, 2)
+            v_gain(2)
+            blend(2, 1, 1)
+            v_gain(3)
             score(2, 0)
-            v_gain(0, 3)
+            x_scale_out(4)
             score(2, 1)
-            score_out(3, 3)
-            score_out(3, 2)
 
             for s in range(1, N_PAIRS - 4):
                 step(s)
@@ -665,50 +658,49 @@ def tile_mixturedenserandomsynthesizer_t_kernel(tc, x_bytes, x_scale, w, rnd, mi
             s = 12
             exponent(s, 1)
             exponent(s, 0)
-            p_quantize(s - 3)
-            x_quantize(s + 3)
             invert(s - 1)
-            v_quantize(6, slice(0, D // 2))
+            quantize_words(s, slice(0, WORDS))
             divide(s - 1, 0)
             divide_by_scalar(s - 1, 1)
             gain(s)
             product(s - 3, 0)
             product(s - 3, 1)
             mix_out_of_psum(s + 1, 1)
-            v_product(6, 2)
+            v_product(26)
             mix_out_of_psum(s + 1, 0)
-            v_product(6, 3)
+            v_product(27)
             logit_out(s + 1, 1)
-            v_product(7, 0)
+            v_product(28)
+            logit_out(s + 1, 0)
+            v_product(29)
             store(s - 3, 1)
             store(s - 3, 0)
-            logit_out(s + 1, 0)
-            v_product(7, 1)
             turn_out(s - 2, 0)
             turn_out(s - 2, 1)
+            maximum(s + 1, SECOND)
+            v_gain(27)
             score_turned(s + 3, 2)
             score_turned(s + 3, 3)
-            v_gain(6, 3)
-            v_gain(6, 2)
             blend(s + 2, 0, 1)
+            v_gain(26)
             turn(s - 1, 1)
             blend(s + 2, 1, 1)
             turn(s - 1, 0)
-            v_gain(7, 1)
+            v_gain(29)
             score(s + 2, 0)
-            maximum(s + 1)
-            v_gain(7, 0)
+            v_gain(28)
             score(s + 2, 1)
+            maximum(s + 1, FIRST)
             score_out(s + 3, 3)
             score_out(s + 3, 2)
 
             s = 13
             exponent(s, 1)
             exponent(s, 0)
-            p_quantize(s - 3)
-            v_quantize(6, slice(D // 2, D))
+            v_quantize(13)
+            v_quantize(14)
             invert(s - 1)
-            v_quantize(7, slice(0, D // 2))
+            p_quantize(s - 3)
             divide(s - 1, 0, slice(0, BANK))
             divide_by_scalar(s - 1, 1)
             divide_by_scalar(s - 1, 0, slice(BANK, S))
@@ -716,9 +708,9 @@ def tile_mixturedenserandomsynthesizer_t_kernel(tc, x_bytes, x_scale, w, rnd, mi
             product(s - 3, 0)
             product(s - 3, 1)
             mix_out_of_psum(s + 1, 1)
-            v_product(7, 2)
+            v_product(30)
             mix_out_of_psum(s + 1, 0)
-            v_product(7, 3)
+            v_product(31)
             logit_out(s + 1, 1)
             turn_out(s - 2, 0)
             turn_out(s - 2, 1)
@@ -727,10 +719,10 @@ def tile_mixturedenserandomsynthesizer_t_kernel(tc, x_bytes, x_scale, w, rnd, mi
             turn(s - 1, 1)
             blend(s + 2, 1, 1)
             turn(s - 1, 0)
-            v_gain(7, 3)
+            v_gain(31)
             score(s + 2, 0)
             maximum(s + 1)
-            v_gain(7, 2)
+            v_gain(30)
             score(s + 2, 1)
             store(s - 3, 1)
             turn_out(s - 1, 1)
@@ -741,7 +733,7 @@ def tile_mixturedenserandomsynthesizer_t_kernel(tc, x_bytes, x_scale, w, rnd, mi
             exponent(s, 1)
             exponent(s, 0)
             p_quantize(s - 3)
-            v_quantize(7, slice(D // 2, D))
+            v_quantize(15)
             invert(s - 1)
             p_quantize(s - 2)
             divide(s - 1, 0)
@@ -760,10 +752,9 @@ def tile_mixturedenserandomsynthesizer_t_kernel(tc, x_bytes, x_scale, w, rnd, mi
             store(s - 3, 0)
             turn_out(s - 1, 0)
             turn_out(s - 1, 1)
-            store(s - 2, 0, by_vector)
             product(s - 2, 1)
             maximum(s + 1)
-            store(s - 3, 1)
+            store(s - 2, 0)
             p_quantize(s - 1)
             divide(s, 0, slice(0, S), nc.vector)
             product(s - 1, 0, "vector")
@@ -772,39 +763,40 @@ def tile_mixturedenserandomsynthesizer_t_kernel(tc, x_bytes, x_scale, w, rnd, mi
             exponent(s, 0)
             exponent(s, 1)
             divide_and_gain(s - 1, 1, 0)
+            invert(s, FIRST)
             divide_and_gain(s - 1, 1, 1)
             turn(s - 1, 0)
             product(s - 2, 1, "vector")
-            turn(s - 1, 1)
-            invert(s, FIRST)
-            store(s - 2, 0, by_vector)
+            turn(s - 1, 1, BOTH, "vector")
             turn_out(s - 1, 0)
-            store(s - 3, 1)
+            store(s - 4, 1)
             turn_out(s - 1, 1)
-            store(s - 2, 1)
+            store(s - 3, 1)
             divide_and_gain(s, 0, 0)
-            p_quantize(s - 1, FIRST)
             invert(s, SECOND)
             divide_and_gain(s, 0, 1)
-            product(s - 1, 0, "vector")
+            p_quantize(s - 1, FIRST)
             turn(s, 0)
+            product(s - 1, 0, "vector")
             divide_and_gain(s, 1, 0)
             p_quantize(s - 1, SECOND)
             divide_and_gain(s, 1, 1)
             turn(s, 1, FIRST)
-            turn(s, 1, SECOND)
             product(s - 1, 1)
+            turn(s, 1, SECOND)
             turn_out(s, 0)
+            store(s - 2, 0, by_vector)
             turn_out(s, 1, FIRST)
-            store(s - 1, 0, by_vector)
             p_quantize(s, FIRST)
+            store(s - 2, 1)
             turn_out(s, 1, SECOND)
             product(s, 0)
             quantize_half(s, 1, 0)
+            store(s - 1, 0, by_vector)
             quantize_half(s, 1, 1)
             last_product(0)
             last_product(1)
             store(s - 1, 1)
-            store(s, 0, by_vector)
-            last_store(1, by_scalar)
+            store(s, 0)
             last_store(0, by_vector)
+            last_store(1, by_scalar)

@@ -28,7 +28,8 @@ FLOPS = 2 * B * S * D * S + 2 * B * S * D * D + 2 * B * S * S * D
 
 BOTH, FIRST, SECOND = slice(0, 2), slice(0, 1), slice(1, 2)
 ROW = BANK + 8
-VECTOR_COLUMNS = 96
+VECTOR_COLUMNS = 160
+SHARED_STEPS = range(5, 11)
 LAG = 3
 P_WORDS, X_WORDS, V_WORDS = slice(0, 4 * P), slice(4 * P, 6 * P), slice(6 * P, 8 * P)
 WORDS = 8 * P
@@ -500,14 +501,14 @@ def tile_mixturedenserandomsynthesizer_t_kernel(tc, x_bytes, x_scale, w, rnd, mi
             exponent(s, 1)
             exponent(s, 0)
             if s == 1:
-                score_out(3, 3)
-                score_out(3, 2)
-            if s == 1:
                 v_quantize(0)
             invert(s - 1)
             quantize_words(s, slice(0 if live(s - 3) else X_WORDS.start, WORDS))
             divide(s - 1, 0)
             divide_by_scalar(s - 1, 1)
+            if s == 1:
+                score_out(3, 3)
+                score_out(3, 2)
             gain(s)
             if live(s - 3):
                 product(s - 3, 0)
@@ -524,7 +525,10 @@ def tile_mixturedenserandomsynthesizer_t_kernel(tc, x_bytes, x_scale, w, rnd, mi
             blend(s + 2, 0, 1)
             if live(s - 3):
                 store(s - 3, 1)
-                store_part(s - 3, 0, slice(VECTOR_COLUMNS, D))
+                if s in SHARED_STEPS:
+                    store_part(s - 3, 0, slice(VECTOR_COLUMNS, D))
+                else:
+                    store(s - 3, 0)
             elif s + 2 < PAIRS:
                 rnd_scale(s + 2, 0)
                 rnd_scale(s + 2, 1)
@@ -540,7 +544,7 @@ def tile_mixturedenserandomsynthesizer_t_kernel(tc, x_bytes, x_scale, w, rnd, mi
             turn(s - 1, 1)
             v_gain(2 * s + 2)
             x_scale_out(s + 4)
-            if live(s - 3):
+            if s in SHARED_STEPS:
                 store(s - 3, 0, by_vector, slice(0, VECTOR_COLUMNS))
             turn(s - 1, 0)
             if live(s + 5):
@@ -556,21 +560,22 @@ def tile_mixturedenserandomsynthesizer_t_kernel(tc, x_bytes, x_scale, w, rnd, mi
             x_turn(0, FIRST)
             x_turn(0, SECOND)
             x_widen(1)
-            w_group(0, 0, by_vector)
+            w_group(0, 0, copy_by_gpsimd)
             w_group(0, 1, by_scalar)
-            by_vector(out=mix_column[0:2], in_=mix_raw[:])
-            mix_spread()
             x_turn(1)
             w_group(1, 0, by_scalar)
             w_group(1, 1, by_scalar)
             x_widen(2)
             x_scale_out(0, FIRST)
             x_scale_out(0, SECOND)
+            by_vector(out=mix_column[0:2], in_=mix_raw[:])
             by_vector(out=c_4[:], in_=c_raw[:].rearrange("p g t -> p (g t)"))
-            mix_out()
+            mix_spread()
             c_spread(0)
             w_quantize(0)
             x_quantize(0)
+            mix_out()
+            rnd_scale_by_gpsimd(0, 0)
             score(0, 0)
             score(0, 1)
             blend_open(0, 0, 1)
@@ -581,7 +586,6 @@ def tile_mixturedenserandomsynthesizer_t_kernel(tc, x_bytes, x_scale, w, rnd, mi
             wv_group()
             rnd_scale_by_gpsimd(1, 0)
             rnd_scale_by_gpsimd(1, 1)
-            rnd_scale(0, 0)
             rnd_scale(0, 1)
             x_widen(3)
             by_scalar(out=u_f[:], in_=u_raw[:])
@@ -596,8 +600,8 @@ def tile_mixturedenserandomsynthesizer_t_kernel(tc, x_bytes, x_scale, w, rnd, mi
             score_out(0, 3)
             score_turned(1, 1)
             x_turn(3)
-            score_turned(1, 2)
             blend_close(0, 0, 1)
+            score_turned(1, 2)
             score_turned(1, 3)
             blend_close(0, 1, 1)
             first_minimum(0, 0)
@@ -638,8 +642,6 @@ def tile_mixturedenserandomsynthesizer_t_kernel(tc, x_bytes, x_scale, w, rnd, mi
             score_out(2, 2)
             logit_out(1, 0, 1, True)
             x_turn(4)
-            score_turned(3, 2)
-            score_turned(3, 3)
             logit_out(1, 1, 1, True)
             blend(2, 0, 1)
             rnd_scale(2, 0)
@@ -651,6 +653,8 @@ def tile_mixturedenserandomsynthesizer_t_kernel(tc, x_bytes, x_scale, w, rnd, mi
             score(2, 0)
             x_scale_out(4)
             score(2, 1)
+            score_turned(3, 2)
+            score_turned(3, 3)
 
             for s in range(1, N_PAIRS - 4):
                 step(s)

@@ -28,8 +28,6 @@ FLOPS = 2 * B * S * D * S + 2 * B * S * D * D + 2 * B * S * S * D
 
 BOTH, FIRST, SECOND = slice(0, 2), slice(0, 1), slice(1, 2)
 ROW = BANK + 8
-VECTOR_COLUMNS = 160
-SHARED_STEPS = range(5, 11)
 LAG = 3
 P_WORDS, X_WORDS, V_WORDS = slice(0, 4 * P), slice(4 * P, 6 * P), slice(6 * P, 8 * P)
 WORDS = 8 * P
@@ -107,7 +105,7 @@ def tile_mixturedenserandomsynthesizer_t_kernel(tc, x_bytes, x_scale, w, rnd, mi
         mix_f = keep.tile([P, 1], F32, name="mix_f")
         mix_negated = keep.tile([P, 2], F32, name="mix_negated")
         rnd_f = []
-        for k in range(PAIRS):
+        for k in range(PAIRS - 1):
             rnd_f.append(keep.tile([P, 2, BANK], F32, name="rnd_f%d" % k))
         u_f = keep.tile([P, HALVES, PACK], F32, name="u_f")
         c_4 = keep.tile([P, HALVES * PACK], F32, name="c_4")
@@ -115,7 +113,7 @@ def tile_mixturedenserandomsynthesizer_t_kernel(tc, x_bytes, x_scale, w, rnd, mi
         mix_diag = keep.tile([P, P], BF16, name="mix_diag")
         w_grouped, w_codes, w_scales = [], [], []
         for g in range(HALVES):
-            w_grouped.append(keep.tile([P, BANK, PACK], BF16, name="gained%d" % (1 - g), align_bytes=64))
+            w_grouped.append(keep.tile([P, BANK, PACK], BF16, name="rnd_f3" if g else "gained0", align_bytes=64))
             w_codes.append(keep.tile([P, BANK], U32, name="w_codes%d" % g, align_bytes=64))
             w_scales.append(keep.tile([P, BANK], U8, name="w_scales%d" % g, align_bytes=64))
         wv_grouped = []
@@ -180,7 +178,7 @@ def tile_mixturedenserandomsynthesizer_t_kernel(tc, x_bytes, x_scale, w, rnd, mi
             quantize(w_codes[g][:], w_scales[g][:], w_grouped[g][:].rearrange("p n j -> p (n j)"))
 
         def wv_group():
-            wv_grouped.append(keep.tile([P, D, PACK], BF16, name="gained0", align_bytes=64))
+            wv_grouped.append(keep.tile([P, D, PACK], BF16, name="rnd_f3", align_bytes=64))
             copy_by_gpsimd(wv_grouped[0][:], wv_raw[:].rearrange("p j n -> p n j"))
 
         def wv_quantize():
@@ -195,6 +193,8 @@ def tile_mixturedenserandomsynthesizer_t_kernel(tc, x_bytes, x_scale, w, rnd, mi
             )
 
         def rnd_scale_by_gpsimd(k, j):
+            if k == len(rnd_f):
+                rnd_f.append(keep.tile([P, 2, BANK], F32, name="rnd_f3", align_bytes=64))
             nc.gpsimd.tensor_scalar(
                 out=column_split(rnd_f[k][:, j]),
                 in0=key_split(rnd_raw[k][:, j, 0:BANK]),
@@ -225,7 +225,7 @@ def tile_mixturedenserandomsynthesizer_t_kernel(tc, x_bytes, x_scale, w, rnd, mi
 
         def x_widen(q):
             b, h, t = q // PAIRS, (q % PAIRS) // 2, 2 * (q % 2)
-            x_wide[q] = work.tile([P, 2 * D], BF16, name="wide", bufs=2)
+            x_wide[q] = work.tile([P, 2 * D], BF16, name="wide", bufs=7)
             nc.scalar.copy(
                 out=x_wide[q][:], in_=x_raw.get((b, h))[:, t : t + 2, :].rearrange("p t k -> p (t k)").bitcast(FP8)
             )
@@ -480,9 +480,6 @@ def tile_mixturedenserandomsynthesizer_t_kernel(tc, x_bytes, x_scale, w, rnd, mi
                 rows_out[q] = work.tile([P, 2, D], F32, name="rows_out", bufs=4)
             return rows_out[q]
 
-        def store_part(q, j, cols):
-            nc.scalar.copy(out=rows_tile(q)[:, j, cols], in_=held.get(("out", q, j))[2][:, cols])
-
         def store(q, j, copy=nc.scalar.copy, cols=slice(0, D)):
             b, h, t = q // PAIRS, (q % PAIRS) // 2, 2 * (q % 2)
             copy(out=rows_tile(q)[:, j, cols], in_=give_bank(("out", q, j))[:, cols])
@@ -525,13 +522,7 @@ def tile_mixturedenserandomsynthesizer_t_kernel(tc, x_bytes, x_scale, w, rnd, mi
             blend(s + 2, 0, 1)
             if live(s - 3):
                 store(s - 3, 1)
-                if s in SHARED_STEPS:
-                    store_part(s - 3, 0, slice(VECTOR_COLUMNS, D))
-                else:
-                    store(s - 3, 0)
-            elif s + 2 < PAIRS:
-                rnd_scale(s + 2, 0)
-                rnd_scale(s + 2, 1)
+                store(s - 3, 0)
             if live(s - 2):
                 turn_out(s - 2, 0)
                 turn_out(s - 2, 1)
@@ -544,11 +535,12 @@ def tile_mixturedenserandomsynthesizer_t_kernel(tc, x_bytes, x_scale, w, rnd, mi
             turn(s - 1, 1)
             v_gain(2 * s + 2)
             x_scale_out(s + 4)
-            if s in SHARED_STEPS:
-                store(s - 3, 0, by_vector, slice(0, VECTOR_COLUMNS))
             turn(s - 1, 0)
-            if live(s + 5):
-                x_widen(s + 5)
+            if s == 1:
+                for q in (8, 9, 10):
+                    x_widen(q)
+            elif s % 2 == 0:
+                x_widen(10 + s // 2)
             score(s + 2, 0)
             score(s + 2, 1)
             maximum(s + 1, FIRST)
@@ -586,6 +578,7 @@ def tile_mixturedenserandomsynthesizer_t_kernel(tc, x_bytes, x_scale, w, rnd, mi
             wv_group()
             rnd_scale_by_gpsimd(1, 0)
             rnd_scale_by_gpsimd(1, 1)
+            rnd_scale_by_gpsimd(2, 0)
             rnd_scale(0, 1)
             x_widen(3)
             by_scalar(out=u_f[:], in_=u_raw[:])
@@ -621,6 +614,8 @@ def tile_mixturedenserandomsynthesizer_t_kernel(tc, x_bytes, x_scale, w, rnd, mi
             x_quantize(2)
             wv_quantize()
             x_quantize(3)
+            rnd_scale_by_gpsimd(3, 0)
+            rnd_scale_by_gpsimd(3, 1)
 
             exponent(0, 0)
             exponent(0, 1)
@@ -630,6 +625,7 @@ def tile_mixturedenserandomsynthesizer_t_kernel(tc, x_bytes, x_scale, w, rnd, mi
             score_turned(2, 2)
             score_turned(2, 3)
             x_widen(4)
+            x_widen(5)
             logit_out(1, 0, 0)
             logit_out(1, 1, 0)
             blend(1, 0, 1)
@@ -644,9 +640,9 @@ def tile_mixturedenserandomsynthesizer_t_kernel(tc, x_bytes, x_scale, w, rnd, mi
             x_turn(4)
             logit_out(1, 1, 1, True)
             blend(2, 0, 1)
-            rnd_scale(2, 0)
             rnd_scale(2, 1)
-            x_widen(5)
+            x_widen(6)
+            x_widen(7)
             v_gain(2)
             blend(2, 1, 1)
             v_gain(3)

@@ -31,6 +31,8 @@ ROW = BANK + 8
 LAG = 3
 P_WORDS, X_WORDS, V_WORDS = slice(0, 4 * P), slice(4 * P, 6 * P), slice(6 * P, 8 * P)
 WORDS = 8 * P
+VECTOR_COLUMNS = 192
+SCALAR_KEYS = 256
 RING = 4
 FIRST_TILEWISE_PAIR = N_PAIRS - 5
 
@@ -480,6 +482,9 @@ def tile_mixturedenserandomsynthesizer_t_kernel(tc, x_bytes, x_scale, w, rnd, mi
                 rows_out[q] = work.tile([P, 2, D], F32, name="rows_out", bufs=4)
             return rows_out[q]
 
+        def store_part(q, j, cols):
+            nc.scalar.copy(out=rows_tile(q)[:, j, cols], in_=held.get(("out", q, j))[2][:, cols])
+
         def store(q, j, copy=nc.scalar.copy, cols=slice(0, D)):
             b, h, t = q // PAIRS, (q % PAIRS) // 2, 2 * (q % 2)
             copy(out=rows_tile(q)[:, j, cols], in_=give_bank(("out", q, j))[:, cols])
@@ -501,7 +506,11 @@ def tile_mixturedenserandomsynthesizer_t_kernel(tc, x_bytes, x_scale, w, rnd, mi
                 v_quantize(0)
             invert(s - 1)
             quantize_words(s, slice(0 if live(s - 3) else X_WORDS.start, WORDS))
-            divide(s - 1, 0)
+            if s % 2 == 1:
+                divide(s - 1, 0, slice(0, S - SCALAR_KEYS))
+                divide_by_scalar(s - 1, 0, slice(S - SCALAR_KEYS, S))
+            else:
+                divide(s - 1, 0)
             divide_by_scalar(s - 1, 1)
             if s == 1:
                 score_out(3, 3)
@@ -522,7 +531,10 @@ def tile_mixturedenserandomsynthesizer_t_kernel(tc, x_bytes, x_scale, w, rnd, mi
             blend(s + 2, 0, 1)
             if live(s - 3):
                 store(s - 3, 1)
-                store(s - 3, 0)
+                if s % 2 == 0:
+                    store_part(s - 3, 0, slice(VECTOR_COLUMNS, D))
+                else:
+                    store(s - 3, 0)
             if live(s - 2):
                 turn_out(s - 2, 0)
                 turn_out(s - 2, 1)
@@ -535,6 +547,8 @@ def tile_mixturedenserandomsynthesizer_t_kernel(tc, x_bytes, x_scale, w, rnd, mi
             turn(s - 1, 1)
             v_gain(2 * s + 2)
             x_scale_out(s + 4)
+            if live(s - 3) and s % 2 == 0:
+                store(s - 3, 0, by_vector, slice(0, VECTOR_COLUMNS))
             turn(s - 1, 0)
             if s == 1:
                 for q in (8, 9, 10):
@@ -752,9 +766,10 @@ def tile_mixturedenserandomsynthesizer_t_kernel(tc, x_bytes, x_scale, w, rnd, mi
             store(s - 3, 0)
             turn_out(s - 1, 0)
             turn_out(s - 1, 1)
+            store(s - 2, 0, by_vector)
             product(s - 2, 1)
             maximum(s + 1)
-            store(s - 2, 0)
+            store(s - 3, 1)
             p_quantize(s - 1)
             divide(s, 0, slice(0, S), nc.vector)
             product(s - 1, 0, "vector")
@@ -769,34 +784,33 @@ def tile_mixturedenserandomsynthesizer_t_kernel(tc, x_bytes, x_scale, w, rnd, mi
             product(s - 2, 1, "vector")
             turn(s - 1, 1, BOTH, "vector")
             turn_out(s - 1, 0)
-            store(s - 4, 1)
-            turn_out(s - 1, 1)
             store(s - 3, 1)
+            turn_out(s - 1, 1)
             divide_and_gain(s, 0, 0)
             invert(s, SECOND)
             divide_and_gain(s, 0, 1)
             p_quantize(s - 1, FIRST)
             turn(s, 0)
-            product(s - 1, 0, "vector")
+            product(s - 1, 0)
             divide_and_gain(s, 1, 0)
             p_quantize(s - 1, SECOND)
             divide_and_gain(s, 1, 1)
             turn(s, 1, FIRST)
-            product(s - 1, 1)
-            turn(s, 1, SECOND)
+            product(s - 1, 1, "vector")
             turn_out(s, 0)
-            store(s - 2, 0, by_vector)
+            turn(s, 1, SECOND)
+            store(s - 2, 1)
             turn_out(s, 1, FIRST)
             p_quantize(s, FIRST)
-            store(s - 2, 1)
-            turn_out(s, 1, SECOND)
             product(s, 0)
+            store(s - 2, 0, by_vector)
+            store(s - 1, 0)
+            turn_out(s, 1, SECOND)
             quantize_half(s, 1, 0)
-            store(s - 1, 0, by_vector)
+            store(s - 1, 1, by_vector)
             quantize_half(s, 1, 1)
+            store(s, 0)
             last_product(0)
             last_product(1)
-            store(s - 1, 1)
-            store(s, 0)
-            last_store(0, by_vector)
             last_store(1, by_scalar)
+            last_store(0, by_vector)

@@ -504,8 +504,12 @@ def tile_mixturedenserandomsynthesizer_t_kernel(tc, x_bytes, x_scale, w, rnd, mi
             exponent(s, 0)
             if s == 1:
                 v_quantize(0)
+            elif s == 2:
+                x_quantize(5)
+            else:
+                p_quantize(s - 3)
             invert(s - 1)
-            quantize_words(s, slice(0 if live(s - 3) else X_WORDS.start, WORDS))
+            quantize_words(s, V_WORDS if s == 2 else slice(X_WORDS.start, WORDS))
             if s % 2 == 1:
                 divide(s - 1, 0, slice(0, S - SCALAR_KEYS))
                 divide_by_scalar(s - 1, 0, slice(S - SCALAR_KEYS, S))
@@ -522,13 +526,12 @@ def tile_mixturedenserandomsynthesizer_t_kernel(tc, x_bytes, x_scale, w, rnd, mi
             else:
                 score_turned(s + 3, 3)
             mix_out_of_psum(s + 1, 1)
-            v_product(2 * s + 2)
-            mix_out_of_psum(s + 1, 0)
-            v_product(2 * s + 3)
-            logit_out(s + 1, 1)
             x_turn(s + 4)
+            mix_out_of_psum(s + 1, 0)
+            v_product(2 * s + 2)
+            logit_out(s + 1, 1)
+            v_product(2 * s + 3)
             logit_out(s + 1, 0)
-            blend(s + 2, 0, 1)
             if live(s - 3):
                 store(s - 3, 1)
                 if s % 2 == 0:
@@ -538,18 +541,19 @@ def tile_mixturedenserandomsynthesizer_t_kernel(tc, x_bytes, x_scale, w, rnd, mi
             if live(s - 2):
                 turn_out(s - 2, 0)
                 turn_out(s - 2, 1)
-            maximum(s + 1, SECOND)
-            v_gain(2 * s + 3)
             score_turned(s + 3, 2)
             if live(s - 3):
                 score_turned(s + 3, 3)
-            blend(s + 2, 1, 1)
-            turn(s - 1, 1)
-            v_gain(2 * s + 2)
+            blend(s + 2, 0, 1)
             x_scale_out(s + 4)
             if live(s - 3) and s % 2 == 0:
                 store(s - 3, 0, by_vector, slice(0, VECTOR_COLUMNS))
+            turn(s - 1, 1)
+            blend(s + 2, 1, 1)
             turn(s - 1, 0)
+            v_gain(2 * s + 3)
+            maximum(s + 1)
+            v_gain(2 * s + 2)
             if s == 1:
                 for q in (8, 9, 10):
                     x_widen(q)
@@ -557,7 +561,6 @@ def tile_mixturedenserandomsynthesizer_t_kernel(tc, x_bytes, x_scale, w, rnd, mi
                 x_widen(10 + s // 2)
             score(s + 2, 0)
             score(s + 2, 1)
-            maximum(s + 1, FIRST)
             for n in (3, 2) if live(s - 3) else (2, 3):
                 score_out(s + 3, n)
 
@@ -672,8 +675,9 @@ def tile_mixturedenserandomsynthesizer_t_kernel(tc, x_bytes, x_scale, w, rnd, mi
             s = 12
             exponent(s, 1)
             exponent(s, 0)
+            p_quantize(s - 3)
             invert(s - 1)
-            quantize_words(s, slice(0, WORDS))
+            quantize_words(s, slice(X_WORDS.start, WORDS))
             divide(s - 1, 0)
             divide_by_scalar(s - 1, 1)
             gain(s)

@@ -6,13 +6,11 @@ from concourse.masks import make_identity
 B, S, D = 4, 1024, 512
 P = 128
 PACK = 4
-HALF = P * PACK
-HALVES = S // HALF
+HALVES = S // (P * PACK)
 PAIRS = S // (2 * P)
 N_PAIRS = B * PAIRS
 BANK = 512
 QUARTERS = D // P
-N_QUARTERS = B * HALVES * QUARTERS
 
 F32 = mybir.dt.float32
 BF16 = mybir.dt.bfloat16
@@ -28,13 +26,17 @@ FLOPS = 2 * B * S * D * S + 2 * B * S * D * D + 2 * B * S * S * D
 
 BOTH, FIRST, SECOND = slice(0, 2), slice(0, 1), slice(1, 2)
 ROW = BANK + 8
+RING = 4
 LAG = 3
 P_WORDS, X_WORDS, V_WORDS = slice(0, 4 * P), slice(4 * P, 6 * P), slice(6 * P, 8 * P)
 WORDS = 8 * P
 VECTOR_COLUMNS = 192
 SCALAR_KEYS = 256
-RING = 4
+WIDE_AHEAD = (8, 9, 10)
+WIDE_BUFS = 7
+CODE_BUFS = 8
 FIRST_TILEWISE_PAIR = N_PAIRS - 5
+LAST_FULL_STEP = N_PAIRS - 5
 
 
 def tile_mixturedenserandomsynthesizer_t_kernel(tc, x_bytes, x_scale, w, rnd, mix, wv, c, u, out):
@@ -70,8 +72,14 @@ def tile_mixturedenserandomsynthesizer_t_kernel(tc, x_bytes, x_scale, w, rnd, mi
         wv_raw = keep.tile([P, PACK, D], BF16, name="wv_raw")
 
         def load_x(b, h):
-            x_raw[(b, h)] = keep.tile([P, PACK, D], U8, name="x_raw%d%d" % (b, h), align_bytes=64)
-            nc.sync.dma_start(out=x_raw.get((b, h))[:], in_=x_rows[b, h])
+            tile = keep.tile([P, PACK, D], U8, name="x_raw%d%d" % (b, h), align_bytes=64)
+            nc.sync.dma_start(out=tile[:], in_=x_rows[b, h])
+            for i in range(2):
+                x_raw[PAIRS * b + 2 * h + i] = tile[:, 2 * i : 2 * i + 2]
+
+        def load_x_pair(q):
+            x_raw[q] = keep.tile([P, 2, D], U8, name="x_pair%d" % q, align_bytes=64)[:]
+            nc.sync.dma_start(out=x_raw[q], in_=x_rows[0, 0, :, 2 * q : 2 * q + 2])
 
         def load_w(g):
             w_raw[g] = keep.tile([P, PACK, BANK], BF16, name="w_raw%d" % g)
@@ -81,7 +89,8 @@ def tile_mixturedenserandomsynthesizer_t_kernel(tc, x_bytes, x_scale, w, rnd, mi
             rnd_raw[k] = keep.tile([P, 2, S], BF16, name="rnd_raw%d" % k)
             nc.sync.dma_start(out=rnd_raw[k][:], in_=rnd_rows[k // 2, :, 2 * (k % 2) : 2 * (k % 2) + 2])
 
-        load_x(0, 0)
+        load_x_pair(0)
+        load_x_pair(1)
         load_w(0)
         nc.sync.dma_start(out=scale_4[:], in_=x_scale.rearrange("a b (p t) -> p (a b t)", t=PACK))
         nc.sync.dma_start(out=mix_raw[:], in_=mix.rearrange("(p o) -> p o", o=1))
@@ -102,6 +111,8 @@ def tile_mixturedenserandomsynthesizer_t_kernel(tc, x_bytes, x_scale, w, rnd, mi
 
         ident = keep.tile([P, P], F32, name="ident")
         make_identity(nc, ident[:])
+        ident_bf = keep.tile([P, P], BF16, name="ident_bf")
+        make_identity(nc, ident_bf[:])
         mix_column = keep.tile([P, 1], F32, name="mix_column")
         nc.vector.memset(mix_column[:], 0.0)
         mix_f = keep.tile([P, 1], F32, name="mix_f")
@@ -110,7 +121,6 @@ def tile_mixturedenserandomsynthesizer_t_kernel(tc, x_bytes, x_scale, w, rnd, mi
         for k in range(PAIRS - 1):
             rnd_f.append(keep.tile([P, 2, BANK], F32, name="rnd_f%d" % k))
         u_f = keep.tile([P, HALVES, PACK], F32, name="u_f")
-        c_4 = keep.tile([P, HALVES * PACK], F32, name="c_4")
         c_f = keep.tile([P, S], F32, name="c_f")
         mix_diag = keep.tile([P, P], BF16, name="mix_diag")
         w_grouped, w_codes, w_scales = [], [], []
@@ -144,26 +154,24 @@ def tile_mixturedenserandomsynthesizer_t_kernel(tc, x_bytes, x_scale, w, rnd, mi
         def column_split(ap):
             return ap.rearrange("p (h m e) -> p h m e", h=2, e=2)
 
-        def spread(columns, key):
-            bank = take_bank("scalar", key)
-            for t in range(PACK):
-                nc.tensor.transpose(bank[:, t, :], columns[:, t : t + 1].to_broadcast([P, P]), ident[:])
-
         def mix_spread():
             bank = take_bank("scalar", "mix")
             nc.tensor.transpose(bank[:, 0, :], mix_column[:].to_broadcast([P, P]), ident[:])
 
         def mix_out():
             bank = give_bank("mix")
+            nc.vector.tensor_scalar(out=mix_diag[:], in0=ident[:], scalar1=bank[:, 0, 1:2], scalar2=None, op0=Alu.mult)
             nc.vector.tensor_copy(out=mix_f[:], in_=bank[:, 0, 0:1])
             nc.vector.tensor_scalar(out=mix_negated[:], in0=bank[:, 0, 0:2], scalar1=-1.0, scalar2=None, op0=Alu.mult)
-            nc.vector.tensor_scalar(out=mix_diag[:], in0=ident[:], scalar1=bank[:, 0, 1:2], scalar2=None, op0=Alu.mult)
 
         def c_spread(g):
-            spread(c_4[:, g * PACK : (g + 1) * PACK], ("c", g))
+            bank = take_bank("scalar", ("c", g))
+            for t in range(PACK):
+                column = c_raw[:, g, t : t + 1].to_broadcast([P, P])
+                nc.tensor.matmul(bank[:, t, :], lhsT=column, rhs=ident_bf[:], start=True, stop=True)
 
-        def c_out(g, copy):
-            copy(
+        def c_out(g):
+            nc.scalar.copy(
                 out=column_split(c_f[:, g * BANK : (g + 1) * BANK]),
                 in_=give_bank(("c", g))[:].rearrange("p (h e) m -> p h m e", h=2),
             )
@@ -215,8 +223,8 @@ def tile_mixturedenserandomsynthesizer_t_kernel(tc, x_bytes, x_scale, w, rnd, mi
 
         def quantize_words(s, words):
             if s not in codes:
-                codes[s] = work.tile([P, WORDS], U32, name="codes", bufs=8, align_bytes=64)
-                scales[s] = work.tile([P, WORDS], U8, name="scales", bufs=8, align_bytes=64)
+                codes[s] = work.tile([P, WORDS], U32, name="codes", bufs=CODE_BUFS, align_bytes=64)
+                scales[s] = work.tile([P, WORDS], U8, name="scales", bufs=CODE_BUFS, align_bytes=64)
             quantize(codes[s][:, words], scales[s][:, words], grouped[s][:, words].rearrange("p n t -> p (n t)"))
 
         def x_operand(q, rows=slice(0, 2 * P)):
@@ -226,11 +234,8 @@ def tile_mixturedenserandomsynthesizer_t_kernel(tc, x_bytes, x_scale, w, rnd, mi
         x_wide = {}
 
         def x_widen(q):
-            b, h, t = q // PAIRS, (q % PAIRS) // 2, 2 * (q % 2)
-            x_wide[q] = work.tile([P, 2 * D], BF16, name="wide", bufs=7)
-            nc.scalar.copy(
-                out=x_wide[q][:], in_=x_raw.get((b, h))[:, t : t + 2, :].rearrange("p t k -> p (t k)").bitcast(FP8)
-            )
+            x_wide[q] = work.tile([P, 2 * D], BF16, name="wide", bufs=WIDE_BUFS)
+            nc.scalar.copy(out=x_wide[q][:], in_=x_raw[q].rearrange("p t k -> p (t k)").bitcast(FP8))
 
         def x_turn(q, tiles=BOTH):
             words = x_wide[q][:].bitcast(F32)
@@ -460,13 +465,11 @@ def tile_mixturedenserandomsynthesizer_t_kernel(tc, x_bytes, x_scale, w, rnd, mi
                 for n in range(2):
                     product_pass(bank[:, n * D // 2 : (n + 1) * D // 2], q, j, g, n, g + n == 0, g + n == 2)
 
-        last_sums = {}
-
         def last_product(g):
             for n, ring in enumerate(("vector", "scalar")):
                 if g == 0:
-                    last_sums[n] = take_bank(ring, ("last", n), (P, D // 2))
-                product_pass(last_sums[n][:], N_PAIRS - 1, 1, g, n, g == 0, g == HALVES - 1)
+                    take_bank(ring, ("last", n), (P, D // 2))
+                product_pass(held.get(("last", n))[2][:], N_PAIRS - 1, 1, g, n, g == 0, g == HALVES - 1)
 
         def last_store(n, copy):
             d_cols = slice(n * D // 2, (n + 1) * D // 2)
@@ -496,18 +499,16 @@ def tile_mixturedenserandomsynthesizer_t_kernel(tc, x_bytes, x_scale, w, rnd, mi
 
         by_scalar, by_vector = nc.scalar.copy, nc.vector.tensor_copy
 
-        def live(q):
-            return 0 <= q < N_PAIRS
-
         def step(s):
+            stored = s - LAG
             exponent(s, 1)
             exponent(s, 0)
             if s == 1:
                 v_quantize(0)
             elif s == 2:
-                x_quantize(5)
+                x_quantize(s + LAG)
             else:
-                p_quantize(s - 3)
+                p_quantize(stored)
             invert(s - 1)
             quantize_words(s, V_WORDS if s == 2 else slice(X_WORDS.start, WORDS))
             if s % 2 == 1:
@@ -520,11 +521,12 @@ def tile_mixturedenserandomsynthesizer_t_kernel(tc, x_bytes, x_scale, w, rnd, mi
                 score_out(3, 3)
                 score_out(3, 2)
             gain(s)
-            if live(s - 3):
-                product(s - 3, 0)
-                product(s - 3, 1)
+            if stored >= 0:
+                product(stored, 0)
+                product(stored, 1)
             else:
                 score_turned(s + 3, 3)
+                score_turned(s + 3, 2)
             mix_out_of_psum(s + 1, 1)
             x_turn(s + 4)
             mix_out_of_psum(s + 1, 0)
@@ -532,22 +534,22 @@ def tile_mixturedenserandomsynthesizer_t_kernel(tc, x_bytes, x_scale, w, rnd, mi
             logit_out(s + 1, 1)
             v_product(2 * s + 3)
             logit_out(s + 1, 0)
-            if live(s - 3):
-                store(s - 3, 1)
+            if stored >= 0:
+                store(stored, 1)
                 if s % 2 == 0:
-                    store_part(s - 3, 0, slice(VECTOR_COLUMNS, D))
+                    store_part(stored, 0, slice(VECTOR_COLUMNS, D))
                 else:
-                    store(s - 3, 0)
-            if live(s - 2):
+                    store(stored, 0)
+            if s >= 2:
                 turn_out(s - 2, 0)
                 turn_out(s - 2, 1)
-            score_turned(s + 3, 2)
-            if live(s - 3):
+            if stored >= 0:
+                score_turned(s + 3, 2)
                 score_turned(s + 3, 3)
             blend(s + 2, 0, 1)
             x_scale_out(s + 4)
-            if live(s - 3) and s % 2 == 0:
-                store(s - 3, 0, by_vector, slice(0, VECTOR_COLUMNS))
+            if stored >= 0 and s % 2 == 0:
+                store(stored, 0, by_vector, slice(0, VECTOR_COLUMNS))
             turn(s - 1, 1)
             blend(s + 2, 1, 1)
             turn(s - 1, 0)
@@ -555,13 +557,13 @@ def tile_mixturedenserandomsynthesizer_t_kernel(tc, x_bytes, x_scale, w, rnd, mi
             maximum(s + 1)
             v_gain(2 * s + 2)
             if s == 1:
-                for q in (8, 9, 10):
+                for q in WIDE_AHEAD:
                     x_widen(q)
             elif s % 2 == 0:
-                x_widen(10 + s // 2)
+                x_widen(WIDE_AHEAD[-1] + s // 2)
             score(s + 2, 0)
             score(s + 2, 1)
-            for n in (3, 2) if live(s - 3) else (2, 3):
+            for n in (3, 2) if stored >= 0 else (2, 3):
                 score_out(s + 3, n)
 
         with tc.manual_schedule():
@@ -578,7 +580,6 @@ def tile_mixturedenserandomsynthesizer_t_kernel(tc, x_bytes, x_scale, w, rnd, mi
             x_scale_out(0, FIRST)
             x_scale_out(0, SECOND)
             by_vector(out=mix_column[0:2], in_=mix_raw[:])
-            by_vector(out=c_4[:], in_=c_raw[:].rearrange("p g t -> p (g t)"))
             mix_spread()
             c_spread(0)
             w_quantize(0)
@@ -605,7 +606,7 @@ def tile_mixturedenserandomsynthesizer_t_kernel(tc, x_bytes, x_scale, w, rnd, mi
             x_turn(2)
             score_turned(1, 0)
             mix_out_of_psum(0, 1)
-            c_out(0, by_scalar)
+            c_out(0)
             score_out(0, 2)
             score_out(0, 3)
             score_turned(1, 1)
@@ -623,7 +624,7 @@ def tile_mixturedenserandomsynthesizer_t_kernel(tc, x_bytes, x_scale, w, rnd, mi
             score_out(1, 1)
             score_out(1, 2)
             score_out(1, 3)
-            c_out(1, by_scalar)
+            c_out(1)
             blend(1, 0, 0)
             blend(1, 1, 0)
             logit_out(0, 0, 1, True)
@@ -637,10 +638,10 @@ def tile_mixturedenserandomsynthesizer_t_kernel(tc, x_bytes, x_scale, w, rnd, mi
             exponent(0, 0)
             exponent(0, 1)
             gain(0)
-            v_product(0)
-            v_product(1)
             score_turned(2, 2)
             score_turned(2, 3)
+            v_product(0)
+            v_product(1)
             x_widen(4)
             x_widen(5)
             logit_out(1, 0, 0)
@@ -669,13 +670,13 @@ def tile_mixturedenserandomsynthesizer_t_kernel(tc, x_bytes, x_scale, w, rnd, mi
             score_turned(3, 2)
             score_turned(3, 3)
 
-            for s in range(1, N_PAIRS - 4):
+            for s in range(1, LAST_FULL_STEP + 1):
                 step(s)
 
-            s = 12
+            s = LAST_FULL_STEP + 1
             exponent(s, 1)
             exponent(s, 0)
-            p_quantize(s - 3)
+            p_quantize(s - LAG)
             invert(s - 1)
             quantize_words(s, slice(X_WORDS.start, WORDS))
             divide(s - 1, 0)
@@ -684,41 +685,41 @@ def tile_mixturedenserandomsynthesizer_t_kernel(tc, x_bytes, x_scale, w, rnd, mi
             product(s - 3, 0)
             product(s - 3, 1)
             mix_out_of_psum(s + 1, 1)
-            v_product(26)
+            v_product(2 * s + 2)
             mix_out_of_psum(s + 1, 0)
-            v_product(27)
+            v_product(2 * s + 3)
             logit_out(s + 1, 1)
-            v_product(28)
+            v_product(2 * s + 4)
             logit_out(s + 1, 0)
-            v_product(29)
+            v_product(2 * s + 5)
             store(s - 3, 1)
             store(s - 3, 0)
             turn_out(s - 2, 0)
             turn_out(s - 2, 1)
             maximum(s + 1, SECOND)
-            v_gain(27)
+            v_gain(2 * s + 3)
             score_turned(s + 3, 2)
             score_turned(s + 3, 3)
             blend(s + 2, 0, 1)
-            v_gain(26)
+            v_gain(2 * s + 2)
             turn(s - 1, 1)
             blend(s + 2, 1, 1)
             turn(s - 1, 0)
-            v_gain(29)
+            v_gain(2 * s + 5)
             score(s + 2, 0)
-            v_gain(28)
+            v_gain(2 * s + 4)
             score(s + 2, 1)
             maximum(s + 1, FIRST)
             score_out(s + 3, 3)
             score_out(s + 3, 2)
 
-            s = 13
+            s += 1
             exponent(s, 1)
             exponent(s, 0)
-            v_quantize(13)
-            v_quantize(14)
+            v_quantize(s)
+            v_quantize(s + 1)
             invert(s - 1)
-            p_quantize(s - 3)
+            p_quantize(s - LAG)
             divide(s - 1, 0, slice(0, BANK))
             divide_by_scalar(s - 1, 1)
             divide_by_scalar(s - 1, 0, slice(BANK, S))
@@ -726,9 +727,9 @@ def tile_mixturedenserandomsynthesizer_t_kernel(tc, x_bytes, x_scale, w, rnd, mi
             product(s - 3, 0)
             product(s - 3, 1)
             mix_out_of_psum(s + 1, 1)
-            v_product(30)
+            v_product(2 * s + 4)
             mix_out_of_psum(s + 1, 0)
-            v_product(31)
+            v_product(2 * s + 5)
             logit_out(s + 1, 1)
             turn_out(s - 2, 0)
             turn_out(s - 2, 1)
@@ -737,21 +738,21 @@ def tile_mixturedenserandomsynthesizer_t_kernel(tc, x_bytes, x_scale, w, rnd, mi
             turn(s - 1, 1)
             blend(s + 2, 1, 1)
             turn(s - 1, 0)
-            v_gain(31)
+            v_gain(2 * s + 5)
             score(s + 2, 0)
             maximum(s + 1)
-            v_gain(30)
+            v_gain(2 * s + 4)
             score(s + 2, 1)
             store(s - 3, 1)
             turn_out(s - 1, 1)
             turn_out(s - 1, 0)
             store(s - 3, 0, by_vector)
 
-            s = 14
+            s += 1
             exponent(s, 1)
             exponent(s, 0)
-            p_quantize(s - 3)
-            v_quantize(15)
+            p_quantize(s - LAG)
+            v_quantize(s + 1)
             invert(s - 1)
             p_quantize(s - 2)
             divide(s - 1, 0)
@@ -778,7 +779,7 @@ def tile_mixturedenserandomsynthesizer_t_kernel(tc, x_bytes, x_scale, w, rnd, mi
             divide(s, 0, slice(0, S), nc.vector)
             product(s - 1, 0, "vector")
 
-            s = 15
+            s += 1
             exponent(s, 0)
             exponent(s, 1)
             divide_and_gain(s - 1, 1, 0)

from contextlib import ExitStack

import concourse.mybir as mybir
from concourse.masks import make_identity

B, S, D = 4, 1024, 512
P = 128
PACK = 4
HALVES = S // (P * PACK)
PAIRS = S // (2 * P)
N_PAIRS = B * PAIRS
BANK = 512
QUARTERS = D // P

F32 = mybir.dt.float32
BF16 = mybir.dt.bfloat16
U32 = mybir.dt.uint32
U8 = mybir.dt.uint8
FP8 = mybir.dt.float8_e4m3fn
FP8X4 = mybir.dt.float8_e4m3fn_x4
Alu = mybir.AluOpType
Act = mybir.ActivationFunctionType
AX = mybir.AxisListType

FLOPS = 2 * B * S * D * S + 2 * B * S * D * D + 2 * B * S * S * D

BOTH, FIRST, SECOND = slice(0, 2), slice(0, 1), slice(1, 2)
ROW = BANK + 8
RING = 4
LAG = 3
P_WORDS, X_WORDS, V_WORDS = slice(0, 4 * P), slice(4 * P, 6 * P), slice(6 * P, 8 * P)
WORDS = 8 * P
VECTOR_COLUMNS = 192
SCALAR_KEYS = 256
WIDE_AHEAD = (8, 9, 10)
WIDE_BUFS = 7
CODE_BUFS = 8
FIRST_TILEWISE_PAIR = N_PAIRS - 5
LAST_FULL_STEP = N_PAIRS - 5


def tile_mixturedenserandomsynthesizer_t_kernel(tc, x_bytes, x_scale, w, rnd, mix, wv, c, u, out):
    nc = tc.nc
    with ExitStack() as ctx:
        keep = ctx.enter_context(tc.tile_pool(name="keep", bufs=1))
        work = ctx.enter_context(tc.tile_pool(name="work", bufs=2))
        psum = ctx.enter_context(tc.psum_pool(name="psum", bufs=1))

        free_banks = {"vector": list(range(RING)), "scalar": list(range(RING, 2 * RING))}
        held = {}

        def take_bank(ring, key, shape=(P, PACK, P)):
            k = free_banks[ring][0]
            free_banks[ring].remove(k)
            held[key] = (ring, k, psum.tile(list(shape), F32, name="bank%d" % k))
            return held.get(key)[2]

        def give_bank(key):
            ring, k, bank = held.get(key)
            free_banks[ring].append(k)
            return bank

        scale_4 = keep.tile([P, PACK], F32, name="scale_4")
        mix_raw = keep.tile([2, 1], BF16, name="mix_raw")
        c_raw = keep.tile([P, HALVES, PACK], BF16, name="c_raw")
        u_raw = keep.tile([P, HALVES, PACK], BF16, name="u_raw")

        x_rows = x_bytes.rearrange("b (h m t) k -> b h m t k", m=P, t=PACK)
        rnd_rows = rnd.rearrange("(h m t) k -> h m t k", m=P, t=PACK)
        w_rows = w.rearrange("(p j) n -> p j n", j=PACK)
        x_raw, rnd_raw, w_raw = {}, {}, {}
        wv_raw = keep.tile([P, PACK, D], BF16, name="wv_raw")

        def load_x(b, h):
            tile = keep.tile([P, PACK, D], U8, name="x_raw%d%d" % (b, h), align_bytes=64)
            nc.sync.dma_start(out=tile[:], in_=x_rows[b, h])
            for i in range(2):
                x_raw[PAIRS * b + 2 * h + i] = tile[:, 2 * i : 2 * i + 2]

        def load_x_pair(q):
            x_raw[q] = keep.tile([P, 2, D], U8, name="x_pair%d" % q, align_bytes=64)[:]
            nc.sync.dma_start(out=x_raw[q], in_=x_rows[0, 0, :, 2 * q : 2 * q + 2])

        def load_w(g):
            w_raw[g] = keep.tile([P, PACK, BANK], BF16, name="w_raw%d" % g)
            nc.sync.dma_start(out=w_raw[g][:], in_=w_rows[:, :, g * BANK : (g + 1) * BANK])

        def load_rnd(k):
            rnd_raw[k] = keep.tile([P, 2, S], BF16, name="rnd_raw%d" % k)
            nc.sync.dma_start(out=rnd_raw[k][:], in_=rnd_rows[k // 2, :, 2 * (k % 2) : 2 * (k % 2) + 2])

        load_x_pair(0)
        load_x_pair(1)
        load_w(0)
        nc.sync.dma_start(out=scale_4[:], in_=x_scale.rearrange("a b (p t) -> p (a b t)", t=PACK))
        nc.sync.dma_start(out=mix_raw[:], in_=mix.rearrange("(p o) -> p o", o=1))
        nc.sync.dma_start(out=c_raw[:], in_=c.rearrange("(g p t) -> p g t", p=P, t=PACK))
        load_w(1)
        load_x(0, 1)
        load_rnd(0)
        nc.sync.dma_start(out=wv_raw[:], in_=wv.rearrange("(p j) n -> p j n", j=PACK))
        nc.sync.dma_start(out=u_raw[:], in_=u.rearrange("(h p t) -> p h t", p=P, t=PACK))
        load_rnd(1)
        load_x(1, 0)
        load_rnd(2)
        load_rnd(3)
        load_x(1, 1)
        for b in range(2, B):
            for h in range(HALVES):
                load_x(b, h)

        ident = keep.tile([P, P], F32, name="ident")
        make_identity(nc, ident[:])
        ident_bf = keep.tile([P, P], BF16, name="ident_bf")
        make_identity(nc, ident_bf[:])
        mix_column = keep.tile([P, 1], F32, name="mix_column")
        nc.vector.memset(mix_column[:], 0.0)
        mix_f = keep.tile([P, 1], F32, name="mix_f")
        mix_negated = keep.tile([P, 2], F32, name="mix_negated")
        rnd_f = []
        for k in range(PAIRS - 1):
            rnd_f.append(keep.tile([P, 2, BANK], F32, name="rnd_f%d" % k))
        u_f = keep.tile([P, HALVES, PACK], F32, name="u_f")
        c_f = keep.tile([P, S], F32, name="c_f")
        mix_diag = keep.tile([P, P], BF16, name="mix_diag")
        w_grouped, w_codes, w_scales = [], [], []
        for g in range(HALVES):
            w_grouped.append(keep.tile([P, BANK, PACK], BF16, name="rnd_f3" if g else "gained0", align_bytes=64))
            w_codes.append(keep.tile([P, BANK], U32, name="w_codes%d" % g, align_bytes=64))
            w_scales.append(keep.tile([P, BANK], U8, name="w_scales%d" % g, align_bytes=64))
        wv_grouped = []
        wv_codes = keep.tile([P, D], U32, name="wv_codes", align_bytes=64)
        wv_scales = keep.tile([P, D], U8, name="wv_scales", align_bytes=64)

        out_rows = out.rearrange("b (h m t) d -> b h m t d", m=P, t=PACK)

        def quantize(codes, scales, grouped):
            nc.vector.quantize_mx(out=codes.bitcast(FP8X4), scales=scales, in_=grouped)

        def multiply(sums, lhs_codes, lhs_scales, rhs_codes, rhs_scales, start, stop):
            nc.tensor.matmul_mx(
                out=sums,
                lhsT=lhs_codes.bitcast(FP8X4),
                lhsT_scale=lhs_scales,
                rhs=rhs_codes.bitcast(FP8X4),
                rhs_scale=rhs_scales,
                start=start,
                stop=stop,
            )

        def key_split(ap):
            return ap.rearrange("p (m h e) -> p h m e", h=2, e=2)

        def column_split(ap):
            return ap.rearrange("p (h m e) -> p h m e", h=2, e=2)

        def mix_spread():
            bank = take_bank("scalar", "mix")
            nc.tensor.transpose(bank[:, 0, :], mix_column[:].to_broadcast([P, P]), ident[:])

        def mix_out():
            bank = give_bank("mix")
            nc.vector.tensor_scalar(out=mix_diag[:], in0=ident[:], scalar1=bank[:, 0, 1:2], scalar2=None, op0=Alu.mult)
            nc.vector.tensor_copy(out=mix_f[:], in_=bank[:, 0, 0:1])
            nc.vector.tensor_scalar(out=mix_negated[:], in0=bank[:, 0, 0:2], scalar1=-1.0, scalar2=None, op0=Alu.mult)

        def c_spread(g):
            bank = take_bank("scalar", ("c", g))
            for t in range(PACK):
                column = c_raw[:, g, t : t + 1].to_broadcast([P, P])
                nc.tensor.matmul(bank[:, t, :], lhsT=column, rhs=ident_bf[:], start=True, stop=True)

        def c_out(g):
            nc.scalar.copy(
                out=column_split(c_f[:, g * BANK : (g + 1) * BANK]),
                in_=give_bank(("c", g))[:].rearrange("p (h e) m -> p h m e", h=2),
            )

        def copy_by_gpsimd(out, in_):
            nc.gpsimd.tensor_scalar(out=out, in0=in_, scalar1=1.0, scalar2=0.0, op0=Alu.mult, op1=Alu.add)

        def w_group(g, h, copy):
            src = w_raw[g][:].rearrange("p j (m h e) -> p h m e j", h=2, e=2)
            dst = w_grouped[g][:].rearrange("p (h m e) j -> p h m e j", h=2, e=2)
            copy(out=dst[:, h], in_=src[:, h])

        def w_quantize(g):
            quantize(w_codes[g][:], w_scales[g][:], w_grouped[g][:].rearrange("p n j -> p (n j)"))

        def wv_group():
            wv_grouped.append(keep.tile([P, D, PACK], BF16, name="rnd_f3", align_bytes=64))
            copy_by_gpsimd(wv_grouped[0][:], wv_raw[:].rearrange("p j n -> p n j"))

        def wv_quantize():
            quantize(wv_codes[:], wv_scales[:], wv_grouped[0][:].rearrange("p n j -> p (n j)"))

        def rnd_scale(k, j):
            nc.scalar.activation(
                out=column_split(rnd_f[k][:, j]),
                in_=key_split(rnd_raw[k][:, j, 0:BANK]),
                func=Act.Copy,
                scale=mix_negated[:, 1:2],
            )

        def rnd_scale_by_gpsimd(k, j):
            if k == len(rnd_f):
                rnd_f.append(keep.tile([P, 2, BANK], F32, name="rnd_f3", align_bytes=64))
            nc.gpsimd.tensor_scalar(
                out=column_split(rnd_f[k][:, j]),
                in0=key_split(rnd_raw[k][:, j, 0:BANK]),
                scalar1=mix_negated[:, 1:2],
                scalar2=0.0,
                op0=Alu.mult,
                op1=Alu.add,
            )

        grouped, codes, scales = {}, {}, {}

        def grouped_tile(s):
            if s not in grouped:
                grouped[s] = work.tile([P, WORDS, PACK], BF16, name="grouped", align_bytes=64)
            return grouped[s]

        def quantize_words(s, words):
            if s not in codes:
                codes[s] = work.tile([P, WORDS], U32, name="codes", bufs=CODE_BUFS, align_bytes=64)
                scales[s] = work.tile([P, WORDS], U8, name="scales", bufs=CODE_BUFS, align_bytes=64)
            quantize(codes[s][:, words], scales[s][:, words], grouped[s][:, words].rearrange("p n t -> p (n t)"))

        def x_operand(q, rows=slice(0, 2 * P)):
            words = slice(X_WORDS.start + rows.start, X_WORDS.start + rows.stop)
            return codes[q - LAG][:, words], scales[q - LAG][:, words]

        x_wide = {}

        def x_widen(q):
            x_wide[q] = work.tile([P, 2 * D], BF16, name="wide", bufs=WIDE_BUFS)
            nc.scalar.copy(out=x_wide[q][:], in_=x_raw[q].rearrange("p t k -> p (t k)").bitcast(FP8))

        def x_turn(q, tiles=BOTH):
            words = x_wide[q][:].bitcast(F32)
            bank = take_bank("vector", ("x", q, tiles.start))
            for j in range(tiles.start, tiles.stop):
                for h in range(2):
                    nc.tensor.transpose(bank[:, 2 * h + j, :], words[:, 2 * P * j + h : 2 * P * (j + 1) : 2], ident[:])

        def x_scale_out(q, tiles=BOTH):
            bank = give_bank(("x", q, tiles.start))
            values = bank[:].rearrange("p n q -> p (n q)").bitcast(BF16).rearrange("p (h q e) -> p q h e", h=2, e=2)
            tokens = slice(tiles.start * P, tiles.stop * P)
            count = tokens.stop - tokens.start
            nc.vector.tensor_tensor(
                out=grouped_tile(q - LAG)[:, X_WORDS].rearrange("p q (h e) -> p q h e", e=2)[:, tokens],
                in0=values[:, tokens],
                in1=scale_4[:].rearrange("p (o h e) -> p o h e", o=1, e=2).to_broadcast([P, count, 2, 2]),
                op=Alu.mult,
            )

        def x_quantize(q):
            quantize_words(q - LAG, X_WORDS)

        def v_product(n):
            sums = take_bank("vector", ("v", n))
            hh, i = divmod(n, QUARTERS)
            d_cols = slice(i * P, (i + 1) * P)
            for t in range(PACK):
                x_codes, x_scales = x_operand(2 * hh + t // 2, slice((t % 2) * P, (t % 2 + 1) * P))
                multiply(sums[:, t, :], x_codes, x_scales, wv_codes[:, d_cols], wv_scales[:, d_cols], True, True)

        def v_gain(n):
            h = n // QUARTERS % HALVES
            first = V_WORDS.start + n % 2 * P
            nc.vector.tensor_tensor(
                out=grouped_tile(n // 2)[:, first : first + P, :],
                in0=give_bank(("v", n))[:].rearrange("p t d -> p d t"),
                in1=u_f[:, h : h + 1, :].to_broadcast([P, P, PACK]),
                op=Alu.mult,
            )

        def v_quantize(s):
            quantize_words(s, V_WORDS)

        mixed_scores = {}
        logits, maxima, exps, totals, inverses = {}, {}, {}, {}, {}
        gained, pcs, rows_out = {}, {}, {}

        def score_turned(q, n):
            bank = take_bank("scalar", ("score", q, n), (P, 2, 2 * P))
            for i in range(2):
                keys = slice((2 * (n % 2) + i) * P, (2 * (n % 2) + i + 1) * P)
                multiply(
                    bank[:, i, :], w_codes[n // 2][:, keys], w_scales[n // 2][:, keys],
                    *x_operand(q), True, True,
                )

        def score_out(q, n):
            if (q, n // 2) not in mixed_scores:
                mixed_scores[(q, n // 2)] = work.tile([P, PACK, 2 * P], F32, name="mixed_scores%d" % (n // 2))
            nc.scalar.activation(
                out=mixed_scores.get((q, n // 2))[:, 2 * (n % 2) : 2 * (n % 2) + 2],
                in_=give_bank(("score", q, n))[:],
                func=Act.Copy,
                scale=mix_f[:],
            )

        def blend_open(q, j, g):
            bank = take_bank("vector", ("logit", q, j, g), (P, BANK))
            nc.tensor.matmul(
                bank[:].rearrange("p (h m e) -> p m h e", h=2, e=2),
                lhsT=mix_diag[:],
                rhs=rnd_raw[q % PAIRS][:, j, g * BANK : (g + 1) * BANK].rearrange("p (m h e) -> p m h e", h=2, e=2),
                start=True,
                stop=False,
            )

        def blend_close(q, j, g):
            for n in range(PACK):
                nc.tensor.matmul(
                    held.get(("logit", q, j, g))[2][:, n * P : (n + 1) * P],
                    lhsT=mixed_scores.get((q, g))[:, n, j * P : (j + 1) * P],
                    rhs=ident[:],
                    start=False,
                    stop=n == PACK - 1,
                    is_transpose=True,
                )

        def blend(q, j, g):
            blend_open(q, j, g)
            blend_close(q, j, g)

        def score(q, j):
            bank = take_bank("vector", ("score", q, j, 0), (P, BANK))
            multiply(bank[:], *x_operand(q, slice(j * P, (j + 1) * P)), w_codes[0][:], w_scales[0][:], True, True)

        def logit_tile(q):
            if q not in logits:
                logits[q] = work.tile([P, 2, 2, ROW], F32, name="logit")
                maxima[q] = work.tile([P, 2], F32, name="maximum")
            return logits[q]

        def mix_out_of_psum(q, j):
            nc.vector.scalar_tensor_tensor(
                out=logit_tile(q)[:, j, 0, 0:BANK],
                in0=give_bank(("score", q, j, 0))[:],
                scalar=mix_negated[:, 0:1],
                in1=rnd_f[q % PAIRS][:, j],
                op0=Alu.mult,
                op1=Alu.add,
            )

        def logit_out(q, j, g=1, last=False):
            least = logit_tile(q)[:, j, 0, BANK : BANK + 1]
            nc.vector.tensor_scalar(
                out=logit_tile(q)[:, j, g, 0:BANK],
                in0=give_bank(("logit", q, j, g))[:],
                scalar1=-1.0,
                scalar2=least if last else None,
                op0=Alu.mult,
                op1=Alu.min,
                accum_out=maxima[q][:, j : j + 1] if last else least,
            )

        def maximum(q, tiles=BOTH):
            nc.vector.tensor_reduce(
                out=maxima[q][:, tiles], in_=logits[q][:, tiles, 0, 0 : BANK + 1], axis=AX.X, op=Alu.min
            )

        def first_minimum(q, j):
            row = logits[q][:, j, 0]
            nc.vector.tensor_reduce(out=row[:, BANK : BANK + 1], in_=row[:, 0:BANK], axis=AX.X, op=Alu.min)

        def exponent(q, j):
            if q not in exps:
                exps[q] = work.tile([P, 2 * S], F32, name="exp")
                totals[q] = work.tile([P, 2], F32, name="total")
            nc.scalar.activation(
                out=exps[q][:, j * S : (j + 1) * S].rearrange("p (g k) -> p g k", g=HALVES),
                in_=logits[q][:, j, :, 0:BANK],
                func=Act.Exp,
                bias=maxima[q][:, j : j + 1],
                scale=-1.0,
                accum_out=totals[q][:, j : j + 1],
            )

        def invert(q, tiles=BOTH):
            if q not in inverses:
                inverses[q] = work.tile([P, 2], F32, name="inverse")
            nc.vector.reciprocal(out=inverses[q][:, tiles], in_=totals[q][:, tiles])

        def gain(q, tiles=BOTH):
            gained[q] = keep.tile([P, 2, S], F32, name="gained%d" % (q % 2), align_bytes=64)
            count = tiles.stop - tiles.start
            nc.gpsimd.tensor_tensor(
                out=gained[q][:, tiles],
                in0=exps[q][:].rearrange("p (j k) -> p j k", j=2)[:, tiles],
                in1=c_f[:].rearrange("p (o k) -> p o k", o=1).to_broadcast([P, count, S]),
                op=Alu.mult,
            )

        def pc_tile(q):
            if q not in pcs:
                pcs[q] = work.tile([P, 2 * S], BF16, name="pc")
            return pcs[q]

        def divide(q, j, keys=slice(0, S), engine=nc.gpsimd):
            engine.tensor_scalar(
                out=pc_tile(q)[:, j * S + keys.start : j * S + keys.stop],
                in0=gained[q][:, j, keys],
                scalar1=inverses[q][:, j : j + 1],
                scalar2=0.0,
                op0=Alu.mult,
                op1=Alu.add,
            )

        def divide_by_scalar(q, j, keys=slice(0, S)):
            nc.scalar.activation(
                out=pc_tile(q)[:, j * S + keys.start : j * S + keys.stop],
                in_=gained[q][:, j, keys],
                func=Act.Copy,
                scale=inverses[q][:, j : j + 1],
            )

        def divide_and_gain(q, j, g):
            columns = slice(j * S + g * BANK, j * S + (g + 1) * BANK)
            nc.vector.scalar_tensor_tensor(
                out=pc_tile(q)[:, columns],
                in0=exps[q][:, columns],
                scalar=inverses[q][:, j : j + 1],
                in1=c_f[:, g * BANK : (g + 1) * BANK],
                op0=Alu.mult,
                op1=Alu.mult,
            )

        def turn(q, j, halves=BOTH, ring="scalar"):
            words = pcs[q][:, j * S : (j + 1) * S].bitcast(F32)
            bank = take_bank(ring, ("pc", q, j, halves.start))
            for n in range(2 * halves.start, 2 * halves.stop):
                nc.tensor.transpose(bank[:, n, :], words[:, n * P : (n + 1) * P], ident[:])

        def turn_out(q, j, halves=BOTH):
            target = grouped_tile(q + LAG)[:, P_WORDS].rearrange("p (j g q) t -> p j g q t", j=2, g=HALVES)
            bank = give_bank(("pc", q, j, halves.start))
            nc.scalar.copy(
                out=target[:, j, halves].bitcast(F32),
                in_=bank[:, 2 * halves.start : 2 * halves.stop].rearrange("p (g h) q -> p g q h", h=2),
            )

        def p_quantize(q, tiles=BOTH):
            quantize_words(q + LAG, slice(tiles.start * HALVES * P, tiles.stop * HALVES * P))

        def quantize_half(q, j, g):
            quantize_words(q + LAG, slice((2 * j + g) * P, (2 * j + g + 1) * P))

        def product_pass(sums, q, j, g, n, start, stop):
            words = slice((2 * j + g) * P, (2 * j + g + 1) * P)
            s = 2 * (HALVES * (q // PAIRS) + g) + n
            multiply(
                sums, codes[q + LAG][:, words], scales[q + LAG][:, words],
                codes[s][:, V_WORDS], scales[s][:, V_WORDS], start, stop,
            )

        def product(q, j, ring="scalar"):
            bank = take_bank(ring, ("out", q, j), (P, D))
            for g in range(HALVES):
                for n in range(2):
                    product_pass(bank[:, n * D // 2 : (n + 1) * D // 2], q, j, g, n, g + n == 0, g + n == 2)

        def last_product(g):
            for n, ring in enumerate(("vector", "scalar")):
                if g == 0:
                    take_bank(ring, ("last", n), (P, D // 2))
                product_pass(held.get(("last", n))[2][:], N_PAIRS - 1, 1, g, n, g == 0, g == HALVES - 1)

        def last_store(n, copy):
            d_cols = slice(n * D // 2, (n + 1) * D // 2)
            copy(out=rows_out[N_PAIRS - 1][:, 1, d_cols], in_=give_bank(("last", n))[:])
            nc.sync.dma_start(
                out=out_rows[B - 1, HALVES - 1, :, PACK - 1, d_cols], in_=rows_out[N_PAIRS - 1][:, 1, d_cols]
            )

        stored_tiles = {}

        def rows_tile(q):
            if q not in rows_out:
                rows_out[q] = work.tile([P, 2, D], F32, name="rows_out", bufs=4)
            return rows_out[q]

        def store_part(q, j, cols):
            nc.scalar.copy(out=rows_tile(q)[:, j, cols], in_=held.get(("out", q, j))[2][:, cols])

        def store(q, j, copy=nc.scalar.copy, cols=slice(0, D)):
            b, h, t = q // PAIRS, (q % PAIRS) // 2, 2 * (q % 2)
            copy(out=rows_tile(q)[:, j, cols], in_=give_bank(("out", q, j))[:, cols])
            stored_tiles[q] = stored_tiles.get(q, 0) + 1
            if q >= FIRST_TILEWISE_PAIR:
                nc.sync.dma_start(out=out_rows[b, h, :, t + j], in_=rows_out[q][:, j])
            elif stored_tiles[q] == 2:
                nc.sync.dma_start(out=out_rows[b, h, :, t : t + 2], in_=rows_out[q][:])

        by_scalar, by_vector = nc.scalar.copy, nc.vector.tensor_copy

        def step(s):
            stored = s - LAG
            exponent(s, 1)
            exponent(s, 0)
            if s == 1:
                v_quantize(0)
            elif s == 2:
                x_quantize(s + LAG)
            else:
                p_quantize(stored)
            invert(s - 1)
            quantize_words(s, V_WORDS if s == 2 else slice(X_WORDS.start, WORDS))
            if s % 2 == 1:
                divide(s - 1, 0, slice(0, S - SCALAR_KEYS))
                divide_by_scalar(s - 1, 0, slice(S - SCALAR_KEYS, S))
            else:
                divide(s - 1, 0)
            divide_by_scalar(s - 1, 1)
            if s == 1:
                score_out(3, 3)
                score_out(3, 2)
            gain(s)
            if stored >= 0:
                product(stored, 0)
                product(stored, 1)
            else:
                score_turned(s + 3, 3)
                score_turned(s + 3, 2)
            mix_out_of_psum(s + 1, 1)
            x_turn(s + 4)
            mix_out_of_psum(s + 1, 0)
            v_product(2 * s + 2)
            logit_out(s + 1, 1)
            v_product(2 * s + 3)
            logit_out(s + 1, 0)
            if stored >= 0:
                store(stored, 1)
                if s % 2 == 0:
                    store_part(stored, 0, slice(VECTOR_COLUMNS, D))
                else:
                    store(stored, 0)
            if s >= 2:
                turn_out(s - 2, 0)
                turn_out(s - 2, 1)
            if stored >= 0:
                score_turned(s + 3, 2)
                score_turned(s + 3, 3)
            blend(s + 2, 0, 1)
            x_scale_out(s + 4)
            if stored >= 0 and s % 2 == 0:
                store(stored, 0, by_vector, slice(0, VECTOR_COLUMNS))
            turn(s - 1, 1)
            blend(s + 2, 1, 1)
            turn(s - 1, 0)
            v_gain(2 * s + 3)
            maximum(s + 1)
            v_gain(2 * s + 2)
            if s == 1:
                for q in WIDE_AHEAD:
                    x_widen(q)
            elif s % 2 == 0:
                x_widen(WIDE_AHEAD[-1] + s // 2)
            score(s + 2, 0)
            score(s + 2, 1)
            for n in (3, 2) if stored >= 0 else (2, 3):
                score_out(s + 3, n)

        with tc.manual_schedule():
            x_widen(0)
            x_turn(0, FIRST)
            x_turn(0, SECOND)
            x_widen(1)
            w_group(0, 0, copy_by_gpsimd)
            w_group(0, 1, by_scalar)
            x_turn(1)
            w_group(1, 0, by_scalar)
            w_group(1, 1, by_scalar)
            x_widen(2)
            x_scale_out(0, FIRST)
            x_scale_out(0, SECOND)
            by_vector(out=mix_column[0:2], in_=mix_raw[:])
            mix_spread()
            c_spread(0)
            w_quantize(0)
            x_quantize(0)
            mix_out()
            rnd_scale_by_gpsimd(0, 0)
            score(0, 0)
            score(0, 1)
            blend_open(0, 0, 1)
            x_scale_out(1)
            blend_open(0, 1, 1)
            w_quantize(1)
            x_quantize(1)
            wv_group()
            rnd_scale_by_gpsimd(1, 0)
            rnd_scale_by_gpsimd(1, 1)
            rnd_scale_by_gpsimd(2, 0)
            rnd_scale(0, 1)
            x_widen(3)
            by_scalar(out=u_f[:], in_=u_raw[:])
            score_turned(0, 2)
            score_turned(0, 3)
            mix_out_of_psum(0, 0)
            x_turn(2)
            score_turned(1, 0)
            mix_out_of_psum(0, 1)
            c_out(0)
            score_out(0, 2)
            score_out(0, 3)
            score_turned(1, 1)
            x_turn(3)
            blend_close(0, 0, 1)
            score_turned(1, 2)
            score_turned(1, 3)
            blend_close(0, 1, 1)
            first_minimum(0, 0)
            first_minimum(0, 1)
            x_scale_out(2)
            x_scale_out(3)
            score_out(1, 0)
            c_spread(1)
            score_out(1, 1)
            score_out(1, 2)
            score_out(1, 3)
            c_out(1)
            blend(1, 0, 0)
            blend(1, 1, 0)
            logit_out(0, 0, 1, True)
            logit_out(0, 1, 1, True)
            x_quantize(2)
            wv_quantize()
            x_quantize(3)
            rnd_scale_by_gpsimd(3, 0)
            rnd_scale_by_gpsimd(3, 1)

            exponent(0, 0)
            exponent(0, 1)
            gain(0)
            score_turned(2, 2)
            score_turned(2, 3)
            v_product(0)
            v_product(1)
            x_widen(4)
            x_widen(5)
            logit_out(1, 0, 0)
            logit_out(1, 1, 0)
            blend(1, 0, 1)
            blend(1, 1, 1)
            v_gain(0)
            v_product(2)
            v_gain(1)
            v_product(3)
            score_out(2, 3)
            score_out(2, 2)
            logit_out(1, 0, 1, True)
            x_turn(4)
            logit_out(1, 1, 1, True)
            blend(2, 0, 1)
            rnd_scale(2, 1)
            x_widen(6)
            x_widen(7)
            v_gain(2)
            blend(2, 1, 1)
            v_gain(3)
            score(2, 0)
            x_scale_out(4)
            score(2, 1)
            score_turned(3, 2)
            score_turned(3, 3)

            for s in range(1, LAST_FULL_STEP + 1):
                step(s)

            s = LAST_FULL_STEP + 1
            exponent(s, 1)
            exponent(s, 0)
            p_quantize(s - LAG)
            invert(s - 1)
            quantize_words(s, slice(X_WORDS.start, WORDS))
            divide(s - 1, 0)
            divide_by_scalar(s - 1, 1)
            gain(s)
            product(s - 3, 0)
            product(s - 3, 1)
            mix_out_of_psum(s + 1, 1)
            v_product(2 * s + 2)
            mix_out_of_psum(s + 1, 0)
            v_product(2 * s + 3)
            logit_out(s + 1, 1)
            v_product(2 * s + 4)
            logit_out(s + 1, 0)
            v_product(2 * s + 5)
            store(s - 3, 1)
            store(s - 3, 0)
            turn_out(s - 2, 0)
            turn_out(s - 2, 1)
            maximum(s + 1, SECOND)
            v_gain(2 * s + 3)
            score_turned(s + 3, 2)
            score_turned(s + 3, 3)
            blend(s + 2, 0, 1)
            v_gain(2 * s + 2)
            turn(s - 1, 1)
            blend(s + 2, 1, 1)
            turn(s - 1, 0)
            v_gain(2 * s + 5)
            score(s + 2, 0)
            v_gain(2 * s + 4)
            score(s + 2, 1)
            maximum(s + 1, FIRST)
            score_out(s + 3, 3)
            score_out(s + 3, 2)

            s += 1
            exponent(s, 1)
            exponent(s, 0)
            v_quantize(s)
            v_quantize(s + 1)
            invert(s - 1)
            p_quantize(s - LAG)
            divide(s - 1, 0, slice(0, BANK))
            divide_by_scalar(s - 1, 1)
            divide_by_scalar(s - 1, 0, slice(BANK, S))
            gain(s)
            product(s - 3, 0)
            product(s - 3, 1)
            mix_out_of_psum(s + 1, 1)
            v_product(2 * s + 4)
            mix_out_of_psum(s + 1, 0)
            v_product(2 * s + 5)
            logit_out(s + 1, 1)
            turn_out(s - 2, 0)
            turn_out(s - 2, 1)
            logit_out(s + 1, 0)
            blend(s + 2, 0, 1)
            turn(s - 1, 1)
            blend(s + 2, 1, 1)
            turn(s - 1, 0)
            v_gain(2 * s + 5)
            score(s + 2, 0)
            maximum(s + 1)
            v_gain(2 * s + 4)
            score(s + 2, 1)
            store(s - 3, 1)
            turn_out(s - 1, 1)
            turn_out(s - 1, 0)
            store(s - 3, 0, by_vector)

            s += 1
            exponent(s, 1)
            exponent(s, 0)
            p_quantize(s - LAG)
            v_quantize(s + 1)
            invert(s - 1)
            p_quantize(s - 2)
            divide(s - 1, 0)
            divide_by_scalar(s - 1, 1)
            gain(s, FIRST)
            product(s - 3, 0)
            logit_out(s + 1, 1)
            product(s - 2, 0, "vector")
            logit_out(s + 1, 0)
            mix_out_of_psum(s + 1, 1)
            mix_out_of_psum(s + 1, 0)
            turn(s - 1, 0)
            turn(s - 1, 1)
            product(s - 3, 1)
            invert(s)
            store(s - 3, 0)
            turn_out(s - 1, 0)
            turn_out(s - 1, 1)
            store(s - 2, 0, by_vector)
            product(s - 2, 1)
            maximum(s + 1)
            store(s - 3, 1)
            p_quantize(s - 1)
            divide(s, 0, slice(0, S), nc.vector)
            product(s - 1, 0, "vector")

            s += 1
            exponent(s, 0)
            exponent(s, 1)
            divide_and_gain(s - 1, 1, 0)
            invert(s, FIRST)
            divide_and_gain(s - 1, 1, 1)
            turn(s - 1, 0)
            product(s - 2, 1, "vector")
            turn(s - 1, 1, BOTH, "vector")
            turn_out(s - 1, 0)
            store(s - 3, 1)
            turn_out(s - 1, 1)
            divide_and_gain(s, 0, 0)
            invert(s, SECOND)
            divide_and_gain(s, 0, 1)
            p_quantize(s - 1, FIRST)
            turn(s, 0)
            product(s - 1, 0)
            divide_and_gain(s, 1, 0)
            p_quantize(s - 1, SECOND)
            divide_and_gain(s, 1, 1)
            turn(s, 1, FIRST)
            product(s - 1, 1, "vector")
            turn_out(s, 0)
            turn(s, 1, SECOND)
            store(s - 2, 1)
            turn_out(s, 1, FIRST)
            p_quantize(s, FIRST)
            product(s, 0)
            store(s - 2, 0, by_vector)
            store(s - 1, 0)
            turn_out(s, 1, SECOND)
            quantize_half(s, 1, 0)
            store(s - 1, 1, by_vector)
            quantize_half(s, 1, 1)
            store(s, 0)
            last_product(0)
            last_product(1)
            last_store(1, by_scalar)
            last_store(0, by_vector)
